import numpy as np, ml_dtypes
CORES = [5,29,101,125,133,157,229,253]
N = 8
BF = ml_dtypes.bfloat16
D, L, H, S1, S2, VI = 1760, 128, 64, 4, 1, 4
def effects(rng):
    cap = rng.integers(1, 256, (N, 8, 1, D))
    return np.minimum((rng.random((N, 8, 16, D)) * (cap + 1)).astype(np.int64), cap)
def near(rng, n, share, few=64):
    pop = rng.integers(0, D, (N, 8, few)); v = rng.integers(0, D, (N, 8, 16, n))
    c = np.take_along_axis(pop, rng.integers(0, few, (N, 8, 16 * n)), 2).reshape(N, 8, 16, n)
    return np.where(rng.random(v.shape) < share, c, v)
def rows(rng, n):
    return np.argsort(np.argsort(rng.random((N, 8, 16, L)), axis=2), axis=2) < n
def forest(rng, filled, own, deep):
    o = np.argsort(np.where(filled, rng.random(filled.shape), 2.0), axis=2); r = np.arange(16)[:, None]
    u = rng.random(filled.shape); b = np.minimum((rng.random(filled.shape) * (r + 1)).astype(np.int64), r)
    b = np.where(u < own, r, np.where(u > 1 - deep, np.maximum(r - 1, 0), b))
    w = np.zeros(filled.shape, np.int64); np.put_along_axis(w, o, np.take_along_axis(o, b, 2), 2)
    return np.where(filled, w, 0)
def pack(eff, rem, lim, drugs, why, filled):
    return {"eff": np.ascontiguousarray(eff.reshape(N, 128, D)).astype(np.float32).astype(BF), "rem": np.ascontiguousarray(rem.reshape(N, 128, D)).astype(np.int32),
            "lim": np.repeat(lim, 16, axis=1)[:, :, None].astype(np.int32), "drugs": np.ascontiguousarray(np.where(filled, drugs, D).reshape(N, 128, L)).astype(np.int32),
            "why": np.ascontiguousarray(np.where(filled, why, 0).reshape(N, 128, L)).astype(np.int32)}
def setup_inputs(rng):
    n = np.maximum(rng.integers(0, 17, (N, 8, 1, L)), rng.integers(0, 17, (N, 8, 1, L)))
    filled = rows(rng, n); why = forest(rng, filled, 0.3, 0.3)
    return pack(effects(rng), near(rng, D, 0.3), rng.integers(6000, 20000, (N, 8)), near(rng, L, 0.3), why, filled)
def setup_inputs_ties(rng):
    v = rng.integers(0, 256, (N, 8, 16)); v[:, :, 0] = 255
    sh = rng.integers(0, 16, (N, 8, 1, D)); sh[:, ::2, :, 1::2] = sh[:, ::2, :, ::2] + 8
    ix = (np.arange(16)[:, None] + sh) % 16
    eff = np.take_along_axis(v, ix.reshape(N, 8, 16 * D), 2).reshape(N, 8, 16, D)
    lim = np.minimum(rng.integers(3, 12, (N, 8)) * np.add.reduce(v, axis=2), 65280)
    filled = rows(rng, rng.integers(1, 17, (N, 8, 1, L))); drugs = near(rng, L, 0.9, 6)
    pair = rng.random((N, 8, 1, L)) < 0.5; pair[:, 1::2] = False
    twin = np.repeat(drugs[:, :, ::2], 2, axis=2); twin[:, :, 1::2] = twin[:, :, 1::2] ^ 1
    drugs = np.where(pair, twin, drugs); filled = np.where(pair, np.repeat(filled[:, :, ::2], 2, axis=2), filled)
    why = forest(rng, filled, 0.4, 0.2)
    return pack(eff, near(rng, D, 0.7, 6), lim, drugs, why, filled)
def setup_inputs_corners(rng):
    eff = effects(rng); eff[..., 0] = 0; eff[..., D - 1] = 255
    lim = rng.choice(np.array([1, 12000, 65280]), (N, 8)); lim[:, 1] = 1; lim[:, 2] = 65280
    kind = rng.integers(0, 10, (N, 8, 1, L)); m = np.arange(16)[:, None]; hv = rng.random((N, 8, 1, L)) < 0.5
    filled = rows(rng, np.where(kind == 6, 15, rng.integers(0, 17, (N, 8, 1, L))))
    filled = filled | (kind == 1) | (kind == 2) | (kind == 5) | (kind == 8) | (kind == 9)
    filled = np.where(kind == 0, False, np.where(kind == 3, m == 15, np.where(kind == 4, m == 0, filled)))
    why = forest(rng, filled, 0.2, 0.2)
    for k, w in ((1, np.maximum(m - 1, 0)), (2, m), (5, 0 * m), (8, np.minimum(m + 1, 15)), (9, 0 * m + 15)):
        why = np.where(kind == k, w, why)
    drugs = near(rng, L, 0.3)
    low = (kind == 1) | (kind == 5); high = (kind == 8) | (kind == 9)
    top = (low & (m == np.where(hv, 0, 15))) | (high & (m == np.where(hv, 15, 0)))
    drugs = np.where(top | (kind == 3), D - 1, np.where(kind == 4, 0, drugs))
    return pack(eff, near(rng, D, 0.3), lim, drugs, why, filled)
def setup_inputs_great(rng):
    low = np.array([11, 0, 1, 0, 11, 0, 0, 11]).reshape(8, 1, 1); lane = np.arange(L)
    eff = effects(rng); rem = near(rng, D, 0.3); drugs = near(rng, L, 0.3); lim = rng.integers(6000, 20000, (N, 8))
    filled = rows(rng, rng.integers(low, 16, (N, 8, 1, L)))
    for g in (1, 6):
        eff[:, g] = rng.integers(0, 16, (N, 16, D)) < np.array([0, 1, 2, 4, 6, 8, 12, 16])[np.arange(D) % 8]
        lim[:, g] = 1
        h = np.maximum(rng.integers(-4, 8, (N, 1, L)), 0); pure = rng.random((N, 1, L)) < 0.6
        drugs[:, g] = np.where(pure, drugs[:, g] // 8 * 8 + h, drugs[:, g])
        filled[:, g] = filled[:, g] | (pure & (h == 0))
        faint = rng.random((N, 1, D)) < 0.3
        rem[:, g] = np.where(faint, rem[:, g] // 8 * 8 + rng.integers(0, 2, (N, 16, D)), rem[:, g])
    eff[:, 2] = rng.integers(0, 101, (N, 16, D)); lim[:, 2] = 1
    for q in range(N):
        o = rng.permutation(D); i = rng.integers(0, 16, L)
        eff[q, 2][:, o[:L]] = rng.integers(128, 256, (16, L))
        v = rng.choice(o[L:], (16, L)); v[i, lane] = o[:L]; drugs[q, 2] = v
        filled[q, 2][i, lane] = True
    for g in (0, 4, 7):
        eff[:, g] = rng.integers(0, 32, (N, 16, D)) + rng.integers(192, 225, (N, 1, 1))
        if g == 7:
            eff[:, g, :, 7::8] = 255
            drugs[:, g, :, L - 1] = drugs[:, g, :, L - 1] // 8 * 8 + 7
            filled[:, g, :, L - 1] = np.arange(16)[None, :] != rng.integers(0, 16, (N, 1))
        e = np.add.reduce(eff[:, g], axis=1)
        b = np.add.reduce(np.where(filled[:, g], np.take_along_axis(e, drugs[:, g].reshape(N, 16 * L), 1).reshape(N, 16, L), 0), axis=1)
        i = np.argmax(rng.random((N, L)) * (b % 128 > 0), axis=1); v = b[np.arange(N), i]
        lim[:, g] = v + (v % 256 > 128)
    lim[N - 1, 7] = 61200
    filled[0] = True; filled[2] = True
    o = rng.permutation(8 * L)[:int(rng.integers(100, 201))]
    for j in o: filled[2, j // L, :, j % L] = False
    return pack(eff, rem, lim, drugs, forest(rng, filled, 0.3, 0.3), filled)
def setup_inputs_spread(rng):
    cap = np.exp2(8 * rng.random((N, 8, 1, D))).astype(np.int64); cap = np.minimum(cap, 255)
    eff = np.minimum((rng.random((N, 8, 16, D)) * (cap + 1)).astype(np.int64), cap)
    e = rng.choice(np.array([1.0, 3.0, 8.0]), (N, 8, 1, 1))
    rem = np.minimum((D * rng.random((N, 8, 16, D)) ** 3).astype(np.int64), D - 1); drugs = np.minimum((D * rng.random((N, 8, 16, L)) ** e).astype(np.int64), D - 1)
    lim = np.minimum(np.maximum(np.exp2(16 * rng.random((N, 8))).astype(np.int64), 1), 65280); lim[:, 5] = rng.integers(3000, 9000, N)
    filled = rows(rng, rng.integers(0, 17, (N, 8, 1, L))); why = forest(rng, filled, rng.random((N, 8, 1, L)), 0.3)
    return pack(eff, rem, lim, drugs, why, filled)
def setup_inputs_ends(rng):
    eff = 255 * (rng.random((N, 8, 16, D)) < rng.choice(np.array([0.0, 0.5, 1.0]), (N, 8, 1, D))).astype(np.int64)
    case = rng.integers(0, 4, (N, 8)); case[0, 0] = 1; case[N - 1, 7] = 0; case[:, 4] = 2
    a = np.where((case == 0) | (case == 3), 255, np.where(case == 1, 0, -1))[:, :, None]; b = np.where(case == 0, 255, np.where((case == 1) | (case == 3), 0, -1))[:, :, None]
    eff[..., 0] = np.where(a >= 0, a, eff[..., 0]); eff[..., D - 1] = np.where(b >= 0, b, eff[..., D - 1])
    rem = (D - 1) * rng.integers(0, 2, (N, 8, 16, D))
    lim = np.where(rng.random((N, 8)) < 0.5, 1, 65280); lim[:, 0] = 1; lim[:, 7] = 65280
    filled = rng.random((N, 8, 16, L)) < 0.65; filled[:, :, 0] = True; filled[:, :, 15] = True
    none = rng.random((N, 8, 1, L)) < 0.05; full = rng.random((N, 8, 1, L)) < 0.1; full[..., 1] = True; full[..., L - 1] = True
    filled = full | (filled & ~none)
    drugs = np.where(rng.random((N, 8, 16, L)) < 0.7, 0, D - 1); drugs[..., 1] = 0; drugs[..., L - 1] = D - 1
    why = 15 * rng.integers(0, 2, (N, 8, 16, L)); z = rng.integers(0, 2, (N, 8, L))
    why[:, :, 0] = 15 * z; why[:, :, 15] = np.where(z == 1, 15, why[:, :, 15])
    return pack(eff, rem, lim, drugs, why, filled)
def check_inputs(d):
    bad = []
    for k, lo, hi in (("eff", 0, 255), ("rem", 0, D - 1), ("lim", 1, 65280), ("drugs", 0, D), ("why", 0, 15)):
        v = np.asarray(d[k]).astype(np.float64)
        if not (np.min(v) >= lo and np.max(v) <= hi): bad.append("range of " + k)
        elif k == "eff" and np.any(v != np.floor(v)): bad.append("whole numbers in eff")
    v = np.asarray(d["lim"]).reshape(N, 8, 16)
    if np.any(v != v[:, :, :1]): bad.append("lim alike in a group")
    if "range of drugs" in bad or "range of why" in bad: return bad
    filled = np.asarray(d["drugs"]).reshape(N, 8, 16, L) < D; w = np.asarray(d["why"]).astype(np.int64).reshape(N, 8, 16, L)
    if np.any(~filled & (w != 0)): bad.append("why is 0 in empty rows")
    if np.any(filled & ~np.take_along_axis(filled, w, 2)): bad.append("reasons are filled rows")
    c = w
    for _ in range(4): c = np.take_along_axis(c, c, 2)
    if np.any(filled & (np.take_along_axis(w, c, 2) != c)): bad.append("reasons end in a row that is its own reason")
    return bad
def stand(A, a, t):
    return np.concatenate([A[(a - S1 * t) % N][..., :H], A[(a - S2 * t) % N][..., H:]], axis=2)
def reference(eff, rem, lim, drugs, why):
    X = eff.astype(np.float32).astype(np.int32).reshape(N, 8, 16, D)
    X = np.concatenate([X, np.zeros((N, 8, 16, 1), np.int32)], axis=3)
    R = rem.astype(np.int64).reshape(N, 8, 16, D); B = lim.astype(np.int64).reshape(N, 8, 16)[:, :, :1]
    P = drugs.astype(np.int64).reshape(N, 8, 16, L); Q = why.astype(np.int64).reshape(N, 8, 16, L)
    m16 = np.arange(16)[None, :, None]; c = np.zeros(N, np.int64)
    for t in range(VI):
        NP = np.zeros_like(P); NQ = np.zeros_like(Q); stops = np.zeros(N, np.int64)
        for a in range(N):
            p = stand(P, a, t); w = stand(Q, a, t); filled = p < D
            x = np.take_along_axis(X[a], p.reshape(8, 1, 16 * L), 2).reshape(8, 16, 16, L)
            T = np.add.reduce(x, axis=2); burden = np.add.reduce(T, axis=1)
            stop = np.any(filled, axis=1) & ((burden >= B[a] + c[a]) | np.all(filled, axis=1))
            s = np.argmax(np.where(filled, np.add.reduce(x, axis=1), -1), axis=1)[:, None, :]
            cur = np.broadcast_to(m16, p.shape); reach = np.zeros(p.shape, bool)
            for _ in range(16):
                reach = reach | (cur == s); cur = np.take_along_axis(w, cur, 1)
            gone = reach & filled & stop[:, None, :]
            d = np.take_along_axis(p, s, 1)[:, 0]; xs = np.take_along_axis(x, s[:, None], 2)[:, :, 0]; xn = (xs + (T >> 4)) >> 1
            p = np.where(gone, D, p); w = np.where(gone, 0, w); filled = p < D; some = np.any(filled, axis=1)
            U = np.add.reduce(np.where(filled[:, None], x, 0), axis=2)
            f = np.argmax(U, axis=1)
            k = np.argmax(np.where(filled, np.take_along_axis(x, f[:, None, None, :], 1)[:, 0], -1), axis=1)
            dk = np.minimum(np.take_along_axis(p, k[:, None, :], 1), D - 1)
            cand = np.take_along_axis(R[a], dk, 2)
            xc = np.take_along_axis(X[a], cand.reshape(8, 1, 16 * L), 2).reshape(8, 16, 16, L)
            score = np.add.reduce(np.abs(255 - xc - (U >> 4)[:, :, None, :]), axis=1)
            new = np.take_along_axis(cand, np.argmin(score, axis=1)[:, None, :], 1)
            put = (m16 == np.argmin(filled, axis=1)[:, None, :]) & some[:, None, :]
            p = np.where(put, new, p); w = np.where(put, k[:, None, :], w)
            for A, v in ((NP, p), (NQ, w)):
                A[(a - S1 * t) % N, :, :, :H] = v[..., :H]; A[(a - S2 * t) % N, :, :, H:] = v[..., H:]
            for g in range(8):
                lanes = np.flatnonzero(stop[g]); u, i = np.unique(d[g, lanes], return_index=True)
                X[a, g][:, u] = xn[g][:, lanes[i]]
            stops[a] = np.count_nonzero(stop)
        P, Q, c = NP, NQ, stops & 255
    yp = np.stack([stand(P, a, VI - 1) for a in range(N)]); yq = np.stack([stand(Q, a, VI - 1) for a in range(N)])
    return {"yp": yp.reshape(N, 128, L).astype(np.float32), "yq": yq.reshape(N, 128, L).astype(np.float32),
            "yx": np.ascontiguousarray(X[..., :D]).reshape(N, 128, D).astype(np.float32).astype(BF)}

@@ -1,0 +1,605 @@
+import numpy as np
+from concourse.bass import DstId, RemoteDMATransfer, IndirectOffsetOnAxis
+from concourse.mybir import dt, AluOpType, AxisListType, ActivationFunctionType
+
+A = AluOpType
+F = ActivationFunctionType
+NR, VI, H, L, D = 8, 4, 64, 128, 1760
+STRIDE = (4, 1)
+XW = 16 + D + 128
+f32, b16, h16, i32, u16 = "float32", "bfloat16", "float16", "int32", "uint16"
+SB = {
+    "X": (XW, b16), "R": (16 + D, i32), "dr0": (L, i32), "wy0": (L, i32), "lmI": (1, i32),
+    "kI": (1, i32), "aI": (1, i32), "gI": (1, i32), "kc": (1, f32), "ac": (1, f32), "gc": (1, f32),
+    "cid": (128, f32), "mro": (128, f32), "g8": (8, f32), "j16": (16, f32),
+    "I32": (128, f32), "I16": (128, h16), "Ib": (128, b16), "I16b": (128, b16), "Im16": (128, h16),
+    "bo": (128, b16), "bo32": (128, f32), "bo256": (128, b16),
+    "bo8": (8, b16), "bo8h": (8, h16), "wm16": (8, b16), "w32": (8, b16), "bo8a": (8, b16), "bo8b": (8, b16),
+    "on": (128, b16), "on32": (128, f32), "on16": (128, h16), "tie16": (128, b16), "tief": (128, f32),
+    "m15": (16, f32), "m16": (16, h16), "cm": (128, b16), "d0m": (128, f32), "d0s": (128, f32), "d0p": (128, f32), "d0b": (2048, b16),
+    "pw2": (16, f32), "one16": (16, f32), "pwo": (16, f32), "m64": (1, f32), "dum": (1, f32),
+    "bit": (128, f32), "tri": (512, b16), "limb": (8, f32), "limf": (1, f32), "lim8": (8, f32),
+    "pofI": (128, i32), "pof16": (128, h16),
+    "IF": (1024, b16), "IG": (1024, b16), "PA": (2048, b16), "PB": (2048, b16), "CA": (2048, b16), "CB": (2048, b16),
+    "LW": (2048, b16), "lf": (128, f32), "lu1": (128, u16), "lu2": (128, u16), "lu4": (128, u16), "lu8": (128, u16),
+    "qf0": (128, f32), "fil": (128, f32), "aP0": (128, f32), "w0": (128, f32),
+    "x": (2048, b16), "x2": (2048, b16), "xc": (2048, b16), "mn": (2048, b16), "vf": (2048, b16), "bs": (2048, h16),
+    "eR": (128, b16), "e2": (128, b16), "q16": (128, h16), "aa": (128, i32), "aF": (128, f32), "aM": (128, f32),
+    "n0": (8, f32), "n1": (8, f32), "n2": (8, f32), "thr": (8, f32), "mx": (128, f32), "sm": (128, f32), "stp": (8, f32),
+    "oh": (128, f32), "pw": (128, f32), "pr": (128, i32), "bb": (128, i32), "q2P": (128, h16), "q2u": (128, u16), "q2h": (128, h16),
+    "fR": (128, b16), "vv": (128, f32), "lo": (128, h16), "u1": (128, h16), "eP": (128, f32), "eQ": (128, f32),
+    "mk": (128, f32), "zi": (8, i32), "r16": (8, f32), "ok": (128, h16), "pk": (128, f32), "sk": (128, f32), "AL": (128, h16), "lk": (8, u16),
+    "cd": (128, u16), "cd16": (128, h16), "oka": (128, f32), "t3": (128, f32), "xk": (128, f32), "ky": (128, f32),
+    "ms": (128, f32), "oj": (128, f32), "pn": (128, f32), "sn": (128, f32), "AN": (128, h16),
+    "on1": (128, f32), "pq": (128, f32), "sq": (128, f32), "dg": (1024, h16), "eq": (1024, b16), "du": (8, f32), "uu": (8, f32), "ut": (8, f32), "of": (8, f32), "AS": (128, h16), "ls": (8, u16),
+    "ti": (128, i32), "xs": (128, f32), "xn": (128, i32), "cn": (1, f32), "ci": (1, i32), "cj": (1, i32), "c16": (1, f32),
+    "yt": (128, f32), "yo": (128, f32), "vI": (128, i32), "yw": (128, f32),
+}
+ALONE = ("X", "R", "dr0", "wy0", "lmI", "yt", "yw", "IF", "IG")
+ALIAS, SCRATCH, _wide = {}, {}, {}
+for _k, (_w, _d) in SB.items():
+    if _w > 1024 or _k in ALONE:
+        SCRATCH[_k] = ("sbuf", [128, _w], _d)
+    else:
+        ALIAS[_k] = ("p_" + _d, _wide.get(_d, 0))
+        _wide[_d] = _wide.get(_d, 0) + -(-_w // 16) * 16
+for _d, _w in _wide.items():
+    SCRATCH["p_" + _d] = ("sbuf", [128, _w], _d)
+for _t in range(VI):
+    SCRATCH["q%d" % _t] = ("sbuf", [128, L], u16)
+    SCRATCH["v%d" % _t] = ("sbuf", [128, L], i32)
+for _t in range(1, VI):
+    SCRATCH["qo%d" % _t] = ("sbuf", [128, L], u16)
+    SCRATCH["vo%d" % _t] = ("sbuf", [128, L], i32)
+    SCRATCH["rq%d" % _t] = ("sbuf", [128, H], u16)
+    SCRATCH["rv%d" % _t] = ("sbuf", [128, H], i32)
+PS = ("pW", "pT", "pU", "pS", "pQ", "pA", "pL", "pD")
+for _p in PS:
+    SCRATCH[_p] = ("psum", [128, 512], f32)
+SEMAPHORES = ["ev", "es", "et", "eg", "loc"] + ["ld%d" % _t for _t in range(5)] + ["st%d" % _t for _t in range(3)]
+for _t in range(1, VI):
+    SEMAPHORES += ["%s%d" % (_n, _t) for _n in ("qL", "qH", "vL", "vH", "rq", "rv")]
+HV = ((0, 64), (64, 128))
+
+
+def relay_of(core, dst, topo):
+    c = [k for k in topo.cores_of(core) if k != core and topo.may_write(k, dst)]
+    return ([k for k in c if topo.die(k) == topo.die(core)] + c)[0]
+
+
+def bits(topo, src, dst, n, top):
+    e = topo.engines(src, dst)
+    e = e[len(e) - n:] if top else e[:n]
+    return sum(1 << k for k in e)
+
+
+def rank_program(g, core, T, topo):
+    rank = T.rank_of(core)
+    if rank is None:
+        for r, c in enumerate(T.cores):
+            dst = T.cores[(r + STRIDE[1]) % NR]
+            if relay_of(c, dst, topo) == core:
+                relay(g, core, dst, T, topo)
+        return
+    member(g, core, rank, T, topo)
+
+
+def relay(g, core, dst, T, topo):
+    rid, pid = topo.addr(dst, core)
+    m = bits(topo, core, dst, 8, False)
+    n = 0
+    for t in range(1, VI):
+        for k in ("q", "v"):
+            g.wait_ge(T.sem["r%s%d" % (k, t)], 8)
+            g.remote_dma(T["%s%d" % (k, t)][:, H:L], T["r%s%d" % (k, t)][:, :], T.sem["%sH%d" % (k, t)], T.sem["loc"], pid, rid, m)
+            n += 8
+    g.wait_ge(T.sem["loc"], n)
+
+
+def member(g, core, rank, T, topo):
+    Q = {"v": g.vector, "s": g.scalar, "t": g.tensor, "g": g, "y": g.sync}
+    ES = {"v": "ev", "s": "es", "t": "et", "g": "eg"}
+    cnt = {}
+    known = {q: {} for q in Q}
+    snap = {}
+    recs = {}
+    psum = set(PS)
+
+    def vw(name, lo=0, hi=None, st=1, r0=0, r1=128):
+        if hi is None:
+            hi = SB[name][0] if name in SB else SCRATCH[name][1][1]
+        if name in ALIAS:
+            name, o = ALIAS[name]
+            lo, hi = lo + o, hi + o
+        ap = T[name][r0:r1, lo:hi:st] if st > 1 else T[name][r0:r1, lo:hi]
+        return {"ap": ap, "n": name, "lo": lo, "hi": hi, "st": st, "x": None}
+
+    def ind(w, o):
+        return {"ap": w["ap"].indirect(o["ap"]), "n": w["n"], "lo": w["lo"], "hi": w["hi"], "st": 1, "x": o}
+
+    def clash(a, b):
+        if a["n"] in psum:
+            return True
+        if a["lo"] >= b["hi"] or b["lo"] >= a["hi"]:
+            return False
+        return not (a["st"] > 1 and a["st"] == b["st"] and (a["lo"] - b["lo"]) % a["st"])
+
+    def need(q, tok):
+        s, n = tok
+        if known[q].get(s, 0) >= n:
+            return
+        Q[q].wait_ge(T.sem[s], n)
+        known[q][s] = n
+        for k, m in snap.get(tok, {}).items():
+            if known[q].get(k, 0) < m:
+                known[q][k] = m
+
+    def expand(vs):
+        r = []
+        for a in vs:
+            if isinstance(a, dict):
+                r.append(a)
+                if a["x"]:
+                    r.append(a["x"])
+        return r
+
+    def deps(q, outs, ins):
+        best = {}
+        for a, wr in [(a, True) for a in outs] + [(a, False) for a in ins]:
+            for b, bw, tok, bq in recs.get(a["n"], []):
+                if not clash(a, b):
+                    continue
+                if a["n"] in psum:
+                    over = not (a["lo"] >= b["hi"] or b["lo"] >= a["hi"])
+                    if bq == q and (q == "t" or not (over and bw and not wr)):
+                        continue
+                else:
+                    if not wr and not bw:
+                        continue
+                    if bq == q and q != "y" and not bw:
+                        continue
+                best[tok[0]] = max(best.get(tok[0], 0), tok[1])
+        for s in sorted(best):
+            need(q, (s, best[s]))
+
+    def note(q, tok, outs, ins):
+        for a, wr in [(a, True) for a in outs] + [(a, False) for a in ins]:
+            l = recs.setdefault(a["n"], [])
+            if wr and a["st"] == 1 and a["n"] not in psum:
+                l[:] = [b for b in l if not (a["lo"] <= b[0]["lo"] and b[0]["hi"] <= a["hi"])]
+            elif a["n"] in psum or not wr:
+                l[:] = [b for b in l if not (b[3] == q and b[1] == wr and b[0]["lo"] == a["lo"] and b[0]["hi"] == a["hi"] and b[0]["st"] == a["st"])]
+            l.append((a, wr, tok, q))
+
+    def op(q, outs, ins, fn, sem=None, inc=1):
+        ins = expand(ins + [a["x"] for a in outs])
+        deps(q, outs, ins)
+        s = sem or ES[q]
+        fn().then_inc(T.sem[s], inc)
+        cnt[s] = cnt.get(s, 0) + inc
+        tok = (s, cnt[s])
+        snap[tok] = dict(known[q])
+        note(q, tok, outs, ins)
+
+    def P(a):
+        return a["ap"] if isinstance(a, dict) else a
+
+    def copy(o, i):
+        op("v", [o], [i], lambda: g.vector.tensor_copy(P(o), P(i)))
+
+    def tt(o, a, b, f):
+        op("v", [o], [a, b], lambda: g.vector.tensor_tensor(P(o), P(a), P(b), f))
+
+    def ts(o, a, s1, f1, s2=None, f2=None):
+        if s2 is None:
+            op("v", [o], [a, s1], lambda: g.vector.tensor_scalar(P(o), P(a), P(s1), None, f1))
+        else:
+            op("v", [o], [a, s1, s2], lambda: g.vector.tensor_scalar(P(o), P(a), P(s1), P(s2), f1, f2))
+
+    def scan(o, d0, d1, f0, f1, init=0.0):
+        op("v", [o], [d0, d1], lambda: g.vector.tensor_tensor_scan(P(o), P(d0), P(d1), init, f0, f1))
+
+    def fill(o, c):
+        op("v", [o], [], lambda: g.vector.memset(P(o), c))
+
+    def act(o, i, scale=1.0, bias=0.0, func=F.Identity):
+        op("s", [o], [i, scale], lambda: g.scalar.activation(P(o), P(i), func, bias=bias, scale=P(scale)))
+
+    def mm(o, a, b, start=True, stop=True):
+        op("t", [o], [a, b], lambda: g.tensor.matmul(P(o), P(a), P(b), start, stop))
+
+    def load(o, src, sem, q="y"):
+        op(q, [o], [], lambda: Q[q].dma_start(P(o), src), sem, 16)
+
+    def store(dst, i, sem, q="y"):
+        op(q, [], [i], lambda: Q[q].dma_start(dst, P(i)), sem, 16)
+
+    def iota(o, pat, base, cm, fl=True):
+        op("g", [o], [], lambda: g.iota(P(o), pat, base, cm, allow_small_or_imprecise_dtypes=True) if fl else g.iota(P(o), pat, base, cm))
+
+    def gfill(o, n, c, fl=True):
+        iota(o, [[0, n]], c, 0, fl)
+
+    def sel(o, pat, f, c, base, cm):
+        op("g", [o], [o], lambda: g.affine_select(P(o), P(o), pat, f, c, base, cm))
+
+    def half(name, h):
+        return vw(name, 1024 * h, 1024 * h + 1024)
+
+    load(vw("wy0"), T.why[:, :], "ld0")
+    load(vw("dr0"), T.drugs[:, :], "ld1", "s")
+    load(vw("X", 16, 16 + D), T.eff[:, :], "ld2")
+    load(vw("lmI"), T.lim[:, :], "ld3", "s")
+    load(vw("R", 16, 16 + D), T.rem[:, :], "ld4")
+    iota(vw("kI"), [[1, 1]], 0, 1, False)
+    iota(vw("mro"), [[0, 8], [1, 16]], 0, 0)
+    iota(vw("pofI"), [[0, 2], [16, 64]], 0, 0, False)
+    iota(vw("g8"), [[1, 8]], 0, 0)
+    iota(vw("cid"), [[1, 128]], 0, 0)
+    iota(vw("j16"), [[1, 16]], 0, 0)
+    fill(vw("LW"), 0.0)
+    ts(vw("aI"), vw("kI"), 15, A.bitwise_and)
+    copy(vw("ac"), vw("aI"))
+    ts(vw("IF", 0, 128), vw("mro"), vw("ac"), A.is_equal)
+    for h in (128, 256, 512):
+        copy(vw("IF", h, 2 * h), vw("IF", 0, h))
+    act(vw("IG"), vw("IF"))
+    ts(vw("gI"), vw("kI"), 4, A.arith_shift_right)
+    copy(vw("gc"), vw("gI"))
+    copy(vw("kc"), vw("kI"))
+    ts(vw("bo8"), vw("g8"), vw("gc"), A.is_equal)
+    ts(vw("bo8a"), vw("bo8"), vw("ac"), A.mult)
+    tt(vw("lf"), vw("wy0"), vw("pofI"), A.add)
+    copy(vw("lu1"), vw("lf"))
+
+    def win(name, h):
+        return vw("IF") if name == "IF" else half(name, h)
+
+    def pgath(q, dst, src, lst, h):
+        o, w, f = half(dst, h), win(src, h), vw(lst, *HV[h])
+        if q == "s":
+            act(o, ind(w, f))
+        else:
+            copy(o, ind(w, f))
+
+    def cgath(dst, src, lst, h, by=None):
+        o, w, f = half(dst, h), win(src, h), vw(lst, *HV[h])
+        d = vw("IG") if src == "IF" else half("xc", h)
+        if by == "s":
+            act(d, w)
+        elif by == "v":
+            copy(d, w)
+        tt(o, ind(w, f), d, A.max)
+
+    def xgath(q, dst, lst, c0, c1, conv=False, lo=0):
+        o, w, f = vw(dst, 16 * c0, 16 * c1), vw("X", lo, 16 + D), vw(lst, c0, c1)
+        if q == "s":
+            act(o, ind(w, f), 16.0, -2048.0) if conv else act(o, ind(w, f))
+        elif conv:
+            ts(o, ind(w, f), 16.0, A.mult, -2048.0, A.add)
+        else:
+            copy(o, ind(w, f))
+
+    def conv(src, h):
+        o = vw("pU" if h == 0 else "pS", 0, 64)
+        mm(o, vw("I16"), vw("pof16", *HV[h]), True, False)
+        for m in range(16):
+            mm(o, vw("LW", 128 * m, 128 * m + 128), vw(src, 1024 * h + m, 1024 * h + 1024, 16), False, m == 15)
+
+    def convd(lst, h):
+        copy(vw(lst, *HV[h]), vw("pU" if h == 0 else "pS", 0, 64))
+    pgath("s", "PA", "IF", "lu1", 0)
+    pgath("v", "PA", "IF", "lu1", 1)
+    for m in range(16):
+        o = vw("LW", 128 * m + m, 128 * m + 128, 16)
+        act(o, vw("bo8a")) if m % 4 else copy(o, vw("bo8a"))
+    pgath("s", "PB", "PA", "lu1", 0)
+    ts(vw("I32"), vw("cid"), vw("kc"), A.is_equal)
+    copy(vw("I16"), vw("I32"))
+    copy(vw("pof16"), vw("pofI"))
+    pgath("v", "PB", "PA", "lu1", 1)
+    conv("PB", 0)
+    conv("PB", 1)
+    gfill(vw("X", 0, 16), 16, -1)
+    gfill(vw("X", 16 + D, XW), 128, 0)
+    gfill(vw("R", 0, 16), 16, 0, False)
+    gfill(vw("d0b"), 2048, 1)
+    sel(vw("d0b"), [[0, 128], [1, 16]], A.not_equal, -8192.0, 0, 0)
+    for n, c, z in (("d0s", 1, 0.0), ("d0m", 0, -16777216.0), ("d0p", 2, 0.0)):
+        gfill(vw(n), 128, c)
+        sel(vw(n), [[0, 8], [1, 16]], A.not_equal, z, 0, 0)
+    gfill(vw("on32"), 128, 1)
+    gfill(vw("on"), 128, 1)
+    gfill(vw("bo32"), 128, 1)
+    gfill(vw("cm"), 128, 65)
+    sel(vw("cm"), [[1, 128]], A.is_gt, 1.0, 0, -1)
+    sel(vw("cm"), [[1, 128]], A.not_equal, -31.0, 0, -1)
+    for n in ("bo32", "cm"):
+        sel(vw(n), [[-16, 8], [0, 16]], A.is_ge, 0.0, 0, 1)
+        sel(vw(n), [[16, 8], [0, 16]], A.is_ge, 0.0, 15, -1)
+    gfill(vw("tri"), 512, 4096)
+    sel(vw("tri"), [[0, 4], [-1, 128]], A.is_ge, 0.0, 0, 1)
+    cgath("CA", "IF", "lu1", 0)
+    convd("lu2", 0)
+    pgath("s", "mn", "PB", "lu2", 0)
+    conv("mn", 0)
+    convd("lu2", 1)
+    cgath("CA", "IF", "lu1", 1)
+    ts(vw("fil"), vw("dr0"), D, A.is_lt)
+    ts(vw("qf0"), vw("dr0"), 16, A.add)
+    tt(vw("qf0"), vw("qf0"), vw("fil"), A.mult)
+    copy(vw("q0"), vw("qf0"))
+    pgath("s", "mn", "PB", "lu2", 1)
+    conv("mn", 1)
+    cgath("CB", "CA", "lu2", 0, "v")
+    convd("lu4", 0)
+    act(half("xc", 1), half("CA", 1))
+    pgath("s", "PB", "mn", "lu4", 0)
+    conv("PB", 0)
+    cgath("CB", "CA", "lu2", 1)
+    convd("lu4", 1)
+    pgath("s", "PB", "mn", "lu4", 1)
+    conv("PB", 1)
+    xgath("s", "x", "q0", 0, 64)
+    ts(vw("pw2"), vw("j16"), vw("ac"), A.is_lt, 1.0, A.add)
+    fill(vw("one16"), 1.0)
+    scan(vw("pwo"), vw("pw2"), vw("one16"), A.mult, A.mult, 1.0)
+    pcol = vw("pwo", 15, 16)
+    ts(vw("bo8b"), vw("bo8"), pcol, A.mult)
+    cgath("CA", "CB", "lu4", 0, "v")
+    convd("lu8", 0)
+    act(half("xc", 0), half("CA", 0))
+    cgath("CA", "CB", "lu4", 1, "v")
+    convd("lu8", 1)
+    act(half("xc", 1), half("CA", 1))
+    xgath("s", "x", "q0", 64, 128)
+    act(vw("Ib"), vw("I32"))
+    act(vw("wm16"), vw("bo8"), -16.0)
+    act(vw("w32"), vw("bo8"), 32.0)
+    act(vw("bo"), vw("bo32"))
+    act(vw("I16b"), vw("I32"), 16.0)
+    act(vw("bo256"), vw("bo32"), 256.0)
+    act(vw("tie16"), vw("mro"), -16.0, 240.0)
+    act(vw("tief"), vw("mro"), -1.0, 15.0)
+    act(vw("m15"), vw("mro", 0, 16), -1.0, 15.0)
+    act(vw("bit"), vw("on32"), pcol)
+    copy(vw("limf"), vw("lmI"))
+    ts(vw("lim8"), vw("I32", 0, 128, 16), vw("limf"), A.mult)
+    cgath("CB", "CA", "lu8", 0)
+    cgath("CB", "CA", "lu8", 1)
+
+    def late_constants():
+        fill(vw("on16"), 1.0)
+        ts(vw("Im16"), vw("I32"), -16.0, A.mult)
+        copy(vw("bo8h"), vw("bo8"))
+        copy(vw("m16"), vw("IF", 0, 16))
+        ts(vw("m64"), vw("ac"), 65536.0, A.mult)
+        ts(vw("dum"), vw("kc"), float(16 + D), A.add)
+
+    def stopped():
+        ts(vw("on1"), vw("pw"), 1.0, A.is_equal)
+        tt(vw("pq"), vw("on1"), vw("pQ", 0, 128), A.mult)
+        scan(vw("sq"), vw("d0s"), vw("pq"), A.mult, A.add)
+        for w in range(8):
+            ts(vw("dg", 128 * w, 128 * w + 128), vw("I16"), vw("sq", 16 * w + 15, 16 * w + 16), A.mult)
+
+    def spread():
+        for b, p in ((0, "pD"), (1, "pT")):
+            mm(vw(p), vw("Ib"), vw("tri"), True, False)
+            mm(vw(p), vw("on16"), vw("dg", 512 * b, 512 * b + 512), False, True)
+
+    def equal():
+        for w in range(8):
+            p = vw("pD" if w < 4 else "pT", 128 * (w % 4), 128 * (w % 4) + 128)
+            ts(vw("eq", 128 * w, 128 * w + 128), p, vw("sq", 16 * w + 15, 16 * w + 16), A.is_equal)
+
+    def dedupe():
+        ts(vw("du"), vw("pL", 272, 280), 0.5, A.is_lt)
+        tt(vw("uu"), vw("du"), vw("sq", 15, 128, 16), A.mult)
+        ts(vw("ut"), vw("uu"), 0.0, A.is_equal, vw("dum"), A.mult)
+        tt(vw("of"), vw("uu"), vw("ut"), A.add)
+        for w in range(8):
+            ts(vw("AS", 16 * w, 16 * w + 16), vw("m16"), vw("of", w, w + 1), A.mult)
+        mm(vw("pL", 264, 272), vw("AS"), vw("bo8h"))
+        copy(vw("ls"), vw("pL", 264, 272))
+
+    def update():
+        tt(vw("xs"), ind(vw("X"), vw("ls")), vw("ti"), A.add)
+        ts(vw("xn"), vw("xs"), 0.5, A.mult, -0.25, A.add)
+
+    def scatter():
+        copy(ind(vw("X"), vw("ls")), vw("xn"))
+
+    def sums():
+        for m in range(16):
+            mm(vw("pT", 0, 128), vw("Ib"), vw("x", m, 2048, 16), m == 0, False)
+        mm(vw("pT", 0, 128), vw("bo"), vw("eR"), False, True)
+
+    def tsixteenth():
+        ts(vw("ti"), vw("pT", 0, 128), 0.0625, A.mult, -0.46875, A.add)
+
+    def stops():
+        mm(vw("pT", 128, 136), vw("on32"), vw("stp"))
+        o, i = vw("cn"), vw("pT", 128, 136)
+        op("v", [o], [i], lambda: g.vector.tensor_reduce(P(o), P(i), AxisListType.X, A.add))
+        copy(vw("ci"), vw("cn"))
+        ts(vw("cj"), vw("ci"), 255, A.bitwise_and)
+        copy(vw("c16"), vw("cj"))
+
+    def rowsums(h):
+        for m in range(16):
+            mm(vw("pW", m, 128, 16, *HV[h]), vw("x", 1024 * h + m, 1024 * h + 1024, 16), vw("bo8"))
+
+    for t in range(VI):
+        q, v = "q%d" % t, "v%d" % t
+        if t:
+            for k, h in (("q", 0), ("v", 0), ("q", 1), ("v", 1)):
+                s = "%s%s%d" % (k, "LH"[h], t)
+                cnt[s] = 8
+                snap[(s, 8)] = {}
+                recs.setdefault("%s%d" % (k, t), []).append((vw("%s%d" % (k, t), *HV[h]), True, (s, 8), "remote"))
+            xgath("v", "x", q, 0, 32)
+            xgath("s", "x", q, 32, 64)
+        ts(vw("eR"), vw(q), 0, A.is_equal)
+        if t:
+            xgath("v", "x", q, 64, 96)
+            xgath("s", "x", q, 96, 128)
+        rowsums(0)
+        mm(vw("pT", 256, 264), vw("eR"), vw("bo8"))
+        rowsums(1)
+        ts(vw("q16"), vw(q), 0.0, A.add)
+        mm(vw("pQ", 0, 128), vw("q16"), vw("I16"))
+        if t:
+            ts(vw("n1"), vw("pT", 256, 264), -16.0, A.mult, vw("c16"), A.add)
+        else:
+            mm(vw("pT", 264, 272), vw("on32"), vw("lim8"))
+            copy(vw("limb"), vw("pT", 264, 272))
+            ts(vw("n1"), vw("pT", 256, 264), -16.0, A.mult)
+        ts(vw("n0"), vw("pT", 256, 264), 0.0, A.is_equal, -4194304.0, A.mult)
+        tt(vw("n2"), vw("n1"), vw("limb"), A.add)
+        tt(vw("thr"), vw("n2"), vw("n0"), A.add)
+        if t:
+            ts(vw("aa"), vw(v), 65535, A.bitwise_and)
+            copy(vw("aF"), vw("aa"))
+            mm(vw("pA", 0, 128), vw("aF"), vw("I32"))
+        else:
+            for m in range(16):
+                mm(vw("pA", m, 128, 16), vw("CB", m, 2048, 16), vw("bo8b"))
+        if t == VI - 1:
+            sums()
+        key = vw("pW", 0, 128)
+        scan(vw("sm"), vw("d0s"), key, A.mult, A.add)
+        scan(vw("mx"), vw("d0m"), key, A.add, A.max)
+        tt(vw("stp"), vw("sm", 15, 128, 16), vw("thr"), A.is_ge)
+        for w in range(8):
+            ts(vw("oh", 16 * w, 16 * w + 16), vw("mx", 16 * w, 16 * w + 16), vw("mx", 16 * w + 15, 16 * w + 16), A.is_equal, vw("stp", w, w + 1), A.mult)
+        scan(vw("pw"), vw("d0p"), vw("oh"), A.mult, A.max)
+        for w in range(8):
+            ts(vw("pr", 16 * w, 16 * w + 16), vw("pA", 16 * w, 16 * w + 16), vw("pw", 16 * w + 15, 16 * w + 16), A.mult)
+        ts(vw("bb"), vw("pr"), 32768, A.bitwise_and)
+        tt(vw("q2P"), vw("pQ", 0, 128), vw("bb"), A.subtract)
+        mm(vw("pL", 384, 512), vw("q2P"), vw("I16"))
+        copy(vw("q2u"), vw("pL", 384, 512))
+        xgath("s", "x2", "q2u", 64, 128, True)
+        ts(vw("e2"), vw("q2u"), 0, A.is_equal)
+        xgath("v", "x2", "q2u", 0, 64, True)
+        if t == 0:
+            late_constants()
+        mm(vw("pL", 0, 128), vw("e2"), vw("cm"))
+        mm(vw("pL", 128, 256), vw("cm"), vw("e2"))
+        scan(vw("bs", 0, 1024), vw("d0b", 0, 1024), vw("x2", 0, 1024), A.add, A.max)
+        scan(vw("bs", 1024, 2048), vw("d0b", 1024, 2048), vw("x2", 1024, 2048), A.add, A.max)
+        bl = vw("bs", 15, 2048, 16)
+        ts(vw("lo"), bl, 0.0625, A.mult, 1280 - 0.46875, A.add)
+        ku = vw("pU", 0, 128)
+        mm(ku, vw("on", 0, 128, 1, 0, 1), vw("tie16", 0, 128, 1, 0, 1), True, False)
+        mm(ku, vw("e2"), vw("bo256"), False, False)
+        for m in range(16):
+            mm(ku, vw("x2", m, 2048, 16), vw("I16b"), False, False)
+        mm(ku, bl, vw("I16"), False, False)
+        mm(ku, vw("lo"), vw("Im16"), False, True)
+        ts(vw("eP"), vw("pL", 0, 128), -16.5, A.is_lt)
+        ts(vw("eQ"), vw("pL", 128, 256), -16.5, A.is_lt)
+        if t == VI - 1:
+            tsixteenth()
+        stopped()
+        if t == 0:
+            act(vw("aP0"), vw("pA", 0, 128))
+        ts(vw("u1"), ku, 1.0 / 4096, A.mult, 1156.5 + 1.0 / 8192, A.add)
+        mm(vw("pS", 128, 256), vw("u1"), vw("I16"))
+        for j in range(16):
+            act(vw("vf", j, 2048, 16), vw("pS", 128, 256), -1.0, 1279.0)
+        scan(vw("mk"), vw("d0m"), ku, A.add, A.max)
+        kk = vw("mk", 15, 128, 16)
+        ts(vw("zi"), kk, 0.0625, A.mult, -0.46875, A.add)
+        ts(vw("r16"), vw("zi"), 16.0, A.mult)
+        for w in range(8):
+            ts(vw("ok", 16 * w, 16 * w + 16), vw("m15"), vw("r16", w, w + 1), A.add, vw("mk", 16 * w + 15, 16 * w + 16), A.is_equal)
+        tt(vw("pk"), vw("ok"), vw("pQ", 0, 128), A.mult)
+        scan(vw("sk"), vw("d0s"), vw("pk"), A.mult, A.add)
+        for w in range(8):
+            ts(vw("AL", 16 * w, 16 * w + 16), vw("m16"), vw("sk", 16 * w + 15, 16 * w + 16), A.mult)
+        mm(vw("pL", 256, 264), vw("AL"), vw("bo8h"))
+        copy(vw("lk"), vw("pL", 256, 264))
+        copy(vw("cd"), ind(vw("R"), vw("lk")))
+        spread()
+        mm(vw("pA", 256, 384), vw("ok"), vw("I16"))
+        if t == 0:
+            mm(vw("pA", 384, 512), vw("aP0"), vw("I32"))
+        for a, b in ((0, 64), (64, 96), (96, 128)):
+            d = vw("mn", 16 * a, 16 * b)
+            tt(d, ind(vw("X", 16, 16 + D), vw("cd", a, b)), vw("vf", 16 * a, 16 * b), A.subtract)
+            act(vw("xc", 16 * a, 16 * b), d, 1.0, 0.0, F.Abs)
+            for j in range(16):
+                mm(vw("pS", j, 128, 16, a, b), vw("xc", 16 * a + j, 16 * b, 16), vw("wm16"))
+        if t == 0:
+            tt(vw("aF"), vw("pA", 384, 512), vw("fil"), A.mult)
+            ts(vw("w0"), vw("wy0"), 65536.0, A.mult)
+            tt(vw("v0"), vw("aF"), vw("w0"), A.add)
+        ts(vw("aM"), vw("aF"), vw("m64"), A.add)
+        tt(vw("oka"), vw("pA", 256, 384), vw("aM"), A.mult)
+        ts(vw("cd16"), vw("cd"), 16.0, A.add)
+        ts(vw("fR"), vw("q2u"), 0, A.is_gt)
+        tt(vw("vv"), vw(v), vw("fR"), A.mult)
+        ts(vw("q2h"), vw("q2u"), 0.0, A.add)
+        equal()
+        mm(vw("pQ", 128, 256), vw("cd16"), vw("I16"))
+        for w in range(8):
+            mm(vw("pL", 272 + w, 273 + w), vw("eq", 128 * w, 128 * w + 128), vw("on", 0, 1))
+        mm(vw("pA", 128, 256), vw("bo32"), vw("oka"), True, False)
+        mm(vw("pA", 128, 256), vw("I32"), vw("bit"), False, True)
+
+        def send(k):
+            src = "%so%d" % (k, t + 1)
+            lowd = T.cores[(rank + STRIDE[0]) % NR]
+            hid = relay_of(core, T.cores[(rank + STRIDE[1]) % NR], topo)
+            r1, p1 = topo.addr(lowd, core)
+            r2, p2 = topo.addr(hid, core)
+            tr = [RemoteDMATransfer(dst_ids=[DstId(rid=r1, pnc=p1)], dma_engine_mask=bits(topo, core, lowd, 8, False), remote_sem=T.sem["%sL%d" % (k, t + 1)],
+                                    src=T[src][:, 0:H], dst=T["%s%d" % (k, t + 1)][:, 0:H]),
+                  RemoteDMATransfer(dst_ids=[DstId(rid=r2, pnc=p2)], dma_engine_mask=bits(topo, core, hid, 8, True), remote_sem=T.sem["r%s%d" % (k, t + 1)],
+                                    src=T[src][:, H:L], dst=T["r%s%d" % (k, t + 1)][:, :])]
+            deps("g", [], [vw(src)])
+            g.remote_dma_fused(tr, local_sem=T.sem["loc"])
+            cnt["loc"] = cnt.get("loc", 0) + 16
+        if t == VI - 1:
+            dedupe()
+            update()
+            scatter()
+            store(T.yx[:, :], vw("X", 16, 16 + D), "st0")
+        tt(vw("ky"), vw("pS", 0, 128), vw("tief"), A.add)
+        scan(vw("ms"), vw("d0m"), vw("ky"), A.add, A.max)
+        for w in range(8):
+            ts(vw("oj", 16 * w, 16 * w + 16), vw("ky", 16 * w, 16 * w + 16), vw("ms", 16 * w + 15, 16 * w + 16), A.is_equal)
+        tt(vw("pn"), vw("oj"), vw("pQ", 128, 256), A.mult)
+        scan(vw("sn"), vw("d0s"), vw("pn"), A.mult, A.add)
+        for w in range(8):
+            ts(vw("AN", 16 * w, 16 * w + 16), vw("eP", 16 * w, 16 * w + 16), vw("sn", 16 * w + 15, 16 * w + 16), A.mult)
+        nq = vw("pL", 384, 512)
+        mm(nq, vw("I16"), vw("q2h"), True, False)
+        mm(nq, vw("AN"), vw("I16"), False, True)
+        if t < VI - 1:
+            copy(vw("qo%d" % (t + 1)), nq)
+            send("q")
+        else:
+            ts(vw("yo"), nq, 0.0, A.is_equal, float(16 + D), A.mult)
+            tt(vw("yo"), vw("yo"), nq, A.add)
+            ts(vw("yt"), vw("yo"), -16.0, A.add)
+            store(T.yp[:, :], vw("yt"), "st2")
+        tt(vw("t3"), vw("pA", 128, 256), vw("eQ"), A.mult)
+        tt(vw("vo%d" % (t + 1) if t < VI - 1 else "vI"), vw("vv"), vw("t3"), A.add)
+        if t < VI - 1:
+            send("v")
+            sums()
+            dedupe()
+            stops()
+            tsixteenth()
+            update()
+            scatter()
+        else:
+            ts(vw("bb"), vw("vI"), 16, A.arith_shift_right)
+            copy(vw("yw"), vw("bb"))
+            store(T.yq[:, :], vw("yw"), "st1")
+    for s in SEMAPHORES:
+        if cnt.get(s):
+            g.wait_ge(T.sem[s], cnt[s])

@@ -6,36 +6,40 @@ A = AluOpType
 F = ActivationFunctionType
 NR, VI, H, L, D = 8, 4, 64, 128, 1760
 STRIDE = (4, 1)
-XW = 16 + D + 128
+X0 = 32
+XS = X0 + D + 16
+XW = XS + 128
+BIG = 16777216.0
 f32, b16, h16, i32, u16 = "float32", "bfloat16", "float16", "int32", "uint16"
 SB = {
-    "X": (XW, b16), "R": (16 + D, i32), "dr0": (L, i32), "wy0": (L, i32), "lmI": (1, i32),
-    "kI": (1, i32), "aI": (1, i32), "gI": (1, i32), "kc": (1, f32), "ac": (1, f32), "gc": (1, f32),
-    "cid": (128, f32), "mro": (128, f32), "g8": (8, f32), "j16": (16, f32),
-    "I32": (128, f32), "I16": (128, h16), "Ib": (128, b16), "I16b": (128, b16), "Im16": (128, h16),
-    "bo": (128, b16), "bo32": (128, f32), "bo256": (128, b16),
-    "bo8": (8, b16), "bo8h": (8, h16), "wm16": (8, b16), "w32": (8, b16), "bo8a": (8, b16), "bo8b": (8, b16),
-    "on": (128, b16), "on32": (128, f32), "on16": (128, h16), "tie16": (128, b16), "tief": (128, f32),
-    "m15": (16, f32), "m16": (16, h16), "cm": (128, b16), "d0m": (128, f32), "d0s": (128, f32), "d0p": (128, f32), "d0b": (2048, b16),
-    "pw2": (16, f32), "one16": (16, f32), "pwo": (16, f32), "m64": (1, f32), "dum": (1, f32),
-    "bit": (128, f32), "tri": (512, b16), "limb": (8, f32), "limf": (1, f32), "lim8": (8, f32),
-    "pofI": (128, i32), "pof16": (128, h16),
-    "IF": (1024, b16), "IG": (1024, b16), "PA": (2048, b16), "PB": (2048, b16), "CA": (2048, b16), "CB": (2048, b16),
-    "LW": (2048, b16), "lf": (128, f32), "lu1": (128, u16), "lu2": (128, u16), "lu4": (128, u16), "lu8": (128, u16),
-    "qf0": (128, f32), "fil": (128, f32), "aP0": (128, f32), "w0": (128, f32),
-    "x": (2048, b16), "x2": (2048, b16), "xc": (2048, b16), "mn": (2048, b16), "vf": (2048, b16), "bs": (2048, h16),
-    "eR": (128, b16), "e2": (128, b16), "q16": (128, h16), "aa": (128, i32), "aF": (128, f32), "aM": (128, f32),
-    "n0": (8, f32), "n1": (8, f32), "n2": (8, f32), "thr": (8, f32), "mx": (128, f32), "sm": (128, f32), "stp": (8, f32),
-    "oh": (128, f32), "pw": (128, f32), "pr": (128, i32), "bb": (128, i32), "q2P": (128, h16), "q2u": (128, u16), "q2h": (128, h16),
-    "fR": (128, b16), "vv": (128, f32), "lo": (128, h16), "u1": (128, h16), "eP": (128, f32), "eQ": (128, f32),
-    "mk": (128, f32), "zi": (8, i32), "r16": (8, f32), "ok": (128, h16), "pk": (128, f32), "sk": (128, f32), "AL": (128, h16), "lk": (8, u16),
-    "cd": (128, u16), "cd16": (128, h16), "oka": (128, f32), "t3": (128, f32), "xk": (128, f32), "ky": (128, f32),
+    "X": (XW, b16), "R": (32 + D, i32), "dr0": (L, i32), "wy0": (L, i32), "lmI": (1, i32),
+    "kI": (1, i32), "aI": (1, i32), "gI": (1, i32), "hI": (1, i32), "kc": (1, f32), "ac": (1, f32), "gc": (1, f32), "hc": (1, f32),
+    "a16": (1, f32), "a32": (1, f32), "c14": (1, f32), "c15": (1, f32), "n15": (1, f32), "ndum": (1, f32), "dum": (1, f32), "b16p": (1, f32),
+    "wI": (256, b16), "dl": (256, b16), "Kc": (256, b16), "K": (256, b16), "cid": (144, f32), "Z": (144, b16), "g8": (8, f32),
+    "I32": (128, f32), "Im32": (128, f32), "Ib": (128, b16), "I256": (128, b16), "Im16": (128, b16), "ImQ": (128, b16), "I32th": (128, b16),
+    "bo": (128, b16), "bo32": (128, f32), "bo16": (128, b16), "Dm": (128, b16), "cm": (128, b16),
+    "bo8": (8, b16), "bo8n": (8, b16), "wm16": (8, b16), "bo8b": (8, b16), "bo8m": (8, b16), "bo8d": (8, h16), "bo8k": (8, h16),
+    "on": (128, b16), "on32": (128, f32), "m15": (128, b16), "tie16": (128, b16), "m16": (128, b16),
+    "d0s": (128, f32), "d0m": (128, f32), "d0p": (128, f32), "d0b": (1024, b16), "pwr": (128, b16), "hlf": (128, f32), "zer": (128, f32),
+    "wr": (128, b16), "wc": (1, b16), "wt": (1, f32), "eI": (512, b16), "E": (512, b16), "sl8": (1024, b16),
+    "lbI": (8, i32), "l8I": (8, i32), "LB": (8, u16), "L8": (8, u16),
+    "limf": (1, f32), "limc": (1, f32), "lim8": (8, f32), "pofI": (128, i32), "pofm": (128, h16),
+    "WA": (2048, b16), "WB": (2048, b16), "lf": (128, f32), "l0": (128, u16),
+    "lu1": (128, u16), "lu2": (128, u16), "lu4": (128, u16), "lu8": (128, u16), "wyb": (128, b16),
+    "x": (2048, b16), "x2": (2048, b16), "xc": (2048, b16), "mn": (2048, b16), "vf": (2048, b16), "bs": (2048, h16), "RA": (2048, f32),
+    "eR": (128, b16), "e2": (128, b16), "q16": (128, h16), "aP": (128, f32), "aM": (128, f32), "a1": (128, f32), "a2": (128, f32),
+    "n0": (8, f32), "thr": (8, f32), "mx": (128, f32), "sm": (128, f32), "nst": (8, b16), "mx8": (8, f32),
+    "oh": (128, f32), "pw": (128, f32), "pw8": (8, f32), "pr": (128, i32), "bb": (128, i32), "q2P": (128, h16), "q2u": (128, u16), "q2h": (128, h16),
+    "lo": (128, h16), "Uh": (128, h16), "cP": (128, h16), "e0": (256, f32), "e1": (256, b16),
+    "mk": (128, i32), "r8": (8, i32), "ok": (128, b16), "AL": (128, h16), "lk": (8, u16),
+    "cd": (128, u16), "cd16": (128, h16), "oka": (128, f32), "okb": (128, b16), "t3": (128, f32),
     "ms": (128, f32), "oj": (128, f32), "pn": (128, f32), "sn": (128, f32), "AN": (128, h16),
-    "on1": (128, f32), "pq": (128, f32), "sq": (128, f32), "dg": (1024, h16), "eq": (1024, b16), "du": (8, f32), "uu": (8, f32), "ut": (8, f32), "of": (8, f32), "AS": (128, h16), "ls": (8, u16),
-    "ti": (128, i32), "xs": (128, f32), "xn": (128, i32), "cn": (1, f32), "ci": (1, i32), "cj": (1, i32), "c16": (1, f32),
-    "yt": (128, f32), "yo": (128, f32), "vI": (128, i32), "yw": (128, f32),
+    "pq": (128, f32), "sq": (128, f32), "y8": (8, f32), "y16": (8, h16), "yT": (128, h16), "eq": (1024, b16),
+    "du": (8, f32), "ya": (8, f32), "of": (8, f32), "AS": (128, h16), "ls": (8, u16),
+    "ti": (128, f32), "xs": (128, f32), "xn": (128, i32), "cj": (8, f32), "cn": (1, f32), "cz": (1, h16), "cc": (1, f32),
+    "yt": (128, f32), "yo": (128, f32), "yw": (128, f32), "fR": (128, f32), "fr": (128, f32),
 }
-ALONE = ("X", "R", "dr0", "wy0", "lmI", "yt", "yw", "IF", "IG")
+ALONE = ("X", "R", "dr0", "wy0", "lmI", "yt", "yw")
 ALIAS, SCRATCH, _wide = {}, {}, {}
 for _k, (_w, _d) in SB.items():
     if _w > 1024 or _k in ALONE:
@@ -47,13 +51,13 @@ for _d, _w in _wide.items():
     SCRATCH["p_" + _d] = ("sbuf", [128, _w], _d)
 for _t in range(VI):
     SCRATCH["q%d" % _t] = ("sbuf", [128, L], u16)
-    SCRATCH["v%d" % _t] = ("sbuf", [128, L], i32)
+    SCRATCH["v%d" % _t] = ("sbuf", [128, L], f32)
 for _t in range(1, VI):
     SCRATCH["qo%d" % _t] = ("sbuf", [128, L], u16)
-    SCRATCH["vo%d" % _t] = ("sbuf", [128, L], i32)
+    SCRATCH["vo%d" % _t] = ("sbuf", [128, L], f32)
     SCRATCH["rq%d" % _t] = ("sbuf", [128, H], u16)
-    SCRATCH["rv%d" % _t] = ("sbuf", [128, H], i32)
-PS = ("pW", "pT", "pU", "pS", "pQ", "pA", "pL", "pD")
+    SCRATCH["rv%d" % _t] = ("sbuf", [128, H], f32)
+PS = ("pA", "pB", "pC", "pD", "pE", "pF", "pG", "pH")
 for _p in PS:
     SCRATCH[_p] = ("psum", [128, 512], f32)
 SEMAPHORES = ["ev", "es", "et", "eg", "loc"] + ["ld%d" % _t for _t in range(5)] + ["st%d" % _t for _t in range(3)]
@@ -89,7 +93,7 @@ def relay(g, core, dst, T, topo):
     m = bits(topo, core, dst, 8, False)
     n = 0
     for t in range(1, VI):
-        for k in ("q", "v"):
+        for k in ("v", "q"):
             g.wait_ge(T.sem["r%s%d" % (k, t)], 8)
             g.remote_dma(T["%s%d" % (k, t)][:, H:L], T["r%s%d" % (k, t)][:, :], T.sem["%sH%d" % (k, t)], T.sem["loc"], pid, rid, m)
             n += 8
@@ -112,17 +116,20 @@ def member(g, core, rank, T, topo):
             name, o = ALIAS[name]
             lo, hi = lo + o, hi + o
         ap = T[name][r0:r1, lo:hi:st] if st > 1 else T[name][r0:r1, lo:hi]
-        return {"ap": ap, "n": name, "lo": lo, "hi": hi, "st": st, "x": None}
+        return {"ap": ap, "n": name, "lo": lo, "hi": hi, "st": st, "x": None, "r0": r0, "r1": r1}
 
     def ind(w, o):
-        return {"ap": w["ap"].indirect(o["ap"]), "n": w["n"], "lo": w["lo"], "hi": w["hi"], "st": 1, "x": o}
+        return dict(w, ap=w["ap"].indirect(o["ap"]), x=o)
 
     def clash(a, b):
         if a["n"] in psum:
             return True
-        if a["lo"] >= b["hi"] or b["lo"] >= a["hi"]:
+        if a["lo"] >= b["hi"] or b["lo"] >= a["hi"] or a["r0"] >= b["r1"] or b["r0"] >= a["r1"]:
             return False
         return not (a["st"] > 1 and a["st"] == b["st"] and (a["lo"] - b["lo"]) % a["st"])
+
+    def covers(a, b):
+        return a["lo"] <= b["lo"] and b["hi"] <= a["hi"] and a["r0"] <= b["r0"] and b["r1"] <= a["r1"]
 
     def need(q, tok):
         s, n = tok
@@ -166,9 +173,9 @@ def member(g, core, rank, T, topo):
         for a, wr in [(a, True) for a in outs] + [(a, False) for a in ins]:
             l = recs.setdefault(a["n"], [])
             if wr and a["st"] == 1 and a["n"] not in psum:
-                l[:] = [b for b in l if not (a["lo"] <= b[0]["lo"] and b[0]["hi"] <= a["hi"])]
+                l[:] = [b for b in l if not covers(a, b[0])]
             elif a["n"] in psum or not wr:
-                l[:] = [b for b in l if not (b[3] == q and b[1] == wr and b[0]["lo"] == a["lo"] and b[0]["hi"] == a["hi"] and b[0]["st"] == a["st"])]
+                l[:] = [b for b in l if not (b[3] == q and b[1] == wr and b[0]["st"] == a["st"] and covers(a, b[0]) and covers(b[0], a))]
             l.append((a, wr, tok, q))
 
     def op(q, outs, ins, fn, sem=None, inc=1):
@@ -202,8 +209,11 @@ def member(g, core, rank, T, topo):
     def fill(o, c):
         op("v", [o], [], lambda: g.vector.memset(P(o), c))
 
-    def act(o, i, scale=1.0, bias=0.0, func=F.Identity):
-        op("s", [o], [i, scale], lambda: g.scalar.activation(P(o), P(i), func, bias=bias, scale=P(scale)))
+    def act(o, i, scale=1.0, bias=0.0, func=F.Identity, acc=None):
+        if acc is None:
+            op("s", [o], [i, scale, bias], lambda: g.scalar.activation(P(o), P(i), func, bias=P(bias), scale=P(scale)))
+        else:
+            op("s", [o, acc], [i, scale, bias], lambda: g.scalar.activation(P(o), P(i), func, bias=P(bias), scale=P(scale), accum_out=P(acc)))
 
     def mm(o, a, b, start=True, stop=True):
         op("t", [o], [a, b], lambda: g.tensor.matmul(P(o), P(a), P(b), start, stop))
@@ -223,383 +233,450 @@ def member(g, core, rank, T, topo):
     def sel(o, pat, f, c, base, cm):
         op("g", [o], [o], lambda: g.affine_select(P(o), P(o), pat, f, c, base, cm))
 
-    def half(name, h):
-        return vw(name, 1024 * h, 1024 * h + 1024)
+    def flat(name, a, b, m=None):
+        return vw(name, 16 * a, 16 * b) if m is None else vw(name, 16 * a + m, 16 * b, 16)
+
+    def last(name):
+        return vw(name, 15, 128, 16)
+
+    def row(name, lo=0, hi=128):
+        return vw(name, lo, hi, 1, 0, 1)
+
+    def gath(q, o, w, f, scale=1.0, bias=0.0):
+        if q == "s":
+            act(o, ind(w, f), scale, bias)
+        elif scale != 1.0:
+            ts(o, ind(w, f), scale, A.mult, bias, A.add)
+        else:
+            copy(o, ind(w, f))
+    XG = vw("X", 16, XS)
+
+    def xgath(q, dst, lst, a, b, scale=1.0, bias=0.0):
+        gath(q, flat(dst, a, b), XG, vw(lst, a, b), scale, bias)
 
     load(vw("wy0"), T.why[:, :], "ld0")
     load(vw("dr0"), T.drugs[:, :], "ld1", "s")
-    load(vw("X", 16, 16 + D), T.eff[:, :], "ld2")
+    load(vw("X", X0, X0 + D), T.eff[:, :], "ld2")
     load(vw("lmI"), T.lim[:, :], "ld3", "s")
     load(vw("R", 16, 16 + D), T.rem[:, :], "ld4")
     iota(vw("kI"), [[1, 1]], 0, 1, False)
-    iota(vw("mro"), [[0, 8], [1, 16]], 0, 0)
+    iota(vw("wI"), [[0, 16], [1, 16]], 0, 0)
+    iota(vw("dl"), [[-1, 16], [1, 16]], 0, 0)
     iota(vw("pofI"), [[0, 2], [16, 64]], 0, 0, False)
-    iota(vw("g8"), [[1, 8]], 0, 0)
-    iota(vw("cid"), [[1, 128]], 0, 0)
-    iota(vw("j16"), [[1, 16]], 0, 0)
-    fill(vw("LW"), 0.0)
+    iota(vw("cid"), [[1, 144]], 0, 0)
     ts(vw("aI"), vw("kI"), 15, A.bitwise_and)
     copy(vw("ac"), vw("aI"))
-    ts(vw("IF", 0, 128), vw("mro"), vw("ac"), A.is_equal)
-    for h in (128, 256, 512):
-        copy(vw("IF", h, 2 * h), vw("IF", 0, h))
-    act(vw("IG"), vw("IF"))
-    ts(vw("gI"), vw("kI"), 4, A.arith_shift_right)
-    copy(vw("gc"), vw("gI"))
     copy(vw("kc"), vw("kI"))
-    ts(vw("bo8"), vw("g8"), vw("gc"), A.is_equal)
-    ts(vw("bo8a"), vw("bo8"), vw("ac"), A.mult)
+    ts(vw("c15"), vw("ac"), 15.0, A.is_equal)
+    ts(vw("c14"), vw("ac"), 14.0, A.is_equal, 2.0, A.mult)
+    ts(vw("a16"), vw("ac"), 16.0, A.mult)
+    ts(vw("K"), vw("wI"), vw("ac"), A.is_equal)
+    ts(vw("K", 15, 256, 16), vw("wI", 0, 16), 0.0, A.mult, vw("c14"), A.add)
+    fill(vw("K", 0, 256, 17), 0.0)
+    ts(vw("Kc"), vw("dl"), vw("c15"), A.mult)
+    ts(vw("l0"), vw("wy0"), vw("a16"), A.add)
+    tt(vw("K"), vw("K"), vw("Kc"), A.add)
+    gath("s", flat("WA", 64, 128), vw("K"), vw("l0", 64, 128))
+    ts(vw("q0"), vw("dr0"), 16.0, A.add)
     tt(vw("lf"), vw("wy0"), vw("pofI"), A.add)
     copy(vw("lu1"), vw("lf"))
-
-    def win(name, h):
-        return vw("IF") if name == "IF" else half(name, h)
-
-    def pgath(q, dst, src, lst, h):
-        o, w, f = half(dst, h), win(src, h), vw(lst, *HV[h])
-        if q == "s":
-            act(o, ind(w, f))
-        else:
-            copy(o, ind(w, f))
-
-    def cgath(dst, src, lst, h, by=None):
-        o, w, f = half(dst, h), win(src, h), vw(lst, *HV[h])
-        d = vw("IG") if src == "IF" else half("xc", h)
-        if by == "s":
-            act(d, w)
-        elif by == "v":
-            copy(d, w)
-        tt(o, ind(w, f), d, A.max)
-
-    def xgath(q, dst, lst, c0, c1, conv=False, lo=0):
-        o, w, f = vw(dst, 16 * c0, 16 * c1), vw("X", lo, 16 + D), vw(lst, c0, c1)
-        if q == "s":
-            act(o, ind(w, f), 16.0, -2048.0) if conv else act(o, ind(w, f))
-        elif conv:
-            ts(o, ind(w, f), 16.0, A.mult, -2048.0, A.add)
-        else:
-            copy(o, ind(w, f))
-
-    def conv(src, h):
-        o = vw("pU" if h == 0 else "pS", 0, 64)
-        mm(o, vw("I16"), vw("pof16", *HV[h]), True, False)
-        for m in range(16):
-            mm(o, vw("LW", 128 * m, 128 * m + 128), vw(src, 1024 * h + m, 1024 * h + 1024, 16), False, m == 15)
-
-    def convd(lst, h):
-        copy(vw(lst, *HV[h]), vw("pU" if h == 0 else "pS", 0, 64))
-    pgath("s", "PA", "IF", "lu1", 0)
-    pgath("v", "PA", "IF", "lu1", 1)
-    for m in range(16):
-        o = vw("LW", 128 * m + m, 128 * m + 128, 16)
-        act(o, vw("bo8a")) if m % 4 else copy(o, vw("bo8a"))
-    pgath("s", "PB", "PA", "lu1", 0)
-    ts(vw("I32"), vw("cid"), vw("kc"), A.is_equal)
-    copy(vw("I16"), vw("I32"))
-    copy(vw("pof16"), vw("pofI"))
-    pgath("v", "PB", "PA", "lu1", 1)
-    conv("PB", 0)
-    conv("PB", 1)
-    gfill(vw("X", 0, 16), 16, -1)
-    gfill(vw("X", 16 + D, XW), 128, 0)
-    gfill(vw("R", 0, 16), 16, 0, False)
-    gfill(vw("d0b"), 2048, 1)
-    sel(vw("d0b"), [[0, 128], [1, 16]], A.not_equal, -8192.0, 0, 0)
-    for n, c, z in (("d0s", 1, 0.0), ("d0m", 0, -16777216.0), ("d0p", 2, 0.0)):
+    gath("v", flat("WA", 0, 64), vw("K"), vw("l0", 0, 64))
+    gfill(vw("X", 0, 16), 16, 0)
+    gfill(vw("X", 16, 32), 16, -1)
+    gfill(vw("X", X0 + D, XS), 16, -1)
+    gfill(vw("R", 0, 16), 16, -16, False)
+    gfill(vw("R", 16 + D, 32 + D), 16, -16, False)
+    iota(vw("g8"), [[1, 8]], 0, 0)
+    iota(vw("lbI"), [[16, 8]], 15, 0, False)
+    iota(vw("l8I"), [[1, 8]], 0, 0, False)
+    gfill(vw("on"), 128, 1)
+    gfill(vw("on32"), 128, 1)
+    for n, c, z in (("d0p", 2, 0.0), ("d0s", 1, 0.0), ("d0m", 0, -BIG)):
         gfill(vw(n), 128, c)
         sel(vw(n), [[0, 8], [1, 16]], A.not_equal, z, 0, 0)
-    gfill(vw("on32"), 128, 1)
-    gfill(vw("on"), 128, 1)
+    for n, z in (("I32", 1.0), ("ImQ", -float(16 + D))):
+        gfill(vw(n), 128, 0)
+        sel(vw(n), [[1, 128]], A.not_equal, z, 0, -1)
+    iota(vw("m15"), [[0, 8], [-1, 16]], 15, 0)
+    iota(vw("tie16"), [[0, 8], [-16, 16]], 240, 0)
+    gfill(vw("X", XS, XW), 128, 0)
+    gfill(vw("zer"), 128, 0)
+    gfill(vw("hlf"), 128, 0)
+    sel(vw("hlf"), [[0, 128]], A.not_equal, 0.5, 0, 0)
     gfill(vw("bo32"), 128, 1)
     gfill(vw("cm"), 128, 65)
     sel(vw("cm"), [[1, 128]], A.is_gt, 1.0, 0, -1)
     sel(vw("cm"), [[1, 128]], A.not_equal, -31.0, 0, -1)
-    for n in ("bo32", "cm"):
+    gfill(vw("Dm"), 128, 0)
+    sel(vw("Dm"), [[1, 128]], A.not_equal, 1.0, 0, -1)
+    sel(vw("Dm"), [[1, 128]], A.not_equal, -1.0, 1, -1)
+    for n in ("bo32", "Dm", "cm"):
         sel(vw(n), [[-16, 8], [0, 16]], A.is_ge, 0.0, 0, 1)
         sel(vw(n), [[16, 8], [0, 16]], A.is_ge, 0.0, 15, -1)
-    gfill(vw("tri"), 512, 4096)
-    sel(vw("tri"), [[0, 4], [-1, 128]], A.is_ge, 0.0, 0, 1)
-    cgath("CA", "IF", "lu1", 0)
-    convd("lu2", 0)
-    pgath("s", "mn", "PB", "lu2", 0)
-    conv("mn", 0)
-    convd("lu2", 1)
-    cgath("CA", "IF", "lu1", 1)
-    ts(vw("fil"), vw("dr0"), D, A.is_lt)
-    ts(vw("qf0"), vw("dr0"), 16, A.add)
-    tt(vw("qf0"), vw("qf0"), vw("fil"), A.mult)
-    copy(vw("q0"), vw("qf0"))
-    pgath("s", "mn", "PB", "lu2", 1)
-    conv("mn", 1)
-    cgath("CB", "CA", "lu2", 0, "v")
-    convd("lu4", 0)
-    act(half("xc", 1), half("CA", 1))
-    pgath("s", "PB", "mn", "lu4", 0)
-    conv("PB", 0)
-    cgath("CB", "CA", "lu2", 1)
-    convd("lu4", 1)
-    pgath("s", "PB", "mn", "lu4", 1)
-    conv("PB", 1)
+    iota(vw("eI"), [[1, 32], [0, 16]], 0, 0)
+    gfill(vw("d0b"), 1024, 1)
+    sel(vw("d0b"), [[0, 64], [1, 16]], A.not_equal, -8192.0, 0, 0)
+    gfill(vw("sl8", 0, 1024, 1, 0, 8), 1024, 1)
+    sel(vw("sl8", 0, 1024, 1, 0, 8), [[1, 8], [0, 128]], A.is_equal, 0.0, 0, -1)
+
+    def double(dst, src, lst, h):
+        tt(flat(dst, *HV[h]), ind(flat(src, *HV[h]), vw(lst, *HV[h])), flat("xc", *HV[h]), A.add)
+
+    def twin(src, h):
+        act(flat("xc", *HV[h]), flat(src, *HV[h]))
+
+    def conv(src, h):
+        o = vw("pE" if h == 0 else "pF", 0, 64)
+        mm(o, vw("Ib"), vw("pofm", *HV[h]), True, False)
+        for m in range(16):
+            mm(o, vw("Z", 15 - m, 143 - m), flat(src, HV[h][0], HV[h][1], m), False, m == 15)
+
+    def convd(lst, h):
+        copy(vw(lst, *HV[h]), vw("pE" if h == 0 else "pF", 0, 64))
+
+    def rowsums(a, b):
+        for m in range(16):
+            mm(vw("pA", m, 128, 16, a, b), flat("x", a, b, m), vw("bo8"))
+
+    def remedies(q):
+        for a, b in HV:
+            gath("s", flat("RA", a, b), vw("R"), vw(q, a, b), 1.0, 16.0)
+
+    ts(vw("Z"), vw("cid"), vw("kc"), A.is_equal, vw("c15"), A.mult)
+    ts(vw("Ib"), vw("cid", 0, 128), vw("kc"), A.is_equal)
+    ts(vw("pofm"), vw("pofI"), vw("ac"), A.add)
+    copy(flat("xc", 0, 64), flat("WA", 0, 64))
+    twin("WA", 1)
     xgath("s", "x", "q0", 0, 64)
-    ts(vw("pw2"), vw("j16"), vw("ac"), A.is_lt, 1.0, A.add)
-    fill(vw("one16"), 1.0)
-    scan(vw("pwo"), vw("pw2"), vw("one16"), A.mult, A.mult, 1.0)
-    pcol = vw("pwo", 15, 16)
-    ts(vw("bo8b"), vw("bo8"), pcol, A.mult)
-    cgath("CA", "CB", "lu4", 0, "v")
-    convd("lu8", 0)
-    act(half("xc", 0), half("CA", 0))
-    cgath("CA", "CB", "lu4", 1, "v")
-    convd("lu8", 1)
-    act(half("xc", 1), half("CA", 1))
-    xgath("s", "x", "q0", 64, 128)
-    act(vw("Ib"), vw("I32"))
-    act(vw("wm16"), vw("bo8"), -16.0)
-    act(vw("w32"), vw("bo8"), 32.0)
-    act(vw("bo"), vw("bo32"))
-    act(vw("I16b"), vw("I32"), 16.0)
-    act(vw("bo256"), vw("bo32"), 256.0)
-    act(vw("tie16"), vw("mro"), -16.0, 240.0)
-    act(vw("tief"), vw("mro"), -1.0, 15.0)
-    act(vw("m15"), vw("mro", 0, 16), -1.0, 15.0)
-    act(vw("bit"), vw("on32"), pcol)
+    double("WB", "WA", "lu1", 0)
+    conv("WB", 0)
+    twin("WB", 0)
+    xgath("s", "x", "q0", 64, 96)
+    ts(vw("gI"), vw("kI"), 4, A.arith_shift_right)
+    ts(vw("hI"), vw("kI"), 31, A.bitwise_and)
+    ts(vw("n15"), vw("ac"), 15.0, A.is_lt)
+    copy(vw("gc"), vw("gI"))
+    copy(vw("hc"), vw("hI"))
     copy(vw("limf"), vw("lmI"))
-    ts(vw("lim8"), vw("I32", 0, 128, 16), vw("limf"), A.mult)
-    cgath("CB", "CA", "lu8", 0)
-    cgath("CB", "CA", "lu8", 1)
+    ts(vw("bo8"), vw("g8"), vw("gc"), A.is_equal)
+    double("WB", "WA", "lu1", 1)
+    conv("WB", 1)
+    twin("WB", 1)
+    xgath("s", "x", "q0", 96, 128)
+    convd("lu2", 0)
+    scan(vw("pwr"), vw("d0p"), vw("on32"), A.mult, A.max)
+    double("WA", "WB", "lu2", 0)
+    mm(vw("pG", 0, 1), row("pwr"), row("on", 0, 1))
+    conv("WA", 0)
+    twin("WA", 0)
+    act(vw("bo8m"), vw("bo8"), vw("n15"))
+    act(vw("eR"), vw("dr0"), 1.0, -float(D - 1), F.Relu)
+    convd("lu2", 1)
+    copy(vw("LB"), vw("lbI"))
+    copy(vw("L8"), vw("l8I"))
+    double("WA", "WB", "lu2", 1)
+    conv("WA", 1)
+    twin("WA", 1)
+    rowsums(0, 128)
+    act(vw("wm16"), vw("bo8"), -16.0)
+    act(vw("lim8"), vw("I32", 0, 128, 16), vw("limf"))
+    act(vw("q16"), vw("dr0"), 1.0, 32.0)
+    remedies("q0")
+    convd("lu4", 0)
+    ts(vw("bo8b"), vw("bo8m"), vw("pG", 0, 1), A.mult)
+    ts(vw("m16"), vw("wI", 0, 128), vw("ac"), A.is_equal)
+    double("WB", "WA", "lu4", 0)
+    conv("WB", 0)
+    convd("lu4", 1)
+    double("WB", "WA", "lu4", 1)
 
     def late_constants():
-        fill(vw("on16"), 1.0)
-        ts(vw("Im16"), vw("I32"), -16.0, A.mult)
-        copy(vw("bo8h"), vw("bo8"))
-        copy(vw("m16"), vw("IF", 0, 16))
-        ts(vw("m64"), vw("ac"), 65536.0, A.mult)
-        ts(vw("dum"), vw("kc"), float(16 + D), A.add)
+        act(vw("bo"), vw("bo32"))
+        act(vw("bo16"), vw("bo32"), 16.0)
+        act(vw("I256"), vw("Ib"), 256.0)
+        act(vw("Im16"), vw("Ib"), -16.0)
+        act(vw("b16p"), vw("kc"), 16.0, 15.0)
+        act(vw("bo8k"), vw("bo8"), vw("b16p"))
+        act(vw("bo8n"), vw("bo8"), -1.0)
+        act(vw("wyb"), vw("wy0"))
+        act(vw("I32th"), vw("Ib"), 1.0 / 32)
 
-    def stopped():
-        ts(vw("on1"), vw("pw"), 1.0, A.is_equal)
-        tt(vw("pq"), vw("on1"), vw("pQ", 0, 128), A.mult)
-        scan(vw("sq"), vw("d0s"), vw("pq"), A.mult, A.add)
-        for w in range(8):
-            ts(vw("dg", 128 * w, 128 * w + 128), vw("I16"), vw("sq", 16 * w + 15, 16 * w + 16), A.mult)
+    def last_constants():
+        act(vw("Im32"), vw("Ib"), -1.0)
+        act(vw("a32"), vw("ac"), 1.0 / 32)
+        act(vw("dum"), vw("kc"), 1.0, float(XS))
+        act(vw("ndum"), vw("kc"), -1.0, -float(XS))
+        act(vw("bo8d"), vw("bo8"), vw("dum"))
 
-    def spread():
-        for b, p in ((0, "pD"), (1, "pT")):
-            mm(vw(p), vw("Ib"), vw("tri"), True, False)
-            mm(vw(p), vw("on16"), vw("dg", 512 * b, 512 * b + 512), False, True)
+    def measures(t):
+        mm(vw("pB", 0, 8), vw("eR"), vw("bo8"))
+        mm(vw("pB", 8, 16), vw("eR"), vw("wm16"), True, False)
+        mm(vw("pB", 8, 16), vw("on32"), vw("lim8"), False, True)
 
-    def equal():
-        for w in range(8):
-            p = vw("pD" if w < 4 else "pT", 128 * (w % 4), 128 * (w % 4) + 128)
+    def lists(t):
+        mm(vw("pB", 128, 256), vw("q16"), vw("Ib"), True, t > 0)
+        if t == 0:
+            mm(vw("pB", 128, 256), vw("eR"), vw("ImQ"), False, True)
+        mm(vw("pB", 256, 384), vw("q16"), vw("Dm"))
+
+    def threshold():
+        ts(vw("n0"), vw("pB", 0, 8), BIG, A.mult, -1000.0, A.add)
+        tt(vw("thr"), vw("pB", 8, 16), vw("n0"), A.min)
+
+    def decide():
+        key = vw("pA", 0, 128)
+        scan(vw("sm"), vw("d0s"), key, A.mult, A.add)
+        scan(vw("mx"), vw("d0m"), key, A.add, A.max)
+        tt(vw("nst"), last("sm"), vw("thr"), A.is_lt)
+        tt(vw("mx8"), last("mx"), vw("nst"), A.add)
+        tt(vw("oh"), ind(vw("mx8"), vw("L8")), vw("mx"), A.is_equal)
+        scan(vw("pw"), vw("d0p"), vw("oh"), A.mult, A.max)
+
+    def sums(lo, hi):
+        for m in range(lo, hi):
+            if m < 16:
+                mm(vw("pG", 0, 128), vw("Ib"), flat("x", 0, 128, m), m == 0, False)
+            else:
+                mm(vw("pG", 0, 128), vw("bo"), vw("eR"), False, True)
+
+    def masks(v):
+        act(vw("a1"), vw(v), 1.0, 8388608.0)
+        act(vw("a2"), vw("a1"), 1.0, -8388608.0)
+        act(vw("aM"), vw("a2"), 1.0, vw("a32"))
+
+    measures(0)
+    lists(0)
+    conv("WB", 1)
+    convd("lu8", 0)
+    gath("s", flat("WA", 32, 64), flat("WB", 0, 64), vw("lu8", 32, 64))
+    gath("v", flat("WA", 0, 32), flat("WB", 0, 64), vw("lu8", 0, 32))
+    threshold()
+    scan(row("wr"), row("hlf"), row("zer"), A.mult, A.add, 2.0 ** 64)
+    ts(vw("E"), vw("eI"), vw("hc"), A.is_equal)
+    mm(vw("pH", 0, 1), row("wr"), row("on", 0, 1))
+    an = vw("pC", 384, 512)
+    mm(an, row("on"), row("pwr"), True, False)
+    for m in range(16):
+        mm(vw("pC", 384 + m, 512, 16), flat("WB", 0, 128, m), vw("bo8b"), False, False)
+    convd("lu8", 1)
+    gath("s", flat("WA", 96, 128), flat("WB", 64, 128), vw("lu8", 96, 128))
+    gath("v", flat("WA", 64, 96), flat("WB", 64, 128), vw("lu8", 64, 96))
+    for m in range(16):
+        mm(vw("pC", 384 + m, 512, 16), flat("WA", 0, 128, m), vw("bo8b"), False, m == 15)
+    late_constants()
+    copy(vw("wc"), vw("pH", 0, 1))
+    ts(vw("wt"), vw("pH", 0, 1), 2.5, A.mult)
+    decide()
+    act(vw("aP"), an)
+    last_constants()
+
+    def equal(lo, hi):
+        for w in range(lo, hi):
+            p = vw("pG" if w < 4 else "pH", 128 * (w % 4), 128 * (w % 4) + 128)
             ts(vw("eq", 128 * w, 128 * w + 128), p, vw("sq", 16 * w + 15, 16 * w + 16), A.is_equal)
 
+    def weigh(lo, hi):
+        for w in range(lo, hi):
+            mm(vw("pA", 272 + w, 273 + w), vw("eq", 128 * w, 128 * w + 128), vw("wc"))
+
     def dedupe():
-        ts(vw("du"), vw("pL", 272, 280), 0.5, A.is_lt)
-        tt(vw("uu"), vw("du"), vw("sq", 15, 128, 16), A.mult)
-        ts(vw("ut"), vw("uu"), 0.0, A.is_equal, vw("dum"), A.mult)
-        tt(vw("of"), vw("uu"), vw("ut"), A.add)
-        for w in range(8):
-            ts(vw("AS", 16 * w, 16 * w + 16), vw("m16"), vw("of", w, w + 1), A.mult)
-        mm(vw("pL", 264, 272), vw("AS"), vw("bo8h"))
-        copy(vw("ls"), vw("pL", 264, 272))
+        ts(vw("ya"), last("sq"), vw("ndum"), A.add)
+        ts(vw("du"), vw("pA", 272, 280), vw("wt"), A.is_lt)
+        tt(vw("of"), vw("du"), vw("ya"), A.mult)
+        tt(vw("AS"), ind(vw("of"), vw("L8")), vw("m16"), A.mult)
+        mm(vw("pA", 264, 272), vw("m16"), vw("bo8d"), True, False)
+        mm(vw("pA", 264, 272), vw("AS"), vw("bo8"), False, True)
 
     def update():
+        copy(vw("ls"), vw("pA", 264, 272))
         tt(vw("xs"), ind(vw("X"), vw("ls")), vw("ti"), A.add)
-        ts(vw("xn"), vw("xs"), 0.5, A.mult, -0.25, A.add)
-
-    def scatter():
+        ts(vw("xn"), vw("xs"), 0.5, A.mult, -0.484375, A.add)
         copy(ind(vw("X"), vw("ls")), vw("xn"))
 
-    def sums():
-        for m in range(16):
-            mm(vw("pT", 0, 128), vw("Ib"), vw("x", m, 2048, 16), m == 0, False)
-        mm(vw("pT", 0, 128), vw("bo"), vw("eR"), False, True)
-
-    def tsixteenth():
-        ts(vw("ti"), vw("pT", 0, 128), 0.0625, A.mult, -0.46875, A.add)
-
     def stops():
-        mm(vw("pT", 128, 136), vw("on32"), vw("stp"))
-        o, i = vw("cn"), vw("pT", 128, 136)
-        op("v", [o], [i], lambda: g.vector.tensor_reduce(P(o), P(i), AxisListType.X, A.add))
-        copy(vw("ci"), vw("cn"))
-        ts(vw("cj"), vw("ci"), 255, A.bitwise_and)
-        copy(vw("c16"), vw("cj"))
+        mm(vw("pE", 0, 8), vw("on"), vw("nst"))
+        act(vw("cj"), vw("pE", 0, 8), -1.0, 35328.0, F.Identity, vw("cn"))
+        act(vw("cz"), vw("cn"), 1.0 / 256, -0.498046875)
+        act(vw("cc"), vw("cz"), -256.0, vw("cn"))
+        act(vw("limc"), vw("limf"), 1.0, vw("cc"))
+        act(vw("lim8"), vw("I32", 0, 128, 16), vw("limc"))
 
-    def rowsums(h):
-        for m in range(16):
-            mm(vw("pW", m, 128, 16, *HV[h]), vw("x", 1024 * h + m, 1024 * h + 1024, 16), vw("bo8"))
+    def send(k, t):
+        src = "%so%d" % (k, t)
+        lowd = T.cores[(rank + STRIDE[0]) % NR]
+        hid = relay_of(core, T.cores[(rank + STRIDE[1]) % NR], topo)
+        r1, p1 = topo.addr(lowd, core)
+        r2, p2 = topo.addr(hid, core)
+        tr = [RemoteDMATransfer(dst_ids=[DstId(rid=r1, pnc=p1)], dma_engine_mask=bits(topo, core, lowd, 8, False), remote_sem=T.sem["%sL%d" % (k, t)],
+                                src=T[src][:, 0:H], dst=T["%s%d" % (k, t)][:, 0:H]),
+              RemoteDMATransfer(dst_ids=[DstId(rid=r2, pnc=p2)], dma_engine_mask=bits(topo, core, hid, 8, True), remote_sem=T.sem["r%s%d" % (k, t)],
+                                src=T[src][:, H:L], dst=T["r%s%d" % (k, t)][:, :])]
+        deps("g", [], [vw(src)])
+        g.remote_dma_fused(tr, local_sem=T.sem["loc"])
+        cnt["loc"] = cnt.get("loc", 0) + 16
 
     for t in range(VI):
         q, v = "q%d" % t, "v%d" % t
+        end = t == VI - 1
         if t:
             for k, h in (("q", 0), ("v", 0), ("q", 1), ("v", 1)):
                 s = "%s%s%d" % (k, "LH"[h], t)
                 cnt[s] = 8
                 snap[(s, 8)] = {}
                 recs.setdefault("%s%d" % (k, t), []).append((vw("%s%d" % (k, t), *HV[h]), True, (s, 8), "remote"))
+            mm(an, vw(v), vw("I32"))
+            act(vw("aP"), an)
             xgath("v", "x", q, 0, 32)
             xgath("s", "x", q, 32, 64)
-        ts(vw("eR"), vw(q), 0, A.is_equal)
-        if t:
-            xgath("v", "x", q, 64, 96)
-            xgath("s", "x", q, 96, 128)
-        rowsums(0)
-        mm(vw("pT", 256, 264), vw("eR"), vw("bo8"))
-        rowsums(1)
-        ts(vw("q16"), vw(q), 0.0, A.add)
-        mm(vw("pQ", 0, 128), vw("q16"), vw("I16"))
-        if t:
-            ts(vw("n1"), vw("pT", 256, 264), -16.0, A.mult, vw("c16"), A.add)
-        else:
-            mm(vw("pT", 264, 272), vw("on32"), vw("lim8"))
-            copy(vw("limb"), vw("pT", 264, 272))
-            ts(vw("n1"), vw("pT", 256, 264), -16.0, A.mult)
-        ts(vw("n0"), vw("pT", 256, 264), 0.0, A.is_equal, -4194304.0, A.mult)
-        tt(vw("n2"), vw("n1"), vw("limb"), A.add)
-        tt(vw("thr"), vw("n2"), vw("n0"), A.add)
-        if t:
-            ts(vw("aa"), vw(v), 65535, A.bitwise_and)
-            copy(vw("aF"), vw("aa"))
-            mm(vw("pA", 0, 128), vw("aF"), vw("I32"))
-        else:
-            for m in range(16):
-                mm(vw("pA", m, 128, 16), vw("CB", m, 2048, 16), vw("bo8b"))
-        if t == VI - 1:
-            sums()
-        key = vw("pW", 0, 128)
-        scan(vw("sm"), vw("d0s"), key, A.mult, A.add)
-        scan(vw("mx"), vw("d0m"), key, A.add, A.max)
-        tt(vw("stp"), vw("sm", 15, 128, 16), vw("thr"), A.is_ge)
-        for w in range(8):
-            ts(vw("oh", 16 * w, 16 * w + 16), vw("mx", 16 * w, 16 * w + 16), vw("mx", 16 * w + 15, 16 * w + 16), A.is_equal, vw("stp", w, w + 1), A.mult)
-        scan(vw("pw"), vw("d0p"), vw("oh"), A.mult, A.max)
-        for w in range(8):
-            ts(vw("pr", 16 * w, 16 * w + 16), vw("pA", 16 * w, 16 * w + 16), vw("pw", 16 * w + 15, 16 * w + 16), A.mult)
+            masks(v)
+            rowsums(0, 64)
+            for e, a in (("v", 64), ("s", 80), ("v", 96), ("s", 112)):
+                xgath(e, "x", q, a, a + 16)
+            rowsums(64, 96)
+            ts(vw("eR"), vw(q), 0, A.is_equal)
+            ts(vw("q16"), vw(q), 16.0, A.add)
+            remedies(q)
+            measures(t)
+            rowsums(96, 128)
+            lists(t)
+            threshold()
+            decide()
+        sums(0, 12)
+        tt(vw("pr"), ind(vw("pw"), vw("LB")), vw("aP"), A.mult)
         ts(vw("bb"), vw("pr"), 32768, A.bitwise_and)
-        tt(vw("q2P"), vw("pQ", 0, 128), vw("bb"), A.subtract)
-        mm(vw("pL", 384, 512), vw("q2P"), vw("I16"))
-        copy(vw("q2u"), vw("pL", 384, 512))
-        xgath("s", "x2", "q2u", 64, 128, True)
-        ts(vw("e2"), vw("q2u"), 0, A.is_equal)
-        xgath("v", "x2", "q2u", 0, 64, True)
+        tt(vw("q2P"), vw("pB", 128, 256), vw("bb"), A.subtract)
+        mm(vw("pA", 128, 256), vw("q2P"), vw("Ib"))
+        sums(12, 17)
         if t == 0:
-            late_constants()
-        mm(vw("pL", 0, 128), vw("e2"), vw("cm"))
-        mm(vw("pL", 128, 256), vw("cm"), vw("e2"))
-        scan(vw("bs", 0, 1024), vw("d0b", 0, 1024), vw("x2", 0, 1024), A.add, A.max)
-        scan(vw("bs", 1024, 2048), vw("d0b", 1024, 2048), vw("x2", 1024, 2048), A.add, A.max)
+            mm(vw("pH", 0, 128), vw("aP"), vw("I32"), True, False)
+            mm(vw("pH", 0, 128), vw("I32th"), vw("wyb"), False, True)
+        ts(vw("q2u"), vw("pA", 128, 256), -16.0, A.add)
+        xgath("s", "x2", "q2u", 32, 64, 16.0, -2048.0)
+        xgath("v", "x2", "q2u", 0, 32, 16.0, -2048.0)
+        ts(vw("e2"), vw("q2u"), 0, A.is_equal)
+        xgath("s", "x2", "q2u", 96, 128, 16.0, -2048.0)
+        xgath("v", "x2", "q2u", 64, 96, 16.0, -2048.0)
+        for a, b in HV:
+            u = vw("pC", a, b)
+            for m in range(16):
+                mm(u, vw("Ib"), flat("x2", a, b, m), m == 0, False)
+            mm(u, vw("bo16"), vw("e2", a, b), False, True)
+        for a, b in HV:
+            scan(flat("bs", a, b), vw("d0b"), flat("x2", a, b), A.add, A.max)
         bl = vw("bs", 15, 2048, 16)
         ts(vw("lo"), bl, 0.0625, A.mult, 1280 - 0.46875, A.add)
-        ku = vw("pU", 0, 128)
-        mm(ku, vw("on", 0, 128, 1, 0, 1), vw("tie16", 0, 128, 1, 0, 1), True, False)
-        mm(ku, vw("e2"), vw("bo256"), False, False)
-        for m in range(16):
-            mm(ku, vw("x2", m, 2048, 16), vw("I16b"), False, False)
-        mm(ku, bl, vw("I16"), False, False)
-        mm(ku, vw("lo"), vw("Im16"), False, True)
-        ts(vw("eP"), vw("pL", 0, 128), -16.5, A.is_lt)
-        ts(vw("eQ"), vw("pL", 128, 256), -16.5, A.is_lt)
-        if t == VI - 1:
-            tsixteenth()
-        stopped()
+        act(vw("ti"), vw("pG", 0, 128), 0.0625)
         if t == 0:
-            act(vw("aP0"), vw("pA", 0, 128))
-        ts(vw("u1"), ku, 1.0 / 4096, A.mult, 1156.5 + 1.0 / 8192, A.add)
-        mm(vw("pS", 128, 256), vw("u1"), vw("I16"))
-        for j in range(16):
-            act(vw("vf", j, 2048, 16), vw("pS", 128, 256), -1.0, 1279.0)
-        scan(vw("mk"), vw("d0m"), ku, A.add, A.max)
-        kk = vw("mk", 15, 128, 16)
-        ts(vw("zi"), kk, 0.0625, A.mult, -0.46875, A.add)
-        ts(vw("r16"), vw("zi"), 16.0, A.mult)
-        for w in range(8):
-            ts(vw("ok", 16 * w, 16 * w + 16), vw("m15"), vw("r16", w, w + 1), A.add, vw("mk", 16 * w + 15, 16 * w + 16), A.is_equal)
-        tt(vw("pk"), vw("ok"), vw("pQ", 0, 128), A.mult)
-        scan(vw("sk"), vw("d0s"), vw("pk"), A.mult, A.add)
-        for w in range(8):
-            ts(vw("AL", 16 * w, 16 * w + 16), vw("m16"), vw("sk", 16 * w + 15, 16 * w + 16), A.mult)
-        mm(vw("pL", 256, 264), vw("AL"), vw("bo8h"))
-        copy(vw("lk"), vw("pL", 256, 264))
-        copy(vw("cd"), ind(vw("R"), vw("lk")))
-        spread()
-        mm(vw("pA", 256, 384), vw("ok"), vw("I16"))
-        if t == 0:
-            mm(vw("pA", 384, 512), vw("aP0"), vw("I32"))
-        for a, b in ((0, 64), (64, 96), (96, 128)):
-            d = vw("mn", 16 * a, 16 * b)
-            tt(d, ind(vw("X", 16, 16 + D), vw("cd", a, b)), vw("vf", 16 * a, 16 * b), A.subtract)
-            act(vw("xc", 16 * a, 16 * b), d, 1.0, 0.0, F.Abs)
-            for j in range(16):
-                mm(vw("pS", j, 128, 16, a, b), vw("xc", 16 * a + j, 16 * b, 16), vw("wm16"))
-        if t == 0:
-            tt(vw("aF"), vw("pA", 384, 512), vw("fil"), A.mult)
-            ts(vw("w0"), vw("wy0"), 65536.0, A.mult)
-            tt(vw("v0"), vw("aF"), vw("w0"), A.add)
-        ts(vw("aM"), vw("aF"), vw("m64"), A.add)
-        tt(vw("oka"), vw("pA", 256, 384), vw("aM"), A.mult)
-        ts(vw("cd16"), vw("cd"), 16.0, A.add)
-        ts(vw("fR"), vw("q2u"), 0, A.is_gt)
-        tt(vw("vv"), vw(v), vw("fR"), A.mult)
-        ts(vw("q2h"), vw("q2u"), 0.0, A.add)
-        equal()
-        mm(vw("pQ", 128, 256), vw("cd16"), vw("I16"))
-        for w in range(8):
-            mm(vw("pL", 272 + w, 273 + w), vw("eq", 128 * w, 128 * w + 128), vw("on", 0, 1))
-        mm(vw("pA", 128, 256), vw("bo32"), vw("oka"), True, False)
-        mm(vw("pA", 128, 256), vw("I32"), vw("bit"), False, True)
+            act(vw("v0"), vw("pH", 0, 128))
+            masks("v0")
+        act(vw("Uh"), vw("pC", 0, 128), 0.0625)
+        ku = vw("pD", 0, 128)
+        mm(ku, row("on"), row("tie16"), True, False)
+        mm(ku, bl, vw("Ib"), False, False)
+        mm(vw("pE", 0, 128), vw("Uh"), vw("Ib"))
+        mm(ku, vw("lo"), vw("Im16"), False, False)
+        mm(ku, vw("Uh"), vw("I256"), False, True)
+        act(vw("cP"), vw("pE", 0, 128), -0.0625, 1227.46875)
+        tt(vw("pq"), vw("pB", 256, 384), vw("oh"), A.mult)
+        scan(vw("sq"), vw("d0s"), vw("pq"), A.mult, A.add)
 
-        def send(k):
-            src = "%so%d" % (k, t + 1)
-            lowd = T.cores[(rank + STRIDE[0]) % NR]
-            hid = relay_of(core, T.cores[(rank + STRIDE[1]) % NR], topo)
-            r1, p1 = topo.addr(lowd, core)
-            r2, p2 = topo.addr(hid, core)
-            tr = [RemoteDMATransfer(dst_ids=[DstId(rid=r1, pnc=p1)], dma_engine_mask=bits(topo, core, lowd, 8, False), remote_sem=T.sem["%sL%d" % (k, t + 1)],
-                                    src=T[src][:, 0:H], dst=T["%s%d" % (k, t + 1)][:, 0:H]),
-                  RemoteDMATransfer(dst_ids=[DstId(rid=r2, pnc=p2)], dma_engine_mask=bits(topo, core, hid, 8, True), remote_sem=T.sem["r%s%d" % (k, t + 1)],
-                                    src=T[src][:, H:L], dst=T["r%s%d" % (k, t + 1)][:, :])]
-            deps("g", [], [vw(src)])
-            g.remote_dma_fused(tr, local_sem=T.sem["loc"])
-            cnt["loc"] = cnt.get("loc", 0) + 16
-        if t == VI - 1:
+        def spread(n):
+            p = vw("pF" if n % 2 == 0 else "pE")
+            mm(p, vw("cP", 0, 128, 1, 32 * n, 32 * n + 32), vw("E", 0, 512, 1, 32 * n, 32 * n + 32))
+            act(flat("vf", 32 * n, 32 * n + 32), p, 1.0, -1100.0)
+        scan(vw("mk"), vw("d0m"), ku, A.add, A.max)
+        spread(0)
+        ts(vw("r8"), last("mk"), 15, A.bitwise_and)
+        tt(vw("AL"), ind(vw("r8"), vw("L8")), vw("m16"), A.mult)
+        mm(vw("pA", 256, 264), vw("m16"), vw("bo8k"), True, False)
+        mm(vw("pA", 256, 264), vw("AL"), vw("bo8n"), False, True)
+        copy(vw("lk"), vw("pA", 256, 264))
+        copy(vw("cd"), ind(vw("RA"), vw("lk")))
+        spread(1)
+        mm(vw("pC", 128, 256), vw("e2"), vw("cm"))
+        mm(vw("pC", 256, 384), vw("cm"), vw("e2"))
+        sc = vw("pD", 128, 256)
+        mm(sc, row("on"), row("m15"), True, False)
+
+        def piece(n):
+            a, b = 32 * n, 32 * n + 32
+            tt(flat("mn", a, b), ind(XG, vw("cd", a, b)), flat("vf", a, b), A.subtract)
+
+        def score(n):
+            a, b = 32 * n, 32 * n + 32
+            act(flat("xc", a, b), flat("mn", a, b), 1.0, 0.0, F.Abs)
+            for j in range(16):
+                mm(vw("pD", 128 + j, 256, 16, a, b), flat("xc", a, b, j), vw("wm16"), False, j == 15)
+        piece(0)
+        tt(vw("ok"), ind(vw("r8"), vw("L8")), vw("m15"), A.is_equal)
+        ts(vw("cd16"), vw("cd"), 0.0, A.add)
+        ts(vw("q2h"), vw("q2u"), 0.0, A.add)
+        act(vw("y16"), last("sq"))
+        spread(2)
+        mm(vw("pH", 0, 128, 1, 0, 8), vw("y16"), vw("Ib"))
+        piece(1)
+        act(vw("yT", 0, 128, 1, 0, 8), vw("pH", 0, 128, 1, 0, 8))
+        spread(3)
+        score(0)
+        mm(vw("pB", 256, 384), vw("ok"), vw("Ib"))
+        mm(vw("pB", 384, 512), vw("cd16"), vw("Dm"))
+        for w in range(8):
+            mm(vw("pG" if w < 4 else "pH", 128 * (w % 4), 128 * (w % 4) + 128), vw("sl8", 128 * w, 128 * w + 128, 1, 0, 8), vw("yT", 0, 128, 1, 0, 8))
+        piece(2)
+        score(1)
+        act(vw("e0"), vw("pC", 128, 384), 1.0, 17.0, F.Relu)
+        act(vw("e1"), vw("e0"), -1.0, 1.0, F.Relu)
+        eP, eQ = vw("e1", 0, 128), vw("e1", 128, 256)
+        nv = vw("pB", 128, 256)
+        if not end:
+            mm(nv, row("pwr"), row("on"), True, False)
+            mm(nv, vw("Im32"), vw(v), False, False)
+        piece(3)
+        score(2)
+        score(3)
+        if not end:
+            tt(vw("oka"), vw("pB", 256, 384), vw("aM"), A.mult)
+            mm(nv, vw("bo32"), vw("oka"), False, True)
+            equal(0, 3)
+            tt(vw("t3"), nv, eQ, A.mult)
+            tt(vw("vo%d" % (t + 1)), vw(v), vw("t3"), A.add)
+            send("v", t + 1)
+        else:
+            equal(0, 8)
+            weigh(0, 8)
+            ts(vw("okb"), vw("pB", 256, 384), vw("ac"), A.mult)
+            dedupe()
+            mm(nv, vw("bo"), vw("okb"))
+            ts(vw("fR"), vw("q2u"), 0, A.is_gt, 32.0, A.mult)
+            update()
+            store(T.yx[:, :], vw("X", X0, X0 + D), "st0")
+        scan(vw("ms"), vw("d0m"), sc, A.add, A.max)
+        copy(vw("mx8"), last("ms"))
+        tt(vw("oj"), ind(vw("mx8"), vw("L8")), vw("ms"), A.is_equal)
+        tt(vw("pn"), vw("pB", 384, 512), vw("oj"), A.mult)
+        scan(vw("sn"), vw("d0s"), vw("pn"), A.mult, A.add)
+        tt(vw("AN"), ind(vw("sn"), vw("LB")), eP, A.mult)
+        nq = vw("pA", 384, 512)
+        mm(nq, vw("Ib"), vw("q2h"), True, False)
+        mm(nq, vw("AN"), vw("Ib"), False, True)
+        if not end:
+            copy(vw("qo%d" % (t + 1)), nq)
+            send("q", t + 1)
+            equal(3, 8)
+            weigh(0, 8)
+            stops()
             dedupe()
             update()
-            scatter()
-            store(T.yx[:, :], vw("X", 16, 16 + D), "st0")
-        tt(vw("ky"), vw("pS", 0, 128), vw("tief"), A.add)
-        scan(vw("ms"), vw("d0m"), vw("ky"), A.add, A.max)
-        for w in range(8):
-            ts(vw("oj", 16 * w, 16 * w + 16), vw("ky", 16 * w, 16 * w + 16), vw("ms", 16 * w + 15, 16 * w + 16), A.is_equal)
-        tt(vw("pn"), vw("oj"), vw("pQ", 128, 256), A.mult)
-        scan(vw("sn"), vw("d0s"), vw("pn"), A.mult, A.add)
-        for w in range(8):
-            ts(vw("AN", 16 * w, 16 * w + 16), vw("eP", 16 * w, 16 * w + 16), vw("sn", 16 * w + 15, 16 * w + 16), A.mult)
-        nq = vw("pL", 384, 512)
-        mm(nq, vw("I16"), vw("q2h"), True, False)
-        mm(nq, vw("AN"), vw("I16"), False, True)
-        if t < VI - 1:
-            copy(vw("qo%d" % (t + 1)), nq)
-            send("q")
         else:
+            tt(vw("fr"), vw(v), vw("a2"), A.subtract)
             ts(vw("yo"), nq, 0.0, A.is_equal, float(16 + D), A.mult)
             tt(vw("yo"), vw("yo"), nq, A.add)
             ts(vw("yt"), vw("yo"), -16.0, A.add)
             store(T.yp[:, :], vw("yt"), "st2")
-        tt(vw("t3"), vw("pA", 128, 256), vw("eQ"), A.mult)
-        tt(vw("vo%d" % (t + 1) if t < VI - 1 else "vI"), vw("vv"), vw("t3"), A.add)
-        if t < VI - 1:
-            send("v")
-            sums()
-            dedupe()
-            stops()
-            tsixteenth()
-            update()
-            scatter()
-        else:
-            ts(vw("bb"), vw("vI"), 16, A.arith_shift_right)
-            copy(vw("yw"), vw("bb"))
-            store(T.yq[:, :], vw("yw"), "st1")
+            tt(vw("fr"), vw("fr"), vw("fR"), A.mult)
+            tt(vw("t3"), nv, eQ, A.mult)
+            tt(vw("yw"), vw("fr"), vw("t3"), A.add)
+            store(T.yq[:, :], vw("yw"), "st1", "s")
     for s in SEMAPHORES:
         if cnt.get(s):
             g.wait_ge(T.sem[s], cnt[s])

@@ -16,7 +16,7 @@ SB = {
     "kI": (1, i32), "aI": (1, i32), "gI": (1, i32), "hI": (1, i32), "kc": (1, f32), "ac": (1, f32), "gc": (1, f32), "hc": (1, f32),
     "a16": (1, f32), "a32": (1, f32), "c14": (1, f32), "c15": (1, f32), "n15": (1, f32), "ndum": (1, f32), "dum": (1, f32), "b16p": (1, f32),
     "wI": (256, b16), "dl": (256, b16), "Kc": (256, b16), "K": (256, b16), "cid": (144, f32), "Z": (144, b16), "g8": (8, f32),
-    "I32": (128, f32), "Im32": (128, f32), "Ib": (128, b16), "I256": (128, b16), "Im16": (128, b16), "ImQ": (128, b16), "I32th": (128, b16),
+    "I32": (128, f32), "Im32": (128, f32), "Ib": (128, b16), "I256": (128, b16), "Im16": (128, b16), "ImQ": (128, b16), "IpQ": (128, b16), "I32th": (128, b16),
     "bo": (128, b16), "bo32": (128, f32), "bo16": (128, b16), "Dm": (128, b16), "cm": (128, b16),
     "bo8": (8, b16), "bo8n": (8, b16), "wm16": (8, b16), "bo8b": (8, b16), "bo8m": (8, b16), "bo8d": (8, h16), "bo8k": (8, h16),
     "on": (128, b16), "on32": (128, f32), "m15": (128, b16), "tie16": (128, b16), "m16": (128, b16),
@@ -314,6 +314,9 @@ def member(g, core, rank, T, topo):
         sel(vw(n), [[-16, 8], [0, 16]], A.is_ge, 0.0, 0, 1)
         sel(vw(n), [[16, 8], [0, 16]], A.is_ge, 0.0, 15, -1)
     iota(vw("eI"), [[1, 32], [0, 16]], 0, 0)
+    for n, z in (("I32th", 1.0 / 32), ("Im32", -1.0)):
+        gfill(vw(n), 128, 0)
+        sel(vw(n), [[1, 128]], A.not_equal, z, 0, -1)
     gfill(vw("d0b"), 1024, 1)
     sel(vw("d0b"), [[0, 64], [1, 16]], A.not_equal, -8192.0, 0, 0)
     gfill(vw("sl8", 0, 1024, 1, 0, 8), 1024, 1)
@@ -338,9 +341,8 @@ def member(g, core, rank, T, topo):
         for m in range(16):
             mm(vw("pA", m, 128, 16, a, b), flat("x", a, b, m), vw("bo8"))
 
-    def remedies(q):
-        for a, b in HV:
-            gath("s", flat("RA", a, b), vw("R"), vw(q, a, b), 1.0, 16.0)
+    def remedies(q, a, b):
+        gath("s", flat("RA", a, b), vw("R"), vw(q, a, b), 1.0, 16.0)
 
     ts(vw("Z"), vw("cid"), vw("kc"), A.is_equal, vw("c15"), A.mult)
     ts(vw("Ib"), vw("cid", 0, 128), vw("kc"), A.is_equal)
@@ -381,7 +383,7 @@ def member(g, core, rank, T, topo):
     act(vw("wm16"), vw("bo8"), -16.0)
     act(vw("lim8"), vw("I32", 0, 128, 16), vw("limf"))
     act(vw("q16"), vw("dr0"), 1.0, 32.0)
-    remedies("q0")
+    remedies("q0", 0, 80)
     convd("lu4", 0)
     ts(vw("bo8b"), vw("bo8m"), vw("pG", 0, 1), A.mult)
     ts(vw("m16"), vw("wI", 0, 128), vw("ac"), A.is_equal)
@@ -399,14 +401,13 @@ def member(g, core, rank, T, topo):
         act(vw("bo8k"), vw("bo8"), vw("b16p"))
         act(vw("bo8n"), vw("bo8"), -1.0)
         act(vw("wyb"), vw("wy0"))
-        act(vw("I32th"), vw("Ib"), 1.0 / 32)
+        act(vw("a32"), vw("ac"), 1.0 / 32)
 
     def last_constants():
-        act(vw("Im32"), vw("Ib"), -1.0)
-        act(vw("a32"), vw("ac"), 1.0 / 32)
         act(vw("dum"), vw("kc"), 1.0, float(XS))
         act(vw("ndum"), vw("kc"), -1.0, -float(XS))
         act(vw("bo8d"), vw("bo8"), vw("dum"))
+        act(vw("IpQ"), vw("Ib"), float(16 + D))
 
     def measures(t):
         mm(vw("pB", 0, 8), vw("eR"), vw("bo8"))
@@ -439,10 +440,11 @@ def member(g, core, rank, T, topo):
             else:
                 mm(vw("pG", 0, 128), vw("bo"), vw("eR"), False, True)
 
-    def masks(v):
+    def masks(v, end):
         act(vw("a1"), vw(v), 1.0, 8388608.0)
         act(vw("a2"), vw("a1"), 1.0, -8388608.0)
-        act(vw("aM"), vw("a2"), 1.0, vw("a32"))
+        if not end:
+            act(vw("aM"), vw("a2"), 1.0, vw("a32"))
 
     measures(0)
     lists(0)
@@ -468,7 +470,12 @@ def member(g, core, rank, T, topo):
     ts(vw("wt"), vw("pH", 0, 1), 2.5, A.mult)
     decide()
     act(vw("aP"), an)
-    last_constants()
+    remedies("q0", 80, 128)
+    nv = vw("pH", 128, 256)
+
+    def opened(v):
+        mm(nv, row("pwr"), row("on"), True, False)
+        mm(nv, vw("Im32"), vw(v), False, False)
 
     def equal(lo, hi):
         for w in range(lo, hi):
@@ -525,36 +532,45 @@ def member(g, core, rank, T, topo):
                 snap[(s, 8)] = {}
                 recs.setdefault("%s%d" % (k, t), []).append((vw("%s%d" % (k, t), *HV[h]), True, (s, 8), "remote"))
             mm(an, vw(v), vw("I32"))
-            act(vw("aP"), an)
+            if not end:
+                opened(v)
             xgath("v", "x", q, 0, 32)
             xgath("s", "x", q, 32, 64)
-            masks(v)
             rowsums(0, 64)
+            remedies(q, 0, 32)
+            act(vw("aP"), an)
+            ts(vw("eR"), vw(q), 0, A.is_equal)
+            measures(t)
             for e, a in (("v", 64), ("s", 80), ("v", 96), ("s", 112)):
                 xgath(e, "x", q, a, a + 16)
             rowsums(64, 96)
-            ts(vw("eR"), vw(q), 0, A.is_equal)
             ts(vw("q16"), vw(q), 16.0, A.add)
-            remedies(q)
-            measures(t)
+            remedies(q, 32, 128)
+            masks(v, end)
             rowsums(96, 128)
-            lists(t)
             threshold()
+            lists(t)
             decide()
         sums(0, 12)
         tt(vw("pr"), ind(vw("pw"), vw("LB")), vw("aP"), A.mult)
         ts(vw("bb"), vw("pr"), 32768, A.bitwise_and)
         tt(vw("q2P"), vw("pB", 128, 256), vw("bb"), A.subtract)
         mm(vw("pA", 128, 256), vw("q2P"), vw("Ib"))
+        tt(vw("pq"), vw("pB", 256, 384), vw("oh"), A.mult)
         sums(12, 17)
+        ts(vw("q2u"), vw("pA", 128, 256), -16.0, A.add)
+        xgath("s", "x2", "q2u", 32, 64, 16.0, -2048.0)
+        ts(vw("e2"), vw("q2u"), 0, A.is_equal)
+        xgath("v", "x2", "q2u", 0, 32, 16.0, -2048.0)
+        mm(vw("pF", 0, 128), vw("e2"), vw("cm"))
+        mm(vw("pF", 128, 256), vw("cm"), vw("e2"))
+        ku = vw("pD", 0, 128)
+        mm(ku, row("on"), row("tie16"), True, False)
         if t == 0:
             mm(vw("pH", 0, 128), vw("aP"), vw("I32"), True, False)
             mm(vw("pH", 0, 128), vw("I32th"), vw("wyb"), False, True)
-        ts(vw("q2u"), vw("pA", 128, 256), -16.0, A.add)
-        xgath("s", "x2", "q2u", 32, 64, 16.0, -2048.0)
-        xgath("v", "x2", "q2u", 0, 32, 16.0, -2048.0)
-        ts(vw("e2"), vw("q2u"), 0, A.is_equal)
         xgath("s", "x2", "q2u", 96, 128, 16.0, -2048.0)
+        scan(vw("sq"), vw("d0s"), vw("pq"), A.mult, A.add)
         xgath("v", "x2", "q2u", 64, 96, 16.0, -2048.0)
         for a, b in HV:
             u = vw("pC", a, b)
@@ -565,20 +581,25 @@ def member(g, core, rank, T, topo):
             scan(flat("bs", a, b), vw("d0b"), flat("x2", a, b), A.add, A.max)
         bl = vw("bs", 15, 2048, 16)
         ts(vw("lo"), bl, 0.0625, A.mult, 1280 - 0.46875, A.add)
-        act(vw("ti"), vw("pG", 0, 128), 0.0625)
+        ts(vw("q2h"), vw("q2u"), 0.0, A.add)
+        act(vw("y16"), last("sq"))
+        act(vw("e0"), vw("pF", 0, 256), 1.0, 17.0, F.Relu)
+        act(vw("e1"), vw("e0"), -1.0, 1.0, F.Relu)
+        eP, eQ = vw("e1", 0, 128), vw("e1", 128, 256)
         if t == 0:
             act(vw("v0"), vw("pH", 0, 128))
-            masks("v0")
-        act(vw("Uh"), vw("pC", 0, 128), 0.0625)
-        ku = vw("pD", 0, 128)
-        mm(ku, row("on"), row("tie16"), True, False)
+        act(vw("ti"), vw("pG", 0, 128), 0.0625)
+        ts(vw("Uh"), vw("pC", 0, 128), 0.0625, A.mult)
+        yT = vw("pG", 128, 256, 1, 0, 8)
         mm(ku, bl, vw("Ib"), False, False)
-        mm(vw("pE", 0, 128), vw("Uh"), vw("Ib"))
         mm(ku, vw("lo"), vw("Im16"), False, False)
+        mm(vw("pE", 0, 128), vw("Uh"), vw("Ib"))
         mm(ku, vw("Uh"), vw("I256"), False, True)
+        mm(yT, vw("y16"), vw("Ib"))
+        if t == 0:
+            masks(v, end)
         act(vw("cP"), vw("pE", 0, 128), -0.0625, 1227.46875)
-        tt(vw("pq"), vw("pB", 256, 384), vw("oh"), A.mult)
-        scan(vw("sq"), vw("d0s"), vw("pq"), A.mult, A.add)
+        act(vw("yT", 0, 128, 1, 0, 8), yT)
 
         def spread(n):
             p = vw("pF" if n % 2 == 0 else "pE")
@@ -590,13 +611,12 @@ def member(g, core, rank, T, topo):
         tt(vw("AL"), ind(vw("r8"), vw("L8")), vw("m16"), A.mult)
         mm(vw("pA", 256, 264), vw("m16"), vw("bo8k"), True, False)
         mm(vw("pA", 256, 264), vw("AL"), vw("bo8n"), False, True)
+        tt(vw("ok"), ind(vw("r8"), vw("L8")), vw("m15"), A.is_equal)
         copy(vw("lk"), vw("pA", 256, 264))
         copy(vw("cd"), ind(vw("RA"), vw("lk")))
         spread(1)
-        mm(vw("pC", 128, 256), vw("e2"), vw("cm"))
-        mm(vw("pC", 256, 384), vw("cm"), vw("e2"))
+        spread(2)
         sc = vw("pD", 128, 256)
-        mm(sc, row("on"), row("m15"), True, False)
 
         def piece(n):
             a, b = 32 * n, 32 * n + 32
@@ -607,76 +627,86 @@ def member(g, core, rank, T, topo):
             act(flat("xc", a, b), flat("mn", a, b), 1.0, 0.0, F.Abs)
             for j in range(16):
                 mm(vw("pD", 128 + j, 256, 16, a, b), flat("xc", a, b, j), vw("wm16"), False, j == 15)
-        piece(0)
-        tt(vw("ok"), ind(vw("r8"), vw("L8")), vw("m15"), A.is_equal)
-        ts(vw("cd16"), vw("cd"), 0.0, A.add)
-        ts(vw("q2h"), vw("q2u"), 0.0, A.add)
-        act(vw("y16"), last("sq"))
-        spread(2)
-        mm(vw("pH", 0, 128, 1, 0, 8), vw("y16"), vw("Ib"))
-        piece(1)
-        act(vw("yT", 0, 128, 1, 0, 8), vw("pH", 0, 128, 1, 0, 8))
-        spread(3)
-        score(0)
+
+        def shown(lo, hi):
+            for w in range(lo, hi):
+                mm(vw("pG" if w < 4 else "pH", 128 * (w % 4), 128 * (w % 4) + 128), vw("sl8", 128 * w, 128 * w + 128, 1, 0, 8), vw("yT", 0, 128, 1, 0, 8))
+
+        def carried():
+            tt(vw("t3"), nv, eQ, A.mult)
+            tt(vw("vo%d" % (t + 1)), vw(v), vw("t3"), A.add)
+            send("v", t + 1)
+        nq = vw("pA", 384, 512)
         mm(vw("pB", 256, 384), vw("ok"), vw("Ib"))
-        mm(vw("pB", 384, 512), vw("cd16"), vw("Dm"))
-        for w in range(8):
-            mm(vw("pG" if w < 4 else "pH", 128 * (w % 4), 128 * (w % 4) + 128), vw("sl8", 128 * w, 128 * w + 128, 1, 0, 8), vw("yT", 0, 128, 1, 0, 8))
-        piece(2)
-        score(1)
-        act(vw("e0"), vw("pC", 128, 384), 1.0, 17.0, F.Relu)
-        act(vw("e1"), vw("e0"), -1.0, 1.0, F.Relu)
-        eP, eQ = vw("e1", 0, 128), vw("e1", 128, 256)
-        nv = vw("pB", 128, 256)
+        piece(0)
+        ts(vw("cd16"), vw("cd"), 0.0, A.add)
         if not end:
-            mm(nv, row("pwr"), row("on"), True, False)
-            mm(nv, vw("Im32"), vw(v), False, False)
+            tt(vw("oka"), vw("pB", 256, 384), vw("aM"), A.mult)
+        else:
+            ts(vw("okb"), vw("pB", 256, 384), vw("ac"), A.mult)
+        if t == 0:
+            opened(v)
+            mm(nv, vw("bo32"), vw("oka"), False, True)
+        spread(3)
+        piece(1)
+        if t == 0:
+            carried()
+        mm(sc, row("on"), row("m15"), True, False)
+        shown(0, 4)
+        if end:
+            mm(vw("pB", 128, 256), vw("bo"), vw("okb"))
+            shown(4, 8)
+        elif t:
+            mm(nv, vw("bo32"), vw("oka"), False, True)
+        score(0)
+        piece(2)
+        mm(vw("pB", 384, 512), vw("cd16"), vw("Dm"))
+        score(1)
         piece(3)
         score(2)
         score(3)
         if not end:
-            tt(vw("oka"), vw("pB", 256, 384), vw("aM"), A.mult)
-            mm(nv, vw("bo32"), vw("oka"), False, True)
-            equal(0, 3)
-            tt(vw("t3"), nv, eQ, A.mult)
-            tt(vw("vo%d" % (t + 1)), vw(v), vw("t3"), A.add)
-            send("v", t + 1)
+            if t:
+                carried()
+            equal(0, 4)
+            shown(4, 8)
         else:
             equal(0, 8)
             weigh(0, 8)
-            ts(vw("okb"), vw("pB", 256, 384), vw("ac"), A.mult)
+            tt(vw("fr"), vw(v), vw("a2"), A.subtract)
             dedupe()
-            mm(nv, vw("bo"), vw("okb"))
             ts(vw("fR"), vw("q2u"), 0, A.is_gt, 32.0, A.mult)
             update()
             store(T.yx[:, :], vw("X", X0, X0 + D), "st0")
+            mm(nq, vw("ImQ"), eQ, True, False)
+            mm(nq, vw("IpQ"), vw("e2"), False, False)
         scan(vw("ms"), vw("d0m"), sc, A.add, A.max)
         copy(vw("mx8"), last("ms"))
         tt(vw("oj"), ind(vw("mx8"), vw("L8")), vw("ms"), A.is_equal)
         tt(vw("pn"), vw("pB", 384, 512), vw("oj"), A.mult)
         scan(vw("sn"), vw("d0s"), vw("pn"), A.mult, A.add)
         tt(vw("AN"), ind(vw("sn"), vw("LB")), eP, A.mult)
-        nq = vw("pA", 384, 512)
-        mm(nq, vw("Ib"), vw("q2h"), True, False)
+        mm(nq, vw("Ib"), vw("q2h"), not end, False)
         mm(nq, vw("AN"), vw("Ib"), False, True)
         if not end:
+            equal(4, 6)
             copy(vw("qo%d" % (t + 1)), nq)
             send("q", t + 1)
-            equal(3, 8)
-            weigh(0, 8)
+            weigh(0, 6)
+            equal(6, 8)
+            weigh(6, 8)
+            if t == 0:
+                last_constants()
             stops()
             dedupe()
             update()
         else:
-            tt(vw("fr"), vw(v), vw("a2"), A.subtract)
-            ts(vw("yo"), nq, 0.0, A.is_equal, float(16 + D), A.mult)
-            tt(vw("yo"), vw("yo"), nq, A.add)
-            ts(vw("yt"), vw("yo"), -16.0, A.add)
-            store(T.yp[:, :], vw("yt"), "st2")
+            act(vw("yt"), nq, 1.0, -16.0)
+            store(T.yp[:, :], vw("yt"), "st2", "s")
             tt(vw("fr"), vw("fr"), vw("fR"), A.mult)
-            tt(vw("t3"), nv, eQ, A.mult)
+            tt(vw("t3"), vw("pB", 128, 256), eQ, A.mult)
             tt(vw("yw"), vw("fr"), vw("t3"), A.add)
-            store(T.yq[:, :], vw("yw"), "st1", "s")
+            store(T.yq[:, :], vw("yw"), "st1")
     for s in SEMAPHORES:
         if cnt.get(s):
             g.wait_ge(T.sem[s], cnt[s])

@@ -16,28 +16,29 @@ SB = {
     "kI": (1, i32), "aI": (1, i32), "gI": (1, i32), "hI": (1, i32), "kc": (1, f32), "ac": (1, f32), "gc": (1, f32), "hc": (1, f32),
     "a16": (1, f32), "a32": (1, f32), "c14": (1, f32), "c15": (1, f32), "n15": (1, f32), "ndum": (1, f32), "dum": (1, f32), "b16p": (1, f32),
     "wI": (256, b16), "dl": (256, b16), "Kc": (256, b16), "K": (256, b16), "cid": (144, f32), "Z": (144, b16), "g8": (8, f32),
-    "I32": (128, f32), "Im32": (128, f32), "Ib": (128, b16), "I256": (128, b16), "Im16": (128, b16), "ImQ": (128, b16), "IpQ": (128, b16), "I32th": (128, b16),
-    "bo": (128, b16), "bo32": (128, f32), "bo16": (128, b16), "Dm": (128, b16), "cm": (128, b16),
-    "bo8": (8, b16), "bo8n": (8, b16), "wm16": (8, b16), "bo8b": (8, b16), "bo8m": (8, b16), "bo8d": (8, h16), "bo8k": (8, h16),
+    "I32": (128, f32), "Im32": (128, f32), "Ib": (128, b16), "I256": (128, b16), "Im16": (128, b16), "ImQ": (128, b16), "IpQ": (128, b16),
+    "I32th": (128, b16), "bo": (128, b16), "bo32": (128, f32), "bo16": (128, b16), "Dm": (128, b16), "cm": (128, b16),
+    "bo8": (8, b16), "bo8n": (8, b16), "wm16": (8, b16), "wp16": (8, b16), "wm32": (8, b16),
+    "bo8b": (8, b16), "bo8m": (8, b16), "bo8d": (8, h16), "bo8k": (8, h16),
     "on": (128, b16), "on32": (128, f32), "m15": (128, b16), "tie16": (128, b16), "m16": (128, b16),
-    "d0s": (128, f32), "d0m": (128, f32), "d0p": (128, f32), "d0b": (1024, b16), "pwr": (128, b16), "hlf": (128, f32), "zer": (128, f32),
+    "d0s": (128, f32), "d0m": (128, f32), "d0p": (128, f32), "d0b": (512, b16), "pwr": (128, b16), "hlf": (128, f32), "zer": (128, f32),
     "wr": (128, b16), "wc": (1, b16), "wt": (1, f32), "eI": (512, b16), "E": (512, b16), "sl8": (1024, b16),
     "lbI": (8, i32), "l8I": (8, i32), "LB": (8, u16), "L8": (8, u16),
     "limf": (1, f32), "limc": (1, f32), "lim8": (8, f32), "pofI": (128, i32), "pofm": (128, h16),
     "WA": (2048, b16), "WB": (2048, b16), "lf": (128, f32), "l0": (128, u16),
     "lu1": (128, u16), "lu2": (128, u16), "lu4": (128, u16), "lu8": (128, u16), "wyb": (128, b16),
-    "x": (2048, b16), "x2": (2048, b16), "xc": (2048, b16), "mn": (2048, b16), "vf": (2048, b16), "bs": (2048, h16), "RA": (2048, f32),
-    "eR": (128, b16), "e2": (128, b16), "q16": (128, h16), "aP": (128, f32), "aM": (128, f32), "a1": (128, f32), "a2": (128, f32),
-    "n0": (8, f32), "thr": (8, f32), "mx": (128, f32), "sm": (128, f32), "nst": (8, b16), "mx8": (8, f32),
-    "oh": (128, f32), "pw": (128, f32), "pw8": (8, f32), "pr": (128, i32), "bb": (128, i32), "q2P": (128, h16), "q2u": (128, u16), "q2h": (128, h16),
+    "x": (2048, b16), "x2": (2048, b16), "xc": (2048, b16), "mn": (2048, b16), "vf": (1024, b16), "bs": (2048, h16), "RA": (2048, f32),
+    "eR": (128, b16), "e2": (128, b16), "q16": (128, h16), "aP": (128, f32), "aS": (128, f32), "aM": (128, f32), "a1": (128, f32), "a2": (128, f32),
+    "n0": (8, f32), "thr": (8, f32), "mx": (128, f32), "my": (128, f32), "sm": (128, f32), "stp": (8, f32), "stb": (8, b16), "pw8": (8, f32),
+    "oh": (128, f32), "pw": (128, f32), "pr": (128, i32), "bb": (128, i32), "q2P": (128, h16), "q2u": (128, u16), "q2h": (128, h16),
     "lo": (128, h16), "Uh": (128, h16), "cP": (128, h16), "e0": (256, f32), "e1": (256, b16),
     "mk": (128, i32), "r8": (8, i32), "ok": (128, b16), "AL": (128, h16), "lk": (8, u16),
     "cd": (128, u16), "cd16": (128, h16), "oka": (128, f32), "okb": (128, b16), "t3": (128, f32),
-    "ms": (128, f32), "oj": (128, f32), "pn": (128, f32), "sn": (128, f32), "AN": (128, h16),
+    "oj": (128, f32), "pn": (128, f32), "sn": (128, f32), "AN": (128, h16),
     "pq": (128, f32), "sq": (128, f32), "y8": (8, f32), "y16": (8, h16), "yT": (128, h16), "eq": (1024, b16),
     "du": (8, f32), "ya": (8, f32), "of": (8, f32), "AS": (128, h16), "ls": (8, u16),
     "ti": (128, f32), "xs": (128, f32), "xn": (128, i32), "cj": (8, f32), "cn": (1, f32), "cz": (1, h16), "cc": (1, f32),
-    "yt": (128, f32), "yo": (128, f32), "yw": (128, f32), "fR": (128, f32), "fr": (128, f32),
+    "yt": (128, f32), "yw": (128, f32), "fR": (128, f32), "fr": (128, f32),
 }
 ALONE = ("X", "R", "dr0", "wy0", "lmI", "yt", "yw")
 ALIAS, SCRATCH, _wide = {}, {}, {}
@@ -67,8 +68,8 @@ HV = ((0, 64), (64, 128))
 
 
 def relay_of(core, dst, topo):
-    c = [k for k in topo.cores_of(core) if k != core and topo.may_write(k, dst)]
-    return ([k for k in c if topo.die(k) == topo.die(core)] + c)[0]
+    c = [n for n in topo.cores_of(core) if n != core and topo.may_write(n, dst)]
+    return ([n for n in c if topo.die(n) == topo.die(core)] + c)[0]
 
 
 def bits(topo, src, dst, n, top):
@@ -91,13 +92,11 @@ def rank_program(g, core, T, topo):
 def relay(g, core, dst, T, topo):
     rid, pid = topo.addr(dst, core)
     m = bits(topo, core, dst, 8, False)
-    n = 0
     for t in range(1, VI):
         for k in ("v", "q"):
             g.wait_ge(T.sem["r%s%d" % (k, t)], 8)
             g.remote_dma(T["%s%d" % (k, t)][:, H:L], T["r%s%d" % (k, t)][:, :], T.sem["%sH%d" % (k, t)], T.sem["loc"], pid, rid, m)
-            n += 8
-    g.wait_ge(T.sem["loc"], n)
+    g.wait_ge(T.sem["loc"], 16 * (VI - 1))
 
 
 def member(g, core, rank, T, topo):
@@ -265,65 +264,64 @@ def member(g, core, rank, T, topo):
     iota(vw("pofI"), [[0, 2], [16, 64]], 0, 0, False)
     iota(vw("cid"), [[1, 144]], 0, 0)
     ts(vw("aI"), vw("kI"), 15, A.bitwise_and)
-    copy(vw("ac"), vw("aI"))
     copy(vw("kc"), vw("kI"))
-    ts(vw("c15"), vw("ac"), 15.0, A.is_equal)
-    ts(vw("c14"), vw("ac"), 14.0, A.is_equal, 2.0, A.mult)
-    ts(vw("a16"), vw("ac"), 16.0, A.mult)
-    ts(vw("K"), vw("wI"), vw("ac"), A.is_equal)
-    ts(vw("K", 15, 256, 16), vw("wI", 0, 16), 0.0, A.mult, vw("c14"), A.add)
-    fill(vw("K", 0, 256, 17), 0.0)
-    ts(vw("Kc"), vw("dl"), vw("c15"), A.mult)
-    ts(vw("l0"), vw("wy0"), vw("a16"), A.add)
+    ts(vw("gI"), vw("kI"), 4, A.arith_shift_right)
+    ts(vw("hI"), vw("kI"), 31, A.bitwise_and)
+    copy(vw("ac"), vw("aI"))
+    ts(vw("c15"), vw("aI"), 15.0, A.is_equal)
+    ts(vw("c14"), vw("aI"), 14.0, A.is_equal, 2.0, A.mult)
+    ts(vw("a16"), vw("aI"), 16.0, A.mult)
+    ts(vw("n15"), vw("aI"), 15.0, A.is_lt)
+    copy(vw("gc"), vw("gI"))
+    copy(vw("hc"), vw("hI"))
+    ts(vw("Kc"), vw("wI"), vw("ac"), A.is_equal)
+    ts(vw("Kc", 15, 256, 16), vw("wI", 0, 16), 0.0, A.mult, vw("c14"), A.add)
+    ts(vw("K"), vw("dl"), vw("c15"), A.mult)
+    fill(vw("Kc", 0, 256, 17), 0.0)
     tt(vw("K"), vw("K"), vw("Kc"), A.add)
-    gath("s", flat("WA", 64, 128), vw("K"), vw("l0", 64, 128))
-    ts(vw("q0"), vw("dr0"), 16.0, A.add)
+    ts(vw("l0"), vw("wy0"), vw("a16"), A.add)
     tt(vw("lf"), vw("wy0"), vw("pofI"), A.add)
-    copy(vw("lu1"), vw("lf"))
+    gath("s", flat("WA", 64, 128), vw("K"), vw("l0", 64, 128))
     gath("v", flat("WA", 0, 64), vw("K"), vw("l0", 0, 64))
     gfill(vw("X", 0, 16), 16, 0)
     gfill(vw("X", 16, 32), 16, -1)
     gfill(vw("X", X0 + D, XS), 16, -1)
-    gfill(vw("R", 0, 16), 16, -16, False)
-    gfill(vw("R", 16 + D, 32 + D), 16, -16, False)
     iota(vw("g8"), [[1, 8]], 0, 0)
+    gfill(vw("on32"), 128, 1)
+    gfill(vw("on"), 128, 1)
+    for n, c in (("d0p", 2), ("d0s", 1), ("d0m", 0), ("I32", 0), ("ImQ", 0), ("Dm", 0)):
+        gfill(vw(n), 128, c)
+    for n, z in (("d0p", 0.0), ("d0s", 0.0), ("d0m", -BIG)):
+        sel(vw(n), [[0, 8], [1, 16]], A.not_equal, z, 0, 0)
     iota(vw("lbI"), [[16, 8]], 15, 0, False)
     iota(vw("l8I"), [[1, 8]], 0, 0, False)
-    gfill(vw("on"), 128, 1)
-    gfill(vw("on32"), 128, 1)
-    for n, c, z in (("d0p", 2, 0.0), ("d0s", 1, 0.0), ("d0m", 0, -BIG)):
+    gfill(vw("R", 0, 16), 16, -16, False)
+    gfill(vw("R", 16 + D, 32 + D), 16, -16, False)
+    for n, z in (("I32", 1.0), ("ImQ", -float(16 + D)), ("Dm", 1.0)):
+        sel(vw(n), [[1, 128]], A.not_equal, z, 0, -1)
+    for n, c in (("bo32", 1), ("cm", 65), ("hlf", 0), ("zer", 0)):
         gfill(vw(n), 128, c)
-        sel(vw(n), [[0, 8], [1, 16]], A.not_equal, z, 0, 0)
-    for n, z in (("I32", 1.0), ("ImQ", -float(16 + D))):
-        gfill(vw(n), 128, 0)
-        sel(vw(n), [[1, 128]], A.not_equal, z, 0, -1)
-    iota(vw("m15"), [[0, 8], [-1, 16]], 15, 0)
-    iota(vw("tie16"), [[0, 8], [-16, 16]], 240, 0)
-    gfill(vw("X", XS, XW), 128, 0)
-    gfill(vw("zer"), 128, 0)
-    gfill(vw("hlf"), 128, 0)
-    sel(vw("hlf"), [[0, 128]], A.not_equal, 0.5, 0, 0)
-    gfill(vw("bo32"), 128, 1)
-    gfill(vw("cm"), 128, 65)
-    sel(vw("cm"), [[1, 128]], A.is_gt, 1.0, 0, -1)
-    sel(vw("cm"), [[1, 128]], A.not_equal, -31.0, 0, -1)
-    gfill(vw("Dm"), 128, 0)
-    sel(vw("Dm"), [[1, 128]], A.not_equal, 1.0, 0, -1)
     sel(vw("Dm"), [[1, 128]], A.not_equal, -1.0, 1, -1)
-    for n in ("bo32", "Dm", "cm"):
-        sel(vw(n), [[-16, 8], [0, 16]], A.is_ge, 0.0, 0, 1)
-        sel(vw(n), [[16, 8], [0, 16]], A.is_ge, 0.0, 15, -1)
+    sel(vw("cm"), [[1, 128]], A.is_gt, 1.0, 0, -1)
+    sel(vw("hlf"), [[0, 128]], A.not_equal, 0.5, 0, 0)
+    sel(vw("cm"), [[1, 128]], A.not_equal, -31.0, 0, -1)
+    for pat, base, cm in (([[-16, 8], [0, 16]], 0, 1), ([[16, 8], [0, 16]], 15, -1)):
+        for n in ("Dm", "bo32", "cm"):
+            sel(vw(n), pat, A.is_ge, 0.0, base, cm)
     iota(vw("eI"), [[1, 32], [0, 16]], 0, 0)
-    for n, z in (("I32th", 1.0 / 32), ("Im32", -1.0)):
-        gfill(vw(n), 128, 0)
-        sel(vw(n), [[1, 128]], A.not_equal, z, 0, -1)
-    gfill(vw("d0b"), 1024, 1)
-    sel(vw("d0b"), [[0, 64], [1, 16]], A.not_equal, -8192.0, 0, 0)
     gfill(vw("sl8", 0, 1024, 1, 0, 8), 1024, 1)
+    gfill(vw("d0b"), 512, 1)
     sel(vw("sl8", 0, 1024, 1, 0, 8), [[1, 8], [0, 128]], A.is_equal, 0.0, 0, -1)
+    sel(vw("d0b"), [[0, 32], [1, 16]], A.not_equal, -8192.0, 0, 0)
+    iota(vw("tie16"), [[0, 8], [-16, 16]], 240, 0)
+    iota(vw("m15"), [[0, 8], [-1, 16]], 15, 0)
+    gfill(vw("X", XS, XW), 128, 0)
 
-    def double(dst, src, lst, h):
-        tt(flat(dst, *HV[h]), ind(flat(src, *HV[h]), vw(lst, *HV[h])), flat("xc", *HV[h]), A.add)
+    def double(dst, src, lst, h, between):
+        lo, hi = HV[h]
+        tt(flat(dst, lo, hi - 16), ind(flat(src, lo, hi), vw(lst, lo, hi - 16)), flat("xc", lo, hi - 16), A.add)
+        between()
+        tt(flat(dst, hi - 16, hi), ind(flat(src, lo, hi), vw(lst, hi - 16, hi)), flat("xc", hi - 16, hi), A.add)
 
     def twin(src, h):
         act(flat("xc", *HV[h]), flat(src, *HV[h]))
@@ -344,72 +342,7 @@ def member(g, core, rank, T, topo):
     def remedies(q, a, b):
         gath("s", flat("RA", a, b), vw("R"), vw(q, a, b), 1.0, 16.0)
 
-    ts(vw("Z"), vw("cid"), vw("kc"), A.is_equal, vw("c15"), A.mult)
-    ts(vw("Ib"), vw("cid", 0, 128), vw("kc"), A.is_equal)
-    ts(vw("pofm"), vw("pofI"), vw("ac"), A.add)
-    copy(flat("xc", 0, 64), flat("WA", 0, 64))
-    twin("WA", 1)
-    xgath("s", "x", "q0", 0, 64)
-    double("WB", "WA", "lu1", 0)
-    conv("WB", 0)
-    twin("WB", 0)
-    xgath("s", "x", "q0", 64, 96)
-    ts(vw("gI"), vw("kI"), 4, A.arith_shift_right)
-    ts(vw("hI"), vw("kI"), 31, A.bitwise_and)
-    ts(vw("n15"), vw("ac"), 15.0, A.is_lt)
-    copy(vw("gc"), vw("gI"))
-    copy(vw("hc"), vw("hI"))
-    copy(vw("limf"), vw("lmI"))
-    ts(vw("bo8"), vw("g8"), vw("gc"), A.is_equal)
-    double("WB", "WA", "lu1", 1)
-    conv("WB", 1)
-    twin("WB", 1)
-    xgath("s", "x", "q0", 96, 128)
-    convd("lu2", 0)
-    scan(vw("pwr"), vw("d0p"), vw("on32"), A.mult, A.max)
-    double("WA", "WB", "lu2", 0)
-    mm(vw("pG", 0, 1), row("pwr"), row("on", 0, 1))
-    conv("WA", 0)
-    twin("WA", 0)
-    act(vw("bo8m"), vw("bo8"), vw("n15"))
-    act(vw("eR"), vw("dr0"), 1.0, -float(D - 1), F.Relu)
-    convd("lu2", 1)
-    copy(vw("LB"), vw("lbI"))
-    copy(vw("L8"), vw("l8I"))
-    double("WA", "WB", "lu2", 1)
-    conv("WA", 1)
-    twin("WA", 1)
-    rowsums(0, 128)
-    act(vw("wm16"), vw("bo8"), -16.0)
-    act(vw("lim8"), vw("I32", 0, 128, 16), vw("limf"))
-    act(vw("q16"), vw("dr0"), 1.0, 32.0)
-    remedies("q0", 0, 80)
-    convd("lu4", 0)
-    ts(vw("bo8b"), vw("bo8m"), vw("pG", 0, 1), A.mult)
-    ts(vw("m16"), vw("wI", 0, 128), vw("ac"), A.is_equal)
-    double("WB", "WA", "lu4", 0)
-    conv("WB", 0)
-    convd("lu4", 1)
-    double("WB", "WA", "lu4", 1)
-
-    def late_constants():
-        act(vw("bo"), vw("bo32"))
-        act(vw("bo16"), vw("bo32"), 16.0)
-        act(vw("I256"), vw("Ib"), 256.0)
-        act(vw("Im16"), vw("Ib"), -16.0)
-        act(vw("b16p"), vw("kc"), 16.0, 15.0)
-        act(vw("bo8k"), vw("bo8"), vw("b16p"))
-        act(vw("bo8n"), vw("bo8"), -1.0)
-        act(vw("wyb"), vw("wy0"))
-        act(vw("a32"), vw("ac"), 1.0 / 32)
-
-    def last_constants():
-        act(vw("dum"), vw("kc"), 1.0, float(XS))
-        act(vw("ndum"), vw("kc"), -1.0, -float(XS))
-        act(vw("bo8d"), vw("bo8"), vw("dum"))
-        act(vw("IpQ"), vw("Ib"), float(16 + D))
-
-    def measures(t):
+    def measures():
         mm(vw("pB", 0, 8), vw("eR"), vw("bo8"))
         mm(vw("pB", 8, 16), vw("eR"), vw("wm16"), True, False)
         mm(vw("pB", 8, 16), vw("on32"), vw("lim8"), False, True)
@@ -420,25 +353,10 @@ def member(g, core, rank, T, topo):
             mm(vw("pB", 128, 256), vw("eR"), vw("ImQ"), False, True)
         mm(vw("pB", 256, 384), vw("q16"), vw("Dm"))
 
-    def threshold():
-        ts(vw("n0"), vw("pB", 0, 8), BIG, A.mult, -1000.0, A.add)
-        tt(vw("thr"), vw("pB", 8, 16), vw("n0"), A.min)
-
-    def decide():
-        key = vw("pA", 0, 128)
-        scan(vw("sm"), vw("d0s"), key, A.mult, A.add)
-        scan(vw("mx"), vw("d0m"), key, A.add, A.max)
-        tt(vw("nst"), last("sm"), vw("thr"), A.is_lt)
-        tt(vw("mx8"), last("mx"), vw("nst"), A.add)
-        tt(vw("oh"), ind(vw("mx8"), vw("L8")), vw("mx"), A.is_equal)
-        scan(vw("pw"), vw("d0p"), vw("oh"), A.mult, A.max)
-
-    def sums(lo, hi):
-        for m in range(lo, hi):
-            if m < 16:
-                mm(vw("pG", 0, 128), vw("Ib"), flat("x", 0, 128, m), m == 0, False)
-            else:
-                mm(vw("pG", 0, 128), vw("bo"), vw("eR"), False, True)
+    def sums():
+        for m in range(16):
+            mm(vw("pD", 256, 384), vw("Ib"), flat("x", 0, 128, m), m == 0, False)
+        mm(vw("pD", 256, 384), vw("bo"), vw("eR"), False, True)
 
     def masks(v, end):
         act(vw("a1"), vw(v), 1.0, 8388608.0)
@@ -446,63 +364,115 @@ def member(g, core, rank, T, topo):
         if not end:
             act(vw("aM"), vw("a2"), 1.0, vw("a32"))
 
-    measures(0)
-    lists(0)
+    def decide(t):
+        key = vw("pA", 0, 128)
+        scan(vw("sm"), vw("d0s"), key, A.mult, A.add)
+        scan(vw("mx"), vw("d0m"), key, A.add, A.max)
+        scan(vw("my"), vw("d0m"), key, A.add, A.max)
+        tt(vw("stp"), last("sm"), vw("thr"), A.is_ge)
+        tt(vw("oh"), ind(vw("mx"), vw("LB")), vw("my"), A.is_equal)
+        if t:
+            tt(vw("aS"), ind(vw("stp"), vw("L8")), vw("aP"), A.mult)
+        scan(vw("pw"), vw("d0p"), vw("oh"), A.mult, A.max)
+        tt(vw("pq"), vw("pB", 256, 384), vw("oh"), A.mult)
+
+    copy(flat("xc", 0, 64), flat("WA", 0, 64))
+    copy(vw("lu1"), vw("lf"))
+    ts(vw("q0"), vw("dr0"), 16.0, A.add)
+    ts(vw("Z"), vw("cid"), vw("kc"), A.is_equal, vw("c15"), A.mult)
+    twin("WA", 1)
+    xgath("s", "x", "q0", 0, 64)
+
+    def first():
+        ts(vw("Ib"), vw("cid", 0, 128), vw("kc"), A.is_equal)
+        ts(vw("pofm"), vw("pofI"), vw("ac"), A.add)
+        copy(vw("limf"), vw("lmI"))
+        ts(vw("bo8"), vw("g8"), vw("gc"), A.is_equal)
+    double("WB", "WA", "lu1", 0, first)
+    conv("WB", 0)
+    twin("WB", 0)
+    xgath("s", "x", "q0", 64, 96)
+    double("WB", "WA", "lu1", 1, lambda: convd("lu2", 0))
     conv("WB", 1)
-    convd("lu8", 0)
+    twin("WB", 1)
+    xgath("s", "x", "q0", 96, 128)
+    scan(vw("pwr"), vw("d0p"), vw("on32"), A.mult, A.max)
+    double("WA", "WB", "lu2", 0, lambda: convd("lu2", 1))
+    mm(vw("pG", 0, 1), row("pwr"), row("on", 0, 1))
+    conv("WA", 0)
+    twin("WA", 0)
+    act(vw("bo8m"), vw("bo8"), vw("n15"))
+    act(vw("eR"), vw("dr0"), 1.0, -float(D - 1), F.Relu)
+    act(vw("wm16"), vw("bo8"), -16.0)
+    act(vw("lim8"), vw("I32", 0, 128, 16), vw("limf"))
+    act(vw("q16"), vw("dr0"), 1.0, 32.0)
+    double("WA", "WB", "lu2", 1, lambda: convd("lu4", 0))
+    conv("WA", 1)
+    twin("WA", 1)
+    rowsums(0, 128)
+    measures()
+    remedies("q0", 0, 112)
+    ts(vw("bo8b"), vw("bo8m"), vw("pG", 0, 1), A.mult)
+    copy(vw("LB"), vw("lbI"))
+    copy(vw("L8"), vw("l8I"))
+    double("WB", "WA", "lu4", 0, lambda: convd("lu4", 1))
+    conv("WB", 0)
+    ts(vw("n0"), vw("pB", 0, 8), BIG, A.mult, -1000.0, A.add)
+    double("WB", "WA", "lu4", 1, lambda: convd("lu8", 0))
+    conv("WB", 1)
     gath("s", flat("WA", 32, 64), flat("WB", 0, 64), vw("lu8", 32, 64))
+    tt(vw("thr"), vw("pB", 8, 16), vw("n0"), A.min)
     gath("v", flat("WA", 0, 32), flat("WB", 0, 64), vw("lu8", 0, 32))
-    threshold()
-    scan(row("wr"), row("hlf"), row("zer"), A.mult, A.add, 2.0 ** 64)
-    ts(vw("E"), vw("eI"), vw("hc"), A.is_equal)
-    mm(vw("pH", 0, 1), row("wr"), row("on", 0, 1))
+    lists(0)
     an = vw("pC", 384, 512)
     mm(an, row("on"), row("pwr"), True, False)
     for m in range(16):
         mm(vw("pC", 384 + m, 512, 16), flat("WB", 0, 128, m), vw("bo8b"), False, False)
     convd("lu8", 1)
-    gath("s", flat("WA", 96, 128), flat("WB", 64, 128), vw("lu8", 96, 128))
-    gath("v", flat("WA", 64, 96), flat("WB", 64, 128), vw("lu8", 64, 96))
+    scan(row("wr"), row("hlf"), row("zer"), A.mult, A.add, 2.0 ** 64)
+    ts(vw("m16"), vw("wI", 0, 128), vw("ac"), A.is_equal)
+    gath("s", flat("WA", 88, 128), flat("WB", 64, 128), vw("lu8", 88, 128))
+    gath("v", flat("WA", 64, 88), flat("WB", 64, 128), vw("lu8", 64, 88))
+    mm(vw("pH", 0, 1), row("wr"), row("on", 0, 1))
     for m in range(16):
         mm(vw("pC", 384 + m, 512, 16), flat("WA", 0, 128, m), vw("bo8b"), False, m == 15)
-    late_constants()
-    copy(vw("wc"), vw("pH", 0, 1))
-    ts(vw("wt"), vw("pH", 0, 1), 2.5, A.mult)
-    decide()
+    act(vw("bo"), vw("bo32"))
+    act(vw("wyb"), vw("wy0"))
+    act(vw("I32th"), vw("Ib"), 1.0 / 32)
+    act(vw("dum"), vw("kc"), 1.0, float(XS))
+    act(vw("b16p"), vw("kc"), 16.0, 15.0)
+    decide(0)
     act(vw("aP"), an)
-    remedies("q0", 80, 128)
-    nv = vw("pH", 128, 256)
+    mm(an, vw("aP"), vw("I32"), True, False)
+    mm(an, vw("I32th"), vw("wyb"), False, True)
+    remedies("q0", 112, 128)
+    act(vw("v0"), an)
 
-    def opened(v):
-        mm(nv, row("pwr"), row("on"), True, False)
-        mm(nv, vw("Im32"), vw(v), False, False)
+    def late_constants():
+        for n, src, c in (("bo16", "bo32", 16.0), ("I256", "Ib", 256.0), ("Im16", "Ib", -16.0), ("Im32", "Ib", -1.0), ("IpQ", "Ib", float(16 + D)),
+                          ("bo8k", "bo8", vw("b16p")), ("bo8d", "bo8", vw("dum")), ("bo8n", "bo8", -1.0), ("wp16", "bo8", 16.0), ("wm32", "bo8", -32.0),
+                          ("a32", "ac", 1.0 / 32), ("ndum", "dum", -1.0)):
+            act(vw(n), vw(src), c)
+
+    def shown():
+        act(vw("y16"), vw("y8"))
+        mm(vw("pE", 128, 256, 1, 0, 8), vw("y16"), vw("Ib"))
+        act(vw("yT", 0, 128, 1, 0, 8), vw("pE", 128, 256, 1, 0, 8))
+        for w in range(8):
+            mm(vw("pG" if w < 4 else "pH", 128 * (w % 4), 128 * (w % 4) + 128), vw("sl8", 128 * w, 128 * w + 128, 1, 0, 8), vw("yT", 0, 128, 1, 0, 8))
 
     def equal(lo, hi):
         for w in range(lo, hi):
             p = vw("pG" if w < 4 else "pH", 128 * (w % 4), 128 * (w % 4) + 128)
-            ts(vw("eq", 128 * w, 128 * w + 128), p, vw("sq", 16 * w + 15, 16 * w + 16), A.is_equal)
+            ts(vw("eq", 128 * w, 128 * w + 128), p, vw("y8", w, w + 1), A.is_equal)
 
-    def weigh(lo, hi):
-        for w in range(lo, hi):
-            mm(vw("pA", 272 + w, 273 + w), vw("eq", 128 * w, 128 * w + 128), vw("wc"))
-
-    def dedupe():
-        ts(vw("ya"), last("sq"), vw("ndum"), A.add)
-        ts(vw("du"), vw("pA", 272, 280), vw("wt"), A.is_lt)
-        tt(vw("of"), vw("du"), vw("ya"), A.mult)
-        tt(vw("AS"), ind(vw("of"), vw("L8")), vw("m16"), A.mult)
-        mm(vw("pA", 264, 272), vw("m16"), vw("bo8d"), True, False)
-        mm(vw("pA", 264, 272), vw("AS"), vw("bo8"), False, True)
-
-    def update():
-        copy(vw("ls"), vw("pA", 264, 272))
-        tt(vw("xs"), ind(vw("X"), vw("ls")), vw("ti"), A.add)
-        ts(vw("xn"), vw("xs"), 0.5, A.mult, -0.484375, A.add)
-        copy(ind(vw("X"), vw("ls")), vw("xn"))
+    def weigh():
+        for w in range(8):
+            mm(vw("pC", 256 + w, 257 + w), vw("eq", 128 * w, 128 * w + 128), vw("wc"))
 
     def stops():
-        mm(vw("pE", 0, 8), vw("on"), vw("nst"))
-        act(vw("cj"), vw("pE", 0, 8), -1.0, 35328.0, F.Identity, vw("cn"))
+        mm(vw("pE", 0, 8), vw("on"), vw("stb"))
+        act(vw("cj"), vw("pE", 0, 8), 1.0, 35200.0, F.Identity, vw("cn"))
         act(vw("cz"), vw("cn"), 1.0 / 256, -0.498046875)
         act(vw("cc"), vw("cz"), -256.0, vw("cn"))
         act(vw("limc"), vw("limf"), 1.0, vw("cc"))
@@ -532,181 +502,190 @@ def member(g, core, rank, T, topo):
                 snap[(s, 8)] = {}
                 recs.setdefault("%s%d" % (k, t), []).append((vw("%s%d" % (k, t), *HV[h]), True, (s, 8), "remote"))
             mm(an, vw(v), vw("I32"))
-            if not end:
-                opened(v)
             xgath("v", "x", q, 0, 32)
             xgath("s", "x", q, 32, 64)
+            act(vw("aP"), an)
             rowsums(0, 64)
             remedies(q, 0, 32)
-            act(vw("aP"), an)
             ts(vw("eR"), vw(q), 0, A.is_equal)
-            measures(t)
+            measures()
             for e, a in (("v", 64), ("s", 80), ("v", 96), ("s", 112)):
                 xgath(e, "x", q, a, a + 16)
             rowsums(64, 96)
             ts(vw("q16"), vw(q), 16.0, A.add)
+            ts(vw("n0"), vw("pB", 0, 8), BIG, A.mult, -1000.0, A.add)
             remedies(q, 32, 128)
-            masks(v, end)
             rowsums(96, 128)
-            threshold()
+            tt(vw("thr"), vw("pB", 8, 16), vw("n0"), A.min)
             lists(t)
-            decide()
-        sums(0, 12)
-        tt(vw("pr"), ind(vw("pw"), vw("LB")), vw("aP"), A.mult)
+            decide(t)
+        sums()
+        if t:
+            tt(vw("pr"), ind(vw("pw"), vw("LB")), vw("aS"), A.mult)
+            scan(vw("sq"), vw("d0s"), vw("pq"), A.mult, A.add)
+        else:
+            tt(vw("pw8"), last("pw"), vw("stp"), A.mult)
+            scan(vw("sq"), vw("d0s"), vw("pq"), A.mult, A.add)
+            copy(vw("wc"), vw("pH", 0, 1))
+            ts(vw("wt"), vw("pH", 0, 1), 2.5, A.mult)
+            tt(vw("pr"), ind(vw("pw8"), vw("L8")), vw("aP"), A.mult)
+            ts(vw("E"), vw("eI"), vw("hc"), A.is_equal)
         ts(vw("bb"), vw("pr"), 32768, A.bitwise_and)
+        tt(vw("y8"), last("sq"), vw("stp"), A.mult)
+        copy(vw("stb"), vw("stp"))
         tt(vw("q2P"), vw("pB", 128, 256), vw("bb"), A.subtract)
         mm(vw("pA", 128, 256), vw("q2P"), vw("Ib"))
-        tt(vw("pq"), vw("pB", 256, 384), vw("oh"), A.mult)
-        sums(12, 17)
+        if t == 0:
+            late_constants()
+        shown()
         ts(vw("q2u"), vw("pA", 128, 256), -16.0, A.add)
         xgath("s", "x2", "q2u", 32, 64, 16.0, -2048.0)
         ts(vw("e2"), vw("q2u"), 0, A.is_equal)
         xgath("v", "x2", "q2u", 0, 32, 16.0, -2048.0)
         mm(vw("pF", 0, 128), vw("e2"), vw("cm"))
         mm(vw("pF", 128, 256), vw("cm"), vw("e2"))
-        ku = vw("pD", 0, 128)
-        mm(ku, row("on"), row("tie16"), True, False)
-        if t == 0:
-            mm(vw("pH", 0, 128), vw("aP"), vw("I32"), True, False)
-            mm(vw("pH", 0, 128), vw("I32th"), vw("wyb"), False, True)
         xgath("s", "x2", "q2u", 96, 128, 16.0, -2048.0)
-        scan(vw("sq"), vw("d0s"), vw("pq"), A.mult, A.add)
         xgath("v", "x2", "q2u", 64, 96, 16.0, -2048.0)
         for a, b in HV:
             u = vw("pC", a, b)
             for m in range(16):
                 mm(u, vw("Ib"), flat("x2", a, b, m), m == 0, False)
             mm(u, vw("bo16"), vw("e2", a, b), False, True)
-        for a, b in HV:
-            scan(flat("bs", a, b), vw("d0b"), flat("x2", a, b), A.add, A.max)
-        bl = vw("bs", 15, 2048, 16)
-        ts(vw("lo"), bl, 0.0625, A.mult, 1280 - 0.46875, A.add)
-        ts(vw("q2h"), vw("q2u"), 0.0, A.add)
-        act(vw("y16"), last("sq"))
+        for a in range(0, 128, 32):
+            scan(flat("bs", a, a + 32), vw("d0b"), flat("x2", a, a + 32), A.add, A.max)
+        act(vw("ti"), vw("pD", 256, 384), 0.0625)
         act(vw("e0"), vw("pF", 0, 256), 1.0, 17.0, F.Relu)
+        act(vw("a1"), vw(v), 1.0, 8388608.0)
         act(vw("e1"), vw("e0"), -1.0, 1.0, F.Relu)
+        act(vw("a2"), vw("a1"), 1.0, -8388608.0)
         eP, eQ = vw("e1", 0, 128), vw("e1", 128, 256)
-        if t == 0:
-            act(vw("v0"), vw("pH", 0, 128))
-        act(vw("ti"), vw("pG", 0, 128), 0.0625)
+        bl = vw("bs", 15, 2048, 16)
+        ku = vw("pD", 0, 128)
         ts(vw("Uh"), vw("pC", 0, 128), 0.0625, A.mult)
-        yT = vw("pG", 128, 256, 1, 0, 8)
+        equal(0, 1)
+        ts(vw("lo"), bl, 0.0625, A.mult, 1280 - 0.46875, A.add)
+        mm(ku, row("on"), row("tie16"), True, False)
         mm(ku, bl, vw("Ib"), False, False)
-        mm(ku, vw("lo"), vw("Im16"), False, False)
         mm(vw("pE", 0, 128), vw("Uh"), vw("Ib"))
-        mm(ku, vw("Uh"), vw("I256"), False, True)
-        mm(yT, vw("y16"), vw("Ib"))
-        if t == 0:
-            masks(v, end)
+        mm(ku, vw("Uh"), vw("I256"), False, False)
+        mm(ku, vw("lo"), vw("Im16"), False, True)
         act(vw("cP"), vw("pE", 0, 128), -0.0625, 1227.46875)
-        act(vw("yT", 0, 128, 1, 0, 8), yT)
+        if not end:
+            act(vw("aM"), vw("a2"), 1.0, vw("a32"))
+        equal(1, 5)
 
         def spread(n):
-            p = vw("pF" if n % 2 == 0 else "pE")
-            mm(p, vw("cP", 0, 128, 1, 32 * n, 32 * n + 32), vw("E", 0, 512, 1, 32 * n, 32 * n + 32))
-            act(flat("vf", 32 * n, 32 * n + 32), p, 1.0, -1100.0)
+            p = vw(("pF", "pE", "pG", "pH")[n])
+            mm(p, vw("cP", 0, 128, 1, 32 * n, 32 * n + 32), vw("E", 0, 512, 1, 32 * n, 32 * n + 32), True, n < 2)
+            if n < 2:
+                act(flat("vf", 32 * n, 32 * n + 32), p, 1.0, -1100.0)
         scan(vw("mk"), vw("d0m"), ku, A.add, A.max)
         spread(0)
+        equal(5, 7)
         ts(vw("r8"), last("mk"), 15, A.bitwise_and)
-        tt(vw("AL"), ind(vw("r8"), vw("L8")), vw("m16"), A.mult)
+        equal(7, 8)
+        ts(vw("q2h"), vw("q2u"), 0.0, A.add)
         mm(vw("pA", 256, 264), vw("m16"), vw("bo8k"), True, False)
+        spread(1)
+        weigh()
+        tt(vw("AL"), ind(vw("r8"), vw("L8")), vw("m16"), A.mult)
         mm(vw("pA", 256, 264), vw("AL"), vw("bo8n"), False, True)
         tt(vw("ok"), ind(vw("r8"), vw("L8")), vw("m15"), A.is_equal)
+        ts(vw("ya"), vw("y8"), vw("ndum"), A.add)
+        ts(vw("du"), vw("pC", 256, 264), vw("wt"), A.is_lt)
         copy(vw("lk"), vw("pA", 256, 264))
-        copy(vw("cd"), ind(vw("RA"), vw("lk")))
-        spread(1)
         spread(2)
+        spread(3)
+        mm(vw("pB", 256, 384), vw("ok"), vw("Ib"))
         sc = vw("pD", 128, 256)
+        mm(sc, row("on"), row("m15"), True, False)
+        tt(vw("of"), vw("du"), vw("ya"), A.mult)
+        copy(vw("cd"), ind(vw("RA"), vw("lk")))
+        tt(vw("AS"), ind(vw("of"), vw("L8")), vw("m16"), A.mult)
+        ts(vw("cd16"), vw("cd"), 0.0, A.add)
+        mm(vw("pC", 264, 272), vw("m16"), vw("bo8d"), True, False)
+        mm(vw("pC", 264, 272), vw("AS"), vw("bo8"), False, True)
 
-        def piece(n):
+        def summed(src, n, w, stop):
+            a, b = 32 * n, 32 * n + 32
+            for j in range(16):
+                mm(vw("pD", 128 + j, 256, 16, a, b), flat(src, a, b, j), vw(w), False, stop and j == 15)
+
+        def differences(n):
             a, b = 32 * n, 32 * n + 32
             tt(flat("mn", a, b), ind(XG, vw("cd", a, b)), flat("vf", a, b), A.subtract)
+            summed("mn", n, "wp16", False)
 
-        def score(n):
+        def positive(n):
             a, b = 32 * n, 32 * n + 32
-            act(flat("xc", a, b), flat("mn", a, b), 1.0, 0.0, F.Abs)
-            for j in range(16):
-                mm(vw("pD", 128 + j, 256, 16, a, b), flat("xc", a, b, j), vw("wm16"), False, j == 15)
+            ts(flat("xc", a, b), flat("mn", a, b), 0.0, A.max)
+            summed("xc", n, "wm32", True)
 
-        def shown(lo, hi):
-            for w in range(lo, hi):
-                mm(vw("pG" if w < 4 else "pH", 128 * (w % 4), 128 * (w % 4) + 128), vw("sl8", 128 * w, 128 * w + 128, 1, 0, 8), vw("yT", 0, 128, 1, 0, 8))
+        def negated(n):
+            a, b = 32 * n, 32 * n + 32
+            xgath("s", "mn", "cd", a, b, -1.0)
+            mm(vw(("pG", "pH")[n - 2]), vw("Ib"), flat("mn", a, b), False, True)
 
-        def carried():
-            tt(vw("t3"), nv, eQ, A.mult)
-            tt(vw("vo%d" % (t + 1)), vw(v), vw("t3"), A.add)
-            send("v", t + 1)
+        def absolute(n):
+            act(flat("xc", 32 * n, 32 * n + 32), vw(("pG", "pH")[n - 2]), 1.0, -1100.0, F.Abs)
+            summed("xc", n, "wm16", True)
         nq = vw("pA", 384, 512)
-        mm(vw("pB", 256, 384), vw("ok"), vw("Ib"))
-        piece(0)
-        ts(vw("cd16"), vw("cd"), 0.0, A.add)
+        nv = vw("pB", 128, 256)
+        mm(vw("pB", 384, 512), vw("cd16"), vw("Dm"))
+        if not end:
+            mm(nv, row("pwr"), row("on"), True, False)
+            mm(nv, vw("Im32"), vw(v), False, False)
+        negated(2)
+        differences(0)
+        copy(vw("ls"), vw("pC", 264, 272))
         if not end:
             tt(vw("oka"), vw("pB", 256, 384), vw("aM"), A.mult)
+            mm(nv, vw("bo32"), vw("oka"), False, True)
         else:
             ts(vw("okb"), vw("pB", 256, 384), vw("ac"), A.mult)
-        if t == 0:
-            opened(v)
-            mm(nv, vw("bo32"), vw("oka"), False, True)
-        spread(3)
-        piece(1)
-        if t == 0:
-            carried()
-        mm(sc, row("on"), row("m15"), True, False)
-        shown(0, 4)
+            mm(nv, vw("bo"), vw("okb"))
+        negated(3)
+        differences(1)
+        positive(0)
+        absolute(2)
+        positive(1)
+        absolute(3)
+        tt(vw("xs"), ind(vw("X"), vw("ls")), vw("ti"), A.add)
+        tt(vw("t3"), nv, eQ, A.mult)
         if end:
-            mm(vw("pB", 128, 256), vw("bo"), vw("okb"))
-            shown(4, 8)
-        elif t:
-            mm(nv, vw("bo32"), vw("oka"), False, True)
-        score(0)
-        piece(2)
-        mm(vw("pB", 384, 512), vw("cd16"), vw("Dm"))
-        score(1)
-        piece(3)
-        score(2)
-        score(3)
-        if not end:
-            if t:
-                carried()
-            equal(0, 4)
-            shown(4, 8)
-        else:
-            equal(0, 8)
-            weigh(0, 8)
             tt(vw("fr"), vw(v), vw("a2"), A.subtract)
-            dedupe()
+        ts(vw("xn"), vw("xs"), 0.5, A.mult, -0.484375, A.add)
+        if not end:
+            tt(vw("vo%d" % (t + 1)), vw(v), vw("t3"), A.add)
+            send("v", t + 1)
+            stops()
+            mm(nq, vw("Ib"), vw("q2h"), True, False)
+        else:
             ts(vw("fR"), vw("q2u"), 0, A.is_gt, 32.0, A.mult)
-            update()
+            copy(ind(vw("X"), vw("ls")), vw("xn"))
             store(T.yx[:, :], vw("X", X0, X0 + D), "st0")
             mm(nq, vw("ImQ"), eQ, True, False)
             mm(nq, vw("IpQ"), vw("e2"), False, False)
-        scan(vw("ms"), vw("d0m"), sc, A.add, A.max)
-        copy(vw("mx8"), last("ms"))
-        tt(vw("oj"), ind(vw("mx8"), vw("L8")), vw("ms"), A.is_equal)
+            mm(nq, vw("Ib"), vw("q2h"), False, False)
+        scan(vw("mx"), vw("d0m"), sc, A.add, A.max)
+        scan(vw("my"), vw("d0m"), sc, A.add, A.max)
+        if end:
+            tt(vw("fr"), vw("fr"), vw("fR"), A.mult)
+        tt(vw("oj"), ind(vw("mx"), vw("LB")), vw("my"), A.is_equal)
+        if end:
+            tt(vw("yw"), vw("fr"), vw("t3"), A.add)
+            store(T.yq[:, :], vw("yw"), "st1")
         tt(vw("pn"), vw("pB", 384, 512), vw("oj"), A.mult)
         scan(vw("sn"), vw("d0s"), vw("pn"), A.mult, A.add)
         tt(vw("AN"), ind(vw("sn"), vw("LB")), eP, A.mult)
-        mm(nq, vw("Ib"), vw("q2h"), not end, False)
         mm(nq, vw("AN"), vw("Ib"), False, True)
         if not end:
-            equal(4, 6)
+            copy(ind(vw("X"), vw("ls")), vw("xn"))
             copy(vw("qo%d" % (t + 1)), nq)
             send("q", t + 1)
-            weigh(0, 6)
-            equal(6, 8)
-            weigh(6, 8)
-            if t == 0:
-                last_constants()
-            stops()
-            dedupe()
-            update()
         else:
             act(vw("yt"), nq, 1.0, -16.0)
             store(T.yp[:, :], vw("yt"), "st2", "s")
-            tt(vw("fr"), vw("fr"), vw("fR"), A.mult)
-            tt(vw("t3"), vw("pB", 128, 256), eQ, A.mult)
-            tt(vw("yw"), vw("fr"), vw("t3"), A.add)
-            store(T.yq[:, :], vw("yw"), "st1")
     for s in SEMAPHORES:
         if cnt.get(s):
             g.wait_ge(T.sem[s], cnt[s])

@@ -16,25 +16,30 @@ SB = {
     "kI": (1, i32), "aI": (1, i32), "gI": (1, i32), "hI": (1, i32), "kc": (1, f32), "ac": (1, f32), "gc": (1, f32), "hc": (1, f32),
     "a16": (1, f32), "a32": (1, f32), "c14": (1, f32), "c15": (1, f32), "n15": (1, f32), "ndum": (1, f32), "dum": (1, f32), "b16p": (1, f32),
     "wI": (256, b16), "dl": (256, b16), "Kc": (256, b16), "K": (256, b16), "cid": (144, f32), "Z": (144, b16), "g8": (8, f32),
-    "I32": (128, f32), "Im32": (128, f32), "Ib": (128, b16), "I256": (128, b16), "Im16": (128, b16), "ImQ": (128, b16), "IpQ": (128, b16),
-    "I32th": (128, b16), "bo": (128, b16), "bo32": (128, f32), "bo16": (128, b16), "Dm": (128, b16), "cm": (128, b16),
-    "bo8": (8, b16), "bo8n": (8, b16), "wm16": (8, b16), "wp16": (8, b16), "wm32": (8, b16),
+    "I32": (128, f32), "Im32": (128, f32), "Ib": (128, b16), "I16": (128, b16), "Im16": (128, b16), "ImQ": (128, b16), "IpQ": (128, b16),
+    "I32th": (128, b16), "Im64": (128, b16), "bo": (128, b16), "bo32": (128, f32), "bo256": (128, b16), "Dm": (128, b16), "cm": (128, b16),
+    "bo8": (8, b16), "bo8n": (8, b16), "wm16": (8, b16), "wa": (16, b16), "wd": (16, b16), "wr2": (16, b16), "tie2": (256, b16),
     "bo8b": (8, b16), "bo8m": (8, b16), "bo8d": (8, h16), "bo8k": (8, h16),
     "on": (128, b16), "on32": (128, f32), "m15": (128, b16), "tie16": (128, b16), "m16": (128, b16),
-    "d0s": (128, f32), "d0m": (128, f32), "d0p": (128, f32), "d0b": (512, b16), "pwr": (128, b16), "hlf": (128, f32), "zer": (128, f32),
+    "d0s": (128, f32), "d0m": (256, f32), "d0p": (128, f32), "d0b": (576, b16), "pwr": (128, b16), "hlf": (128, f32), "zer": (128, f32),
     "wr": (128, b16), "wc": (1, b16), "wt": (1, f32), "eI": (512, b16), "E": (512, b16), "sl8": (1024, b16),
-    "lbI": (8, i32), "l8I": (8, i32), "LB": (8, u16), "L8": (8, u16),
-    "limf": (1, f32), "limc": (1, f32), "lim8": (8, f32), "pofI": (128, i32), "pofm": (128, h16),
+    "l3I": (8, i32), "l8I": (8, i32), "L3": (8, u16), "L8": (8, u16),
+    "pay": (384, b16), "w3": (24, b16), "d0h": (128, f32), "d1h": (128, f32), "pwd": (128, f32),
+    "limf": (1, f32), "limc": (1, f32), "lim8": (8, f32), "pofI": (128, b16), "pofm": (128, h16),
+    "TQ": (XS - 16, f32), "pc": (2, f32), "tA": (1, f32), "tB": (1, f32), "k16": (1, f32), "bo4n": (8, b16),
+    "bo8a": (8, b16), "bo64": (8, b16), "bo8s": (8, b16), "bo8p": (8, h16), "payW": (24, b16), "bigW": (24, b16), "tieW": (16, b16), "far": (24, b16),
+    "eN": (128, b16), "e8": (8, f32), "le": (8, u16), "th2": (8, f32), "xe": (128, b16), "nhi": (128, b16), "nlo": (128, h16), "RN": (128, f32),
+    "nq": (128, h16), "kz": (16, i32), "ky": (16, i32),
     "WA": (2048, b16), "WB": (2048, b16), "lf": (128, f32), "l0": (128, u16),
     "lu1": (128, u16), "lu2": (128, u16), "lu4": (128, u16), "lu8": (128, u16), "wyb": (128, b16),
     "x": (2048, b16), "x2": (2048, b16), "xc": (2048, b16), "mn": (2048, b16), "vf": (1024, b16), "bs": (2048, h16), "RA": (2048, f32),
     "eR": (128, b16), "e2": (128, b16), "q16": (128, h16), "aP": (128, f32), "aS": (128, f32), "aM": (128, f32), "a1": (128, f32), "a2": (128, f32),
-    "n0": (8, f32), "thr": (8, f32), "mx": (128, f32), "my": (128, f32), "sm": (128, f32), "stp": (8, f32), "stb": (8, b16), "pw8": (8, f32),
-    "oh": (128, f32), "pw": (128, f32), "pr": (128, i32), "bb": (128, i32), "q2P": (128, h16), "q2u": (128, u16), "q2h": (128, h16),
-    "lo": (128, h16), "Uh": (128, h16), "cP": (128, h16), "e0": (256, f32), "e1": (256, b16),
+    "n0": (8, f32), "thr": (8, f32), "my": (256, i32), "sm": (128, f32), "qhi": (128, b16),
+    "dz": (24, f32), "dy": (24, f32), "nz": (24, i32), "ny": (24, i32), "pz": (24, f32), "yz": (24, f32), "pr": (128, i32), "bb": (128, i32), "q2P": (128, h16), "q2u": (128, u16), "q2h": (128, h16),
+    "lo": (128, h16), "cP": (128, h16), "e0": (256, f32), "e1": (384, b16),
     "mk": (128, i32), "r8": (8, i32), "ok": (128, b16), "AL": (128, h16), "lk": (8, u16),
     "cd": (128, u16), "cd16": (128, h16), "oka": (128, f32), "okb": (128, b16), "t3": (128, f32),
-    "oj": (128, f32), "pn": (128, f32), "sn": (128, f32), "AN": (128, h16),
+    "chi": (128, b16), "ms": (256, i32), "n16": (16, i32), "AN": (256, h16), "pwB": (128, f32),
     "pq": (128, f32), "sq": (128, f32), "y8": (8, f32), "y16": (8, h16), "yT": (128, h16), "eq": (1024, b16),
     "du": (8, f32), "ya": (8, f32), "of": (8, f32), "AS": (128, h16), "ls": (8, u16),
     "ti": (128, f32), "xs": (128, f32), "xn": (128, i32), "cj": (8, f32), "cn": (1, f32), "cz": (1, h16), "cc": (1, f32),
@@ -58,12 +63,16 @@ for _t in range(1, VI):
     SCRATCH["vo%d" % _t] = ("sbuf", [128, L], f32)
     SCRATCH["rq%d" % _t] = ("sbuf", [128, H], u16)
     SCRATCH["rv%d" % _t] = ("sbuf", [128, H], f32)
+    SCRATCH["n%d" % _t] = ("sbuf", [128, 8], u16)
+    SCRATCH["no%d" % _t] = ("sbuf", [128, 8], u16)
+    SCRATCH["rn%d" % _t] = ("sbuf", [128, 4], u16)
 PS = ("pA", "pB", "pC", "pD", "pE", "pF", "pG", "pH")
 for _p in PS:
     SCRATCH[_p] = ("psum", [128, 512], f32)
 SEMAPHORES = ["ev", "es", "et", "eg", "loc"] + ["ld%d" % _t for _t in range(5)] + ["st%d" % _t for _t in range(3)]
 for _t in range(1, VI):
-    SEMAPHORES += ["%s%d" % (_n, _t) for _n in ("qL", "qH", "vL", "vH", "rq", "rv")]
+    SEMAPHORES += ["%s%d" % (_n, _t) for _n in ("qL", "qH", "vL", "vH", "nL", "nH", "rq", "rv", "rn")]
+HALF = {"q": H, "v": H, "n": 4}
 HV = ((0, 64), (64, 128))
 
 
@@ -93,10 +102,10 @@ def relay(g, core, dst, T, topo):
     rid, pid = topo.addr(dst, core)
     m = bits(topo, core, dst, 8, False)
     for t in range(1, VI):
-        for k in ("v", "q"):
+        for k in "qvn":
             g.wait_ge(T.sem["r%s%d" % (k, t)], 8)
-            g.remote_dma(T["%s%d" % (k, t)][:, H:L], T["r%s%d" % (k, t)][:, :], T.sem["%sH%d" % (k, t)], T.sem["loc"], pid, rid, m)
-    g.wait_ge(T.sem["loc"], 16 * (VI - 1))
+            g.remote_dma(T["%s%d" % (k, t)][:, HALF[k]:2 * HALF[k]], T["r%s%d" % (k, t)][:, :], T.sem["%sH%d" % (k, t)], T.sem["loc"], pid, rid, m)
+    g.wait_ge(T.sem["loc"], 24 * (VI - 1))
 
 
 def member(g, core, rank, T, topo):
@@ -261,8 +270,9 @@ def member(g, core, rank, T, topo):
     iota(vw("kI"), [[1, 1]], 0, 1, False)
     iota(vw("wI"), [[0, 16], [1, 16]], 0, 0)
     iota(vw("dl"), [[-1, 16], [1, 16]], 0, 0)
-    iota(vw("pofI"), [[0, 2], [16, 64]], 0, 0, False)
     iota(vw("cid"), [[1, 144]], 0, 0)
+    iota(vw("g8"), [[1, 8]], 0, 0)
+    iota(vw("pofI"), [[0, 2], [16, 64]], 0, 0)
     ts(vw("aI"), vw("kI"), 15, A.bitwise_and)
     copy(vw("kc"), vw("kI"))
     ts(vw("gI"), vw("kI"), 4, A.arith_shift_right)
@@ -280,40 +290,52 @@ def member(g, core, rank, T, topo):
     fill(vw("Kc", 0, 256, 17), 0.0)
     tt(vw("K"), vw("K"), vw("Kc"), A.add)
     ts(vw("l0"), vw("wy0"), vw("a16"), A.add)
-    tt(vw("lf"), vw("wy0"), vw("pofI"), A.add)
-    gath("s", flat("WA", 64, 128), vw("K"), vw("l0", 64, 128))
+    ts(vw("Ib"), vw("cid", 0, 128), vw("kc"), A.is_equal)
+    ts(vw("bo8"), vw("g8"), vw("gc"), A.is_equal)
+    ts(vw("Z"), vw("cid"), vw("kc"), A.is_equal, vw("c15"), A.mult)
+    for n, src, c, b in (("dum", "kc", 1.0, float(XS)), ("ndum", "kc", -1.0, -float(XS)), ("b16p", "kc", 16.0, 15.0), ("a32", "ac", 1.0 / 32, 0.0),
+                         ("k16", "kc", 16.0, 0.0), ("tA", "ac", -256.0, 3840.0 - 128), ("tB", "ac", -256.0, 3840.0 + 8192),
+                         ("limf", "lmI", 1.0, 0.0), ("q16", "dr0", 1.0, 32.0), ("qhi", "dr0", 1.0 / 64, 128.5 - 0.4921875), ("wyb", "wy0", 1.0, 0.0)):
+        act(vw(n), vw(src), c, b)
+    act(vw("eR"), vw("dr0"), 1.0, -float(D - 1), F.Relu)
+    gath("s", flat("xc", 0, 64), vw("K"), vw("l0", 0, 64))
     gath("v", flat("WA", 0, 64), vw("K"), vw("l0", 0, 64))
+    gath("s", flat("WA", 64, 128), vw("K"), vw("l0", 64, 128))
     gfill(vw("X", 0, 16), 16, 0)
     gfill(vw("X", 16, 32), 16, -1)
     gfill(vw("X", X0 + D, XS), 16, -1)
-    iota(vw("g8"), [[1, 8]], 0, 0)
     gfill(vw("on32"), 128, 1)
     gfill(vw("on"), 128, 1)
-    for n, c in (("d0p", 2), ("d0s", 1), ("d0m", 0), ("I32", 0), ("ImQ", 0), ("Dm", 0)):
-        gfill(vw(n), 128, c)
-    for n, z in (("d0p", 0.0), ("d0s", 0.0), ("d0m", -BIG)):
-        sel(vw(n), [[0, 8], [1, 16]], A.not_equal, z, 0, 0)
-    iota(vw("lbI"), [[16, 8]], 15, 0, False)
+    for n, c in (("d0s", 1), ("d0p", 2), ("I32", 0), ("ImQ", 0), ("pay", 0)):
+        gfill(vw(n, 0, 128), 128, c)
+    for n in ("d0s", "d0p"):
+        sel(vw(n), [[0, 8], [1, 16]], A.not_equal, 0.0, 0, 0)
+    gfill(vw("d0m"), 256, 0)
+    iota(vw("l3I"), [[3, 8]], 2, 0, False)
     iota(vw("l8I"), [[1, 8]], 0, 0, False)
     gfill(vw("R", 0, 16), 16, -16, False)
     gfill(vw("R", 16 + D, 32 + D), 16, -16, False)
-    for n, z in (("I32", 1.0), ("ImQ", -float(16 + D)), ("Dm", 1.0)):
+    for n, z in (("I32", 1.0), ("ImQ", -float(16 + D))):
         sel(vw(n), [[1, 128]], A.not_equal, z, 0, -1)
+    sel(vw("d0m"), [[0, 16], [1, 16]], A.not_equal, -2 * BIG, 0, 0)
+    iota(vw("tie2", 0, 128), [[0, 8], [-256, 16]], 3840 - 128, 0)
+    iota(vw("tie2", 128, 256), [[0, 8], [-256, 16]], 3840 + 8192, 0)
+    iota(vw("dz"), [[0, 8], [256, 3]], 0, 0)
+    iota(vw("dy"), [[0, 8], [64, 3]], 0, 0)
+    gfill(vw("nz"), 24, 0, False)
+    gfill(vw("ny"), 24, 0, False)
     for n, c in (("bo32", 1), ("cm", 65), ("hlf", 0), ("zer", 0)):
         gfill(vw(n), 128, c)
-    sel(vw("Dm"), [[1, 128]], A.not_equal, -1.0, 1, -1)
     sel(vw("cm"), [[1, 128]], A.is_gt, 1.0, 0, -1)
     sel(vw("hlf"), [[0, 128]], A.not_equal, 0.5, 0, 0)
     sel(vw("cm"), [[1, 128]], A.not_equal, -31.0, 0, -1)
     for pat, base, cm in (([[-16, 8], [0, 16]], 0, 1), ([[16, 8], [0, 16]], 15, -1)):
-        for n in ("Dm", "bo32", "cm"):
+        for n in ("bo32", "cm"):
             sel(vw(n), pat, A.is_ge, 0.0, base, cm)
     iota(vw("eI"), [[1, 32], [0, 16]], 0, 0)
-    gfill(vw("sl8", 0, 1024, 1, 0, 8), 1024, 1)
-    gfill(vw("d0b"), 512, 1)
-    sel(vw("sl8", 0, 1024, 1, 0, 8), [[1, 8], [0, 128]], A.is_equal, 0.0, 0, -1)
-    sel(vw("d0b"), [[0, 32], [1, 16]], A.not_equal, -8192.0, 0, 0)
+    gfill(vw("d0b"), 576, 1)
     iota(vw("tie16"), [[0, 8], [-16, 16]], 240, 0)
+    sel(vw("d0b"), [[0, 36], [1, 16]], A.not_equal, -8192.0, 0, 0)
     iota(vw("m15"), [[0, 8], [-1, 16]], 15, 0)
     gfill(vw("X", XS, XW), 128, 0)
 
@@ -326,36 +348,52 @@ def member(g, core, rank, T, topo):
     def twin(src, h):
         act(flat("xc", *HV[h]), flat(src, *HV[h]))
 
-    def conv(src, h):
-        o = vw("pE" if h == 0 else "pF", 0, 64)
-        mm(o, vw("Ib"), vw("pofm", *HV[h]), True, False)
+    def conv(src, h, a=None, b=None):
+        a, b = HV[h] if a is None else (a, b)
+        o = vw(("pE", "pF", "pD")[h], 0, b - a)
+        mm(o, vw("Ib"), vw("pofm", a, b), True, False)
         for m in range(16):
-            mm(o, vw("Z", 15 - m, 143 - m), flat(src, HV[h][0], HV[h][1], m), False, m == 15)
+            mm(o, vw("Z", 15 - m, 143 - m), flat(src, a, b, m), False, m == 15)
 
-    def convd(lst, h):
-        copy(vw(lst, *HV[h]), vw("pE" if h == 0 else "pF", 0, 64))
+    def convd(lst, h, a=None, b=None):
+        a, b = HV[h] if a is None else (a, b)
+        copy(vw(lst, a, b), vw(("pE", "pF", "pD")[h], 0, b - a))
 
     def rowsums(a, b):
+        if a == 0:
+            mm(vw("pA", 0, 384), row("on"), row("pay", 0, 384), True, False)
         for m in range(16):
-            mm(vw("pA", m, 128, 16, a, b), flat("x", a, b, m), vw("bo8"))
+            mm(vw("pA", m, 384, 16, a, b), flat("x", a, b, m), vw("w3"), False, m == 15)
 
     def remedies(q, a, b):
         gath("s", flat("RA", a, b), vw("R"), vw(q, a, b), 1.0, 16.0)
 
-    def measures():
-        mm(vw("pB", 0, 8), vw("eR"), vw("bo8"))
-        mm(vw("pB", 8, 16), vw("eR"), vw("wm16"), True, False)
-        mm(vw("pB", 8, 16), vw("on32"), vw("lim8"), False, True)
+    def measures(p="pB"):
+        mm(vw(p, 0, 8), vw("eR"), vw("bo8"))
+        mm(vw(p, 8, 16), vw("eR"), vw("wm16"), True, False)
+        mm(vw(p, 8, 16), vw("on32"), vw("lim8"), False, True)
 
     def lists(t):
-        mm(vw("pB", 128, 256), vw("q16"), vw("Ib"), True, t > 0)
         if t == 0:
+            mm(vw("pB", 128, 256), vw("q16"), vw("Ib"), True, False)
             mm(vw("pB", 128, 256), vw("eR"), vw("ImQ"), False, True)
-        mm(vw("pB", 256, 384), vw("q16"), vw("Dm"))
+        mm(vw("pB", 256, 512), row("on"), row("tie2", 0, 256), True, False)
+        mm(vw("pB", 256, 384), vw("qhi"), vw("Ib"), False, False)
+        mm(vw("pB", 384, 512), vw("q16"), vw("Ib"), False, False)
+        mm(vw("pB", 384, 512), vw("qhi"), vw("Im64"), False, False)
 
-    def sums():
+    def keys():
+        for m in range(16):
+            mm(vw("pB", 256 + m, 512, 16), flat("x", 0, 128, m), vw("wd"), False, m == 15)
+
+    def upper(q):
+        ts(vw("qhi"), vw(q), 1.0 / 64, A.mult, 128.25 - 0.4921875, A.add)
+
+    def sums(t):
         for m in range(16):
             mm(vw("pD", 256, 384), vw("Ib"), flat("x", 0, 128, m), m == 0, False)
+        if t:
+            mm(vw("pD", 256, 384), vw("Ib"), vw("xe"), False, False)
         mm(vw("pD", 256, 384), vw("bo"), vw("eR"), False, True)
 
     def masks(v, end):
@@ -365,98 +403,113 @@ def member(g, core, rank, T, topo):
             act(vw("aM"), vw("a2"), 1.0, vw("a32"))
 
     def decide(t):
-        key = vw("pA", 0, 128)
-        scan(vw("sm"), vw("d0s"), key, A.mult, A.add)
-        scan(vw("mx"), vw("d0m"), key, A.add, A.max)
-        scan(vw("my"), vw("d0m"), key, A.add, A.max)
-        tt(vw("stp"), last("sm"), vw("thr"), A.is_ge)
-        tt(vw("oh"), ind(vw("mx"), vw("LB")), vw("my"), A.is_equal)
-        if t:
-            tt(vw("aS"), ind(vw("stp"), vw("L8")), vw("aP"), A.mult)
-        scan(vw("pw"), vw("d0p"), vw("oh"), A.mult, A.max)
-        tt(vw("pq"), vw("pB", 256, 384), vw("oh"), A.mult)
+        scan(vw("sm"), vw("d0s"), vw("pA", 0, 128), A.mult, A.add)
+        scan(vw("ms"), vw("d0m"), vw("pA", 128, 384), A.add, A.max)
+        if t == 0:
+            gath("v", flat("x2", 64, 96), flat("WB", 64, 128), vw("lu8", 64, 96))
+            convd("lu8", 2, 96, 128)
+        for n in ("dz", "dy"):
+            tt(vw(n, 2, 24, 3), last("sm"), vw("thr"), A.is_ge)
+        for a in (0, 1):
+            ts(vw("nz", a, 24, 3), vw("ms", 128 * a + 15, 128 * a + 128, 16), 255, A.bitwise_and)
+        if t == 0:
+            ts(vw("m16"), vw("wI", 0, 128), vw("ac"), A.is_equal)
+        scan(vw("pz"), vw("dz"), vw("nz"), A.mult, A.add)
 
-    copy(flat("xc", 0, 64), flat("WA", 0, 64))
-    copy(vw("lu1"), vw("lf"))
+    def heaviest():
+        scan(vw("my"), vw("d0m"), vw("pB", 256, 512), A.add, A.max)
+
+    def stopped():
+        for a in (0, 1):
+            ts(vw("ny", a, 24, 3), vw("my", 128 * a + 15, 128 * a + 128, 16), 255, A.bitwise_and)
+
+    mm(vw("pF", 0, 128), vw("Ib"), vw("wyb"), True, False)
+    mm(vw("pF", 0, 128), row("on"), row("pofI"), False, True)
+    copy(vw("lu1"), vw("pF", 0, 128))
     ts(vw("q0"), vw("dr0"), 16.0, A.add)
-    ts(vw("Z"), vw("cid"), vw("kc"), A.is_equal, vw("c15"), A.mult)
-    twin("WA", 1)
-    xgath("s", "x", "q0", 0, 64)
-
-    def first():
-        ts(vw("Ib"), vw("cid", 0, 128), vw("kc"), A.is_equal)
-        ts(vw("pofm"), vw("pofI"), vw("ac"), A.add)
-        copy(vw("limf"), vw("lmI"))
-        ts(vw("bo8"), vw("g8"), vw("gc"), A.is_equal)
-    double("WB", "WA", "lu1", 0, first)
+    ts(vw("pofm"), vw("pofI"), vw("ac"), A.add)
+    double("WB", "WA", "lu1", 0, lambda: copy(flat("xc", 64, 128), flat("WA", 64, 128)))
     conv("WB", 0)
+    xgath("s", "x", "q0", 0, 32)
+    for n, a, c in (("w3", 0, 1.0), ("w3", 8, 512.0), ("w3", 16, 512.0), ("wd", 0, 4096.0), ("wd", 8, 4096.0), ("wm16", 0, -16.0), ("bo8m", 0, vw("n15"))):
+        act(vw(n, a, a + 8), vw("bo8"), c)
+    act(row("d0h"), row("d0s"), 0.5)
+    act(vw("Im64"), vw("Ib"), -64.0)
     twin("WB", 0)
-    xgath("s", "x", "q0", 64, 96)
+    act(row("d1h"), row("d0s"), -32768.0, 32768.0)
+    xgath("s", "x", "q0", 32, 64)
     double("WB", "WA", "lu1", 1, lambda: convd("lu2", 0))
     conv("WB", 1)
     twin("WB", 1)
-    xgath("s", "x", "q0", 96, 128)
+    xgath("s", "x", "q0", 64, 96)
+    act(vw("lim8"), vw("I32", 0, 128, 16), vw("limf"))
     scan(vw("pwr"), vw("d0p"), vw("on32"), A.mult, A.max)
+    scan(row("pwd"), row("d0h"), row("d1h"), A.mult, A.add)
     double("WA", "WB", "lu2", 0, lambda: convd("lu2", 1))
     mm(vw("pG", 0, 1), row("pwr"), row("on", 0, 1))
     conv("WA", 0)
+    measures()
     twin("WA", 0)
-    act(vw("bo8m"), vw("bo8"), vw("n15"))
-    act(vw("eR"), vw("dr0"), 1.0, -float(D - 1), F.Relu)
-    act(vw("wm16"), vw("bo8"), -16.0)
-    act(vw("lim8"), vw("I32", 0, 128, 16), vw("limf"))
-    act(vw("q16"), vw("dr0"), 1.0, 32.0)
-    double("WA", "WB", "lu2", 1, lambda: convd("lu4", 0))
+    xgath("s", "x", "q0", 96, 128)
+
+    def third():
+        convd("lu4", 0)
+        ts(row("pay", 256, 384), row("pwd"), 256.0, A.min)
+        ts(vw("n0"), vw("pB", 0, 8), BIG, A.mult, -1000.0, A.add)
+    double("WA", "WB", "lu2", 1, third)
+    tt(vw("thr"), vw("pB", 8, 16), vw("n0"), A.min)
     conv("WA", 1)
+    act(row("pay", 128, 256), row("pwd"), 1.0 / 256, -0.125)
     twin("WA", 1)
     rowsums(0, 128)
-    measures()
-    remedies("q0", 0, 112)
+    lists(0)
+    remedies("q0", 0, 28)
+    for w in range(8):
+        act(vw("sl8", 128 * w, 128 * w + 128, 1, 0, 8), vw("on", 0, 128, 1, 0, 8), vw("I32", w, w + 1, 1, 0, 8))
     ts(vw("bo8b"), vw("bo8m"), vw("pG", 0, 1), A.mult)
-    copy(vw("LB"), vw("lbI"))
+    copy(vw("L3"), vw("l3I"))
     copy(vw("L8"), vw("l8I"))
     double("WB", "WA", "lu4", 0, lambda: convd("lu4", 1))
     conv("WB", 0)
-    ts(vw("n0"), vw("pB", 0, 8), BIG, A.mult, -1000.0, A.add)
-    double("WB", "WA", "lu4", 1, lambda: convd("lu8", 0))
-    conv("WB", 1)
-    gath("s", flat("WA", 32, 64), flat("WB", 0, 64), vw("lu8", 32, 64))
-    tt(vw("thr"), vw("pB", 8, 16), vw("n0"), A.min)
-    gath("v", flat("WA", 0, 32), flat("WB", 0, 64), vw("lu8", 0, 32))
-    lists(0)
+    keys()
     an = vw("pC", 384, 512)
-    mm(an, row("on"), row("pwr"), True, False)
-    for m in range(16):
-        mm(vw("pC", 384 + m, 512, 16), flat("WB", 0, 128, m), vw("bo8b"), False, False)
-    convd("lu8", 1)
-    scan(row("wr"), row("hlf"), row("zer"), A.mult, A.add, 2.0 ** 64)
-    ts(vw("m16"), vw("wI", 0, 128), vw("ac"), A.is_equal)
-    gath("s", flat("WA", 88, 128), flat("WB", 64, 128), vw("lu8", 88, 128))
-    gath("v", flat("WA", 64, 88), flat("WB", 64, 128), vw("lu8", 64, 88))
-    mm(vw("pH", 0, 1), row("wr"), row("on", 0, 1))
-    for m in range(16):
-        mm(vw("pC", 384 + m, 512, 16), flat("WA", 0, 128, m), vw("bo8b"), False, m == 15)
-    act(vw("bo"), vw("bo32"))
-    act(vw("wyb"), vw("wy0"))
-    act(vw("I32th"), vw("Ib"), 1.0 / 32)
-    act(vw("dum"), vw("kc"), 1.0, float(XS))
-    act(vw("b16p"), vw("kc"), 16.0, 15.0)
-    decide(0)
-    act(vw("aP"), an)
-    mm(an, vw("aP"), vw("I32"), True, False)
-    mm(an, vw("I32th"), vw("wyb"), False, True)
-    remedies("q0", 112, 128)
-    act(vw("v0"), an)
 
-    def late_constants():
-        for n, src, c in (("bo16", "bo32", 16.0), ("I256", "Ib", 256.0), ("Im16", "Ib", -16.0), ("Im32", "Ib", -1.0), ("IpQ", "Ib", float(16 + D)),
-                          ("bo8k", "bo8", vw("b16p")), ("bo8d", "bo8", vw("dum")), ("bo8n", "bo8", -1.0), ("wp16", "bo8", 16.0), ("wm32", "bo8", -32.0),
-                          ("a32", "ac", 1.0 / 32), ("ndum", "dum", -1.0)):
-            act(vw(n), vw(src), c)
+    def masked(src, a, b, stop):
+        for m in range(16):
+            mm(vw("pC", 384 + m, 512, 16, a, b), flat(src, a, b, m), vw("bo8b"), False, stop and m == 15)
+
+    def step(q, dst, src, lst, a, b):
+        if q == "add":
+            tt(flat(dst, a, b), ind(flat(src, 64, 128), vw(lst, a, b)), flat("xc", a, b), A.add)
+        else:
+            gath(q, flat(dst, a, b), flat(src, 64, 128), vw(lst, a, b))
+    step("add", "WB", "WA", "lu4", 64, 96)
+    conv("WB", 1, 64, 96)
+    mm(an, row("on"), row("pwr"), True, False)
+    masked("WB", 0, 64, False)
+    convd("lu8", 0)
+    step("add", "WB", "WA", "lu4", 96, 128)
+    conv("WB", 2, 96, 128)
+    masked("WB", 64, 128, False)
+    gath("s", flat("x2", 0, 64), flat("WB", 0, 64), vw("lu8", 0, 64))
+    convd("lu8", 1, 64, 96)
+    decide(0)
+    step("s", "x2", "WB", "lu8", 108, 128)
+    step("v", "x2", "WB", "lu8", 96, 108)
+    copy(vw("pwB"), ind(vw("pz"), vw("L3")))
+    heaviest()
+    scan(row("wr"), row("hlf"), row("zer"), A.mult, A.add, 2.0 ** 64)
+    for a, b in ((0, 64), (64, 96), (96, 128)):
+        masked("x2", a, b, True)
+    mm(vw("pH", 0, 1), row("wr"), row("on", 0, 1))
+    act(vw("bo"), vw("bo32"))
+    act(vw("I32th"), vw("Ib"), 1.0 / 32)
+    for n, src, c in (("bo256", "bo32", 256.0), ("I16", "Ib", 16.0), ("Im16", "Ib", -16.0), ("Im32", "Ib", -1.0),
+                      ("bo8k", "bo8", vw("b16p")), ("bo8d", "bo8", vw("dum")), ("bo8n", "bo8", -1.0), ("wa", "wd", -1.0), ("wr2", "wd", -2.0)):
+        act(vw(n), vw(src), c)
+
 
     def shown():
-        act(vw("y16"), vw("y8"))
-        mm(vw("pE", 128, 256, 1, 0, 8), vw("y16"), vw("Ib"))
         act(vw("yT", 0, 128, 1, 0, 8), vw("pE", 128, 256, 1, 0, 8))
         for w in range(8):
             mm(vw("pG" if w < 4 else "pH", 128 * (w % 4), 128 * (w % 4) + 128), vw("sl8", 128 * w, 128 * w + 128, 1, 0, 8), vw("yT", 0, 128, 1, 0, 8))
@@ -464,19 +517,11 @@ def member(g, core, rank, T, topo):
     def equal(lo, hi):
         for w in range(lo, hi):
             p = vw("pG" if w < 4 else "pH", 128 * (w % 4), 128 * (w % 4) + 128)
-            ts(vw("eq", 128 * w, 128 * w + 128), p, vw("y8", w, w + 1), A.is_equal)
+            ts(vw("eq", 128 * w, 128 * w + 128), p, vw("yz", 3 * w + 2, 3 * w + 3), A.is_equal)
 
     def weigh():
         for w in range(8):
-            mm(vw("pC", 256 + w, 257 + w), vw("eq", 128 * w, 128 * w + 128), vw("wc"))
-
-    def stops():
-        mm(vw("pE", 0, 8), vw("on"), vw("stb"))
-        act(vw("cj"), vw("pE", 0, 8), 1.0, 35200.0, F.Identity, vw("cn"))
-        act(vw("cz"), vw("cn"), 1.0 / 256, -0.498046875)
-        act(vw("cc"), vw("cz"), -256.0, vw("cn"))
-        act(vw("limc"), vw("limf"), 1.0, vw("cc"))
-        act(vw("lim8"), vw("I32", 0, 128, 16), vw("limc"))
+            mm(vw("pB", 16 + w, 17 + w), vw("eq", 128 * w, 128 * w + 128), vw("wc"))
 
     def send(k, t):
         src = "%so%d" % (k, t)
@@ -485,141 +530,222 @@ def member(g, core, rank, T, topo):
         r1, p1 = topo.addr(lowd, core)
         r2, p2 = topo.addr(hid, core)
         tr = [RemoteDMATransfer(dst_ids=[DstId(rid=r1, pnc=p1)], dma_engine_mask=bits(topo, core, lowd, 8, False), remote_sem=T.sem["%sL%d" % (k, t)],
-                                src=T[src][:, 0:H], dst=T["%s%d" % (k, t)][:, 0:H]),
+                                src=T[src][:, 0:HALF[k]], dst=T["%s%d" % (k, t)][:, 0:HALF[k]]),
               RemoteDMATransfer(dst_ids=[DstId(rid=r2, pnc=p2)], dma_engine_mask=bits(topo, core, hid, 8, True), remote_sem=T.sem["r%s%d" % (k, t)],
-                                src=T[src][:, H:L], dst=T["r%s%d" % (k, t)][:, :])]
+                                src=T[src][:, HALF[k]:2 * HALF[k]], dst=T["r%s%d" % (k, t)][:, :])]
         deps("g", [], [vw(src)])
         g.remote_dma_fused(tr, local_sem=T.sem["loc"])
         cnt["loc"] = cnt.get("loc", 0) + 16
+        for h in (0, 1):
+            s = "%s%s%d" % (k, "LH"[h], t)
+            cnt[s] = 8
+            snap[(s, 8)] = {}
+            recs.setdefault("%s%d" % (k, t), []).append((vw("%s%d" % (k, t), h * HALF[k], (h + 1) * HALF[k]), True, (s, 8), "remote"))
 
+    def entry_constants():
+        for a in (0, 1):
+            mm(vw("pH", 8 + a, 9 + a), row("pay", 128 + 128 * a, 256 + 128 * a), row("on", 0, 1))
+        act(vw("pc"), vw("pH", 8, 10))
+        for n, a, c in (("bo8a", 0, vw("ac")), ("bo64", 0, 64.0), ("bo8s", 0, 0.0625), ("bo4n", 0, -4.0), ("payW", 0, 0.0), ("bo8p", 0, vw("k16")),
+                        ("bigW", 0, 2 * BIG), ("bigW", 8, 2 * BIG), ("bigW", 16, 2 * BIG), ("tieW", 0, vw("tA")), ("tieW", 8, vw("tB")),
+                        ("payW", 8, vw("pc", 0, 1)), ("payW", 16, vw("pc", 1, 2))):
+            act(vw(n, a, a + 8), vw("bo8"), c)
+        act(row("far", 0, 24), row("on", 0, 24), -2 * BIG)
+
+    def ahead(t):
+        q = "q%d" % t
+        mm(vw("pH", 0, 8), vw("on32"), vw("dz", 2, 24, 3))
+        mm(vw("pF", 0, 128), vw("cm"), vw("eR"))
+        remedies(q, 0, 16)
+        act(vw("cj"), vw("pH", 0, 8), 1.0, 35200.0, F.Identity, vw("cn"))
+        act(vw("e0", 0, 128), vw("pF", 0, 128), 1.0, 17.0, F.Relu)
+        xgath("s", "x", q, 44, 64)
+        act(vw("cz"), vw("cn"), 1.0 / 256, -0.498046875)
+        act(vw("eN"), vw("e0", 0, 128), -1.0, 1.0, F.Relu)
+        xgath("s", "x", q, 64, 84)
+        act(vw("cc"), vw("cz"), -256.0, vw("cn"))
+        xgath("s", "x", q, 84, 104)
+        act(vw("limc"), vw("limf"), 1.0, vw("cc"))
+        xgath("s", "x", q, 104, 128)
+        act(vw("lim8"), vw("I32", 0, 128, 16), vw("limc"))
+
+    def kept(t):
+        q, v = "q%d" % t, "v%d" % t
+        mm(vw("pG", 0, 8), vw("eN"), vw("bo8a"))
+        for p, n, w in (("pE", 24, "payW"), ("pF", 16, "tieW")):
+            mm(vw(p, 256, 256 + n), row("on"), row("far", 0, n), True, False)
+            mm(vw(p, 256, 256 + n), vw("eN"), vw("bigW", 0, n), False, False)
+            mm(vw(p, 256, 256 + n), vw("eN"), vw(w), False, False)
+        lists(t)
+        copy(vw("e8"), vw("pG", 0, 8))
+        xgath("v", "x", q, 16, 44)
+        tt(vw("AL"), ind(vw("e8"), vw("L8")), vw("m16"), A.mult)
+        rowsums(0, 128)
+        measures("pH")
+        keys()
+        mm(vw("pB", 128, 256), vw("q16"), vw("Ib"), True, False)
+        mm(an, vw(v), vw("I32"))
+        mm(vw("pG", 8, 16), vw("m16"), vw("bo8p"), True, False)
+        mm(vw("pG", 8, 16), vw("AL"), vw("bo8"), False, True)
+        remedies(q, 16, 72)
+        act(vw("aP"), an)
+        scan(vw("sm"), vw("d0s"), vw("pA", 0, 128), A.mult, A.add)
+        ts(vw("n0"), vw("pH", 0, 8), BIG, A.mult, -BIG - 1000.0, A.add)
+        scan(vw("ms"), vw("d0m"), vw("pA", 128, 384), A.add, A.max)
+        tt(vw("thr"), vw("pH", 8, 16), vw("n0"), A.min)
+        heaviest()
+        tt(vw("th2"), vw("thr"), last("sm"), A.subtract)
+
+    def entered(t):
+        n = vw("n%d" % t)
+        gath("v", vw("xe"), XG, n)
+        gath("s", vw("nhi"), vw("TQ"), n, 1.0 / 64, 128.25 - 0.4921875)
+        gath("s", vw("nlo"), vw("TQ"), n, 1.0, 16.0)
+        gath("s", vw("RN"), vw("R"), n, 1.0, 16.0)
+        remedies("q%d" % t, 72, 128)
+        mm(vw("pE", 256, 280), vw("xe"), vw("w3"), False, True)
+        tt(vw("nq"), ind(vw("TQ"), n), vw("eN"), A.mult)
+        copy(vw("le"), vw("pG", 8, 16))
+        mm(vw("pF", 256, 272), vw("xe"), vw("wd"), False, False)
+        mm(vw("pF", 256, 264), vw("nhi"), vw("bo8s"), False, False)
+        mm(vw("pF", 264, 272), vw("nhi"), vw("bo4n"), False, False)
+        mm(vw("pF", 264, 272), vw("nlo"), vw("bo8s"), False, True)
+        mm(vw("pB", 128, 256), vw("nq"), vw("Ib"), False, True)
+        tt(vw("kz"), vw("pE", 264, 280), vw("ms", 15, 256, 16), A.max)
+        for d in ("dz", "dy"):
+            tt(vw(d, 2, 24, 3), vw("pE", 256, 264), vw("th2"), A.is_ge)
+        for a in (0, 1):
+            ts(vw("nz", a, 24, 3), vw("kz", 8 * a, 8 * a + 8), 255, A.bitwise_and)
+        scan(vw("pz"), vw("dz"), vw("nz"), A.mult, A.add)
+        tt(vw("ky"), vw("pF", 256, 272), vw("my", 15, 256, 16), A.max)
+
+    entry_constants()
     for t in range(VI):
         q, v = "q%d" % t, "v%d" % t
         end = t == VI - 1
         if t:
-            for k, h in (("q", 0), ("v", 0), ("q", 1), ("v", 1)):
-                s = "%s%s%d" % (k, "LH"[h], t)
-                cnt[s] = 8
-                snap[(s, 8)] = {}
-                recs.setdefault("%s%d" % (k, t), []).append((vw("%s%d" % (k, t), *HV[h]), True, (s, 8), "remote"))
-            mm(an, vw(v), vw("I32"))
-            xgath("v", "x", q, 0, 32)
-            xgath("s", "x", q, 32, 64)
-            act(vw("aP"), an)
-            rowsums(0, 64)
-            remedies(q, 0, 32)
-            ts(vw("eR"), vw(q), 0, A.is_equal)
-            measures()
-            for e, a in (("v", 64), ("s", 80), ("v", 96), ("s", 112)):
-                xgath(e, "x", q, a, a + 16)
-            rowsums(64, 96)
-            ts(vw("q16"), vw(q), 16.0, A.add)
-            ts(vw("n0"), vw("pB", 0, 8), BIG, A.mult, -1000.0, A.add)
-            remedies(q, 32, 128)
-            rowsums(96, 128)
-            tt(vw("thr"), vw("pB", 8, 16), vw("n0"), A.min)
-            lists(t)
-            decide(t)
-        sums()
+            kept(t)
+            entered(t)
+        sums(t)
+        q2 = "q2u" if end else "qo%d" % (t + 1)
         if t:
-            tt(vw("pr"), ind(vw("pw"), vw("LB")), vw("aS"), A.mult)
-            scan(vw("sq"), vw("d0s"), vw("pq"), A.mult, A.add)
+            tt(vw("pr"), ind(vw("pz"), vw("L3")), vw("aP"), A.mult)
+            for a in (0, 1):
+                ts(vw("ny", a, 24, 3), vw("ky", 8 * a, 8 * a + 8), 255, A.bitwise_and)
         else:
-            tt(vw("pw8"), last("pw"), vw("stp"), A.mult)
-            scan(vw("sq"), vw("d0s"), vw("pq"), A.mult, A.add)
+            tt(vw("pr"), an, vw("pwB"), A.mult)
+            stopped()
+            act(vw("aP"), an)
+            remedies(q, 28, 52)
             copy(vw("wc"), vw("pH", 0, 1))
             ts(vw("wt"), vw("pH", 0, 1), 2.5, A.mult)
-            tt(vw("pr"), ind(vw("pw8"), vw("L8")), vw("aP"), A.mult)
-            ts(vw("E"), vw("eI"), vw("hc"), A.is_equal)
         ts(vw("bb"), vw("pr"), 32768, A.bitwise_and)
-        tt(vw("y8"), last("sq"), vw("stp"), A.mult)
-        copy(vw("stb"), vw("stp"))
+        scan(vw("yz"), vw("dy"), vw("ny"), A.mult, A.add)
         tt(vw("q2P"), vw("pB", 128, 256), vw("bb"), A.subtract)
         mm(vw("pA", 128, 256), vw("q2P"), vw("Ib"))
         if t == 0:
-            late_constants()
+            ts(vw("E"), vw("eI"), vw("hc"), A.is_equal)
+        else:
+            copy(ind(vw("RA"), vw("le")), vw("RN"))
+        act(vw("y16"), vw("yz", 2, 24, 3))
+        mm(vw("pE", 128, 256, 1, 0, 8), vw("y16"), vw("Ib"))
+        if t == 0:
+            remedies(q, 52, 68)
         shown()
-        ts(vw("q2u"), vw("pA", 128, 256), -16.0, A.add)
-        xgath("s", "x2", "q2u", 32, 64, 16.0, -2048.0)
-        ts(vw("e2"), vw("q2u"), 0, A.is_equal)
-        xgath("v", "x2", "q2u", 0, 32, 16.0, -2048.0)
-        mm(vw("pF", 0, 128), vw("e2"), vw("cm"))
-        mm(vw("pF", 128, 256), vw("cm"), vw("e2"))
-        xgath("s", "x2", "q2u", 96, 128, 16.0, -2048.0)
-        xgath("v", "x2", "q2u", 64, 96, 16.0, -2048.0)
-        for a, b in HV:
-            u = vw("pC", a, b)
-            for m in range(16):
-                mm(u, vw("Ib"), flat("x2", a, b, m), m == 0, False)
-            mm(u, vw("bo16"), vw("e2", a, b), False, True)
-        for a in range(0, 128, 32):
-            scan(flat("bs", a, a + 32), vw("d0b"), flat("x2", a, a + 32), A.add, A.max)
-        act(vw("ti"), vw("pD", 256, 384), 0.0625)
-        act(vw("e0"), vw("pF", 0, 256), 1.0, 17.0, F.Relu)
-        act(vw("a1"), vw(v), 1.0, 8388608.0)
-        act(vw("e1"), vw("e0"), -1.0, 1.0, F.Relu)
-        act(vw("a2"), vw("a1"), 1.0, -8388608.0)
-        eP, eQ = vw("e1", 0, 128), vw("e1", 128, 256)
-        bl = vw("bs", 15, 2048, 16)
-        ku = vw("pD", 0, 128)
-        ts(vw("Uh"), vw("pC", 0, 128), 0.0625, A.mult)
-        equal(0, 1)
-        ts(vw("lo"), bl, 0.0625, A.mult, 1280 - 0.46875, A.add)
-        mm(ku, row("on"), row("tie16"), True, False)
-        mm(ku, bl, vw("Ib"), False, False)
-        mm(vw("pE", 0, 128), vw("Uh"), vw("Ib"))
-        mm(ku, vw("Uh"), vw("I256"), False, False)
-        mm(ku, vw("lo"), vw("Im16"), False, True)
-        act(vw("cP"), vw("pE", 0, 128), -0.0625, 1227.46875)
+        if t == 0:
+            mm(vw("pE", 256, 384), vw("aP"), vw("I32"), True, False)
+            mm(vw("pE", 256, 384), vw("I32th"), vw("wyb"), False, True)
+        ts(vw(q2), vw("pA", 128, 256), -16.0, A.add)
         if not end:
-            act(vw("aM"), vw("a2"), 1.0, vw("a32"))
-        equal(1, 5)
+            send("q", t + 1)
+        if t == 0:
+            iota(vw("TQ"), [[1, XS - 16]], 0, 0)
+        cuts = (0, 28, 56, 92, 128)
+        xgath("s", "x2", q2, cuts[2], cuts[3], 16.0, -2048.0)
+        ts(vw("e2"), vw(q2), 0, A.is_equal)
+        xgath("v", "x2", q2, cuts[0], cuts[1], 16.0, -2048.0)
+        if end:
+            mm(vw("pF", 0, 128), vw("e2"), vw("cm"))
+        mm(vw("pF", 128, 256), vw("cm"), vw("e2"))
+        xgath("s", "x2", q2, cuts[3], cuts[4], 16.0, -2048.0)
+        xgath("v", "x2", q2, cuts[1], cuts[2], 16.0, -2048.0)
+        ku = vw("pC", 0, 128)
+        mm(ku, row("on"), row("tie16"), True, False)
+        mm(ku, vw("e2"), vw("bo256"), False, False)
+        for m in range(16):
+            mm(ku, flat("x2", 0, 128, m), vw("I16"), False, False)
+        for a, b in zip(cuts, cuts[1:]):
+            scan(flat("bs", a, b), flat("d0b", 0, b - a), flat("x2", a, b), A.add, A.max)
+        e = 0 if end else 128
+        act(vw("e0", e, 256), vw("pF", e, 256), 1.0, 17.0, F.Relu)
+        if t == 0:
+            act(vw("v0"), vw("pE", 256, 384))
+            remedies(q, 68, 128)
+        act(vw("ti"), vw("pD", 256, 384), 0.0625)
+        act(vw("a1"), vw(v), 1.0, 8388608.0)
+        eP, eQ = vw("e1", 0, 256), vw("e1", 256, 384)
+        bl = vw("bs", 15, 2048, 16)
+        equal(0, 2)
+        ts(vw("lo"), bl, 0.0625, A.mult, 1280 - 0.46875, A.add)
+        mm(ku, bl, vw("Ib"), False, False)
+        mm(ku, vw("lo"), vw("Im16"), False, True)
+        equal(2, 6)
 
         def spread(n):
             p = vw(("pF", "pE", "pG", "pH")[n])
             mm(p, vw("cP", 0, 128, 1, 32 * n, 32 * n + 32), vw("E", 0, 512, 1, 32 * n, 32 * n + 32), True, n < 2)
             if n < 2:
                 act(flat("vf", 32 * n, 32 * n + 32), p, 1.0, -1100.0)
-        scan(vw("mk"), vw("d0m"), ku, A.add, A.max)
-        spread(0)
-        equal(5, 7)
+        scan(vw("mk"), vw("d0m", 0, 128), ku, A.add, A.max)
+        act(vw("cP"), ku, -1.0 / 4096, 1222.5 - 1.0 / 8192)
+        act(vw("a2"), vw("a1"), 1.0, -8388608.0)
+        act(vw("e1", 128 + e, 384), vw("e0", e, 256), -1.0, 1.0, F.Relu)
+        if not end:
+            act(vw("aM"), vw("a2"), 1.0, vw("a32"))
+        if t == 1:
+            act(vw("IpQ"), vw("Ib"), float(16 + D))
+        if end:
+            act(vw("e1", 0, 128), vw("e0", 0, 128), -64.0, 64.0, F.Relu)
+            act(vw("fR"), vw("e2"), -32.0, 32.0)
+        equal(6, 8)
         ts(vw("r8"), last("mk"), 15, A.bitwise_and)
-        equal(7, 8)
-        ts(vw("q2h"), vw("q2u"), 0.0, A.add)
+        if end:
+            ts(vw("q2h"), vw(q2), 0.0, A.add)
+        ts(vw("ya"), vw("yz", 2, 24, 3), vw("ndum"), A.add)
         mm(vw("pA", 256, 264), vw("m16"), vw("bo8k"), True, False)
-        spread(1)
         weigh()
+        spread(0)
         tt(vw("AL"), ind(vw("r8"), vw("L8")), vw("m16"), A.mult)
         mm(vw("pA", 256, 264), vw("AL"), vw("bo8n"), False, True)
         tt(vw("ok"), ind(vw("r8"), vw("L8")), vw("m15"), A.is_equal)
-        ts(vw("ya"), vw("y8"), vw("ndum"), A.add)
-        ts(vw("du"), vw("pC", 256, 264), vw("wt"), A.is_lt)
+        ts(vw("du"), vw("pB", 16, 24), vw("wt"), A.is_lt)
         copy(vw("lk"), vw("pA", 256, 264))
+        spread(1)
         spread(2)
         spread(3)
         mm(vw("pB", 256, 384), vw("ok"), vw("Ib"))
-        sc = vw("pD", 128, 256)
-        mm(sc, row("on"), row("m15"), True, False)
         tt(vw("of"), vw("du"), vw("ya"), A.mult)
         copy(vw("cd"), ind(vw("RA"), vw("lk")))
         tt(vw("AS"), ind(vw("of"), vw("L8")), vw("m16"), A.mult)
-        ts(vw("cd16"), vw("cd"), 0.0, A.add)
         mm(vw("pC", 264, 272), vw("m16"), vw("bo8d"), True, False)
         mm(vw("pC", 264, 272), vw("AS"), vw("bo8"), False, True)
+        sc = vw("pD", 128, 384)
+        mm(sc, row("on"), row("tie2", 0, 256), True, False)
 
         def summed(src, n, w, stop):
             a, b = 32 * n, 32 * n + 32
             for j in range(16):
-                mm(vw("pD", 128 + j, 256, 16, a, b), flat(src, a, b, j), vw(w), False, stop and j == 15)
+                mm(vw("pD", 128 + j, 384, 16, a, b), flat(src, a, b, j), vw(w), False, stop and j == 15)
 
         def differences(n):
             a, b = 32 * n, 32 * n + 32
             tt(flat("mn", a, b), ind(XG, vw("cd", a, b)), flat("vf", a, b), A.subtract)
-            summed("mn", n, "wp16", False)
+            summed("mn", n, "wd", False)
 
         def positive(n):
             a, b = 32 * n, 32 * n + 32
             ts(flat("xc", a, b), flat("mn", a, b), 0.0, A.max)
-            summed("xc", n, "wm32", True)
+            summed("xc", n, "wr2", True)
 
         def negated(n):
             a, b = 32 * n, 32 * n + 32
@@ -628,16 +754,20 @@ def member(g, core, rank, T, topo):
 
         def absolute(n):
             act(flat("xc", 32 * n, 32 * n + 32), vw(("pG", "pH")[n - 2]), 1.0, -1100.0, F.Abs)
-            summed("xc", n, "wm16", True)
+            summed("xc", n, "wa", True)
         nq = vw("pA", 384, 512)
-        nv = vw("pB", 128, 256)
-        mm(vw("pB", 384, 512), vw("cd16"), vw("Dm"))
+        nv = vw("pC", 0, 128)
         if not end:
             mm(nv, row("pwr"), row("on"), True, False)
             mm(nv, vw("Im32"), vw(v), False, False)
         negated(2)
         differences(0)
+        ts(vw("cd16"), vw("cd"), 0.0, A.add)
+        ts(vw("chi"), vw("cd"), 1.0 / 64, A.mult, 128 - 0.4921875, A.add)
         copy(vw("ls"), vw("pC", 264, 272))
+        mm(vw("pD", 128, 256), vw("chi"), vw("Ib"), False, False)
+        mm(vw("pD", 256, 384), vw("cd16"), vw("Ib"), False, False)
+        mm(vw("pD", 256, 384), vw("chi"), vw("Im64"), False, False)
         if not end:
             tt(vw("oka"), vw("pB", 256, 384), vw("aM"), A.mult)
             mm(nv, vw("bo32"), vw("oka"), False, True)
@@ -651,38 +781,46 @@ def member(g, core, rank, T, topo):
         positive(1)
         absolute(3)
         tt(vw("xs"), ind(vw("X"), vw("ls")), vw("ti"), A.add)
-        tt(vw("t3"), nv, eQ, A.mult)
         if end:
             tt(vw("fr"), vw(v), vw("a2"), A.subtract)
+        else:
+            tt(vw("t3"), nv, eQ, A.mult)
+            ts(vw("eR"), vw("q%d" % (t + 1)), 0, A.is_equal)
         ts(vw("xn"), vw("xs"), 0.5, A.mult, -0.484375, A.add)
         if not end:
             tt(vw("vo%d" % (t + 1)), vw(v), vw("t3"), A.add)
             send("v", t + 1)
-            stops()
-            mm(nq, vw("Ib"), vw("q2h"), True, False)
+            copy(ind(vw("X"), vw("ls")), vw("xn"))
+            ahead(t + 1)
         else:
-            ts(vw("fR"), vw("q2u"), 0, A.is_gt, 32.0, A.mult)
+            tt(vw("fr"), vw("fr"), vw("fR"), A.mult)
             copy(ind(vw("X"), vw("ls")), vw("xn"))
             store(T.yx[:, :], vw("X", X0, X0 + D), "st0")
             mm(nq, vw("ImQ"), eQ, True, False)
             mm(nq, vw("IpQ"), vw("e2"), False, False)
             mm(nq, vw("Ib"), vw("q2h"), False, False)
-        scan(vw("mx"), vw("d0m"), sc, A.add, A.max)
-        scan(vw("my"), vw("d0m"), sc, A.add, A.max)
+        scan(vw("ms"), vw("d0m"), sc, A.add, A.max)
         if end:
-            tt(vw("fr"), vw("fr"), vw("fR"), A.mult)
-        tt(vw("oj"), ind(vw("mx"), vw("LB")), vw("my"), A.is_equal)
+            tt(vw("t3"), nv, eQ, A.mult)
+        else:
+            ts(vw("q16"), vw("q%d" % (t + 1)), 16.0, A.add)
+            upper("q%d" % (t + 1))
+        ts(vw("n16"), vw("ms", 15, 256, 16), 255, A.bitwise_and)
         if end:
             tt(vw("yw"), vw("fr"), vw("t3"), A.add)
             store(T.yq[:, :], vw("yw"), "st1")
-        tt(vw("pn"), vw("pB", 384, 512), vw("oj"), A.mult)
-        scan(vw("sn"), vw("d0s"), vw("pn"), A.mult, A.add)
-        tt(vw("AN"), ind(vw("sn"), vw("LB")), eP, A.mult)
-        mm(nq, vw("AN"), vw("Ib"), False, True)
+        for a in (0, 8):
+            o = vw("AN", 16 * a, 16 * a + 128)
+            if end:
+                tt(o, ind(vw("n16", a, a + 8), vw("L8")), vw("e1", 16 * a, 16 * a + 128), A.mult)
+                mm(nq, o, vw("Ib"), False, a == 8)
+            else:
+                tt(o, ind(vw("n16", a, a + 8), vw("L8")), vw("m16"), A.mult)
+                mm(vw("pA", 384, 392), o, vw("bo8" if a else "bo64"), a == 0, a == 8)
         if not end:
-            copy(ind(vw("X"), vw("ls")), vw("xn"))
-            copy(vw("qo%d" % (t + 1)), nq)
-            send("q", t + 1)
+            xgath("v", "x", "q%d" % (t + 1), 0, 16)
+            copy(vw("no%d" % (t + 1)), vw("pA", 384, 392))
+            send("n", t + 1)
         else:
             act(vw("yt"), nq, 1.0, -16.0)
             store(T.yp[:, :], vw("yt"), "st2", "s")

@@ -1,5 +1,5 @@
 import numpy as np
-from concourse.bass import DstId, RemoteDMATransfer, IndirectOffsetOnAxis
+from concourse.bass import DstId, RemoteDMATransfer
 from concourse.mybir import dt, AluOpType, AxisListType, ActivationFunctionType
 
 A = AluOpType
@@ -7,42 +7,45 @@ F = ActivationFunctionType
 NR, VI, H, L, D = 8, 4, 64, 128, 1760
 STRIDE = (4, 1)
 X0 = 32
-XS = X0 + D + 16
+XS = X0 + D
 XW = XS + 128
 BIG = 16777216.0
+HUGE = 2.0 ** 29
 f32, b16, h16, i32, u16 = "float32", "bfloat16", "float16", "int32", "uint16"
 SB = {
-    "X": (XW, b16), "R": (32 + D, i32), "dr0": (L, i32), "wy0": (L, i32), "lmI": (1, i32),
+    "X": (XW, b16), "Y": (XW, b16), "R": (16 + D, i32), "dr0": (L, i32), "wy0": (L, i32), "lmI": (1, i32),
     "kI": (1, i32), "aI": (1, i32), "gI": (1, i32), "hI": (1, i32), "kc": (1, f32), "ac": (1, f32), "gc": (1, f32), "hc": (1, f32),
-    "a16": (1, f32), "a32": (1, f32), "c14": (1, f32), "c15": (1, f32), "n15": (1, f32), "ndum": (1, f32), "dum": (1, f32), "b16p": (1, f32),
-    "wI": (256, b16), "dl": (256, b16), "Kc": (256, b16), "K": (256, b16), "cid": (144, f32), "Z": (144, b16), "g8": (8, f32),
-    "I32": (128, f32), "Im32": (128, f32), "Ib": (128, b16), "I16": (128, b16), "Im16": (128, b16), "ImQ": (128, b16), "IpQ": (128, b16),
-    "I32th": (128, b16), "Im64": (128, b16), "bo": (128, b16), "bo32": (128, f32), "bo256": (128, b16), "Dm": (128, b16), "cm": (128, b16),
-    "bo8": (8, b16), "bo8n": (8, b16), "wm16": (8, b16), "wa": (16, b16), "wd": (16, b16), "wr2": (16, b16), "tie2": (256, b16),
-    "bo8b": (8, b16), "bo8m": (8, b16), "bo8d": (8, h16), "bo8k": (8, h16),
+    "a32": (1, f32), "ndum": (1, f32), "dum": (1, f32), "b16p": (1, f32), "k16": (1, f32), "k17": (1, f32), "pwc": (1, f32), "pc": (2, f32),
+    "cid": (128, b16), "gid": (128, b16), "aid": (128, b16), "g8": (8, f32), "bj": (16, f32),
+    "I32": (128, f32), "I20": (128, b16), "Im20": (128, b16), "pw20": (128, b16), "I2k": (128, b16), "Im2k": (128, b16), "I4k": (128, b16), "I19": (128, b16), "Im19": (128, b16), "k8": (8, i32), "kl": (128, b16), "Ib": (128, b16), "I16": (128, b16), "Im16": (128, b16),
+    "ImQ": (128, b16), "IpQ": (128, b16), "Im64": (128, b16), "Im256": (128, b16), "I256": (128, b16), "IH": (128, b16), "I2H": (128, b16), "Ig": (128, b16),
+    "bo": (128, b16), "bo32": (128, f32), "bo256": (128, b16), "boS": (128, b16), "boT": (128, b16), "boU": (128, b16), "boE": (128, b16),
+    "Z": (144, b16), "M0": (128, b16), "cm": (128, b16), "c1": (128, b16), "c2": (128, b16), "c3": (128, b16), "mk2": (256, b16), "d0a": (512, b16), "ab": (1024, b16),
+    "bo8": (8, b16), "bo8f": (8, f32), "bo8n": (8, b16), "wm": (8, b16), "wa": (16, b16), "wd": (16, b16), "wr2": (16, b16), "tie2": (256, b16),
+    "bo8d": (8, h16), "bo8k": (8, h16), "bo16": (8, b16), "bo8a": (8, b16), "bo64": (8, b16), "bo8p": (8, h16),
     "on": (128, b16), "on32": (128, f32), "m15": (128, b16), "tie16": (128, b16), "m16": (128, b16),
     "d0s": (128, f32), "d0m": (256, f32), "d0p": (128, f32), "d0b": (576, b16), "pwr": (128, b16), "hlf": (128, f32), "zer": (128, f32),
-    "wr": (128, b16), "wc": (1, b16), "wt": (1, f32), "eI": (512, b16), "E": (512, b16), "sl8": (1024, b16),
-    "l3I": (8, i32), "l8I": (8, i32), "L3": (8, u16), "L8": (8, u16),
+    "wr": (128, b16), "wc": (1, b16), "wt": (1, f32), "eI": (512, b16), "E": (512, b16), "sl": (1024, b16),
+    "l3I": (8, i32), "l8I": (8, i32), "lkI": (8, i32), "L3": (8, u16), "L8": (8, u16), "LK": (8, u16),
     "pay": (384, b16), "w3": (24, b16), "d0h": (128, f32), "d1h": (128, f32), "pwd": (128, f32),
-    "limf": (1, f32), "limc": (1, f32), "lim8": (8, f32), "pofI": (128, b16), "pofm": (128, h16),
-    "TQ": (XS - 16, f32), "pc": (2, f32), "tA": (1, f32), "tB": (1, f32), "k16": (1, f32), "bo4n": (8, b16),
-    "bo8a": (8, b16), "bo64": (8, b16), "bo8s": (8, b16), "bo8p": (8, h16), "payW": (24, b16), "bigW": (24, b16), "tieW": (16, b16), "far": (24, b16),
-    "eN": (128, b16), "e8": (8, f32), "le": (8, u16), "th2": (8, f32), "xe": (128, b16), "nhi": (128, b16), "nlo": (128, h16), "RN": (128, f32),
-    "nq": (128, h16), "kz": (16, i32), "ky": (16, i32),
-    "WA": (2048, b16), "WB": (2048, b16), "lf": (128, f32), "l0": (128, u16),
-    "lu1": (128, u16), "lu2": (128, u16), "lu4": (128, u16), "lu8": (128, u16), "wyb": (128, b16),
+    "limf": (1, f32), "limc": (1, f32), "lim8": (8, f32), "TQ": (XS - 16, f32), "ini": (512, b16), "far": (128, b16), "kr": (256, b16),
+    "B": (2048, b16), "Aj": (2048, b16), "Dn": (1024, b16), "M2": (128, b16), "b1": (16, f32), "n0r": (2048, b16), "N": (2048, b16), "M": (512, b16), "rt": (128, b16), "nw": (128, b16), "wy32": (128, f32),
+    "wI": (256, b16), "dl": (256, b16), "Kc": (256, b16), "Kd": (256, b16), "K": (256, b16), "pofI": (128, b16), "pofm": (128, h16),
+    "c15": (1, f32), "c14": (1, f32), "a16": (1, f32), "n15": (1, f32), "pw14": (1, f32), "Zc": (144, b16), "Zw": (144, b16),
+    "l0": (128, u16), "lu1": (128, u16), "lu2": (128, u16), "lu4": (128, u16), "lu8": (128, u16), "WA": (2048, b16), "WB": (2048, b16),
+    "qa": (128, f32), "qb": (128, f32), "qc": (128, f32),
+    "eN": (128, b16), "e8": (8, f32), "le": (8, u16), "th2": (8, f32), "xe": (128, b16), "RN": (128, f32), "nq": (128, h16),
     "x": (2048, b16), "x2": (2048, b16), "xc": (2048, b16), "mn": (2048, b16), "vf": (1024, b16), "bs": (2048, h16), "RA": (2048, f32),
-    "eR": (128, b16), "e2": (128, b16), "q16": (128, h16), "aP": (128, f32), "aS": (128, f32), "aM": (128, f32), "a1": (128, f32), "a2": (128, f32),
-    "n0": (8, f32), "thr": (8, f32), "my": (256, i32), "sm": (128, f32), "qhi": (128, b16),
-    "dz": (24, f32), "dy": (24, f32), "nz": (24, i32), "ny": (24, i32), "pz": (24, f32), "yz": (24, f32), "pr": (128, i32), "bb": (128, i32), "q2P": (128, h16), "q2u": (128, u16), "q2h": (128, h16),
-    "lo": (128, h16), "cP": (128, h16), "e0": (256, f32), "e1": (384, b16),
-    "mk": (128, i32), "r8": (8, i32), "ok": (128, b16), "AL": (128, h16), "lk": (8, u16),
+    "eR": (128, b16), "e2": (128, b16), "q16": (128, h16), "aM": (128, f32), "a1": (128, f32), "a2": (128, f32),
+    "n0": (8, f32), "thr": (8, f32), "sm": (128, f32), "mr": (384, i32), "dz": (16, f32), "nz": (16, i32), "pz": (16, f32),
+    "slm": (1024, b16), "tri": (512, b16), "ZA": (128, f32), "pwB": (256, b16), "pwR": (128, f32), "tb": (128, h16), "kb": (128, h16), "pr": (256, i32), "bb": (256, i32), "gb": (256, b16), "aP": (256, f32), "s8": (8, i32), "l16I": (16, i32), "L16": (16, u16), "okK": (128, b16),
+    "qd": (512, h16), "sq": (512, h16), "q2u": (128, u16), "w": (128, b16), "rm": (128, h16), "yq": (128, h16), "sg": (128, b16),
+    "lo": (128, h16), "cP": (128, h16), "e0": (128, f32), "e3": (256, f32), "e1": (384, b16),
+    "mk": (128, i32), "r8": (8, i32), "ok": (128, b16), "AL": (128, h16), "AE": (128, h16), "lk": (8, u16),
     "cd": (128, u16), "cd16": (128, h16), "oka": (128, f32), "okb": (128, b16), "t3": (128, f32),
-    "chi": (128, b16), "ms": (256, i32), "n16": (16, i32), "AN": (256, h16), "pwB": (128, f32),
-    "pq": (128, f32), "sq": (128, f32), "y8": (8, f32), "y16": (8, h16), "yT": (128, h16), "eq": (1024, b16),
-    "du": (8, f32), "ya": (8, f32), "of": (8, f32), "AS": (128, h16), "ls": (8, u16),
-    "ti": (128, f32), "xs": (128, f32), "xn": (128, i32), "cj": (8, f32), "cn": (1, f32), "cz": (1, h16), "cc": (1, f32),
+    "chi": (128, b16), "ms": (256, i32), "n16": (32, i32), "AN": (512, h16),
+    "y8": (8, f32), "eq": (1024, b16), "du": (8, f32), "ya": (8, f32), "of": (8, f32), "AS": (128, h16), "ls": (8, u16),
+    "ti": (128, f32), "xs": (128, f32), "xn": (128, i32), "cj": (1, f32), "cn": (1, f32), "cz": (1, h16), "cc": (1, f32),
     "yt": (128, f32), "yw": (128, f32), "fR": (128, f32), "fr": (128, f32),
 }
 ALONE = ("X", "R", "dr0", "wy0", "lmI", "yt", "yw")
@@ -64,16 +67,70 @@ for _t in range(1, VI):
     SCRATCH["rq%d" % _t] = ("sbuf", [128, H], u16)
     SCRATCH["rv%d" % _t] = ("sbuf", [128, H], f32)
     SCRATCH["n%d" % _t] = ("sbuf", [128, 8], u16)
-    SCRATCH["no%d" % _t] = ("sbuf", [128, 8], u16)
+    SCRATCH["no%d" % _t] = ("sbuf", [128, 16], u16)
     SCRATCH["rn%d" % _t] = ("sbuf", [128, 4], u16)
 PS = ("pA", "pB", "pC", "pD", "pE", "pF", "pG", "pH")
 for _p in PS:
     SCRATCH[_p] = ("psum", [128, 512], f32)
-SEMAPHORES = ["ev", "es", "et", "eg", "loc"] + ["ld%d" % _t for _t in range(5)] + ["st%d" % _t for _t in range(3)]
+SEMAPHORES = ["ev", "es", "et", "eg", "loc"] + ["ld%d" % _t for _t in range(6)] + ["st%d" % _t for _t in range(3)]
 for _t in range(1, VI):
     SEMAPHORES += ["%s%d" % (_n, _t) for _n in ("qL", "qH", "vL", "vH", "nL", "nH", "rq", "rv", "rn")]
 HALF = {"q": H, "v": H, "n": 4}
-HV = ((0, 64), (64, 128))
+CYC, PEC, GAT, SCA, WAKE, HOP, DMA = 0.83e-3, 0.42e-3, 1.56, 3.8, 0.2, 1.1, 1.0
+CUT1 = (0, 16, 32, 48, 64, 80, 96, 112, 128)
+CUT2 = (0, 32, 64, 96, 128)
+LATE = 4.0
+SWEEPS = 0
+SPARE = 0.2
+DK = True
+DBL = True
+TWIN = False
+HELP = ()
+ABS = True
+SHARE = 0
+MORE = {'up': 1, 'lk': 1.0, 'xs': 0.75, 'bs': 0.5, 'up2': 1.0, 'e3': 2.0, 'yq': 1.0, 'eN': 0.5, 'aM': 0.5, 'oka': 0.25, 'xn': 0.5, 'x': 0.25, 'pH': 0.25, 'AL': 0.5, 'okK': 0.25, 'pG': 0.5, 'a2': 1.0, 'tb': 0.5, 't3': 0.25, 'cz': 0.5, 'cd16': 1.0, 'pay': 1.0, 'c1': 0.25, 'N': 0.25, 'w3': 2.0, 'sl': 2.0, 'n16': 0.25, 'ls': 0.5}
+TURN = 14.0
+DUE = {"xe0": 0.0, "nq0": 0.0, "qd0": 0.4, "sq0": 0.7, "qo0": 1.1, "xe1": 1.1, "nq1": 1.15, "x2_0": 1.6, "x2_32": 1.4, "qd1": 1.5, "sq1": 1.8, "qo1": 2.2,
+       "w": 2.0, "rm": 2.3, "yq": 2.45, "x2_64": 2.5, "x2_96": 2.45, "e2": 2.4, "bs_0": 2.6, "bs_32": 2.65, "bs_64": 3.3, "bs_96": 3.35, "sg": 3.3,
+       "eq0": 3.35, "eq1": 3.4, "lo": 3.8, "ab0": 3.9, "mk": 4.3, "ab1": 4.35, "ya": 4.2, "cP": 4.5, "r8": 4.6, "du": 4.7, "ok": 4.85, "AS": 4.95,
+       "AL": 5.5, "ls": 5.6, "vf0": 5.3, "vf1": 5.7, "xs": 5.9, "lk": 6.4, "xn": 6.5, "cd": 6.7, "up": 6.9, "mn_0": 7.1, "mn_64": 7.1, "mn_96": 7.8,
+       "mn_32": 7.8, "cd16": 6.7, "chi": 6.8, "pwR": -4.0, "xc0": 8.6, "xc2": 8.6, "xc1": 8.8, "xc3": 9.0, "oka": 5.7, "t3": 5.0, "vo": 6.4, "y8": 2.9, "ms": 10.0, "n16": 10.4,
+       "AN0": 10.6, "AN8": 10.8, "no": 11.5, "x_0": 9.4, "x_16": 9.5, "x_32": 9.6, "x_48": 9.7, "x_64": 10.2, "x_80": 10.6, "x_96": 11.0, "x_112": 11.4,
+       "mr1": 12.2, "nz": 12.6, "mr0": 12.7, "sm": 12.75, "pr": 12.9, "bb": 13.4, "gb0": 13.8, "gb128": 13.8}
+ENG = {k: "s" for k in "kb w eN e1 e2 eR chi cd16 aP gb0 a1 a2 aM ya e0 e3 x_0 x_32 x_64 x_96 cP tb ti cn cz cc limc lim8".split()}
+ENG.update({k: "v" for k in "x_16 x_48 x_80 x_112 gb128".split()})
+DUE = {'pwR': -4.0, 'xe0': -2.8, 'x2_0': 0.03, 'bs_32': 0.4, 'qo0': 0.63, 'rm': 1.38, 'qd1': 1.75, 'nq1': 1.75, 'x2_64': 2.09, 'qo1': 2.42, 'bs_0': 2.5, 'x2_96': 2.55, 'eq0': 2.85, 'AS': 2.9, 'a1': 3.08, 'e2': 3.2, 'eq1': 3.2, 'bs_64': 3.75, 'vf0': 4.2, 'sg': 4.28, 'mk': 4.6, 'ab1': 4.65, 'du': 4.71, 'cP': 4.8, 'ya': 5.2, 'oka': 5.2, 'AL': 5.5, 'lim8': 5.52, 't3': 5.6, 'cd16': 5.8, 'chi': 5.82, 'mn_0': 6.1, 'vf1': 6.7, 'cd': 6.7, 'vo': 6.82, 'mn_32': 7.44, 'pr': 7.6, 'xc0': 8.01, 'AN0': 8.57, 'x_16': 9.22, 'x_0': 9.4, 'x_32': 9.48, 'q16': 9.8, 'ms': 10.0, 'x_48': 10.18, 'x_80': 10.3, 'AN8': 10.55, 'n16': 10.57, 'x_64': 11.2, 'e0': 11.26, 'x_112': 11.8, 'sm': 12.15, 'th2': 13.03, 'mr1': 13.05, 'x_96': 13.07, 's8': 13.45, 'nz': 13.57}
+ENG = {k: "s" for k in "kb w e1 e2 chi cd16 aP gb0 a2 aM e0 e3 x_0 x_32 x_48 x_64 x_96 cP tb ti cn cz cc limc lim8 x2_32 x2_96 y8 sq pwR fR t3".split()}
+ENG.update({k: "v" for k in "eN eR a1 ya x_16 x_80 x_112 gb128 x2_0 x2_64 n0 okb yt".split()})
+DBL, HOP, TURN, DRAIN, WAKE = False, 1.3, 15.5, 0.14, 0.18
+DUE = {'x0_112': -7.99, 'x0_0': -7.52, 'x0_16': -7.22, 'x0_64': -7.19, 'pwR': -4.0, 'nq1': -3.4, 'qd1': -2.4, 'yq': -0.21, 'bs_96': 0.45, 'qd0': 0.48, 'x2_32': 0.8, 'rm': 0.89, 'x2': 0.98, 'sq1': 0.99, 'w': 1.52, 'x2_64': 1.74, 'bs_32': 1.82, 'mk': 1.94, 'x2_0': 2.0, 'bs_0': 2.36, 'x2_96': 2.45, 'e2': 2.83, 'bs_64': 2.94, 'ab0': 4.07, 'cd16': 4.36, 'ab1': 4.75, 'mn_64': 4.9, 'AL': 4.9, 'vo': 5.0, 'ok': 5.01, 'ti': 5.05, 'du': 5.13, 't3': 5.4, 'fr': 5.63, 'chi': 5.98, 'cd': 6.9, 'mn_0': 6.98, 'x_32': 7.98, 'x_0': 8.36, 'x_48': 8.36, 'AN0': 8.97, 'AN8': 9.25, 'n16': 9.27, 'x_64': 9.7, 'x_80': 9.9, 'e0': 10.7, 'q16': 10.72, 'k8': 12.26, 'pr': 12.67, 's8': 13.8, 'th2': 14.58, 'kb': 15.37, 'gb128': 15.44, 'nz': 15.46}
+ENG = {k: "s" for k in "kb e1 chi cd16 aP a2 aM e0 e3 x_0 x_32 x_48 x_64 x_96 cP tb cn cc limc x2_32 x2_96 y8 sq pwR a1 ya x2_0 n0 x0_16 x0_32 x0_48 x0_96 x0_64 kl x0_112 x0_0".split()}
+ENG.update({k: "v" for k in "w e2 gb0 ti cz lim8 fR t3 eN eR x_16 x_80 x_112 gb128 x2_64 okb yt x0_80".split()})
+SUMS = (("mn", 2, "wd"), ("mn", 0, "wd"), ("xc", 2, "wr2"), ("xc", 0, "wr2"), ("xc", 3, "wa"), ("xc", 1, "wa"))
+TURN, GAT, WAKE, DRAIN, VFIX = 15.2, 1.3, 0.23, 0.0, 0.02
+DUE = {'x0_0': -9.2, 'pwR': -4.1, 'qd0': -1.46, 'x2_32': 0.25, 'qd1': 0.31, 'x2_0': 0.51, 'sq0': 0.53, 'yq': 1.07, 'w': 1.74, 'x2_64': 1.95, 'rm': 1.97, 'x2_96': 2.42, 'qo1': 2.72, 'bs_32': 3.47, 'x2': 3.49, 'bs_0': 3.77, 'eq0': 4.76, 'bs_96': 4.93, 'bs_64': 4.95, 'eq1': 4.98, 'mk': 5.63, 'dk': 5.93, 'AL': 5.94, 'ti': 6.0, 'xc2': 6.24, 'AS': 6.28, 'vf0': 6.46, 'vf2': 6.48, 'q16': 6.76, 't3': 6.9, 'cd16': 8.18, 'xc1': 8.46, 'mn_96': 8.68, 'xc3': 8.93, 'mn_32': 9.16, 'mn_0': 9.18, 'xc0': 10.06, 'up': 10.66, 'chi': 10.66, 'lk': 10.68, 'n0': 10.74, 'xn': 10.75, 'nz': 11.1, 'eR': 11.15, 'AN8': 11.24, 'AN0': 11.54, 'ms': 11.84, 'thr': 11.86, 'no': 12.49, 'x_112': 12.79, 'mr1': 13.2, 'k8': 13.72, 'e0': 14.3, 'gb128': 15.5}
+ENG = {k: "s" for k in ("kb e1 chi cd16 aP a2 aM e0 e3 x_0 x_32 x_48 x_64 x_96 cP tb cn x2_32 x2_96 y8 sq a1 ya x2_0 n0 x0_16 x0_32 x0_48 x0_96 x0_64 kl "
+                        "x0_112 x0_0 ti cz fR t3 eN gb128 yt x0_80").split()}
+ENG.update({k: "v" for k in "cc limc pwR w e2 gb0 lim8 eR x_16 x_80 x_112 x2_64 okb".split()})
+SPARE, SFIX, GAT, WAKE, VFIX = 0.1, 0.07, 1.4, 0.18, 0.0
+DUE = {'x0_80': -11.72, 'x0_16': -9.3, 'pwR': -3.4, 'x2_64': -3.15, 'w': -1.96, 'yq': -1.03, 'x2_96': -0.78, 'x2_0': -0.36, 'x2_32': -0.06, 'ti': 0.14, 'qd0': 0.24, 'nq1': 0.54, 'rm': 1.07, 'qo1': 1.22, 'okK': 1.59, 'bs_0': 2.75, 'bs_32': 2.82, 'vf2': 3.15, 'bs_96': 3.51, 'bs_64': 3.53, 'ab0': 4.43, 'lo': 4.75, 'eq1': 4.86, 'ok': 4.95, 'eq0': 5.18, 'du': 5.63, 'mk': 5.65, 'AL': 6.34, 'vf0': 6.56, 'q16': 6.86, 'xn': 6.86, 't3': 8.5, 'dk': 9.38, 'xs': 9.96, 'AN0': 10.04, 'x_48': 10.92, 'mn_0': 11.24, 'x_80': 11.42, 'ms': 11.44, 'mn_64': 11.74, 'mn_96': 11.74, 'mn_32': 11.92, 'AN8': 12.02, 'chi': 12.02, 'lk': 12.04, 'x_112': 12.38, 'no': 12.4, 'up': 12.72, 'eN': 13.2, 'pr': 13.21, 'sm': 13.33, 'bb': 13.71, 'eR': 13.75, 's8': 14.29, 'e0': 14.5, 'up2': 14.57, 'nz': 14.61, 'k8': 14.61, 'mr0': 14.63}
+ENG = {k: "s" for k in ("kb e1 chi cd16 aP a2 aM e0 e3 x_0 x_32 x_64 x_96 cP tb cn x2_32 x2_96 y8 sq a1 ya x2_0 x0_16 x0_32 x0_48 x0_96 x0_64 kl x0_112 x0_0 "
+                        "ti cz fR t3 eN gb128 yt x0_80 cc limc pwR w gb0 lim8 eR x_16 okb").split()}
+ENG.update({k: "v" for k in "x_48 n0 e2 x_80 x_112 x2_64".split()})
+TURN = 15.2
+DUE = {'x0_80': -6.58, 'x0_16': -5.58, 'pwR': -2.5, 'x2_0': -2.25, 'okK': -1.62, 'qd1': 0.24, 'bs_96': 2.76, 'qo1': 2.86, 'x2': 2.98, 'e3': 3.0, 'bs_0': 3.08, 'bs_64': 3.2, 'lo': 3.2, 'bs_32': 3.5, 'okm': 3.6, 'sg': 3.78, 'aM': 3.92, 'eq1': 3.94, 'a2': 4.02, 'du': 4.4, 'AL': 4.42, 'ti': 4.54, 'ya': 4.6, 'oka': 4.78, 'vo': 4.99, 'vf0': 5.19, 'mn_64': 5.19, 't3': 5.21, 'xn': 5.23, 'ls': 5.98, 'xc2': 6.3, 'mn_0': 7.0, 'AN0': 7.16, 'cd': 7.3, 'no': 7.56, 'q16': 7.76, 'xc0': 7.88, 'AN8': 7.96, 'x_80': 8.08, 'x_112': 8.1, 'x_16': 8.14, 'ms': 8.16, 's8': 8.92, 'bb': 8.94, 'xs': 9.1, 'gb0': 9.94, 'nz': 10.84, 'k8': 10.86, 'up2': 11.45, 'mr0': 11.56}
+ENG = {k: "s" for k in ("kb chi cd16 aP a2 aM e0 e3 x_0 x_32 x_48 x_64 x_96 cP tb cn x2_32 x2_96 sq pwR a1 x2_0 x0_16 x0_48 x0_96 x0_64 kl x0_112 x0_0 t3 eN eR "
+                        "gb128 okb x0_80").split()}
+ENG.update({k: "v" for k in "e1 cc limc ya n0 x0_32 w e2 gb0 ti cz lim8 fR x_16 x_80 x_112 x2_64 yt".split()})
+WAKE, GAT, SFIX, SPARE = 0.25, 1.3, 0.03, 0.15
+DUE = {'x0_80': -7.05, 'x0_16': -5.41, 'nq1': -4.47, 'x0_0': -3.43, 'pwR': -2.2, 'x2_96': -0.26, 'yq': 0.59, 'okm': 1.2, 'qo1': 1.26, 'mk': 1.88, 'bs_32': 2.22, 'bs_0': 2.24, 'x2': 2.24, 'bs_96': 2.24, 'bs_64': 2.7, 'vf2': 2.7, 'e3': 2.82, 'e1': 3.08, 'fr': 3.6, 'sg': 3.71, 'du': 4.2, 'ab1': 4.6, 'vo': 4.61, 'vf0': 4.68, 'ya': 4.7, 'aP': 5.48, 't3': 5.61, 'mn_96': 6.7, 'AN0': 7.46, 'chi': 7.54, 'xc0': 7.68, 'xc2': 7.68, 'mn_32': 7.68, 'cd': 7.7, 'AN8': 8.14, 'ms': 8.16, 's8': 10.08, 'mr1': 10.76, 'k8': 10.98, 'x_0': 11.38, 'xn': 11.58, 'eN': 12.13}
+ENG = {k: "s" for k in "kb chi cd16 aP a2 aM e0 x_0 x_32 x_48 x_64 x_96 cP tb cn x2_32 x2_96 sq a1 x2_0 x0_16 x0_48 x0_64 kl x0_0 t3 eN eR gb128 x0_80 cc limc ya ti lim8 x_80".split()}
+ENG.update({k: "v" for k in "e3 pwR x0_96 x0_112 okb e1 n0 x0_32 w e2 gb0 cz fR x_16 x_112 x2_64 yt".split()})
+FIRST, PEC, WAKE = 5.2, 0.54e-3, 0.21
+DUE = {'x0_80': -6.28, 'x2_32': -0.89, 'x2_0': -0.87, 'a2': 1.75, 'qo1': 1.86, 'y8': 1.88, 'vf2': 2.5, 'eq0': 2.78, 'okm': 2.88, 'mk': 3.78, 'lo': 3.88, 'vf0': 4.38, 'sg': 4.46, 'ab0': 5.08, 'ti': 5.1, 'aP': 5.88, 'chi': 6.24, 'mn_64': 6.49, 'vo': 6.51, 'cd16': 7.86, 'xc2': 8.5, 'thr': 8.81, 'x_16': 8.88, 'cd': 9.1, 'ms': 9.16, 'xn': 9.38, 'q16': 9.85, 'e0': 11.54, 'eR': 11.81, 'x_112': 12.52, 'bb': 12.6}
+ENG = {k: "s" for k in "chi cd16 aP a2 x_0 x_32 x_48 x_64 x_96 cP tb x2_32 x2_96 sq a1 x2_0 x0_16 x0_48 x0_64 kl x0_0 t3 gb128 pwR x0_96 aM cn limc ya e3 x0_112 okb x0_32".split()}
+ENG.update({k: "v" for k in "kb ti x_80 e1 e0 eN eR x0_80 cc lim8 n0 w e2 gb0 cz fR x_16 x_112 x2_64 yt y8".split()})
+PLAN = {}
 
 
 def relay_of(core, dst, topo):
@@ -93,437 +150,247 @@ def rank_program(g, core, T, topo):
         for r, c in enumerate(T.cores):
             dst = T.cores[(r + STRIDE[1]) % NR]
             if relay_of(c, dst, topo) == core:
-                relay(g, core, dst, T, topo)
+                relay(g, core, c, dst, T, topo)
         return
     member(g, core, rank, T, topo)
 
 
-def relay(g, core, dst, T, topo):
+def relay(g, core, src, dst, T, topo):
     rid, pid = topo.addr(dst, core)
     m = bits(topo, core, dst, 8, False)
     for t in range(1, VI):
         for k in "qvn":
-            g.wait_ge(T.sem["r%s%d" % (k, t)], 8)
+            g.wait_ge(T.sem["r%s%d" % (k, t)], len(topo.engines(src, core)) if k == "n" else 8)
             g.remote_dma(T["%s%d" % (k, t)][:, HALF[k]:2 * HALF[k]], T["r%s%d" % (k, t)][:, :], T.sem["%sH%d" % (k, t)], T.sem["loc"], pid, rid, m)
     g.wait_ge(T.sem["loc"], 24 * (VI - 1))
+
+
+def clash(a, b):
+    if a["lo"] >= b["hi"] or b["lo"] >= a["hi"] or a["r0"] >= b["r1"] or b["r0"] >= a["r1"]:
+        return False
+    return not (a["st"] > 1 and a["st"] == b["st"] and (a["lo"] - b["lo"]) % a["st"])
+
+
+def covers(a, b):
+    return a["st"] == 1 and a["lo"] <= b["lo"] and b["hi"] <= a["hi"] and a["r0"] <= b["r0"] and b["r1"] <= a["r1"]
+
+
+def links(ops):
+    recs, pre = {}, []
+    for i, o in enumerate(ops):
+        d = dict(o["after"])
+        acc = [(a, True) for a in o["outs"]] + [(a, False) for a in o["ins"]]
+        for a, wr in acc:
+            l = recs.setdefault(a["n"], [])
+            if a["n"] in PS:
+                for b, bw, j in l[-1:] + [r for r in l if r[1] and not wr and "t" not in ops[r[2]]["alts"] and clash(a, r[0])]:
+                    d[j] = d.get(j, False) or (bw and "t" not in ops[j]["alts"])
+                continue
+            for b, bw, j in l:
+                if (wr or bw) and clash(a, b):
+                    d[j] = True
+        for a, wr in acc:
+            l = recs[a["n"]]
+            if wr and a["n"] not in PS:
+                l[:] = [b for b in l if not covers(a, b[0])]
+            l.append((a, wr, i))
+        d.pop(i, None)
+        pre.append(d)
+    return pre
+
+
+def first(l, t):
+    a, b = 0, len(l)
+    while a < b:
+        m = (a + b) // 2
+        if l[m][1] <= t:
+            a = m + 1
+        else:
+            b = m
+    return a
+
+
+def order(ops, pre):
+    n = len(ops)
+    due = [VI * 100.0] * n
+    for i in range(n - 1, -1, -1):
+        o = ops[i]
+        due[i] -= min(c for _, c in o["alts"].values()) + o["lat"]
+        if o["name"] in DUE and o["turn"] is not None:
+            due[i] = o["turn"] * TURN + DUE[o["name"]]
+        for j, hard in pre[i].items():
+            due[j] = min(due[j], due[i] - (WAKE if hard or set(ops[j]["alts"]) != set(o["alts"]) else 0.0))
+    for i in range(n):
+        for j in pre[i]:
+            due[i] = max(due[i], due[j] + 1e-6)
+    busy, place = {}, [None] * n
+    PLAN["due"] = due
+    for i in sorted(range(n), key=lambda k: (due[k], k)):
+        o, best = ops[i], None
+        for q, (_, c) in o["alts"].items():
+            if o["turn"] is not None and ENG.get(o["name"], q) in o["alts"] and ENG.get(o["name"], q) != q:
+                continue
+            t = 0.0
+            for j, hard in pre[i].items():
+                pq, s, e = place[j]
+                t = max(t, e + ops[j]["lat"] + WAKE if hard or pq != q else e)
+            if q != "-":
+                l = busy.setdefault(q, [])
+                k = first(l, t + 1e-9)
+                while k < len(l) and l[k][0] < t + c - 1e-9:
+                    t = l[k][1]
+                    k += 1
+            f = t + c + (SPARE if q == "v" else 0.0)
+            if best is None or f < best[3] - 1e-9:
+                best = (q, t, t + c, f)
+        place[i] = best = best[:3]
+        if best[0] != "-":
+            l = busy[best[0]]
+            l.insert(first(l, best[1] + 1e-9), (best[1], best[2]))
+    return pre, place, sorted(range(n), key=lambda k: (place[k][1], k))
 
 
 def member(g, core, rank, T, topo):
     Q = {"v": g.vector, "s": g.scalar, "t": g.tensor, "g": g, "y": g.sync}
     ES = {"v": "ev", "s": "es", "t": "et", "g": "eg"}
-    cnt = {}
-    known = {q: {} for q in Q}
-    snap = {}
-    recs = {}
-    psum = set(PS)
+    ops = []
+    turn = [None]
 
     def vw(name, lo=0, hi=None, st=1, r0=0, r1=128):
+        d, nm = SB[name][1] if name in SB else SCRATCH[name][2], name.rstrip("0123") if name not in SB else name
         if hi is None:
             hi = SB[name][0] if name in SB else SCRATCH[name][1][1]
         if name in ALIAS:
             name, o = ALIAS[name]
             lo, hi = lo + o, hi + o
         ap = T[name][r0:r1, lo:hi:st] if st > 1 else T[name][r0:r1, lo:hi]
-        return {"ap": ap, "n": name, "lo": lo, "hi": hi, "st": st, "x": None, "r0": r0, "r1": r1}
+        return {"ap": ap, "n": name, "lo": lo, "hi": hi, "st": st, "x": None, "r0": r0, "r1": r1, "k": len(range(lo, hi, st)), "b": 2 if "16" in d else 4, "d": d, "name": nm}
 
     def ind(w, o):
-        return dict(w, ap=w["ap"].indirect(o["ap"]), x=o)
+        return dict(w, ap=w["ap"].indirect(o["ap"]), x=o, k=16 * o["k"])
 
-    def clash(a, b):
-        if a["n"] in psum:
-            return True
-        if a["lo"] >= b["hi"] or b["lo"] >= a["hi"] or a["r0"] >= b["r1"] or b["r0"] >= a["r1"]:
-            return False
-        return not (a["st"] > 1 and a["st"] == b["st"] and (a["lo"] - b["lo"]) % a["st"])
-
-    def covers(a, b):
-        return a["lo"] <= b["lo"] and b["hi"] <= a["hi"] and a["r0"] <= b["r0"] and b["r1"] <= a["r1"]
-
-    def need(q, tok):
-        s, n = tok
-        if known[q].get(s, 0) >= n:
-            return
-        Q[q].wait_ge(T.sem[s], n)
-        known[q][s] = n
-        for k, m in snap.get(tok, {}).items():
-            if known[q].get(k, 0) < m:
-                known[q][k] = m
-
-    def expand(vs):
+    def op(alts, outs, ins, sem=None, inc=1, lat=0.0, after=()):
         r = []
-        for a in vs:
+        for a in ins + [a["x"] for a in outs]:
             if isinstance(a, dict):
                 r.append(a)
                 if a["x"]:
                     r.append(a["x"])
-        return r
+        ops.append({"alts": alts, "outs": outs, "ins": r, "sem": sem, "inc": inc, "lat": lat, "after": list(after),
+                    "name": outs[0]["name"] if outs else "", "turn": turn[0]})
+        return len(ops) - 1
 
-    def deps(q, outs, ins):
-        best = {}
-        for a, wr in [(a, True) for a in outs] + [(a, False) for a in ins]:
-            for b, bw, tok, bq in recs.get(a["n"], []):
-                if not clash(a, b):
-                    continue
-                if a["n"] in psum:
-                    over = not (a["lo"] >= b["hi"] or b["lo"] >= a["hi"])
-                    if bq == q and (q == "t" or not (over and bw and not wr)):
-                        continue
-                else:
-                    if not wr and not bw:
-                        continue
-                    if bq == q and q != "y" and not bw:
-                        continue
-                best[tok[0]] = max(best.get(tok[0], 0), tok[1])
-        for s in sorted(best):
-            need(q, (s, best[s]))
-
-    def note(q, tok, outs, ins):
-        for a, wr in [(a, True) for a in outs] + [(a, False) for a in ins]:
-            l = recs.setdefault(a["n"], [])
-            if wr and a["st"] == 1 and a["n"] not in psum:
-                l[:] = [b for b in l if not covers(a, b[0])]
-            elif a["n"] in psum or not wr:
-                l[:] = [b for b in l if not (b[3] == q and b[1] == wr and b[0]["st"] == a["st"] and covers(a, b[0]) and covers(b[0], a))]
-            l.append((a, wr, tok, q))
-
-    def op(q, outs, ins, fn, sem=None, inc=1):
-        ins = expand(ins + [a["x"] for a in outs])
-        deps(q, outs, ins)
-        s = sem or ES[q]
-        fn().then_inc(T.sem[s], inc)
-        cnt[s] = cnt.get(s, 0) + inc
-        tok = (s, cnt[s])
-        snap[tok] = dict(known[q])
-        note(q, tok, outs, ins)
+    def more(name):
+        ops[-1]["name"] = name
 
     def P(a):
         return a["ap"] if isinstance(a, dict) else a
 
+    def vcost(o, ins, rate=1.0):
+        if o["x"]:
+            return 0.05 + SCA * o["k"] * CYC
+        if ins and ins[0]["x"]:
+            return 0.05 + GAT * o["k"] * CYC
+        if rate == 1.0 and all(a["b"] == 2 for a in [o] + ins):
+            rate /= 2
+        return max(64, rate * o["k"]) * CYC + VFIX
+
+    def scost(o, i):
+        return 0.065 + GAT * o["k"] * CYC if i["x"] else max(64, o["k"]) * CYC + SFIX
+
     def copy(o, i):
-        op("v", [o], [i], lambda: g.vector.tensor_copy(P(o), P(i)))
+        op({"v": (lambda: g.vector.tensor_copy(P(o), P(i)), vcost(o, [i]))}, [o], [i])
 
     def tt(o, a, b, f):
-        op("v", [o], [a, b], lambda: g.vector.tensor_tensor(P(o), P(a), P(b), f))
+        r = 1.0 if a["n"] in PS or b["n"] in PS else 2.0
+        op({"v": (lambda: g.vector.tensor_tensor(P(o), P(a), P(b), f), vcost(o, [a, b], r))}, [o], [a, b])
+
+    def tsf(o, a, s1, f1, s2=None, f2=None):
+        if s2 is None:
+            return lambda: g.vector.tensor_scalar(P(o), P(a), P(s1), None, f1)
+        return lambda: g.vector.tensor_scalar(P(o), P(a), P(s1), P(s2), f1, f2)
 
     def ts(o, a, s1, f1, s2=None, f2=None):
-        if s2 is None:
-            op("v", [o], [a, s1], lambda: g.vector.tensor_scalar(P(o), P(a), P(s1), None, f1))
-        else:
-            op("v", [o], [a, s1, s2], lambda: g.vector.tensor_scalar(P(o), P(a), P(s1), P(s2), f1, f2))
+        op({"v": (tsf(o, a, s1, f1, s2, f2), vcost(o, [a]))}, [o], [a, s1, s2])
 
     def scan(o, d0, d1, f0, f1, init=0.0):
-        op("v", [o], [d0, d1], lambda: g.vector.tensor_tensor_scan(P(o), P(d0), P(d1), init, f0, f1))
+        op({"v": (lambda: g.vector.tensor_tensor_scan(P(o), P(d0), P(d1), init, f0, f1), vcost(o, [d0, d1]))}, [o], [d0, d1])
 
-    def fill(o, c):
-        op("v", [o], [], lambda: g.vector.memset(P(o), c))
+    def least(o, i):
+        op({"v": (lambda: g.vector.tensor_reduce(P(o), P(i), AxisListType.X, A.min, apply_absolute_value=True), max(64, i["k"]) * CYC)}, [o], [i])
+
+    def fill(o, c, qs="v"):
+        alts = {"v": (lambda: g.vector.memset(P(o), c if o["d"] != i32 else int(c)), vcost(o, []))}
+        if "g" in qs:
+            alts["g"] = (iotaf(o, [[0, o["k"]]], int(c), 0), 0.13 + 2 * o["k"] * CYC)
+        op(alts, [o], [])
+
+    def actf(o, i, scale, bias, func):
+        return lambda: g.scalar.activation(P(o), P(i), func, bias=P(bias), scale=P(scale))
 
     def act(o, i, scale=1.0, bias=0.0, func=F.Identity, acc=None):
         if acc is None:
-            op("s", [o], [i, scale, bias], lambda: g.scalar.activation(P(o), P(i), func, bias=P(bias), scale=P(scale)))
+            op({"s": (actf(o, i, scale, bias, func), scost(o, i))}, [o], [i, scale, bias])
         else:
-            op("s", [o, acc], [i, scale, bias], lambda: g.scalar.activation(P(o), P(i), func, bias=P(bias), scale=P(scale), accum_out=P(acc)))
+            op({"s": (lambda: g.scalar.activation(P(o), P(i), func, bias=P(bias), scale=P(scale), accum_out=P(acc)), scost(o, i) + 0.02)}, [o, acc], [i, scale, bias])
+
+    def aff(o, i, scale=1.0, bias=0.0, qs="vs"):
+        if isinstance(scale, float) and isinstance(bias, float) and (scale, bias) == (1.0, 0.0):
+            fv = lambda: g.vector.tensor_copy(P(o), P(i))
+        else:
+            fv = tsf(o, i, scale, A.mult, bias, A.add)
+        alts = {"v": (fv, vcost(o, [i])), "s": (actf(o, i, scale, bias, F.Identity), scost(o, i))}
+        op({q: alts[q] for q in qs}, [o], [i, scale, bias])
+
+    def relu(o, i, bias, qs="vs"):
+        alts = {"v": (tsf(o, i, bias, A.add, 0.0, A.max), vcost(o, [i])), "s": (actf(o, i, 1.0, bias, F.Relu), scost(o, i))}
+        op({q: alts[q] for q in qs}, [o], [i, bias])
+
+    def zero(o, i):
+        op({"v": (tsf(o, i, 0.0, A.is_equal), vcost(o, [i])), "s": (actf(o, i, -1.0, 1.0, F.Relu), scost(o, i))}, [o], [i])
 
     def mm(o, a, b, start=True, stop=True):
-        op("t", [o], [a, b], lambda: g.tensor.matmul(P(o), P(a), P(b), start, stop))
+        c = max(min(64, a["k"]), b["k"]) * (4 if a["b"] == 4 else 1) * PEC
+        op({"t": (lambda: g.tensor.matmul(P(o), P(a), P(b), start, stop), c)}, [o], [a, b], lat=DRAIN)
 
-    def load(o, src, sem, q="y"):
-        op(q, [o], [], lambda: Q[q].dma_start(P(o), src), sem, 16)
+    def run(k):
+        l = ops[-k:]
+        del ops[-k:]
+        fs = [o["alts"]["t"][0] for o in l]
+        op({"t": (lambda: [f() for f in fs][-1], sum(o["alts"]["t"][1] for o in l))}, [a for o in l for a in o["outs"]], [a for o in l for a in o["ins"]], lat=DRAIN)
 
-    def store(dst, i, sem, q="y"):
-        op(q, [], [i], lambda: Q[q].dma_start(dst, P(i)), sem, 16)
+    def load(o, src, sem, q, lat):
+        loaded[q] = [(op({q: (lambda: Q[q].dma_start(P(o), src), 0.05)}, [o], [], sem, 16, lat, loaded.get(q, [])), False)]
+    loaded = {}
 
-    def iota(o, pat, base, cm, fl=True):
-        op("g", [o], [], lambda: g.iota(P(o), pat, base, cm, allow_small_or_imprecise_dtypes=True) if fl else g.iota(P(o), pat, base, cm))
+    def store(dst, i, sem, q, lat):
+        op({q: (lambda: Q[q].dma_start(dst, P(i)), 0.05)}, [], [i], sem, 16, lat)
 
-    def gfill(o, n, c, fl=True):
-        iota(o, [[0, n]], c, 0, fl)
+    def iotaf(o, pat, base, cm):
+        if o["d"] == i32:
+            return lambda: g.iota(P(o), pat, base, cm)
+        return lambda: g.iota(P(o), pat, base, cm, allow_small_or_imprecise_dtypes=True)
 
-    def sel(o, pat, f, c, base, cm):
-        op("g", [o], [o], lambda: g.affine_select(P(o), P(o), pat, f, c, base, cm))
+    def iota(o, pat, base, cm=0):
+        op({"g": (iotaf(o, pat, base, cm), 0.13 + 2 * o["k"] * CYC)}, [o], [])
 
     def flat(name, a, b, m=None):
         return vw(name, 16 * a, 16 * b) if m is None else vw(name, 16 * a + m, 16 * b, 16)
 
-    def last(name):
-        return vw(name, 15, 128, 16)
+    def last(name, lo=0):
+        return vw(name, lo + 15, lo + 128, 16)
 
-    def row(name, lo=0, hi=128):
-        return vw(name, lo, hi, 1, 0, 1)
+    def row(name, lo=0, hi=None, st=1):
+        return vw(name, lo, hi, st, 0, 1)
 
-    def gath(q, o, w, f, scale=1.0, bias=0.0):
-        if q == "s":
-            act(o, ind(w, f), scale, bias)
-        elif scale != 1.0:
-            ts(o, ind(w, f), scale, A.mult, bias, A.add)
-        else:
-            copy(o, ind(w, f))
-    XG = vw("X", 16, XS)
+    def XG(t):
+        return vw("XY"[t % 2], 16, XS)
 
-    def xgath(q, dst, lst, a, b, scale=1.0, bias=0.0):
-        gath(q, flat(dst, a, b), XG, vw(lst, a, b), scale, bias)
+    def xgath(t, dst, lst, a, b, scale=1.0, bias=0.0, qs="vs"):
+        aff(flat(dst, a, b), ind(XG(t), vw(lst, a, b)), scale, bias, qs)
+        more("%s_%d" % (dst, a))
 
-    load(vw("wy0"), T.why[:, :], "ld0")
-    load(vw("dr0"), T.drugs[:, :], "ld1", "s")
-    load(vw("X", X0, X0 + D), T.eff[:, :], "ld2")
-    load(vw("lmI"), T.lim[:, :], "ld3", "s")
-    load(vw("R", 16, 16 + D), T.rem[:, :], "ld4")
-    iota(vw("kI"), [[1, 1]], 0, 1, False)
-    iota(vw("wI"), [[0, 16], [1, 16]], 0, 0)
-    iota(vw("dl"), [[-1, 16], [1, 16]], 0, 0)
-    iota(vw("cid"), [[1, 144]], 0, 0)
-    iota(vw("g8"), [[1, 8]], 0, 0)
-    iota(vw("pofI"), [[0, 2], [16, 64]], 0, 0)
-    ts(vw("aI"), vw("kI"), 15, A.bitwise_and)
-    copy(vw("kc"), vw("kI"))
-    ts(vw("gI"), vw("kI"), 4, A.arith_shift_right)
-    ts(vw("hI"), vw("kI"), 31, A.bitwise_and)
-    copy(vw("ac"), vw("aI"))
-    ts(vw("c15"), vw("aI"), 15.0, A.is_equal)
-    ts(vw("c14"), vw("aI"), 14.0, A.is_equal, 2.0, A.mult)
-    ts(vw("a16"), vw("aI"), 16.0, A.mult)
-    ts(vw("n15"), vw("aI"), 15.0, A.is_lt)
-    copy(vw("gc"), vw("gI"))
-    copy(vw("hc"), vw("hI"))
-    ts(vw("Kc"), vw("wI"), vw("ac"), A.is_equal)
-    ts(vw("Kc", 15, 256, 16), vw("wI", 0, 16), 0.0, A.mult, vw("c14"), A.add)
-    ts(vw("K"), vw("dl"), vw("c15"), A.mult)
-    fill(vw("Kc", 0, 256, 17), 0.0)
-    tt(vw("K"), vw("K"), vw("Kc"), A.add)
-    ts(vw("l0"), vw("wy0"), vw("a16"), A.add)
-    ts(vw("Ib"), vw("cid", 0, 128), vw("kc"), A.is_equal)
-    ts(vw("bo8"), vw("g8"), vw("gc"), A.is_equal)
-    ts(vw("Z"), vw("cid"), vw("kc"), A.is_equal, vw("c15"), A.mult)
-    for n, src, c, b in (("dum", "kc", 1.0, float(XS)), ("ndum", "kc", -1.0, -float(XS)), ("b16p", "kc", 16.0, 15.0), ("a32", "ac", 1.0 / 32, 0.0),
-                         ("k16", "kc", 16.0, 0.0), ("tA", "ac", -256.0, 3840.0 - 128), ("tB", "ac", -256.0, 3840.0 + 8192),
-                         ("limf", "lmI", 1.0, 0.0), ("q16", "dr0", 1.0, 32.0), ("qhi", "dr0", 1.0 / 64, 128.5 - 0.4921875), ("wyb", "wy0", 1.0, 0.0)):
-        act(vw(n), vw(src), c, b)
-    act(vw("eR"), vw("dr0"), 1.0, -float(D - 1), F.Relu)
-    gath("s", flat("xc", 0, 64), vw("K"), vw("l0", 0, 64))
-    gath("v", flat("WA", 0, 64), vw("K"), vw("l0", 0, 64))
-    gath("s", flat("WA", 64, 128), vw("K"), vw("l0", 64, 128))
-    gfill(vw("X", 0, 16), 16, 0)
-    gfill(vw("X", 16, 32), 16, -1)
-    gfill(vw("X", X0 + D, XS), 16, -1)
-    gfill(vw("on32"), 128, 1)
-    gfill(vw("on"), 128, 1)
-    for n, c in (("d0s", 1), ("d0p", 2), ("I32", 0), ("ImQ", 0), ("pay", 0)):
-        gfill(vw(n, 0, 128), 128, c)
-    for n in ("d0s", "d0p"):
-        sel(vw(n), [[0, 8], [1, 16]], A.not_equal, 0.0, 0, 0)
-    gfill(vw("d0m"), 256, 0)
-    iota(vw("l3I"), [[3, 8]], 2, 0, False)
-    iota(vw("l8I"), [[1, 8]], 0, 0, False)
-    gfill(vw("R", 0, 16), 16, -16, False)
-    gfill(vw("R", 16 + D, 32 + D), 16, -16, False)
-    for n, z in (("I32", 1.0), ("ImQ", -float(16 + D))):
-        sel(vw(n), [[1, 128]], A.not_equal, z, 0, -1)
-    sel(vw("d0m"), [[0, 16], [1, 16]], A.not_equal, -2 * BIG, 0, 0)
-    iota(vw("tie2", 0, 128), [[0, 8], [-256, 16]], 3840 - 128, 0)
-    iota(vw("tie2", 128, 256), [[0, 8], [-256, 16]], 3840 + 8192, 0)
-    iota(vw("dz"), [[0, 8], [256, 3]], 0, 0)
-    iota(vw("dy"), [[0, 8], [64, 3]], 0, 0)
-    gfill(vw("nz"), 24, 0, False)
-    gfill(vw("ny"), 24, 0, False)
-    for n, c in (("bo32", 1), ("cm", 65), ("hlf", 0), ("zer", 0)):
-        gfill(vw(n), 128, c)
-    sel(vw("cm"), [[1, 128]], A.is_gt, 1.0, 0, -1)
-    sel(vw("hlf"), [[0, 128]], A.not_equal, 0.5, 0, 0)
-    sel(vw("cm"), [[1, 128]], A.not_equal, -31.0, 0, -1)
-    for pat, base, cm in (([[-16, 8], [0, 16]], 0, 1), ([[16, 8], [0, 16]], 15, -1)):
-        for n in ("bo32", "cm"):
-            sel(vw(n), pat, A.is_ge, 0.0, base, cm)
-    iota(vw("eI"), [[1, 32], [0, 16]], 0, 0)
-    gfill(vw("d0b"), 576, 1)
-    iota(vw("tie16"), [[0, 8], [-16, 16]], 240, 0)
-    sel(vw("d0b"), [[0, 36], [1, 16]], A.not_equal, -8192.0, 0, 0)
-    iota(vw("m15"), [[0, 8], [-1, 16]], 15, 0)
-    gfill(vw("X", XS, XW), 128, 0)
-
-    def double(dst, src, lst, h, between):
-        lo, hi = HV[h]
-        tt(flat(dst, lo, hi - 16), ind(flat(src, lo, hi), vw(lst, lo, hi - 16)), flat("xc", lo, hi - 16), A.add)
-        between()
-        tt(flat(dst, hi - 16, hi), ind(flat(src, lo, hi), vw(lst, hi - 16, hi)), flat("xc", hi - 16, hi), A.add)
-
-    def twin(src, h):
-        act(flat("xc", *HV[h]), flat(src, *HV[h]))
-
-    def conv(src, h, a=None, b=None):
-        a, b = HV[h] if a is None else (a, b)
-        o = vw(("pE", "pF", "pD")[h], 0, b - a)
-        mm(o, vw("Ib"), vw("pofm", a, b), True, False)
-        for m in range(16):
-            mm(o, vw("Z", 15 - m, 143 - m), flat(src, a, b, m), False, m == 15)
-
-    def convd(lst, h, a=None, b=None):
-        a, b = HV[h] if a is None else (a, b)
-        copy(vw(lst, a, b), vw(("pE", "pF", "pD")[h], 0, b - a))
-
-    def rowsums(a, b):
-        if a == 0:
-            mm(vw("pA", 0, 384), row("on"), row("pay", 0, 384), True, False)
-        for m in range(16):
-            mm(vw("pA", m, 384, 16, a, b), flat("x", a, b, m), vw("w3"), False, m == 15)
-
-    def remedies(q, a, b):
-        gath("s", flat("RA", a, b), vw("R"), vw(q, a, b), 1.0, 16.0)
-
-    def measures(p="pB"):
-        mm(vw(p, 0, 8), vw("eR"), vw("bo8"))
-        mm(vw(p, 8, 16), vw("eR"), vw("wm16"), True, False)
-        mm(vw(p, 8, 16), vw("on32"), vw("lim8"), False, True)
-
-    def lists(t):
-        if t == 0:
-            mm(vw("pB", 128, 256), vw("q16"), vw("Ib"), True, False)
-            mm(vw("pB", 128, 256), vw("eR"), vw("ImQ"), False, True)
-        mm(vw("pB", 256, 512), row("on"), row("tie2", 0, 256), True, False)
-        mm(vw("pB", 256, 384), vw("qhi"), vw("Ib"), False, False)
-        mm(vw("pB", 384, 512), vw("q16"), vw("Ib"), False, False)
-        mm(vw("pB", 384, 512), vw("qhi"), vw("Im64"), False, False)
-
-    def keys():
-        for m in range(16):
-            mm(vw("pB", 256 + m, 512, 16), flat("x", 0, 128, m), vw("wd"), False, m == 15)
-
-    def upper(q):
-        ts(vw("qhi"), vw(q), 1.0 / 64, A.mult, 128.25 - 0.4921875, A.add)
-
-    def sums(t):
-        for m in range(16):
-            mm(vw("pD", 256, 384), vw("Ib"), flat("x", 0, 128, m), m == 0, False)
-        if t:
-            mm(vw("pD", 256, 384), vw("Ib"), vw("xe"), False, False)
-        mm(vw("pD", 256, 384), vw("bo"), vw("eR"), False, True)
-
-    def masks(v, end):
-        act(vw("a1"), vw(v), 1.0, 8388608.0)
-        act(vw("a2"), vw("a1"), 1.0, -8388608.0)
-        if not end:
-            act(vw("aM"), vw("a2"), 1.0, vw("a32"))
-
-    def decide(t):
-        scan(vw("sm"), vw("d0s"), vw("pA", 0, 128), A.mult, A.add)
-        scan(vw("ms"), vw("d0m"), vw("pA", 128, 384), A.add, A.max)
-        if t == 0:
-            gath("v", flat("x2", 64, 96), flat("WB", 64, 128), vw("lu8", 64, 96))
-            convd("lu8", 2, 96, 128)
-        for n in ("dz", "dy"):
-            tt(vw(n, 2, 24, 3), last("sm"), vw("thr"), A.is_ge)
-        for a in (0, 1):
-            ts(vw("nz", a, 24, 3), vw("ms", 128 * a + 15, 128 * a + 128, 16), 255, A.bitwise_and)
-        if t == 0:
-            ts(vw("m16"), vw("wI", 0, 128), vw("ac"), A.is_equal)
-        scan(vw("pz"), vw("dz"), vw("nz"), A.mult, A.add)
-
-    def heaviest():
-        scan(vw("my"), vw("d0m"), vw("pB", 256, 512), A.add, A.max)
-
-    def stopped():
-        for a in (0, 1):
-            ts(vw("ny", a, 24, 3), vw("my", 128 * a + 15, 128 * a + 128, 16), 255, A.bitwise_and)
-
-    mm(vw("pF", 0, 128), vw("Ib"), vw("wyb"), True, False)
-    mm(vw("pF", 0, 128), row("on"), row("pofI"), False, True)
-    copy(vw("lu1"), vw("pF", 0, 128))
-    ts(vw("q0"), vw("dr0"), 16.0, A.add)
-    ts(vw("pofm"), vw("pofI"), vw("ac"), A.add)
-    double("WB", "WA", "lu1", 0, lambda: copy(flat("xc", 64, 128), flat("WA", 64, 128)))
-    conv("WB", 0)
-    xgath("s", "x", "q0", 0, 32)
-    for n, a, c in (("w3", 0, 1.0), ("w3", 8, 512.0), ("w3", 16, 512.0), ("wd", 0, 4096.0), ("wd", 8, 4096.0), ("wm16", 0, -16.0), ("bo8m", 0, vw("n15"))):
-        act(vw(n, a, a + 8), vw("bo8"), c)
-    act(row("d0h"), row("d0s"), 0.5)
-    act(vw("Im64"), vw("Ib"), -64.0)
-    twin("WB", 0)
-    act(row("d1h"), row("d0s"), -32768.0, 32768.0)
-    xgath("s", "x", "q0", 32, 64)
-    double("WB", "WA", "lu1", 1, lambda: convd("lu2", 0))
-    conv("WB", 1)
-    twin("WB", 1)
-    xgath("s", "x", "q0", 64, 96)
-    act(vw("lim8"), vw("I32", 0, 128, 16), vw("limf"))
-    scan(vw("pwr"), vw("d0p"), vw("on32"), A.mult, A.max)
-    scan(row("pwd"), row("d0h"), row("d1h"), A.mult, A.add)
-    double("WA", "WB", "lu2", 0, lambda: convd("lu2", 1))
-    mm(vw("pG", 0, 1), row("pwr"), row("on", 0, 1))
-    conv("WA", 0)
-    measures()
-    twin("WA", 0)
-    xgath("s", "x", "q0", 96, 128)
-
-    def third():
-        convd("lu4", 0)
-        ts(row("pay", 256, 384), row("pwd"), 256.0, A.min)
-        ts(vw("n0"), vw("pB", 0, 8), BIG, A.mult, -1000.0, A.add)
-    double("WA", "WB", "lu2", 1, third)
-    tt(vw("thr"), vw("pB", 8, 16), vw("n0"), A.min)
-    conv("WA", 1)
-    act(row("pay", 128, 256), row("pwd"), 1.0 / 256, -0.125)
-    twin("WA", 1)
-    rowsums(0, 128)
-    lists(0)
-    remedies("q0", 0, 28)
-    for w in range(8):
-        act(vw("sl8", 128 * w, 128 * w + 128, 1, 0, 8), vw("on", 0, 128, 1, 0, 8), vw("I32", w, w + 1, 1, 0, 8))
-    ts(vw("bo8b"), vw("bo8m"), vw("pG", 0, 1), A.mult)
-    copy(vw("L3"), vw("l3I"))
-    copy(vw("L8"), vw("l8I"))
-    double("WB", "WA", "lu4", 0, lambda: convd("lu4", 1))
-    conv("WB", 0)
-    keys()
-    an = vw("pC", 384, 512)
-
-    def masked(src, a, b, stop):
-        for m in range(16):
-            mm(vw("pC", 384 + m, 512, 16, a, b), flat(src, a, b, m), vw("bo8b"), False, stop and m == 15)
-
-    def step(q, dst, src, lst, a, b):
-        if q == "add":
-            tt(flat(dst, a, b), ind(flat(src, 64, 128), vw(lst, a, b)), flat("xc", a, b), A.add)
-        else:
-            gath(q, flat(dst, a, b), flat(src, 64, 128), vw(lst, a, b))
-    step("add", "WB", "WA", "lu4", 64, 96)
-    conv("WB", 1, 64, 96)
-    mm(an, row("on"), row("pwr"), True, False)
-    masked("WB", 0, 64, False)
-    convd("lu8", 0)
-    step("add", "WB", "WA", "lu4", 96, 128)
-    conv("WB", 2, 96, 128)
-    masked("WB", 64, 128, False)
-    gath("s", flat("x2", 0, 64), flat("WB", 0, 64), vw("lu8", 0, 64))
-    convd("lu8", 1, 64, 96)
-    decide(0)
-    step("s", "x2", "WB", "lu8", 108, 128)
-    step("v", "x2", "WB", "lu8", 96, 108)
-    copy(vw("pwB"), ind(vw("pz"), vw("L3")))
-    heaviest()
-    scan(row("wr"), row("hlf"), row("zer"), A.mult, A.add, 2.0 ** 64)
-    for a, b in ((0, 64), (64, 96), (96, 128)):
-        masked("x2", a, b, True)
-    mm(vw("pH", 0, 1), row("wr"), row("on", 0, 1))
-    act(vw("bo"), vw("bo32"))
-    act(vw("I32th"), vw("Ib"), 1.0 / 32)
-    for n, src, c in (("bo256", "bo32", 256.0), ("I16", "Ib", 16.0), ("Im16", "Ib", -16.0), ("Im32", "Ib", -1.0),
-                      ("bo8k", "bo8", vw("b16p")), ("bo8d", "bo8", vw("dum")), ("bo8n", "bo8", -1.0), ("wa", "wd", -1.0), ("wr2", "wd", -2.0)):
-        act(vw(n), vw(src), c)
-
-
-    def shown():
-        act(vw("yT", 0, 128, 1, 0, 8), vw("pE", 128, 256, 1, 0, 8))
-        for w in range(8):
-            mm(vw("pG" if w < 4 else "pH", 128 * (w % 4), 128 * (w % 4) + 128), vw("sl8", 128 * w, 128 * w + 128, 1, 0, 8), vw("yT", 0, 128, 1, 0, 8))
-
-    def equal(lo, hi):
-        for w in range(lo, hi):
-            p = vw("pG" if w < 4 else "pH", 128 * (w % 4), 128 * (w % 4) + 128)
-            ts(vw("eq", 128 * w, 128 * w + 128), p, vw("yz", 3 * w + 2, 3 * w + 3), A.is_equal)
-
-    def weigh():
-        for w in range(8):
-            mm(vw("pB", 16 + w, 17 + w), vw("eq", 128 * w, 128 * w + 128), vw("wc"))
-
-    def send(k, t):
+    def send(k, t, half=None):
         src = "%so%d" % (k, t)
         lowd = T.cores[(rank + STRIDE[0]) % NR]
         hid = relay_of(core, T.cores[(rank + STRIDE[1]) % NR], topo)
@@ -533,297 +400,587 @@ def member(g, core, rank, T, topo):
                                 src=T[src][:, 0:HALF[k]], dst=T["%s%d" % (k, t)][:, 0:HALF[k]]),
               RemoteDMATransfer(dst_ids=[DstId(rid=r2, pnc=p2)], dma_engine_mask=bits(topo, core, hid, 8, True), remote_sem=T.sem["r%s%d" % (k, t)],
                                 src=T[src][:, HALF[k]:2 * HALF[k]], dst=T["r%s%d" % (k, t)][:, :])]
-        deps("g", [], [vw(src)])
-        g.remote_dma_fused(tr, local_sem=T.sem["loc"])
-        cnt["loc"] = cnt.get("loc", 0) + 16
+        late = {"n": 0.0, "v": 0.4 * LATE, "q": LATE if sent else FIRST}[k]
+        if half == 1:
+            i = op({"g": (lambda: g.remote_dma(T["rn%d" % t][:, :], T[src][:, 8:12], T.sem["rn%d" % t], T.sem["loc"], p2, r2, topo.mask(core, hid)), 0.1)},
+                   [], [vw(src, 8, 12)], "loc", len(topo.engines(core, hid)), after=sent[-1:])
+        elif half == 0:
+            i = op({"g": (lambda: g.remote_dma(T["n%d" % t][:, 0:4], T[src][:, 4:8], T.sem["nL%d" % t], T.sem["loc"], p1, r1, bits(topo, core, lowd, 8, False)), 0.1)},
+                   [], [vw(src, 4, 8)], "loc", 8, after=sent[-1:])
+        else:
+            i = op({"g": (lambda: g.remote_dma_fused(tr, local_sem=T.sem["loc"]), 0.1)}, [], [vw(src)], "loc", 16, after=sent[-1:])
+        sent.append((i, False))
+        for h in (0, 1) if half is None else (half,):
+            op({"-": (None, (h + 1) * HOP + late)}, [vw("%s%d" % (k, t), h * HALF[k], (h + 1) * HALF[k])], [], "%s%s%d" % (k, "LH"[h], t), 8, after=[(i, True)])
+    sent = []
+
+    load(vw("wy0"), T.why[:, :], "ld0", "y", DMA + 0.3)
+    load(vw("dr0"), T.drugs[:, :], "ld1", "s", DMA + 0.5)
+    load(vw("X", X0, X0 + D), T.eff[:, :], "ld2", "y", DMA + 2.0)
+    load(vw("lmI"), T.lim[:, :], "ld3", "s", DMA + 2.2)
+    load(vw("R", 16, 16 + D), T.rem[:, :], "ld4", "y", DMA + 5.0)
+    load(vw("Y", X0, X0 + D), T.eff[:, :], "ld5", "y", DMA + 7.0)
+    iota(vw("kI"), [[1, 1]], 0, 1)
+    iota(vw("gid"), [[1, 8], [0, 16]], 0)
+    iota(vw("cid"), [[1, 128]], 0)
+    iota(vw("aid"), [[0, 8], [1, 16]], 0)
+    iota(vw("g8"), [[1, 8]], 0)
+    ts(vw("aI"), vw("kI"), 15, A.bitwise_and)
+    ts(vw("gI"), vw("kI"), 4, A.arith_shift_right)
+    ts(vw("hI"), vw("kI"), 31, A.bitwise_and)
+    for n in "kagh":
+        aff(vw(n + "c"), vw(n + "I"))
+    ts(vw("bo"), vw("gid"), vw("gc"), A.is_equal)
+    ts(vw("Ib"), vw("cid"), vw("kc"), A.is_equal)
+    tt(vw("M0"), vw("bo"), vw("Ib"), A.add)
+    ts(vw("bj"), vw("aid", 0, 16), vw("ac"), A.is_equal, -1.0, A.add)
+    ts(vw("b1"), vw("aid", 0, 16), vw("ac"), A.is_equal)
+    ts(vw("c3"), vw("cid"), vw("kc"), A.is_equal, -256.0, A.mult)
+    tt(vw("M2"), vw("c3"), vw("bo"), A.add)
+    ts(vw("bo8f"), vw("g8"), vw("gc"), A.is_equal)
+    ts(vw("m16"), vw("aid"), vw("ac"), A.is_equal)
+    fill(vw("on"), 1.0)
+    fill(vw("on32"), 1.0, "vg")
+    fill(row("kr", 0, 128), 255.0)
+    fill(row("kr", 128, 256), 256.0)
+    for n, c in (("Im256", -256.0), ("I256", 256.0), ("I32", 1.0), ("I20", 131072.0), ("Im20", -131072.0), ("I2k", 2048.0), ("Im2k", -2048.0), ("I4k", 4096.0), ("I19", 2.0 ** 19), ("Im19", -2.0 ** 19), ("I16", 16.0), ("Im16", -16.0),
+                 ("ImQ", -float(16 + D)), ("IpQ", float(16 + D)), ("Im64", -64.0), ("IH", HUGE), ("I2H", 2 * HUGE), ("Ig", -HUGE / 32768)):
+        aff(vw(n), vw("Ib"), c)
+    for n, c in (("bo32", 1.0), ("bo256", 256.0), ("boS", -2048.0), ("boT", 32768.0), ("boU", -32768.0)):
+        aff(vw(n), vw("bo"), c)
+    for n, src, c, b in (("dum", "kc", 1.0, float(XS)), ("ndum", "kc", -1.0, -float(XS)), ("b16p", "kc", 16.0, 15.0), ("a32", "ac", 1.0 / 32, 0.0),
+                         ("k17", "kc", 16.0, 0.0), ("limf", "lmI", 16.0, 120.0), ("m15", "aid", -1.0, 15.0), ("tie16", "aid", -16.0, 240.0)):
+        aff(vw(n), vw(src), c, b)
+    for n, a, c in (("bo8", 0, 1.0), ("w3", 0, 16.0), ("w3", 8, 512.0), ("w3", 16, 512.0), ("wd", 0, 4096.0), ("wd", 8, 4096.0), ("wm", 0, -256.0),
+                    ("wa", 0, -4096.0), ("wa", 8, -4096.0), ("wr2", 0, -8192.0), ("wr2", 8, -8192.0), ("bo8k", 0, vw("b16p")), ("bo8d", 0, vw("dum")),
+                    ("bo8n", 0, -1.0), ("bo16", 0, 16.0), ("bo8a", 0, vw("ac")), ("bo64", 0, 64.0), ("bo8p", 0, vw("k17"))):
+        aff(vw(n, a, a + 8), vw("bo8f"), c)
+    aff(row("tie2", 0, 128), row("aid"), -256.0, 3840.0 - 128)
+    aff(row("tie2", 128, 256), row("aid"), -256.0, 3840.0 + 8192)
+    for n in "XY":
+        fill(vw(n, 0, 16), 0.0, "vg")
+        fill(vw(n, 16, 32), -1.0, "vg")
+        fill(vw(n, XS, XW), 0.0, "vg")
+    fill(vw("R", 0, 16), -16, "vg")
+    for n, c, z in (("d0s", 1.0, 0.0), ("d0m", 0.0, -2 * BIG), ("d0b", 1.0, -8192.0)):
+        fill(vw(n), c, "vg")
+        fill(vw(n, 0, None, 16), z)
+    for n, c, z in (("d0p", 2.0, 0.0), ("d0h", 0.5, 0.0), ("d1h", 0.0, 32768.0)):
+        fill(row(n), c)
+        fill(row(n, 0, None, 16), z)
+    scan(row("pwr"), row("d0p"), row("on32"), A.mult, A.max)
+    scan(row("pwd"), row("d0h"), row("d1h"), A.mult, A.add)
+    aff(row("pay", 0, 128), row("m15"))
+    aff(row("pay", 128, 256), row("pwd"), 1.0 / 256, -0.125)
+    ts(row("pay", 256, 384), row("pwd"), 256.0, A.min)
+    fill(row("hlf"), 2.0)
+    fill(row("hlf", 0, None, 8), 0.0)
+    scan(row("wr"), row("hlf"), row("on"), A.mult, A.max)
+    ts(vw("pz", 0, 1), vw("aI"), 8.0, A.is_lt)
+    ts(vw("pz", 1, 2), vw("aI"), 8.0, A.is_ge)
+    mm(vw("pB", 500, 501), row("wr"), row("on", 0, 1))
+    ts(vw("pc"), vw("pz", 0, 2), vw("pB", 500, 501), A.mult)
+    aff(row("far"), row("pwd"))
+    mm(vw("pB", 502, 503), row("far"), row("on", 0, 1))
+    aff(vw("pwc"), vw("pB", 502, 503))
+    fill(row("pw20"), -131072.0)
+    fill(row("far"), HUGE / 4)
+    fill(vw("n16"), 0, "vg")
+    for s, c in enumerate((1.0, 2.0 ** 22, 2.25 * HUGE, -2.25 * HUGE)):
+        fill(row("ini", s, None, 4), c)
+    for s, c in enumerate((0.0, 2048.0, 2048.0)):
+        fill(vw("qd", s, None, 4), c)
+    for n, st, b, k in (("8", 1, 0, 8), ("k", 16, 15, 8), ("16", 1, 0, 16)):
+        iota(vw("l%sI" % n), [[st, k]], b)
+        copy(vw("L" + n.upper()), vw("l%sI" % n))
+    ts(vw("c1"), vw("cid"), vw("kc"), A.is_gt, 64.0, A.mult)
+    aff(vw("c2"), vw("Ib"), -32.0, 1.0)
+    tt(vw("c1"), vw("c1"), vw("c2"), A.add)
+    tt(vw("cm"), vw("c1"), vw("bo"), A.mult)
+    aff(vw("k16"), vw("ac"), -2048.0, 15 * 2048.0)
+    aff(vw("c3"), vw("bo"), vw("k16"))
+    tt(vw("boE"), vw("c3"), vw("I2H"), A.subtract)
+    aff(row("mk2", 0, 128), row("m15"), 2048.0)
+    aff(row("mk2", 128, 256), row("m15"), -2048.0)
+    fill(vw("d0a"), 0.0, "vg")
+    fill(vw("d0a", 0, None, 128), BIG)
+    fill(vw("Z"), 0.0)
+    aff(vw("Z", 15, 143, 16), vw("bo8f"))
+    iota(vw("eI"), [[1, 32], [0, 16]], 0)
+    ts(vw("E"), vw("eI"), vw("hc"), A.is_equal)
+    for w in range(8):
+        ts(vw("sl", 128 * w, 128 * w + 128), vw("on"), vw("bo8f", w, w + 1), A.mult, 4096.0, A.mult)
+    for w in range(4):
+        ts(vw("tri", 128 * w, 128 * w + 128), vw("cid"), vw("kc"), A.is_ge, BIG, A.mult)
+    iota(vw("TQ"), [[1, XS - 16]], 0)
+
+    an = vw("pC", 0, 128)
+    if DBL:
+        iota(vw("wI"), [[0, 16], [1, 16]], 0)
+        iota(vw("dl"), [[-1, 16], [1, 16]], 0)
+        iota(vw("pofI"), [[0, 2], [16, 64]], 0)
+        ts(vw("c15"), vw("aI"), 15.0, A.is_equal)
+        ts(vw("c14"), vw("aI"), 14.0, A.is_equal, 2.0, A.mult)
+        ts(vw("a16"), vw("aI"), 16.0, A.mult)
+        ts(vw("n15"), vw("aI"), 15.0, A.is_lt)
+        ts(vw("Kc"), vw("wI"), vw("ac"), A.is_equal)
+        ts(vw("Kc", 15, 256, 16), vw("wI", 0, 16), 0.0, A.mult, vw("c14"), A.add)
+        fill(vw("Kc", 0, 256, 17), 0.0)
+        ts(vw("Kd"), vw("dl"), vw("c15"), A.mult)
+        tt(vw("K"), vw("Kd"), vw("Kc"), A.add)
+        ts(vw("l0"), vw("wy0"), vw("a16"), A.add)
+        tt(vw("qc"), vw("wy0"), vw("pofI"), A.add)
+        copy(vw("lu1"), vw("qc"))
+        aff(vw("pofm"), vw("pofI"), 1.0, vw("ac"))
+        fill(vw("Zc", 128, 144), 0.0)
+        aff(vw("Zc", 0, 128), vw("Ib"), vw("c15"))
+        mm(vw("pB", 503, 504), row("pwr"), row("on", 0, 1))
+        ts(vw("pw14"), vw("pB", 503, 504), vw("n15"), A.mult)
+        fill(vw("Zw"), 0.0)
+        aff(vw("Zw", 15, 143, 16), vw("bo8f"), vw("pw14"))
+        turn[0] = 0
+        for a in range(0, 128, 32):
+            aff(flat("WA", a, a + 32), ind(vw("K"), vw("l0", a, a + 32)))
+            more("K_%d" % a)
+        mm(an, row("pwr"), row("on"), True, False)
+
+        def masked(src, a, b, stop):
+            for m in range(16):
+                mm(vw("pC", a, b), vw("Zw", 15 - m, 143 - m), flat(src, a, b, m), False, stop and m == 15)
+            run(16)
+        for r, (src, dst) in enumerate((("WA", "WB"), ("WB", "WA"), ("WA", "WB"))):
+            for h in (0, 1):
+                lo = 64 * h
+                for a in (lo, lo + 32):
+                    if TWIN and a not in HELP:
+                        aff(flat("xc", a, a + 32), flat(src, a, a + 32))
+                        more("tw%d_%d" % (r, a))
+                    if a in HELP:
+                        aff(flat("mn", a, a + 32), ind(flat(src, lo, lo + 64), vw("lu%d" % 2 ** r, a, a + 32)), 1.0, 0.0, "s")
+                        more("g%d_%d" % (r, a))
+                        tt(flat(dst, a, a + 32), flat("mn", a, a + 32), flat(src, a, a + 32), A.add)
+                    else:
+                        tt(flat(dst, a, a + 32), ind(flat(src, lo, lo + 64), vw("lu%d" % 2 ** r, a, a + 32)), flat("xc" if TWIN else src, a, a + 32), A.add)
+                    more("d%d_%d" % (r, a))
+                o = vw(("pE", "pF")[h], 0, 64)
+                mm(o, vw("Ib"), vw("pofm", lo, lo + 64), True, False)
+                for m in range(16):
+                    mm(o, vw("Zc", 15 - m, 143 - m), flat(dst, lo, lo + 64, m), False, m == 15)
+                run(16)
+                copy(vw("lu%d" % 2 ** (r + 1), lo, lo + 64), o)
+                more("lu%d_%d" % (r, h))
+        for lo in (0, 64):
+            masked("WB", lo, lo + 64, False)
+        for lo in (0, 64):
+            for a in range(lo, lo + 64, 16):
+                aff(flat("x2", a, a + 16), ind(flat("WB", lo, lo + 64), vw("lu8", a, a + 16)))
+                more("l_%d" % a)
+            masked("x2", lo, lo + 64, lo == 64)
+        turn[0] = None
+    else:
+        aff(vw("nw"), vw("wy0"), -1.0, 16.0)
+        ts(vw("rt"), vw("wy0"), vw("ac"), A.is_equal, 17.0, A.mult)
+        tt(vw("N", 0, 128), vw("nw"), vw("rt"), A.max)
+    for h in (0, 1):
+        for b in () if DBL else (0, 1):
+            aff(vw("M", 128 * h + 64 * b, 128 * h + 64 * b + 64), vw("on", 0, 64), vw("pc", b, b + 1))
+    for s in range(0 if DBL else 16):
+        j = 15 - s
+        bj, n0, n = vw("B", 128 * s, 128 * s + 128), row("n0r", 128 * s, 128 * s + 128), vw("N", 128 * s, 128 * s + 128)
+        relu(bj, vw("M0"), vw("bj", j, j + 1))
+        aff(n0, row("on"), float(16 - j))
+        if s < 15:
+            z = vw(("pC", "pD")[s % 2], 0, 128)
+            mm(z, n0, row("kr", 0, 128), True, False)
+            aj = vw("Aj", 128 * s, 128 * s + 128)
+            ts(aj, vw("M2"), vw("b1", j, j + 1), A.min)
+            mm(z, aj, n, False, True)
+            tt(vw("N", 128 * s + 128, 128 * s + 256), z, n, A.max)
         for h in (0, 1):
-            s = "%s%s%d" % (k, "LH"[h], t)
-            cnt[s] = 8
-            snap[(s, 8)] = {}
-            recs.setdefault("%s%d" % (k, t), []).append((vw("%s%d" % (k, t), h * HALF[k], (h + 1) * HALF[k]), True, (s, 8), "remote"))
+            p = ("pE", "pF", "pG", "pH")[2 * h + s % 2]
+            m, m2 = [vw("M", 256 * k + 128 * h, 256 * k + 128 * h + 128) for k in (s % 2, 1 - s % 2)]
+            if h == 0:
+                aff(vw("Dn", 128 * (s % 8), 128 * (s % 8) + 128), n, -256.0, 256.0 * (16 - j), "s")
+            for b in (0, 64):
+                mm(vw(p, b, b + 64), vw("Ib"), vw("Dn", 128 * (s % 8) + 64 * h, 128 * (s % 8) + 64 * h + 64), b == 0, False)
+            run(2)
+            mm(vw(p, 0, 128), bj, m, False, True)
+            tt(m2, vw(p, 0, 128), m, A.max)
+    for h in () if DBL else (0, 1):
+        mm(vw("pC", 64 * h, 64 * h + 64), vw("Ib"), vw("M", 128 * h, 128 * h + 64), True, False)
+        mm(vw("pC", 64 * h, 64 * h + 64), vw("I256"), vw("M", 128 * h + 64, 128 * h + 128), False, True)
+    aff(vw("wy32"), vw("wy0"), 1.0 / 32)
+    qf, q2f = vw("qd", 3, None, 4), vw("sq", 3, None, 4)
+    ts(vw("eR"), vw("dr0"), float(D), A.is_ge)
+    aff(vw("qa"), vw("dr0"), 1.0, 16.0)
+    aff(vw("qb"), vw("eR"), float(16 + D))
+    tt(qf, vw("qa"), vw("qb"), A.subtract)
+    copy(vw("q0"), qf)
+    aff(vw("lim8"), vw("I32", 0, 128, 16), vw("limf"))
 
-    def entry_constants():
-        for a in (0, 1):
-            mm(vw("pH", 8 + a, 9 + a), row("pay", 128 + 128 * a, 256 + 128 * a), row("on", 0, 1))
-        act(vw("pc"), vw("pH", 8, 10))
-        for n, a, c in (("bo8a", 0, vw("ac")), ("bo64", 0, 64.0), ("bo8s", 0, 0.0625), ("bo4n", 0, -4.0), ("payW", 0, 0.0), ("bo8p", 0, vw("k16")),
-                        ("bigW", 0, 2 * BIG), ("bigW", 8, 2 * BIG), ("bigW", 16, 2 * BIG), ("tieW", 0, vw("tA")), ("tieW", 8, vw("tB")),
-                        ("payW", 8, vw("pc", 0, 1)), ("payW", 16, vw("pc", 1, 2))):
-            act(vw(n, a, a + 8), vw("bo8"), c)
-        act(row("far", 0, 24), row("on", 0, 24), -2 * BIG)
-
-    def ahead(t):
+    def rows(t):
         q = "q%d" % t
-        mm(vw("pH", 0, 8), vw("on32"), vw("dz", 2, 24, 3))
-        mm(vw("pF", 0, 128), vw("cm"), vw("eR"))
-        remedies(q, 0, 16)
-        act(vw("cj"), vw("pH", 0, 8), 1.0, 35200.0, F.Identity, vw("cn"))
-        act(vw("e0", 0, 128), vw("pF", 0, 128), 1.0, 17.0, F.Relu)
-        xgath("s", "x", q, 44, 64)
-        act(vw("cz"), vw("cn"), 1.0 / 256, -0.498046875)
-        act(vw("eN"), vw("e0", 0, 128), -1.0, 1.0, F.Relu)
-        xgath("s", "x", q, 64, 84)
-        act(vw("cc"), vw("cz"), -256.0, vw("cn"))
-        xgath("s", "x", q, 84, 104)
-        act(vw("limc"), vw("limf"), 1.0, vw("cc"))
-        xgath("s", "x", q, 104, 128)
-        act(vw("lim8"), vw("I32", 0, 128, 16), vw("limc"))
+        for a, b in zip(CUT1, CUT1[1:]):
+            turn[0] = 0 if t == 0 else turn[0]
+            xgath(t, "x", q, a, b)
+            if t == 0:
+                more("x0_%d" % a)
+                turn[0] = None
+        p = "pA"
+        mm(vw(p, 384, 392), vw("eR"), vw("bo8"))
+        mm(vw(p, 392, 400), vw("eR"), vw("wm"), True, False)
+        mm(vw(p, 392, 400), vw("on32"), vw("lim8"), False, True)
+        aff(vw("n0"), vw(p, 384, 392), BIG, (-BIG if t else 0.0) - 16000.0)
+        tt(vw("thr"), vw(p, 392, 400), vw("n0"), A.min)
+        mm(vw("pA", 0, 384), row("on"), row("pay"), True, False)
+        for m in range(16):
+            mm(vw("pA", m, 384, 16), flat("x", 0, 128, m), vw("w3"), False, m == 15)
+            if m % 8 == 7:
+                run(8)
+        scan(vw("mr", 128, 384), vw("d0m", 0, 256), vw("pA", 128, 384), A.add, A.max)
+        more("mr1")
+        if t:
+            scan(vw("mr", 0, 128), vw("d0m", 0, 128), vw("pA", 0, 128), A.add, A.max)
+            more("mr0")
+        scan(vw("sm"), vw("d0s"), vw("pA", 0, 128), A.mult, A.add)
+        ts(vw("nz"), vw("mr", 143, 384, 16), 255, A.bitwise_and)
+        if t == 0:
+            for a in (0, 8):
+                tt(vw("dz", a, a + 8), last("sm"), vw("thr"), A.is_ge)
+            tt(vw("pz"), vw("nz"), vw("dz"), A.mult)
+            for a, b in ((0, "I256"), (8, "Ib")):
+                aff(vw("pwB", 16 * a, 16 * a + 128), ind(vw("pz", a, a + 8), vw("L8")))
+                mm(vw("pB", 0, 128), vw("pwB", 16 * a, 16 * a + 128), vw(b), a == 0, a == 8)
+        for a, b in zip(CUT1, CUT1[1:]):
+            if not DK:
+                aff(flat("RA", a, b), ind(vw("R"), vw(q, a, b)), 1.0, 16.0)
+                more("RA_%d" % a)
+
+    def sums(t):
+        for m in range(16):
+            mm(vw("pD", 256, 384), vw("Ib"), flat("x", 0, 128, m), m == 0, False)
+            if m % 4 == 3:
+                run(4)
+        mm(vw("pD", 256, 384), vw("bo"), vw("eR"), False, t == 0)
+
+    QB = ("pC", "pE")
+
+    def quad(s, a, b, stop=False):
+        for h in (0, 1):
+            mm(vw(QB[h], s, 256, 4), a, vw(b, 64 * h, 64 * h + 64), False, stop)
+    win = vw("pB", 128, 256)
 
     def kept(t):
         q, v = "q%d" % t, "v%d" % t
-        mm(vw("pG", 0, 8), vw("eN"), vw("bo8a"))
-        for p, n, w in (("pE", 24, "payW"), ("pF", 16, "tieW")):
-            mm(vw(p, 256, 256 + n), row("on"), row("far", 0, n), True, False)
-            mm(vw(p, 256, 256 + n), vw("eN"), vw("bigW", 0, n), False, False)
-            mm(vw(p, 256, 256 + n), vw("eN"), vw(w), False, False)
-        lists(t)
-        copy(vw("e8"), vw("pG", 0, 8))
-        xgath("v", "x", q, 16, 44)
-        tt(vw("AL"), ind(vw("e8"), vw("L8")), vw("m16"), A.mult)
-        rowsums(0, 128)
-        measures("pH")
-        keys()
-        mm(vw("pB", 128, 256), vw("q16"), vw("Ib"), True, False)
-        mm(an, vw(v), vw("I32"))
-        mm(vw("pG", 8, 16), vw("m16"), vw("bo8p"), True, False)
-        mm(vw("pG", 8, 16), vw("AL"), vw("bo8"), False, True)
-        remedies(q, 16, 72)
-        act(vw("aP"), an)
-        scan(vw("sm"), vw("d0s"), vw("pA", 0, 128), A.mult, A.add)
-        ts(vw("n0"), vw("pH", 0, 8), BIG, A.mult, -BIG - 1000.0, A.add)
-        scan(vw("ms"), vw("d0m"), vw("pA", 128, 384), A.add, A.max)
-        tt(vw("thr"), vw("pH", 8, 16), vw("n0"), A.min)
-        heaviest()
+        ts(vw("q16"), vw(q), 0.0, A.add)
+        zero(vw("eR"), vw("q16"))
+        mm(vw("pF", 0, 128), vw("cm"), vw("eR"))
+        relu(vw("e0"), vw("pF", 0, 128), 17.0)
+        zero(vw("eN"), vw("e0"))
+        if not DK:
+            mm(vw("pF", 128, 136), vw("eN"), vw("bo8a"))
+            aff(vw("e8"), vw("pF", 128, 136))
+            tt(vw("AE"), ind(vw("e8"), vw("L8")), vw("m16"), A.mult)
+            mm(vw("pF", 136, 144), vw("m16"), vw("bo8p"), True, False)
+            mm(vw("pF", 136, 144), vw("AE"), vw("bo8"), False, True)
+            copy(vw("le"), vw("pF", 136, 144))
+        rows(t)
         tt(vw("th2"), vw("thr"), last("sm"), A.subtract)
+        aff(vw("tb"), ind(vw("th2"), vw("L8")), 1.0 / 32, -1024.0)
+        aff(vw("kb"), ind(vw("mr", 0, 128), vw("LK")), 1.0 / 256, 1280 - 0.498046875)
+        ts(vw("k8"), last("mr"), 255, A.bitwise_and)
+        aff(vw("kl"), ind(vw("k8"), vw("L8")))
+        mm(vw("pB", 0, 128), vw(v), vw("I32"))
+        aff(vw("aP", 0, 128), vw("pB", 0, 128), 256.0)
+        aff(vw("aP", 128, 256), vw("pB", 0, 128))
+        tt(vw("pr"), ind(vw("nz"), vw("L16")), vw("aP"), A.mult)
+        ts(vw("bb"), vw("pr"), 32768, A.bitwise_and)
+        for a in (0, 128):
+            aff(vw("gb", a, a + 128), vw("bb", a, a + 128))
+            more("gb%d" % a)
+        ts(vw("s8"), last("mr"), 15, A.bitwise_and)
+        tt(vw("okK"), ind(vw("s8"), vw("L8")), vw("m15"), A.is_equal)
+        for p in QB:
+            mm(vw(p, 0, 256), row("on"), row("ini", 0, 256), True, False)
+            mm(vw(p, 3, 256, 4), row("mk2", 128, 256), row("on", 0, 64), False, False)
+        for s, a, b in ((2, "boE", "eN"), (3, "IH", "eN"), (2, "kb", "Im19"), (3, "kb", "I19"), (2, "kl", "Im2k"), (3, "kl", "I2k"), (1, "tb", "I4k")):
+            quad(s, vw(a), b)
+        for a in (0, 128):
+            for s in (2, 3):
+                quad(s, vw("gb", a, a + 128), "Ig")
+        mm(win, row("on"), row("far"), True, False)
+        mm(win, row("mk2", 0, 128), row("on"), False, False)
+        mm(win, vw("IH"), vw("eN"), False, False)
+        mm(win, vw("kb"), vw("Im19"), False, False)
+        mm(win, vw("kl"), vw("Im2k"), False, False)
+        mm(win, vw("okK"), vw("I2H"), False, False)
+        sums(t)
 
-    def entered(t):
+    def entered(t, q2):
         n = vw("n%d" % t)
-        gath("v", vw("xe"), XG, n)
-        gath("s", vw("nhi"), vw("TQ"), n, 1.0 / 64, 128.25 - 0.4921875)
-        gath("s", vw("nlo"), vw("TQ"), n, 1.0, 16.0)
-        gath("s", vw("RN"), vw("R"), n, 1.0, 16.0)
-        remedies("q%d" % t, 72, 128)
-        mm(vw("pE", 256, 280), vw("xe"), vw("w3"), False, True)
-        tt(vw("nq"), ind(vw("TQ"), n), vw("eN"), A.mult)
-        copy(vw("le"), vw("pG", 8, 16))
-        mm(vw("pF", 256, 272), vw("xe"), vw("wd"), False, False)
-        mm(vw("pF", 256, 264), vw("nhi"), vw("bo8s"), False, False)
-        mm(vw("pF", 264, 272), vw("nhi"), vw("bo4n"), False, False)
-        mm(vw("pF", 264, 272), vw("nlo"), vw("bo8s"), False, True)
-        mm(vw("pB", 128, 256), vw("nq"), vw("Ib"), False, True)
-        tt(vw("kz"), vw("pE", 264, 280), vw("ms", 15, 256, 16), A.max)
-        for d in ("dz", "dy"):
-            tt(vw(d, 2, 24, 3), vw("pE", 256, 264), vw("th2"), A.is_ge)
-        for a in (0, 1):
-            ts(vw("nz", a, 24, 3), vw("kz", 8 * a, 8 * a + 8), 255, A.bitwise_and)
-        scan(vw("pz"), vw("dz"), vw("nz"), A.mult, A.add)
-        tt(vw("ky"), vw("pF", 256, 272), vw("my", 15, 256, 16), A.max)
+        for h in (0, 1):
+            a, b, nh = 64 * h, 64 * h + 64, vw("n%d" % t, 4 * h, 4 * h + 4)
+            aff(vw("xe", a, b), ind(XG(t), nh), 1.0, 0.0, "s")
+            more("xe%d" % h)
+            tt(vw("nq", a, b), ind(vw("TQ"), nh), vw("eN", a, b), A.mult)
+            more("nq%d" % h)
+            tt(vw("qd", 4 * a + 3, 4 * b, 4), vw("q16", a, b), vw("nq", a, b), A.add)
+            more("qd%d" % h)
+            for s, c in ((1, "boS"), (2, "boT"), (3, "boU")):
+                mm(vw(QB[h], s, 256, 4), vw(c), vw("xe", a, b), False, s == 3)
+            run(3)
+            scan(vw("sq", 4 * a, 4 * b), vw(QB[h], 0, 256), vw("qd", 4 * a, 4 * b), A.max, A.min)
+            more("sq%d" % h)
+            copy(vw(q2, a, b), vw("sq", 4 * a + 3, 4 * b, 4))
+            more("qo%d" % h)
+        mm(win, vw("boT"), vw("xe"), False, True)
+        mm(vw("pD", 256, 384), vw("Ib"), vw("xe"), False, True)
+        relu(vw("w"), win, 0.0)
+        if not DK:
+            aff(vw("RN"), ind(vw("R"), n), 1.0, 16.0)
+            copy(ind(vw("RA"), vw("le")), vw("RN"))
 
-    entry_constants()
+    def update(t):
+        tt(vw("rm"), qf, q2f, A.subtract)
+        tt(vw("yq"), vw("rm"), vw("w"), A.min)
+        act(vw("sg"), vw("yq"), 1.0, 0.0, F.Sign, vw("cj"))
+        for p in ("pG", "pH"):
+            mm(vw(p), vw("Ib"), vw("tri"), True, False)
+        for w in range(8):
+            p = vw("pG" if w < 4 else "pH", 128 * (w % 4), 128 * (w % 4) + 128)
+            mm(p, vw("sl", 128 * w, 128 * w + 128), vw("yq"), False, w % 4 == 3)
+            if w % 4 == 3:
+                run(4)
+        mm(vw("pB", 256, 264), vw("yq"), vw("bo8"))
+        aff(vw("y8"), vw("pB", 256, 264), -4096.0)
+        for a, p in ((0, "pG"), (512, "pH")):
+            for w in range(4):
+                act(vw("eq", a + 128 * w, a + 128 * w + 128), vw(p, 128 * w, 128 * w + 128), 1.0, vw("y8", a // 128 + w, a // 128 + w + 1), F.Abs)
+                more("eq%d" % (a // 512))
+            scan(vw("ab", a, a + 512), vw("d0a"), vw("eq", a, a + 512), A.add, A.min)
+            more("ab%d" % (a // 512))
+        mm(vw("pB", 264, 272), vw("yq"), vw("bo8"), True, False)
+        mm(vw("pB", 264, 272), vw("sg"), vw("bo16"), False, True)
+        aff(vw("ya"), vw("pB", 264, 272), -1.0, vw("dum"))
+        tt(vw("du"), vw("ab", 127, 1024, 128), vw("ya"), A.min)
+        if t < VI - 1:
+            mm(vw("pB", 280, 281), vw("on32"), vw("cj"))
+            aff(vw("cn"), vw("pB", 280, 281), 1.0, 281600.0)
+            aff(vw("cz"), vw("cn"), 1.0 / 256, -0.498046875)
+            aff(vw("cc"), vw("cz"), -256.0, vw("cn"))
+            aff(vw("limc"), vw("cc"), 16.0, vw("limf"))
+            aff(vw("lim8"), vw("I32", 0, 128, 16), vw("limc"))
+        tt(vw("AS"), ind(vw("du"), vw("L8")), vw("m16"), A.mult)
+        mm(vw("pB", 288, 296), vw("m16"), vw("bo8d"), True, False)
+        mm(vw("pB", 288, 296), vw("AS"), vw("bo8n"), False, True)
+        copy(vw("ls"), vw("pB", 288, 296))
+        aff(vw("ti"), vw("pD", 256, 384), 0.0625)
+        tt(vw("xs"), ind(vw("XY"[t % 2]), vw("ls")), vw("ti"), A.add)
+        ts(vw("xn"), vw("xs"), 0.5, A.mult, -0.484375, A.add)
+        copy(ind(vw("YX"[t % 2]), vw("ls")), vw("xn"))
+        more("up")
+
     for t in range(VI):
         q, v = "q%d" % t, "v%d" % t
         end = t == VI - 1
-        if t:
-            kept(t)
-            entered(t)
-        sums(t)
         q2 = "q2u" if end else "qo%d" % (t + 1)
         if t:
-            tt(vw("pr"), ind(vw("pz"), vw("L3")), vw("aP"), A.mult)
-            for a in (0, 1):
-                ts(vw("ny", a, 24, 3), vw("ky", 8 * a, 8 * a + 8), 255, A.bitwise_and)
+            kept(t)
+            turn[0] = t
+            entered(t, q2)
         else:
-            tt(vw("pr"), an, vw("pwB"), A.mult)
-            stopped()
-            act(vw("aP"), an)
-            remedies(q, 28, 52)
-            copy(vw("wc"), vw("pH", 0, 1))
-            ts(vw("wt"), vw("pH", 0, 1), 2.5, A.mult)
-        ts(vw("bb"), vw("pr"), 32768, A.bitwise_and)
-        scan(vw("yz"), vw("dy"), vw("ny"), A.mult, A.add)
-        tt(vw("q2P"), vw("pB", 128, 256), vw("bb"), A.subtract)
-        mm(vw("pA", 128, 256), vw("q2P"), vw("Ib"))
-        if t == 0:
-            ts(vw("E"), vw("eI"), vw("hc"), A.is_equal)
-        else:
-            copy(ind(vw("RA"), vw("le")), vw("RN"))
-        act(vw("y16"), vw("yz", 2, 24, 3))
-        mm(vw("pE", 128, 256, 1, 0, 8), vw("y16"), vw("Ib"))
-        if t == 0:
-            remedies(q, 52, 68)
-        shown()
-        if t == 0:
-            mm(vw("pE", 256, 384), vw("aP"), vw("I32"), True, False)
-            mm(vw("pE", 256, 384), vw("I32th"), vw("wyb"), False, True)
-        ts(vw(q2), vw("pA", 128, 256), -16.0, A.add)
+            rows(0)
+            turn[0] = 0
+            aff(vw("pwR"), vw("pB", 0, 128))
+            turn[0] = None
+            ts(vw("w"), vw("pB", 0, 128), vw("pwc"), A.is_equal, 4096.0, A.mult)
+            tt(vw("pr", 0, 128), an, vw("pwR"), A.mult)
+            tt(vw(v), an, vw("wy32"), A.add)
+            ts(vw("bb", 0, 128), vw("pr", 0, 128), 32768, A.bitwise_and)
+            tt(vw("qc"), qf, vw("bb", 0, 128), A.subtract)
+            turn[0] = 0
+            copy(vw(q2), vw("qc"))
+            more("qo0")
+            relu(q2f, vw("qc"), 0.0)
+            sums(0)
         if not end:
             send("q", t + 1)
-        if t == 0:
-            iota(vw("TQ"), [[1, XS - 16]], 0, 0)
-        cuts = (0, 28, 56, 92, 128)
-        xgath("s", "x2", q2, cuts[2], cuts[3], 16.0, -2048.0)
-        ts(vw("e2"), vw(q2), 0, A.is_equal)
-        xgath("v", "x2", q2, cuts[0], cuts[1], 16.0, -2048.0)
-        if end:
-            mm(vw("pF", 0, 128), vw("e2"), vw("cm"))
-        mm(vw("pF", 128, 256), vw("cm"), vw("e2"))
-        xgath("s", "x2", q2, cuts[3], cuts[4], 16.0, -2048.0)
-        xgath("v", "x2", q2, cuts[1], cuts[2], 16.0, -2048.0)
+        zero(vw("e2"), q2f)
+        for a, b in zip(CUT2, CUT2[1:]):
+            xgath(t, "x2", q2, a, b, 16.0, -2048.0, "vs" if t else "s" if a in CUT2[1::2] else "v")
+            if t == 0:
+                more("x2")
         ku = vw("pC", 0, 128)
         mm(ku, row("on"), row("tie16"), True, False)
-        mm(ku, vw("e2"), vw("bo256"), False, False)
         for m in range(16):
             mm(ku, flat("x2", 0, 128, m), vw("I16"), False, False)
-        for a, b in zip(cuts, cuts[1:]):
+        run(16)
+        mm(ku, vw("e2"), vw("bo256"), False, False)
+        for a, b in zip(CUT2, CUT2[1:]):
             scan(flat("bs", a, b), flat("d0b", 0, b - a), flat("x2", a, b), A.add, A.max)
-        e = 0 if end else 128
-        act(vw("e0", e, 256), vw("pF", e, 256), 1.0, 17.0, F.Relu)
-        if t == 0:
-            act(vw("v0"), vw("pE", 256, 384))
-            remedies(q, 68, 128)
-        act(vw("ti"), vw("pD", 256, 384), 0.0625)
-        act(vw("a1"), vw(v), 1.0, 8388608.0)
-        eP, eQ = vw("e1", 0, 256), vw("e1", 256, 384)
+            more("bs_%d" % a)
         bl = vw("bs", 15, 2048, 16)
-        equal(0, 2)
-        ts(vw("lo"), bl, 0.0625, A.mult, 1280 - 0.46875, A.add)
+        aff(vw("lo"), bl, 0.0625, 1280 - 0.46875, "v")
         mm(ku, bl, vw("Ib"), False, False)
         mm(ku, vw("lo"), vw("Im16"), False, True)
-        equal(2, 6)
-
-        def spread(n):
-            p = vw(("pF", "pE", "pG", "pH")[n])
-            mm(p, vw("cP", 0, 128, 1, 32 * n, 32 * n + 32), vw("E", 0, 512, 1, 32 * n, 32 * n + 32), True, n < 2)
-            if n < 2:
-                act(flat("vf", 32 * n, 32 * n + 32), p, 1.0, -1100.0)
+        e = 0 if end else 128
+        if end:
+            mm(vw("pA", 0, 128), vw("e2"), vw("cm"))
+        mm(vw("pA", 128, 256), vw("cm"), vw("e2"))
+        relu(vw("e3", e, 256), vw("pA", e, 256), 17.0)
+        zero(vw("e1", 128 + e, 384), vw("e3", e, 256))
+        eQ = vw("e1", 256, 384)
+        aff(vw("a1"), vw(v), 1.0, 8388608.0)
+        aff(vw("a2"), vw("a1"), 1.0, -8388608.0)
+        if end:
+            aff(vw("e1", 0, 128), vw("e1", 128, 256), 64.0)
+            aff(vw("fR"), vw("e2"), -32.0, 32.0)
+        else:
+            aff(vw("aM"), vw("a2"), 1.0, vw("a32"))
+        update(t)
         scan(vw("mk"), vw("d0m", 0, 128), ku, A.add, A.max)
-        act(vw("cP"), ku, -1.0 / 4096, 1222.5 - 1.0 / 8192)
-        act(vw("a2"), vw("a1"), 1.0, -8388608.0)
-        act(vw("e1", 128 + e, 384), vw("e0", e, 256), -1.0, 1.0, F.Relu)
-        if not end:
-            act(vw("aM"), vw("a2"), 1.0, vw("a32"))
-        if t == 1:
-            act(vw("IpQ"), vw("Ib"), float(16 + D))
-        if end:
-            act(vw("e1", 0, 128), vw("e0", 0, 128), -64.0, 64.0, F.Relu)
-            act(vw("fR"), vw("e2"), -32.0, 32.0)
-        equal(6, 8)
+        aff(vw("cP"), ku, -1.0 / 4096, 1222.5 - 1.0 / 8192)
         ts(vw("r8"), last("mk"), 15, A.bitwise_and)
-        if end:
-            ts(vw("q2h"), vw(q2), 0.0, A.add)
-        ts(vw("ya"), vw("yz", 2, 24, 3), vw("ndum"), A.add)
-        mm(vw("pA", 256, 264), vw("m16"), vw("bo8k"), True, False)
-        weigh()
-        spread(0)
-        tt(vw("AL"), ind(vw("r8"), vw("L8")), vw("m16"), A.mult)
-        mm(vw("pA", 256, 264), vw("AL"), vw("bo8n"), False, True)
-        tt(vw("ok"), ind(vw("r8"), vw("L8")), vw("m15"), A.is_equal)
-        ts(vw("du"), vw("pB", 16, 24), vw("wt"), A.is_lt)
-        copy(vw("lk"), vw("pA", 256, 264))
-        spread(1)
-        spread(2)
-        spread(3)
-        mm(vw("pB", 256, 384), vw("ok"), vw("Ib"))
-        tt(vw("of"), vw("du"), vw("ya"), A.mult)
-        copy(vw("cd"), ind(vw("RA"), vw("lk")))
-        tt(vw("AS"), ind(vw("of"), vw("L8")), vw("m16"), A.mult)
-        mm(vw("pC", 264, 272), vw("m16"), vw("bo8d"), True, False)
-        mm(vw("pC", 264, 272), vw("AS"), vw("bo8"), False, True)
-        sc = vw("pD", 128, 384)
-        mm(sc, row("on"), row("tie2", 0, 256), True, False)
+        if DK:
+            tt(vw("ok"), ind(vw("r8"), vw("L8")), vw("m15"), A.is_equal)
+            mm(vw("pA", 384, 512), vw("ok"), vw("Ib"))
+            more("okm")
+            tt(vw("AL"), vw("pA", 384, 512), q2f, A.mult)
+            if not end:
+                tt(vw("oka"), vw("pA", 384, 512), vw("aM"), A.mult)
+            for c in range(16):
+                mm(vw("pD", 0, 8), vw("Z", 15 - c, 143 - c), vw("AL", c, 128, 16), c == 0, c == 15)
+            run(16)
+            more("dk")
+            copy(vw("lk"), vw("pD", 0, 8))
+            ts(vw("cd"), ind(vw("R"), vw("lk")), 16.0, A.add)
+        else:
+            tt(vw("AL"), ind(vw("r8"), vw("L8")), vw("m16"), A.mult)
+            mm(vw("pA", 256, 264), vw("m16"), vw("bo8k"), True, False)
+            mm(vw("pA", 256, 264), vw("AL"), vw("bo8n"), False, True)
+            copy(vw("lk"), vw("pA", 256, 264))
+            copy(vw("cd"), ind(vw("RA"), vw("lk")))
+            tt(vw("ok"), ind(vw("r8"), vw("L8")), vw("m15"), A.is_equal)
+            mm(vw("pA", 384, 512), vw("ok"), vw("Ib"))
+        nq = vw("pF", 0, 128)
+        nv = vw("pC", 0, 128)
+        if not end:
+            mm(vw("pC", 128, 256), vw("I32"), vw(v), True, False)
+            mm(vw("pC", 128, 256), vw("Im20"), eQ, False, True)
+            aff(vw("t3"), vw("pC", 128, 256))
+            mm(nv, row("pw20"), row("on"), True, False)
+            mm(nv, row("pwr"), row("on"), False, False)
+            mm(nv, vw("I20"), eQ, False, False)
+            if not DK:
+                tt(vw("oka"), vw("pA", 384, 512), vw("aM"), A.mult)
+            mm(nv, vw("bo32"), vw("oka"), False, True)
+            tt(vw("vo%d" % (t + 1)), nv, vw("t3"), A.max)
+            send("v", t + 1)
+        bank = {2: "pF", 3: "pG", 0: "pE", 1: "pH"}
+        for n in (2, 3, 0, 1):
+            mm(vw(bank[n]), vw("cP", 0, 128, 1, 32 * n, 32 * n + 32), vw("E", 0, 512, 1, 32 * n, 32 * n + 32), True, n % 2 == 0)
+            if n % 2 == 0:
+                aff(flat("vf", 16 * n, 16 * n + 32), vw(bank[n]), 1.0, -1100.0, "s")
+                more("vf%d" % n)
+        sb = ("pD", "pD")
+        if DK:
+            aff(vw("cd16"), ind(vw("R"), vw("lk")), 1.0, 16.0)
+            aff(vw("chi"), ind(vw("R"), vw("lk")), 1.0 / 64, 128.25 - 0.4921875)
+        else:
+            ts(vw("cd16"), vw("cd"), 0.0, A.add)
+            ts(vw("chi"), vw("cd"), 1.0 / 64, A.mult, 128 - 0.4921875, A.add)
 
         def summed(src, n, w, stop):
             a, b = 32 * n, 32 * n + 32
             for j in range(16):
-                mm(vw("pD", 128 + j, 384, 16, a, b), flat(src, a, b, j), vw(w), False, stop and j == 15)
-
-        def differences(n):
-            a, b = 32 * n, 32 * n + 32
-            tt(flat("mn", a, b), ind(XG, vw("cd", a, b)), flat("vf", a, b), A.subtract)
-            summed("mn", n, "wd", False)
-
-        def positive(n):
-            a, b = 32 * n, 32 * n + 32
-            ts(flat("xc", a, b), flat("mn", a, b), 0.0, A.max)
-            summed("xc", n, "wr2", True)
-
-        def negated(n):
-            a, b = 32 * n, 32 * n + 32
-            xgath("s", "mn", "cd", a, b, -1.0)
-            mm(vw(("pG", "pH")[n - 2]), vw("Ib"), flat("mn", a, b), False, True)
-
-        def absolute(n):
-            act(flat("xc", 32 * n, 32 * n + 32), vw(("pG", "pH")[n - 2]), 1.0, -1100.0, F.Abs)
-            summed("xc", n, "wa", True)
-        nq = vw("pA", 384, 512)
-        nv = vw("pC", 0, 128)
-        if not end:
-            mm(nv, row("pwr"), row("on"), True, False)
-            mm(nv, vw("Im32"), vw(v), False, False)
-        negated(2)
-        differences(0)
-        ts(vw("cd16"), vw("cd"), 0.0, A.add)
-        ts(vw("chi"), vw("cd"), 1.0 / 64, A.mult, 128 - 0.4921875, A.add)
-        copy(vw("ls"), vw("pC", 264, 272))
+                mm(vw(sb[n // 2], 128 + j, 384, 16, a, b), flat(src, a, b, j), vw(w), False, stop and j == 15)
+            run(16)
+        mm(vw("pD", 128, 384), row("on"), row("tie2"), True, False)
+        for h in (1, 0):
+            lo, hi = 64 * h, 64 * h + 64
+            n = 2 * h
+            tt(flat("mn", lo, lo + 32), ind(XG(t), vw("cd", lo, lo + 32)), flat("vf", 16 * n, 16 * n + 32), A.subtract)
+            more("mn_%d" % lo)
+            c = hi if h else hi - SHARE
+            xgath(t, "mn", "cd", lo + 32, c, -1.0, 0.0, "s")
+            if c < hi:
+                xgath(t, "mn", "cd", c, hi, -1.0, 0.0, "v")
+                more("mn_v")
+            mm(vw(bank[n + 1]), vw("Ib"), flat("mn", lo + 32, hi), False, True)
+            ts(flat("xc", lo, lo + 32), flat("mn", lo, lo + 32), 0.0, A.max, 2.0, A.mult)
+            more("xc%d" % n)
+            act(flat("xc", lo + 32, hi), vw(bank[n + 1]), 1.0, -1100.0, F.Abs)
+            more("xc%d" % (n + 1))
         mm(vw("pD", 128, 256), vw("chi"), vw("Ib"), False, False)
         mm(vw("pD", 256, 384), vw("cd16"), vw("Ib"), False, False)
         mm(vw("pD", 256, 384), vw("chi"), vw("Im64"), False, False)
+        run(3)
+        for n in (2, 0):
+            summed("mn", n, "wd", False)
+        for j in range(16):
+            mm(vw("pD", 128 + j, 384, 16), flat("xc", 0, 128, j), vw("wa"), False, j == 15)
+        run(16)
         if not end:
-            tt(vw("oka"), vw("pB", 256, 384), vw("aM"), A.mult)
-            mm(nv, vw("bo32"), vw("oka"), False, True)
-        else:
-            ts(vw("okb"), vw("pB", 256, 384), vw("ac"), A.mult)
-            mm(nv, vw("bo"), vw("okb"))
-        negated(3)
-        differences(1)
-        positive(0)
-        absolute(2)
-        positive(1)
-        absolute(3)
-        tt(vw("xs"), ind(vw("X"), vw("ls")), vw("ti"), A.add)
+            scan(vw("ms"), vw("d0m", 0, 256), vw("pD", 128, 384), A.add, A.max)
+            ts(vw("n16", 0, 16), vw("ms", 15, 256, 16), 255, A.bitwise_and)
+            for a in (0, 8):
+                o = vw("AN", 16 * a, 16 * a + 128)
+                tt(o, ind(vw("n16", a, a + 8), vw("L8")), vw("m16"), A.mult)
+                more("AN%d" % a)
+                mm(vw("pH", 0, 8), o, vw("bo8" if a else "bo64"), a == 0, a == 8)
+            copy(vw("no%d" % (t + 1), 4, 12), vw("pH", 0, 8))
+            send("n", t + 1, 1)
+            send("n", t + 1, 0)
+            copy(ind(vw("XY"[t % 2]), vw("ls")), vw("xn"))
+            more("up2")
         if end:
+            aff(vw("okb"), vw("pA", 384, 512), vw("ac"))
+            mm(nv, vw("bo"), vw("okb"))
             tt(vw("fr"), vw(v), vw("a2"), A.subtract)
-        else:
-            tt(vw("t3"), nv, eQ, A.mult)
-            ts(vw("eR"), vw("q%d" % (t + 1)), 0, A.is_equal)
-        ts(vw("xn"), vw("xs"), 0.5, A.mult, -0.484375, A.add)
-        if not end:
-            tt(vw("vo%d" % (t + 1)), vw(v), vw("t3"), A.add)
-            send("v", t + 1)
-            copy(ind(vw("X"), vw("ls")), vw("xn"))
-            ahead(t + 1)
-        else:
             tt(vw("fr"), vw("fr"), vw("fR"), A.mult)
-            copy(ind(vw("X"), vw("ls")), vw("xn"))
-            store(T.yx[:, :], vw("X", X0, X0 + D), "st0")
+            tt(vw("t3"), nv, eQ, A.mult)
+            tt(vw("yw"), vw("fr"), vw("t3"), A.add)
+            store(T.yq[:, :], vw("yw"), "st1", "y", DMA + 0.3)
+            store(T.yx[:, :], vw("X", X0, X0 + D), "st0", "y", DMA + 1.6)
             mm(nq, vw("ImQ"), eQ, True, False)
             mm(nq, vw("IpQ"), vw("e2"), False, False)
-            mm(nq, vw("Ib"), vw("q2h"), False, False)
-        scan(vw("ms"), vw("d0m"), sc, A.add, A.max)
-        if end:
-            tt(vw("t3"), nv, eQ, A.mult)
-        else:
-            ts(vw("q16"), vw("q%d" % (t + 1)), 16.0, A.add)
-            upper("q%d" % (t + 1))
-        ts(vw("n16"), vw("ms", 15, 256, 16), 255, A.bitwise_and)
-        if end:
-            tt(vw("yw"), vw("fr"), vw("t3"), A.add)
-            store(T.yq[:, :], vw("yw"), "st1")
-        for a in (0, 8):
-            o = vw("AN", 16 * a, 16 * a + 128)
-            if end:
+            mm(nq, vw("Ib"), q2f, False, False)
+            scan(vw("ms"), vw("d0m", 0, 256), vw("pD", 128, 384), A.add, A.max)
+            ts(vw("n16", 0, 16), vw("ms", 15, 256, 16), 255, A.bitwise_and)
+            for a in (0, 8):
+                o = vw("AN", 16 * a, 16 * a + 128)
                 tt(o, ind(vw("n16", a, a + 8), vw("L8")), vw("e1", 16 * a, 16 * a + 128), A.mult)
+                more("AN%d" % a)
                 mm(nq, o, vw("Ib"), False, a == 8)
-            else:
-                tt(o, ind(vw("n16", a, a + 8), vw("L8")), vw("m16"), A.mult)
-                mm(vw("pA", 384, 392), o, vw("bo8" if a else "bo64"), a == 0, a == 8)
-        if not end:
-            xgath("v", "x", "q%d" % (t + 1), 0, 16)
-            copy(vw("no%d" % (t + 1)), vw("pA", 384, 392))
-            send("n", t + 1)
-        else:
-            act(vw("yt"), nq, 1.0, -16.0)
-            store(T.yp[:, :], vw("yt"), "st2", "s")
+            aff(vw("yt"), nq, 1.0, -16.0)
+            store(T.yp[:, :], vw("yt"), "st2", "s", DMA + 0.3)
+
+    if "plan" not in PLAN:
+        PLAN["plan"] = order(ops, links(ops))
+    pre, place, seq = PLAN["plan"]
+    cnt, tok, snap, known = {}, {}, {}, {q: {} for q in Q}
+    for i in seq:
+        o, q = ops[i], place[i][0]
+        s = o["sem"] or ES[q]
+        cnt[s] = cnt.get(s, 0) + o["inc"]
+        tok[i] = (s, cnt[s])
+        if q == "-":
+            snap[i] = {}
+            continue
+        best = {}
+        for j, hard in pre[i].items():
+            if (hard or place[j][0] != q) and tok[j][0] != "loc" and tok[j][1] > best.get(tok[j][0], (0, 0))[0]:
+                best[tok[j][0]] = (tok[j][1], j)
+        for k, (c, j) in sorted(best.items(), key=lambda e: -place[e[1][1]][2]):
+            if known[q].get(k, 0) < c:
+                Q[q].wait_ge(T.sem[k], c)
+                known[q][k] = c
+                for k2, c2 in snap[j].items():
+                    known[q][k2] = max(known[q].get(k2, 0), c2)
+        r = o["alts"][q][0]()
+        if s != "loc":
+            r.then_inc(T.sem[s], o["inc"])
+        snap[i] = dict(known[q])
     for s in SEMAPHORES:
         if cnt.get(s):
             g.wait_ge(T.sem[s], cnt[s])

@@ -6,49 +6,26 @@ A = AluOpType
 F = ActivationFunctionType
 NR, VI, H, L, D = 8, 4, 64, 128, 1760
 STRIDE = (4, 1)
-X0 = 32
+X0 = 16
 XS = X0 + D
 XW = XS + 128
-BIG = 16777216.0
-HUGE = 2.0 ** 29
+BIG = 2.0 ** 24
+HUGE = 2.0 ** 27
+LN2 = 0.6931471805599453
 f32, b16, h16, i32, u16 = "float32", "bfloat16", "float16", "int32", "uint16"
-SB = {
-    "X": (XW, b16), "Y": (XW, b16), "R": (16 + D, i32), "dr0": (L, i32), "wy0": (L, i32), "lmI": (1, i32),
-    "kI": (1, i32), "aI": (1, i32), "gI": (1, i32), "hI": (1, i32), "kc": (1, f32), "ac": (1, f32), "gc": (1, f32), "hc": (1, f32),
-    "a32": (1, f32), "ndum": (1, f32), "dum": (1, f32), "b16p": (1, f32), "k16": (1, f32), "k17": (1, f32), "pwc": (1, f32), "pc": (2, f32),
-    "cid": (128, b16), "gid": (128, b16), "aid": (128, b16), "g8": (8, f32), "bj": (16, f32),
-    "I32": (128, f32), "I20": (128, b16), "Im20": (128, b16), "pw20": (128, b16), "I2k": (128, b16), "Im2k": (128, b16), "I4k": (128, b16), "I19": (128, b16), "Im19": (128, b16), "k8": (8, i32), "kl": (128, b16), "Ib": (128, b16), "I16": (128, b16), "Im16": (128, b16),
-    "ImQ": (128, b16), "IpQ": (128, b16), "Im64": (128, b16), "Im256": (128, b16), "I256": (128, b16), "IH": (128, b16), "I2H": (128, b16), "Ig": (128, b16),
-    "bo": (128, b16), "bo32": (128, f32), "bo256": (128, b16), "boS": (128, b16), "boT": (128, b16), "boU": (128, b16), "boE": (128, b16),
-    "Z": (144, b16), "M0": (128, b16), "cm": (128, b16), "c1": (128, b16), "c2": (128, b16), "c3": (128, b16), "mk2": (256, b16), "d0a": (512, b16), "ab": (1024, b16),
-    "bo8": (8, b16), "bo8f": (8, f32), "bo8n": (8, b16), "wm": (8, b16), "wa": (16, b16), "wd": (16, b16), "wr2": (16, b16), "tie2": (256, b16),
-    "bo8d": (8, h16), "bo8k": (8, h16), "bo16": (8, b16), "bo8a": (8, b16), "bo64": (8, b16), "bo8p": (8, h16),
-    "on": (128, b16), "on32": (128, f32), "m15": (128, b16), "tie16": (128, b16), "m16": (128, b16),
-    "d0s": (128, f32), "d0m": (256, f32), "d0p": (128, f32), "d0b": (576, b16), "pwr": (128, b16), "hlf": (128, f32), "zer": (128, f32),
-    "wr": (128, b16), "wc": (1, b16), "wt": (1, f32), "eI": (512, b16), "E": (512, b16), "sl": (1024, b16),
-    "l3I": (8, i32), "l8I": (8, i32), "lkI": (8, i32), "L3": (8, u16), "L8": (8, u16), "LK": (8, u16),
-    "pay": (384, b16), "w3": (24, b16), "d0h": (128, f32), "d1h": (128, f32), "pwd": (128, f32),
-    "limf": (1, f32), "limc": (1, f32), "lim8": (8, f32), "TQ": (XS - 16, f32), "ini": (512, b16), "far": (128, b16), "kr": (256, b16),
-    "B": (2048, b16), "Aj": (2048, b16), "Dn": (1024, b16), "M2": (128, b16), "b1": (16, f32), "n0r": (2048, b16), "N": (2048, b16), "M": (512, b16), "rt": (128, b16), "nw": (128, b16), "wy32": (128, f32),
-    "wI": (256, b16), "dl": (256, b16), "Kc": (256, b16), "Kd": (256, b16), "K": (256, b16), "pofI": (128, b16), "pofm": (128, h16),
-    "c15": (1, f32), "c14": (1, f32), "a16": (1, f32), "n15": (1, f32), "pw14": (1, f32), "Zc": (144, b16), "Zw": (144, b16),
-    "l0": (128, u16), "lu1": (128, u16), "lu2": (128, u16), "lu4": (128, u16), "lu8": (128, u16), "WA": (2048, b16), "WB": (2048, b16),
-    "qa": (128, f32), "qb": (128, f32), "qc": (128, f32),
-    "eN": (128, b16), "e8": (8, f32), "le": (8, u16), "th2": (8, f32), "xe": (128, b16), "RN": (128, f32), "nq": (128, h16),
-    "x": (2048, b16), "x2": (2048, b16), "xc": (2048, b16), "mn": (2048, b16), "vf": (1024, b16), "bs": (2048, h16), "RA": (2048, f32),
-    "eR": (128, b16), "e2": (128, b16), "q16": (128, h16), "aM": (128, f32), "a1": (128, f32), "a2": (128, f32),
-    "n0": (8, f32), "thr": (8, f32), "sm": (128, f32), "mr": (384, i32), "dz": (16, f32), "nz": (16, i32), "pz": (16, f32),
-    "slm": (1024, b16), "tri": (512, b16), "ZA": (128, f32), "pwB": (256, b16), "pwR": (128, f32), "tb": (128, h16), "kb": (128, h16), "pr": (256, i32), "bb": (256, i32), "gb": (256, b16), "aP": (256, f32), "s8": (8, i32), "l16I": (16, i32), "L16": (16, u16), "okK": (128, b16),
-    "qd": (512, h16), "sq": (512, h16), "q2u": (128, u16), "w": (128, b16), "rm": (128, h16), "yq": (128, h16), "sg": (128, b16),
-    "lo": (128, h16), "cP": (128, h16), "e0": (128, f32), "e3": (256, f32), "e1": (384, b16),
-    "mk": (128, i32), "r8": (8, i32), "ok": (128, b16), "AL": (128, h16), "AE": (128, h16), "lk": (8, u16),
-    "cd": (128, u16), "cd16": (128, h16), "oka": (128, f32), "okb": (128, b16), "t3": (128, f32),
-    "chi": (128, b16), "ms": (256, i32), "n16": (32, i32), "AN": (512, h16),
-    "y8": (8, f32), "eq": (1024, b16), "du": (8, f32), "ya": (8, f32), "of": (8, f32), "AS": (128, h16), "ls": (8, u16),
-    "ti": (128, f32), "xs": (128, f32), "xn": (128, i32), "cj": (1, f32), "cn": (1, f32), "cz": (1, h16), "cc": (1, f32),
-    "yt": (128, f32), "yw": (128, f32), "fR": (128, f32), "fr": (128, f32),
-}
-ALONE = ("X", "R", "dr0", "wy0", "lmI", "yt", "yw")
+SB = {"X": (XW, b16), "Y": (XW, b16), "R": (XS, i32), "TQ": (XS, f32), "M": (17 * 256, h16)}
+for _w, _d, _names in (
+        (1, i32, "lmI kI aI gI hI tI cI cA"), (1, f32, "kc ac gc hc tc a1c a32 dum pwa limf cj cb"), (1, b16, "pwb cjb"), (4, f32, "pc"),
+        (8, f32, "g8 c4k bo8f lim8 limP n0 thr sn th2 dz pw pz ym ya du"), (8, i32, "nz ke k8 r8"), (8, b16, "bo8 bo8n bo8a bo64 wm w3 sg"), (8, h16, "bo8d"),
+        (8, u16, "L8 l0 ls lk"), (16, i32, "l16I n16"), (16, u16, "L16"), (16, b16, "wa wd"),
+        (64, b16, "cK tri pk pk1 pk2 mid"), (64, f32, "tH"),
+        (128, b16, "on cid gid aid Ib Im I16 Im16 Im32 I64 Im64 I17 I4k Im4k Im1k IH ImH I2H ImQ IpQ Ipw bo bo256 boT boU cm cmb c1 c2 M2 m15 d0s d0r d0k far low less"),
+        (128, f32, "I32 I32m bo32 on32"), (144, b16, "Z"), (256, b16, "m16 d0m ini"), (512, b16, "eI E sl d0a"), (640, b16, "d0b"),
+        (128, i32, "dr0 wy0 mr mk pr bb xn"), (128, b16, "rt wy32 eN eR e2 eQ xe xb pwB gb okK ok okb w chi"), (128, f32, "qa qb a1 t3 sm pwR oka yt yw"),
+        (128, h16, "nq q16 tb kb yq lo cP AL AS cd16 tU"), (128, u16, "q2u cd"), (256, i32, "ms"), (256, h16, "AN"), (512, h16, "qd sq"), (512, b16, "eq ab"),
+        (2048, b16, "B Aj N Dn x x2 xc mn vf"), (2048, h16, "bs")):
+    SB.update({_k: (_w, _d) for _k in _names.split()})
+ALONE = ("dr0", "wy0", "lmI", "yt", "yw")
 ALIAS, SCRATCH, _wide = {}, {}, {}
 for _k, (_w, _d) in SB.items():
     if _w > 1024 or _k in ALONE:
@@ -76,60 +53,35 @@ SEMAPHORES = ["ev", "es", "et", "eg", "loc"] + ["ld%d" % _t for _t in range(6)] 
 for _t in range(1, VI):
     SEMAPHORES += ["%s%d" % (_n, _t) for _n in ("qL", "qH", "vL", "vH", "nL", "nH", "rq", "rv", "rn")]
 HALF = {"q": H, "v": H, "n": 4}
-CYC, PEC, GAT, SCA, WAKE, HOP, DMA = 0.83e-3, 0.42e-3, 1.56, 3.8, 0.2, 1.1, 1.0
-CUT1 = (0, 16, 32, 48, 64, 80, 96, 112, 128)
-CUT2 = (0, 32, 64, 96, 128)
-LATE = 4.0
-SWEEPS = 0
-SPARE = 0.2
-DK = True
-DBL = True
-TWIN = False
-HELP = ()
-ABS = True
-SHARE = 0
-MORE = {'up': 1, 'lk': 1.0, 'xs': 0.75, 'bs': 0.5, 'up2': 1.0, 'e3': 2.0, 'yq': 1.0, 'eN': 0.5, 'aM': 0.5, 'oka': 0.25, 'xn': 0.5, 'x': 0.25, 'pH': 0.25, 'AL': 0.5, 'okK': 0.25, 'pG': 0.5, 'a2': 1.0, 'tb': 0.5, 't3': 0.25, 'cz': 0.5, 'cd16': 1.0, 'pay': 1.0, 'c1': 0.25, 'N': 0.25, 'w3': 2.0, 'sl': 2.0, 'n16': 0.25, 'ls': 0.5}
-TURN = 14.0
-DUE = {"xe0": 0.0, "nq0": 0.0, "qd0": 0.4, "sq0": 0.7, "qo0": 1.1, "xe1": 1.1, "nq1": 1.15, "x2_0": 1.6, "x2_32": 1.4, "qd1": 1.5, "sq1": 1.8, "qo1": 2.2,
-       "w": 2.0, "rm": 2.3, "yq": 2.45, "x2_64": 2.5, "x2_96": 2.45, "e2": 2.4, "bs_0": 2.6, "bs_32": 2.65, "bs_64": 3.3, "bs_96": 3.35, "sg": 3.3,
-       "eq0": 3.35, "eq1": 3.4, "lo": 3.8, "ab0": 3.9, "mk": 4.3, "ab1": 4.35, "ya": 4.2, "cP": 4.5, "r8": 4.6, "du": 4.7, "ok": 4.85, "AS": 4.95,
-       "AL": 5.5, "ls": 5.6, "vf0": 5.3, "vf1": 5.7, "xs": 5.9, "lk": 6.4, "xn": 6.5, "cd": 6.7, "up": 6.9, "mn_0": 7.1, "mn_64": 7.1, "mn_96": 7.8,
-       "mn_32": 7.8, "cd16": 6.7, "chi": 6.8, "pwR": -4.0, "xc0": 8.6, "xc2": 8.6, "xc1": 8.8, "xc3": 9.0, "oka": 5.7, "t3": 5.0, "vo": 6.4, "y8": 2.9, "ms": 10.0, "n16": 10.4,
-       "AN0": 10.6, "AN8": 10.8, "no": 11.5, "x_0": 9.4, "x_16": 9.5, "x_32": 9.6, "x_48": 9.7, "x_64": 10.2, "x_80": 10.6, "x_96": 11.0, "x_112": 11.4,
-       "mr1": 12.2, "nz": 12.6, "mr0": 12.7, "sm": 12.75, "pr": 12.9, "bb": 13.4, "gb0": 13.8, "gb128": 13.8}
-ENG = {k: "s" for k in "kb w eN e1 e2 eR chi cd16 aP gb0 a1 a2 aM ya e0 e3 x_0 x_32 x_64 x_96 cP tb ti cn cz cc limc lim8".split()}
-ENG.update({k: "v" for k in "x_16 x_48 x_80 x_112 gb128".split()})
-DUE = {'pwR': -4.0, 'xe0': -2.8, 'x2_0': 0.03, 'bs_32': 0.4, 'qo0': 0.63, 'rm': 1.38, 'qd1': 1.75, 'nq1': 1.75, 'x2_64': 2.09, 'qo1': 2.42, 'bs_0': 2.5, 'x2_96': 2.55, 'eq0': 2.85, 'AS': 2.9, 'a1': 3.08, 'e2': 3.2, 'eq1': 3.2, 'bs_64': 3.75, 'vf0': 4.2, 'sg': 4.28, 'mk': 4.6, 'ab1': 4.65, 'du': 4.71, 'cP': 4.8, 'ya': 5.2, 'oka': 5.2, 'AL': 5.5, 'lim8': 5.52, 't3': 5.6, 'cd16': 5.8, 'chi': 5.82, 'mn_0': 6.1, 'vf1': 6.7, 'cd': 6.7, 'vo': 6.82, 'mn_32': 7.44, 'pr': 7.6, 'xc0': 8.01, 'AN0': 8.57, 'x_16': 9.22, 'x_0': 9.4, 'x_32': 9.48, 'q16': 9.8, 'ms': 10.0, 'x_48': 10.18, 'x_80': 10.3, 'AN8': 10.55, 'n16': 10.57, 'x_64': 11.2, 'e0': 11.26, 'x_112': 11.8, 'sm': 12.15, 'th2': 13.03, 'mr1': 13.05, 'x_96': 13.07, 's8': 13.45, 'nz': 13.57}
-ENG = {k: "s" for k in "kb w e1 e2 chi cd16 aP gb0 a2 aM e0 e3 x_0 x_32 x_48 x_64 x_96 cP tb ti cn cz cc limc lim8 x2_32 x2_96 y8 sq pwR fR t3".split()}
-ENG.update({k: "v" for k in "eN eR a1 ya x_16 x_80 x_112 gb128 x2_0 x2_64 n0 okb yt".split()})
-DBL, HOP, TURN, DRAIN, WAKE = False, 1.3, 15.5, 0.14, 0.18
-DUE = {'x0_112': -7.99, 'x0_0': -7.52, 'x0_16': -7.22, 'x0_64': -7.19, 'pwR': -4.0, 'nq1': -3.4, 'qd1': -2.4, 'yq': -0.21, 'bs_96': 0.45, 'qd0': 0.48, 'x2_32': 0.8, 'rm': 0.89, 'x2': 0.98, 'sq1': 0.99, 'w': 1.52, 'x2_64': 1.74, 'bs_32': 1.82, 'mk': 1.94, 'x2_0': 2.0, 'bs_0': 2.36, 'x2_96': 2.45, 'e2': 2.83, 'bs_64': 2.94, 'ab0': 4.07, 'cd16': 4.36, 'ab1': 4.75, 'mn_64': 4.9, 'AL': 4.9, 'vo': 5.0, 'ok': 5.01, 'ti': 5.05, 'du': 5.13, 't3': 5.4, 'fr': 5.63, 'chi': 5.98, 'cd': 6.9, 'mn_0': 6.98, 'x_32': 7.98, 'x_0': 8.36, 'x_48': 8.36, 'AN0': 8.97, 'AN8': 9.25, 'n16': 9.27, 'x_64': 9.7, 'x_80': 9.9, 'e0': 10.7, 'q16': 10.72, 'k8': 12.26, 'pr': 12.67, 's8': 13.8, 'th2': 14.58, 'kb': 15.37, 'gb128': 15.44, 'nz': 15.46}
-ENG = {k: "s" for k in "kb e1 chi cd16 aP a2 aM e0 e3 x_0 x_32 x_48 x_64 x_96 cP tb cn cc limc x2_32 x2_96 y8 sq pwR a1 ya x2_0 n0 x0_16 x0_32 x0_48 x0_96 x0_64 kl x0_112 x0_0".split()}
-ENG.update({k: "v" for k in "w e2 gb0 ti cz lim8 fR t3 eN eR x_16 x_80 x_112 gb128 x2_64 okb yt x0_80".split()})
-SUMS = (("mn", 2, "wd"), ("mn", 0, "wd"), ("xc", 2, "wr2"), ("xc", 0, "wr2"), ("xc", 3, "wa"), ("xc", 1, "wa"))
-TURN, GAT, WAKE, DRAIN, VFIX = 15.2, 1.3, 0.23, 0.0, 0.02
-DUE = {'x0_0': -9.2, 'pwR': -4.1, 'qd0': -1.46, 'x2_32': 0.25, 'qd1': 0.31, 'x2_0': 0.51, 'sq0': 0.53, 'yq': 1.07, 'w': 1.74, 'x2_64': 1.95, 'rm': 1.97, 'x2_96': 2.42, 'qo1': 2.72, 'bs_32': 3.47, 'x2': 3.49, 'bs_0': 3.77, 'eq0': 4.76, 'bs_96': 4.93, 'bs_64': 4.95, 'eq1': 4.98, 'mk': 5.63, 'dk': 5.93, 'AL': 5.94, 'ti': 6.0, 'xc2': 6.24, 'AS': 6.28, 'vf0': 6.46, 'vf2': 6.48, 'q16': 6.76, 't3': 6.9, 'cd16': 8.18, 'xc1': 8.46, 'mn_96': 8.68, 'xc3': 8.93, 'mn_32': 9.16, 'mn_0': 9.18, 'xc0': 10.06, 'up': 10.66, 'chi': 10.66, 'lk': 10.68, 'n0': 10.74, 'xn': 10.75, 'nz': 11.1, 'eR': 11.15, 'AN8': 11.24, 'AN0': 11.54, 'ms': 11.84, 'thr': 11.86, 'no': 12.49, 'x_112': 12.79, 'mr1': 13.2, 'k8': 13.72, 'e0': 14.3, 'gb128': 15.5}
-ENG = {k: "s" for k in ("kb e1 chi cd16 aP a2 aM e0 e3 x_0 x_32 x_48 x_64 x_96 cP tb cn x2_32 x2_96 y8 sq a1 ya x2_0 n0 x0_16 x0_32 x0_48 x0_96 x0_64 kl "
-                        "x0_112 x0_0 ti cz fR t3 eN gb128 yt x0_80").split()}
-ENG.update({k: "v" for k in "cc limc pwR w e2 gb0 lim8 eR x_16 x_80 x_112 x2_64 okb".split()})
-SPARE, SFIX, GAT, WAKE, VFIX = 0.1, 0.07, 1.4, 0.18, 0.0
-DUE = {'x0_80': -11.72, 'x0_16': -9.3, 'pwR': -3.4, 'x2_64': -3.15, 'w': -1.96, 'yq': -1.03, 'x2_96': -0.78, 'x2_0': -0.36, 'x2_32': -0.06, 'ti': 0.14, 'qd0': 0.24, 'nq1': 0.54, 'rm': 1.07, 'qo1': 1.22, 'okK': 1.59, 'bs_0': 2.75, 'bs_32': 2.82, 'vf2': 3.15, 'bs_96': 3.51, 'bs_64': 3.53, 'ab0': 4.43, 'lo': 4.75, 'eq1': 4.86, 'ok': 4.95, 'eq0': 5.18, 'du': 5.63, 'mk': 5.65, 'AL': 6.34, 'vf0': 6.56, 'q16': 6.86, 'xn': 6.86, 't3': 8.5, 'dk': 9.38, 'xs': 9.96, 'AN0': 10.04, 'x_48': 10.92, 'mn_0': 11.24, 'x_80': 11.42, 'ms': 11.44, 'mn_64': 11.74, 'mn_96': 11.74, 'mn_32': 11.92, 'AN8': 12.02, 'chi': 12.02, 'lk': 12.04, 'x_112': 12.38, 'no': 12.4, 'up': 12.72, 'eN': 13.2, 'pr': 13.21, 'sm': 13.33, 'bb': 13.71, 'eR': 13.75, 's8': 14.29, 'e0': 14.5, 'up2': 14.57, 'nz': 14.61, 'k8': 14.61, 'mr0': 14.63}
-ENG = {k: "s" for k in ("kb e1 chi cd16 aP a2 aM e0 e3 x_0 x_32 x_64 x_96 cP tb cn x2_32 x2_96 y8 sq a1 ya x2_0 x0_16 x0_32 x0_48 x0_96 x0_64 kl x0_112 x0_0 "
-                        "ti cz fR t3 eN gb128 yt x0_80 cc limc pwR w gb0 lim8 eR x_16 okb").split()}
-ENG.update({k: "v" for k in "x_48 n0 e2 x_80 x_112 x2_64".split()})
-TURN = 15.2
-DUE = {'x0_80': -6.58, 'x0_16': -5.58, 'pwR': -2.5, 'x2_0': -2.25, 'okK': -1.62, 'qd1': 0.24, 'bs_96': 2.76, 'qo1': 2.86, 'x2': 2.98, 'e3': 3.0, 'bs_0': 3.08, 'bs_64': 3.2, 'lo': 3.2, 'bs_32': 3.5, 'okm': 3.6, 'sg': 3.78, 'aM': 3.92, 'eq1': 3.94, 'a2': 4.02, 'du': 4.4, 'AL': 4.42, 'ti': 4.54, 'ya': 4.6, 'oka': 4.78, 'vo': 4.99, 'vf0': 5.19, 'mn_64': 5.19, 't3': 5.21, 'xn': 5.23, 'ls': 5.98, 'xc2': 6.3, 'mn_0': 7.0, 'AN0': 7.16, 'cd': 7.3, 'no': 7.56, 'q16': 7.76, 'xc0': 7.88, 'AN8': 7.96, 'x_80': 8.08, 'x_112': 8.1, 'x_16': 8.14, 'ms': 8.16, 's8': 8.92, 'bb': 8.94, 'xs': 9.1, 'gb0': 9.94, 'nz': 10.84, 'k8': 10.86, 'up2': 11.45, 'mr0': 11.56}
-ENG = {k: "s" for k in ("kb chi cd16 aP a2 aM e0 e3 x_0 x_32 x_48 x_64 x_96 cP tb cn x2_32 x2_96 sq pwR a1 x2_0 x0_16 x0_48 x0_96 x0_64 kl x0_112 x0_0 t3 eN eR "
-                        "gb128 okb x0_80").split()}
-ENG.update({k: "v" for k in "e1 cc limc ya n0 x0_32 w e2 gb0 ti cz lim8 fR x_16 x_80 x_112 x2_64 yt".split()})
-WAKE, GAT, SFIX, SPARE = 0.25, 1.3, 0.03, 0.15
-DUE = {'x0_80': -7.05, 'x0_16': -5.41, 'nq1': -4.47, 'x0_0': -3.43, 'pwR': -2.2, 'x2_96': -0.26, 'yq': 0.59, 'okm': 1.2, 'qo1': 1.26, 'mk': 1.88, 'bs_32': 2.22, 'bs_0': 2.24, 'x2': 2.24, 'bs_96': 2.24, 'bs_64': 2.7, 'vf2': 2.7, 'e3': 2.82, 'e1': 3.08, 'fr': 3.6, 'sg': 3.71, 'du': 4.2, 'ab1': 4.6, 'vo': 4.61, 'vf0': 4.68, 'ya': 4.7, 'aP': 5.48, 't3': 5.61, 'mn_96': 6.7, 'AN0': 7.46, 'chi': 7.54, 'xc0': 7.68, 'xc2': 7.68, 'mn_32': 7.68, 'cd': 7.7, 'AN8': 8.14, 'ms': 8.16, 's8': 10.08, 'mr1': 10.76, 'k8': 10.98, 'x_0': 11.38, 'xn': 11.58, 'eN': 12.13}
-ENG = {k: "s" for k in "kb chi cd16 aP a2 aM e0 x_0 x_32 x_48 x_64 x_96 cP tb cn x2_32 x2_96 sq a1 x2_0 x0_16 x0_48 x0_64 kl x0_0 t3 eN eR gb128 x0_80 cc limc ya ti lim8 x_80".split()}
-ENG.update({k: "v" for k in "e3 pwR x0_96 x0_112 okb e1 n0 x0_32 w e2 gb0 cz fR x_16 x_112 x2_64 yt".split()})
-FIRST, PEC, WAKE = 5.2, 0.54e-3, 0.21
-DUE = {'x0_80': -6.28, 'x2_32': -0.89, 'x2_0': -0.87, 'a2': 1.75, 'qo1': 1.86, 'y8': 1.88, 'vf2': 2.5, 'eq0': 2.78, 'okm': 2.88, 'mk': 3.78, 'lo': 3.88, 'vf0': 4.38, 'sg': 4.46, 'ab0': 5.08, 'ti': 5.1, 'aP': 5.88, 'chi': 6.24, 'mn_64': 6.49, 'vo': 6.51, 'cd16': 7.86, 'xc2': 8.5, 'thr': 8.81, 'x_16': 8.88, 'cd': 9.1, 'ms': 9.16, 'xn': 9.38, 'q16': 9.85, 'e0': 11.54, 'eR': 11.81, 'x_112': 12.52, 'bb': 12.6}
-ENG = {k: "s" for k in "chi cd16 aP a2 x_0 x_32 x_48 x_64 x_96 cP tb x2_32 x2_96 sq a1 x2_0 x0_16 x0_48 x0_64 kl x0_0 t3 gb128 pwR x0_96 aM cn limc ya e3 x0_112 okb x0_32".split()}
-ENG.update({k: "v" for k in "kb ti x_80 e1 e0 eN eR x0_80 cc lim8 n0 w e2 gb0 cz fR x_16 x_112 x2_64 yt y8".split()})
+CUT1, CUT2, SHARE = range(0, 129, 16), (0, 32, 64, 104, 128), 16
+CLOCKS = (((1, 0.86e-3, 1.25e-3, 3.2e-3, 0.48e-3, 0.9, 1.2, 2.5, 1.0, 1.0), 0.2, 1.25),
+          ((1, 0.88e-3, 0.95e-3, 2.0e-3, 0.46e-3, 1.1, 1.5, 3.5, 1.5, 1.5), 0.29, 1.0),
+          ((1, 1.0e-3, 1.1e-3, 2.5e-3, 0.75e-3, 1.0, 1.2, 3.0, 1.5, 1.3), 0.2, 0.5),
+          ((1, 1.2e-3, 1.7e-3, 4.8e-3, 0.6e-3, 1.0, 1.2, 3.0, 1.5, 1.2), 0.2, 0.5))
+TURN, STEP, WIDE, SWAPS, HEAT, SEED = 14.1, 0.52, 1.5, 24000, 0.2, 12
+TABLE = {
+    "v": """x_48 -8.19 eR -7.25 x_112 -4.86 x_96 -4.49 n0 -3.8 q16 -3.75 thr -3.55 sn -3.3 mr -2.76 nz -2.45 sm -2.4 ke -2.29 k8 -2.03 th2 -1.98 pr -1.77 bb -1.46 okK -1.35
+            nq0 -0.86 qd0 -0.53 sq0 -0.22 nq1 0 qd1 0.33 sq1 0.64 w 0.86 qo1 1.06 e2 1.12 tH 1.17 yq 1.32 x2_64 1.43 bs_0 2.28 bs_32 2.5 bs_104 2.72 bs_64 2.89
+            tV 3.16 tU 3.22 ab 3.31 du 3.73 mk 3.95 AS 4.06 r8 4.27 t3 4.33 ok 4.53 a1 4.74 upH 4.96 AL 5.21 upL 5.41 oka 5.67 lk 6.24 cA 6.29 cd 6.49 vo 6.7
+            cd16 7.3 mn_48 6.9 mn_64 7.33 mn_0 8.02 xc2 8.71 xc0 8.93 ms 10.04 cb 10.26 n16 10.46 AN 10.71 no 11.55 0qo 1.06 0sq 1.3 0mr -2.9 0nz -2.6 0sm -2.8 0dz -2.5 0pz -2.05 0w 0.9 0thr -3.7 0sn -3.4""",
+    "s": """x_0 -7.92 x_16 -7.53 x_80 -4.92 eN -4.53 x_32 -4.42 x_64 -4.04 pwB -2.2 tb -1.72 kb -1.5 gb -1.15 xe0 -0.86 xe1 -0.06 qo0 0.2 x2_32 0.46 x2_0 1.16 x2_104 1.87
+            ym 2.41 ya 2.47 eq 2.67 l0 3.11 eQ 3.16 lo 3.36 xs 3.47 cP 4.26 xn 4.37 ls 4.7 sg 4.76 cjb 5.03 vf2 5.09 vf0 5.53 cI 5.95 okb 6.03 mn_96 6.91 mn_32 7.62
+            chi 8 xc3 8.26 xc1 8.7 0pwb -11.2 0pw -2.35 0pwB -1.8 0pwR -1.1 0v 0.6 0limf -5.2 0lim8 -4.9 0limP -4.3 0n0 -4""",
+    "t": """pGcmeR -5.1 pFeRbo8 -6.9 pFeNbo8a -4.19 pGIbtri -4.16 keys -3.45 pBvI32 -2.72 pEonini -2.47 pDonmid -2.35 pEImHeN -2.25 sums7 -2.16 sums15 -1.92 pConini -1.67
+            pCImHeN -1.55 pCtbI4k -1.3 pEtbI4k -1.26 pCkbIm4k -1.07 pCgbIm1k -0.84 pCboUxe -0.52 pEkbIm4k -0.42 pBonfar -0.36 pBIHeN -0.3 pBkbIm4k -0.24
+            pBokKI2H -0.18 pEgbIm1k -0.12 pEboUxe 0.28 pDxepk 0.38 pBboTxe 0.41 pFIbqd 0.64 pFImsq 1.06 pCe2bo256 1.32 pAcme2 1.38 pByqbo8 1.63 near 1.66 pHZyq 2.15
+            pCx2I16 2.65 pCbsIb 3.63 pCloIm16 3.69 pEtUIb 3.75 pEI16xb 3.9 pHlowon -1.9 9pHIbe2 1.5 9pHZyq 3.8 9l0 4.4 9xs 4.7 9pEI16xb 5.1 9xn 5.4 9upH 5.7 9upL 6.1 pAI4ksq 3.96 pBm16bo8d 4.02 pBASbo8n 4.47 far2 4.57 pAokIb 4.94 far0 5 pBoncjb 5.29
+            pClowon 5.32 pDZAL 5.52 pCbo32oka 6.03 pCI17eQ 6.28 pCIpweQ 6.34 pCbookb 6.4 far1 6.46 far3 6.71 pDcd16Ib 7.16 near3 7.82 near1 8.2 pDchiIb 8.4 lin2 8.55
+            lin0 8.91 score 9.35 pHANbo64 11.28 0keys -3.8 0pDonmid 0.1 0sums7 0.2 0sums15 0.8 0pCIbM -0.1 tri 0.5""",
+    "g": "sendq 1.37 sendv 7.01 over0 8.91 sendn 11.8 over1 12 0l16I -6 0cid -5.5 0eI -3.8 0TQ -2.7"}
+DUE = {k: float(t) for l in TABLE.values() for k, t in zip(l.split()[::2], l.split()[1::2])}
+ENG = {k: q for q, l in TABLE.items() for k in l.split()[::2]}
+ENG.update({"0Dn": "s", "0Dv": "v"})
+for _k in range(8):
+    DUE["0x_%d" % (16 * _k)], ENG["0x_%d" % (16 * _k)] = -9.6 + 0.37 * _k, "s"
+DUE.update({"1x_48": -4.86, "1x_32": -4.49, "1x_64": -4.85, "1x_80": -4.45, "1x_96": -4.05, "1x_112": -3.65, "1eR": -4.95, "1pGcmeR": -4.6, "1pFeRbo8": -4.5, "1eN": -3.25,
+            "1q16": -2.0, "1n0": -3.2, "1thr": -2.9, "1sn": -2.6, "1keys": -2.7})
+ENG.update({"1x_48": "v", "1x_32": "v", "1x_96": "s", "1x_112": "s", "1eR": "s", "1n0": "s"})
 PLAN = {}
 
 
@@ -199,62 +151,160 @@ def links(ops):
     return pre
 
 
-def first(l, t):
-    a, b = 0, len(l)
-    while a < b:
-        m = (a + b) // 2
-        if l[m][1] <= t:
-            a = m + 1
-        else:
-            b = m
-    return a
-
-
 def order(ops, pre):
-    n = len(ops)
-    due = [VI * 100.0] * n
-    for i in range(n - 1, -1, -1):
-        o = ops[i]
-        due[i] -= min(c for _, c in o["alts"].values()) + o["lat"]
-        if o["name"] in DUE and o["turn"] is not None:
-            due[i] = o["turn"] * TURN + DUE[o["name"]]
-        for j, hard in pre[i].items():
-            due[j] = min(due[j], due[i] - (WAKE if hard or set(ops[j]["alts"]) != set(o["alts"]) else 0.0))
-    for i in range(n):
-        for j in pre[i]:
-            due[i] = max(due[i], due[j] + 1e-6)
-    busy, place = {}, [None] * n
-    PLAN["due"] = due
-    for i in sorted(range(n), key=lambda k: (due[k], k)):
-        o, best = ops[i], None
-        for q, (_, c) in o["alts"].items():
-            if o["turn"] is not None and ENG.get(o["name"], q) in o["alts"] and ENG.get(o["name"], q) != q:
-                continue
-            t = 0.0
-            for j, hard in pre[i].items():
-                pq, s, e = place[j]
-                t = max(t, e + ops[j]["lat"] + WAKE if hard or pq != q else e)
-            if q != "-":
-                l = busy.setdefault(q, [])
-                k = first(l, t + 1e-9)
-                while k < len(l) and l[k][0] < t + c - 1e-9:
-                    t = l[k][1]
-                    k += 1
-            f = t + c + (SPARE if q == "v" else 0.0)
-            if best is None or f < best[3] - 1e-9:
-                best = (q, t, t + c, f)
-        place[i] = best = best[:3]
-        if best[0] != "-":
-            l = busy[best[0]]
-            l.insert(first(l, best[1] + 1e-9), (best[1], best[2]))
-    return pre, place, sorted(range(n), key=lambda k: (place[k][1], k))
+    n, K = len(ops), range(len(CLOCKS))
+    dot = lambda c, k: sum(a * b for a, b in zip(c, CLOCKS[k][0]))
+    cost = [[{q: dot(c, k) for q, (_, c) in o["alts"].items()} for o in ops] for k in K]
+    lat = [[dot(o["lat"], k) for o in ops] for k in K]
+    pl, behind = [], []
+    for p in pre:
+        b = 0
+        for j in p:
+            b |= behind[j]
+        pl.append([(j, hard) for j, hard in p.items() if not b >> j & 1])
+        for j, hard in p.items():
+            b |= hard << j
+        behind.append(b)
+    pj = [[j for j, _ in p] for p in pl]
+    ends = sorted(set(range(n)) - {j for p in pre for j in p})
+    name = [o["name"] for o in ops]
+    look = lambda table, k: table.get(k, table.get(k.lstrip("19")))
+    wait = [[[(j, lat[k][j] + CLOCKS[k][1], hard) for j, hard in p] for p in pl] for k in K]
+    sure = lambda i, j, hard: hard or not set(cost[0][i]) & set(cost[0][j])
+    firms = [[[(j, d) for j, d, hard in p if sure(i, j, hard)] for i, p in enumerate(w)] for w in wait]
+    softs = [[[(j, d) for j, d, hard in p if not sure(i, j, hard) and len(cost[0][i]) + len(cost[0][j]) > 2] for i, p in enumerate(w)] for w in wait]
+
+    def place():
+        due = [VI * TURN] * n
+        for i in range(n - 1, -1, -1):
+            t = look(DUE, name[i])
+            t = ops[i].get("due") if t is None else ops[i]["visit"] * TURN + t
+            due[i] = due[i] - min(cost[0][i].values()) - lat[0][i] if t is None else t
+            for j, hard in pl[i]:
+                due[j] = min(due[j], due[i] - (CLOCKS[0][1] if hard or set(cost[0][j]) != set(cost[0][i]) else 0.0))
+        for i in range(n):
+            for j in pj[i]:
+                due[i] = max(due[i], due[j] + 1e-6)
+        busy, q, s, e = {k: [] for k in "vstgy-"}, [None] * n, [0.0] * n, [0.0] * n
+        for i in sorted(range(n), key=lambda k: due[k]):
+            best, want = None, look(ENG, name[i])
+            for k, c in cost[0][i].items():
+                if want in cost[0][i] and want != k:
+                    continue
+                t = max([e[j] + d + ops[j]["late"] if hard or q[j] != k else e[j] for j, d, hard in wait[0][i]] + [0.0])
+                for a, b in busy[k]:
+                    if b > t + 1e-9 and a < t + c - 1e-9:
+                        t = b
+                f = t + c + (0.15 if k == "v" else 0.0)
+                if best is None or f < best[0]:
+                    best = (f, k, t, c)
+            _, q[i], s[i], c = best
+            e[i] = s[i] + c
+            if q[i] != "-":
+                busy[q[i]] = sorted(busy[q[i]] + [(s[i], e[i])])
+        return q, sorted(range(n), key=lambda k: (s[k], k))
+
+    def run(q, seq, k):
+        c, firm, soft = cost[k], firms[k], softs[k]
+        e, free = [0.0] * n, {x: 0.0 for x in "vstgy-"}
+        for i in seq:
+            x = q[i]
+            t = free[x]
+            for j, d in firm[i]:
+                if e[j] + d > t:
+                    t = e[j] + d
+            for j, d in soft[i]:
+                if q[j] != x and e[j] + d > t:
+                    t = e[j] + d
+            e[i] = free[x] = t + c[i][x]
+            free["-"] = 0.0
+        return e
+
+    def pairs(q, before, e, k, i):
+        l = []
+        while i is not None:
+            t, y = e[i] - cost[k][i][q[i]] - 1e-9, None
+            for j, d, hard in wait[k][i]:
+                if (e[j] + d if hard or q[j] != q[i] else e[j]) >= t:
+                    y = j
+            if y is None and q[i] != "-" and before[i] is not None and e[before[i]] >= t:
+                y = before[i]
+                l.append((y, i))
+            i = y
+        return l
+
+    def judge(q, key, limit):
+        seq = np.argsort(key, kind="stable").tolist()
+        es, ws = [], []
+        for k in K:
+            es.append(run(q, seq, k))
+            ws.append((max(es[k][i] + lat[k][i] for i in ends) + 0.3 * sum(es[k]) / n) * CLOCKS[k][2])
+            if sum(ws) > limit[k]:
+                return None
+        at = [0.0] * n
+        for p, i in enumerate(seq):
+            at[i] = es[0][i] - cost[0][i][q[i]] + p * 1e-7
+        seq = np.argsort(at, kind="stable").tolist()
+        before, last, l = [None] * n, {}, []
+        for j in seq:
+            before[j], last[q[j]] = last.get(q[j]), j
+        for k, e in enumerate(es):
+            l += pairs(q, before, e, k, max(ends, key=lambda i: e[i] + lat[k][i])) + pairs(q, before, e, k, draw(n))[:4]
+        return sum(ws), l, (q, at, seq), ws, [round(max(e[i] + lat[k][i] for i in ends), 2) for k, e in enumerate(es)]
+    seed = [SEED]
+
+    def draw(k):
+        seed[0] = (seed[0] * 1103515245 + 12345) % 2 ** 31
+        return (seed[0] >> 8) % k
+    seen, kin = {}, {}
+    for i, o in enumerate(ops):
+        k = seen[(o["visit"], name[i])] = seen.get((o["visit"], name[i]), 0) + 1
+        kin.setdefault((name[i], k), []).append(i)
+    kin = {i: l for l in kin.values() for i in l}
+    q, seq = place()
+    now = best = judge(q, np.argsort(seq), [1e9] * len(K))
+    PLAN["ends"] = best[4]
+    for step in range(SWAPS):
+        q, key = list(now[2][0]), list(now[2][1])
+        pull = False
+        for _ in range(1 + (draw(4) == 0)):
+            a, b = now[1][draw(len(now[1]))]
+            i, sign = ((a, 1.0), (b, -1.0))[draw(2)]
+            if len(cost[0][i]) > 1 and draw(3) == 0:
+                k = [k for k in cost[0][i] if k != q[i]][0]
+                for j in kin[i]:
+                    q[j] = k if k in cost[0][j] else q[j]
+            else:
+                d = abs(key[b] - key[a]) + (1e-4, 1e-4, 0.1, 0.3, 0.8, 2.0)[draw(6)]
+                pull = pull or sign < 0
+                for j in kin[i]:
+                    key[j] += sign * d
+        if pull:
+            for i in range(n - 1, -1, -1):
+                x = key[i]
+                for j in pj[i]:
+                    if key[j] >= x:
+                        key[j] = x - 1e-6
+        else:
+            for i in range(n):
+                x = key[i]
+                for j in pj[i]:
+                    if key[j] >= x:
+                        key[i] = x = key[j] + 1e-6
+        r = judge(q, key, [sum(now[3][:k + 1]) + 0.6 for k in K[:-1]] + [now[0] + HEAT * (1 - step / SWAPS) * draw(100) / 100])
+        if r:
+            now = r
+            if r[0] < best[0]:
+                best = r
+    PLAN["ends2"] = best[4]
+    return best[2]
 
 
 def member(g, core, rank, T, topo):
     Q = {"v": g.vector, "s": g.scalar, "t": g.tensor, "g": g, "y": g.sync}
     ES = {"v": "ev", "s": "es", "t": "et", "g": "eg"}
-    ops = []
-    turn = [None]
+    ops, sent, loaded = [], [], {}
+    tag = ["0", 0]
 
     def vw(name, lo=0, hi=None, st=1, r0=0, r1=128):
         d, nm = SB[name][1] if name in SB else SCRATCH[name][2], name.rstrip("0123") if name not in SB else name
@@ -269,37 +319,39 @@ def member(g, core, rank, T, topo):
     def ind(w, o):
         return dict(w, ap=w["ap"].indirect(o["ap"]), x=o, k=16 * o["k"])
 
-    def op(alts, outs, ins, sem=None, inc=1, lat=0.0, after=()):
+    def tm(us=0.0, cyc=0, gat=0, sca=0, pe=0, hop=0, dma=0, first=0, long=0, far=0):
+        return (us, cyc, gat, sca, pe, hop, dma, first, long, far)
+
+    def op(alts, outs, ins, sem=None, inc=1, lat=tm(), after=(), late=0.0):
         r = []
         for a in ins + [a["x"] for a in outs]:
             if isinstance(a, dict):
                 r.append(a)
                 if a["x"]:
                     r.append(a["x"])
-        ops.append({"alts": alts, "outs": outs, "ins": r, "sem": sem, "inc": inc, "lat": lat, "after": list(after),
-                    "name": outs[0]["name"] if outs else "", "turn": turn[0]})
+        ops.append({"alts": alts, "outs": outs, "ins": r, "sem": sem, "inc": inc, "lat": lat, "after": list(after), "late": late, "visit": tag[1],
+                    "name": tag[0] + (outs[0]["name"] if outs else "out")})
         return len(ops) - 1
 
-    def more(name):
-        ops[-1]["name"] = name
+    def more(name, due=None):
+        ops[-1]["name"] = tag[0] + name
+        if due is not None:
+            ops[-1]["due"] = due
 
     def P(a):
         return a["ap"] if isinstance(a, dict) else a
 
     def vcost(o, ins, rate=1.0):
         if o["x"]:
-            return 0.05 + SCA * o["k"] * CYC
+            return tm(0.05, sca=o["k"])
         if ins and ins[0]["x"]:
-            return 0.05 + GAT * o["k"] * CYC
+            return tm(0.05, gat=o["k"])
         if rate == 1.0 and all(a["b"] == 2 for a in [o] + ins):
             rate /= 2
-        return max(64, rate * o["k"]) * CYC + VFIX
+        return tm(cyc=max(64, rate * o["k"]))
 
-    def scost(o, i):
-        return 0.065 + GAT * o["k"] * CYC if i["x"] else max(64, o["k"]) * CYC + SFIX
-
-    def copy(o, i):
-        op({"v": (lambda: g.vector.tensor_copy(P(o), P(i)), vcost(o, [i]))}, [o], [i])
+    def scost(o, i, us=0.0):
+        return tm(0.065, gat=o["k"]) if i["x"] else tm(us, max(64, o["k"]))
 
     def tt(o, a, b, f):
         r = 1.0 if a["n"] in PS or b["n"] in PS else 2.0
@@ -313,26 +365,20 @@ def member(g, core, rank, T, topo):
     def ts(o, a, s1, f1, s2=None, f2=None):
         op({"v": (tsf(o, a, s1, f1, s2, f2), vcost(o, [a]))}, [o], [a, s1, s2])
 
-    def scan(o, d0, d1, f0, f1, init=0.0):
-        op({"v": (lambda: g.vector.tensor_tensor_scan(P(o), P(d0), P(d1), init, f0, f1), vcost(o, [d0, d1]))}, [o], [d0, d1])
+    def scan(o, d0, d1, f0, f1):
+        op({"v": (lambda: g.vector.tensor_tensor_scan(P(o), P(d0), P(d1), 0.0, f0, f1), vcost(o, [d0, d1]))}, [o], [d0, d1])
 
-    def least(o, i):
-        op({"v": (lambda: g.vector.tensor_reduce(P(o), P(i), AxisListType.X, A.min, apply_absolute_value=True), max(64, i["k"]) * CYC)}, [o], [i])
-
-    def fill(o, c, qs="v"):
-        alts = {"v": (lambda: g.vector.memset(P(o), c if o["d"] != i32 else int(c)), vcost(o, []))}
-        if "g" in qs:
-            alts["g"] = (iotaf(o, [[0, o["k"]]], int(c), 0), 0.13 + 2 * o["k"] * CYC)
-        op(alts, [o], [])
+    def fill(o, c):
+        op({"v": (lambda: g.vector.memset(P(o), c), vcost(o, []))}, [o], [])
 
     def actf(o, i, scale, bias, func):
         return lambda: g.scalar.activation(P(o), P(i), func, bias=P(bias), scale=P(scale))
 
-    def act(o, i, scale=1.0, bias=0.0, func=F.Identity, acc=None):
+    def act(o, i, scale, bias, func, acc=None, us=0.0):
         if acc is None:
-            op({"s": (actf(o, i, scale, bias, func), scost(o, i))}, [o], [i, scale, bias])
+            op({"s": (actf(o, i, scale, bias, func), scost(o, i, us))}, [o], [i, scale, bias])
         else:
-            op({"s": (lambda: g.scalar.activation(P(o), P(i), func, bias=P(bias), scale=P(scale), accum_out=P(acc)), scost(o, i) + 0.02)}, [o, acc], [i, scale, bias])
+            op({"s": (lambda: g.scalar.activation(P(o), P(i), func, bias=P(bias), scale=P(scale), accum_out=P(acc)), scost(o, i, 0.02))}, [o, acc], [i, scale, bias])
 
     def aff(o, i, scale=1.0, bias=0.0, qs="vs"):
         if isinstance(scale, float) and isinstance(bias, float) and (scale, bias) == (1.0, 0.0):
@@ -342,29 +388,30 @@ def member(g, core, rank, T, topo):
         alts = {"v": (fv, vcost(o, [i])), "s": (actf(o, i, scale, bias, F.Identity), scost(o, i))}
         op({q: alts[q] for q in qs}, [o], [i, scale, bias])
 
-    def relu(o, i, bias, qs="vs"):
-        alts = {"v": (tsf(o, i, bias, A.add, 0.0, A.max), vcost(o, [i])), "s": (actf(o, i, 1.0, bias, F.Relu), scost(o, i))}
-        op({q: alts[q] for q in qs}, [o], [i, bias])
+    def relu(o, i, scale=1.0):
+        op({"v": (tsf(o, i, scale, A.mult, 0.0, A.max), vcost(o, [i])), "s": (actf(o, i, scale, 0.0, F.Relu), scost(o, i))}, [o], [i])
 
     def zero(o, i):
         op({"v": (tsf(o, i, 0.0, A.is_equal), vcost(o, [i])), "s": (actf(o, i, -1.0, 1.0, F.Relu), scost(o, i))}, [o], [i])
 
     def mm(o, a, b, start=True, stop=True):
-        c = max(min(64, a["k"]), b["k"]) * (4 if a["b"] == 4 else 1) * PEC
-        op({"t": (lambda: g.tensor.matmul(P(o), P(a), P(b), start, stop), c)}, [o], [a, b], lat=DRAIN)
+        c = max(min(64, a["k"]), b["k"]) * (4 if a["b"] == 4 else 1)
+        op({"t": (lambda: g.tensor.matmul(P(o), P(a), P(b), start, stop), tm(pe=c))}, [o], [a, b])
+        more(o["name"] + a["name"] + b["name"])
 
-    def run(k):
+    def run(k, name=None):
         l = ops[-k:]
         del ops[-k:]
         fs = [o["alts"]["t"][0] for o in l]
-        op({"t": (lambda: [f() for f in fs][-1], sum(o["alts"]["t"][1] for o in l))}, [a for o in l for a in o["outs"]], [a for o in l for a in o["ins"]], lat=DRAIN)
+        op({"t": (lambda: [f() for f in fs][-1], tm(pe=sum(o["alts"]["t"][1][4] for o in l)))}, [a for o in l for a in o["outs"]], [a for o in l for a in o["ins"]])
+        ops[-1]["name"] = tag[0] + name if name else l[0]["name"]
 
-    def load(o, src, sem, q, lat):
-        loaded[q] = [(op({q: (lambda: Q[q].dma_start(P(o), src), 0.05)}, [o], [], sem, 16, lat, loaded.get(q, [])), False)]
-    loaded = {}
+    def load(o, src, sem, q, us):
+        loaded[q] = [(op({q: (lambda: Q[q].dma_start(P(o), src), tm(0.05))}, [o], [], sem, 16, tm(dma=1, long=us), loaded.get(q, [])), False)]
 
-    def store(dst, i, sem, q, lat):
-        op({q: (lambda: Q[q].dma_start(dst, P(i)), 0.05)}, [], [i], sem, 16, lat)
+    def store(dst, i, sem, q, us):
+        op({q: (lambda: Q[q].dma_start(dst, P(i)), tm(0.05))}, [], [i], sem, 16, tm(dma=1, long=us))
+        more(sem)
 
     def iotaf(o, pat, base, cm):
         if o["d"] == i32:
@@ -372,23 +419,39 @@ def member(g, core, rank, T, topo):
         return lambda: g.iota(P(o), pat, base, cm, allow_small_or_imprecise_dtypes=True)
 
     def iota(o, pat, base, cm=0):
-        op({"g": (iotaf(o, pat, base, cm), 0.13 + 2 * o["k"] * CYC)}, [o], [])
+        op({"g": (iotaf(o, pat, base, cm), tm(0.13, 2 * o["k"]))}, [o], [])
+
+    def pick(o, i, pat, f, c, base):
+        op({"g": (lambda: g.affine_select(P(o), P(i), pat, f, c, base, 1), tm(0.17, 2 * o["k"]))}, [o], [i])
 
     def flat(name, a, b, m=None):
         return vw(name, 16 * a, 16 * b) if m is None else vw(name, 16 * a + m, 16 * b, 16)
 
-    def last(name, lo=0):
-        return vw(name, lo + 15, lo + 128, 16)
+    def last(name):
+        return vw(name, 15, None, 16)
 
-    def row(name, lo=0, hi=None, st=1):
-        return vw(name, lo, hi, st, 0, 1)
+    def row(name, lo=0, hi=None, st=1, n=1):
+        return vw(name, lo, hi, st, 0, n)
+
+    def pair(name, lo, st, a, b):
+        fill(row(name, lo, None, st, 2), b)
+        fill(row(name, lo, None, st), a)
+
+    def tab(t):
+        return "XY"[t % 2]
 
     def XG(t):
-        return vw("XY"[t % 2], 16, XS)
+        return vw(tab(t), 0, XS)
 
-    def xgath(t, dst, lst, a, b, scale=1.0, bias=0.0, qs="vs"):
-        aff(flat(dst, a, b), ind(XG(t), vw(lst, a, b)), scale, bias, qs)
+    def xgath(t, dst, lst, a, b, scale=1.0, bias=0.0):
+        aff(flat(dst, a, b), ind(XG(t), vw(lst, a, b)), scale, bias)
         more("%s_%d" % (dst, a))
+
+    def listed(o, src, dst):
+        for c in range(16):
+            mm(o, vw("Z", 15 - c, 143 - c), vw(src, c, 128, 16), c == 0, c == 15)
+        run(16)
+        aff(vw(dst), o)
 
     def send(k, t, half=None):
         src = "%so%d" % (k, t)
@@ -400,324 +463,217 @@ def member(g, core, rank, T, topo):
                                 src=T[src][:, 0:HALF[k]], dst=T["%s%d" % (k, t)][:, 0:HALF[k]]),
               RemoteDMATransfer(dst_ids=[DstId(rid=r2, pnc=p2)], dma_engine_mask=bits(topo, core, hid, 8, True), remote_sem=T.sem["r%s%d" % (k, t)],
                                 src=T[src][:, HALF[k]:2 * HALF[k]], dst=T["r%s%d" % (k, t)][:, :])]
-        late = {"n": 0.0, "v": 0.4 * LATE, "q": LATE if sent else FIRST}[k]
         if half == 1:
-            i = op({"g": (lambda: g.remote_dma(T["rn%d" % t][:, :], T[src][:, 8:12], T.sem["rn%d" % t], T.sem["loc"], p2, r2, topo.mask(core, hid)), 0.1)},
+            i = op({"g": (lambda: g.remote_dma(T["rn%d" % t][:, :], T[src][:, 8:12], T.sem["rn%d" % t], T.sem["loc"], p2, r2, topo.mask(core, hid)), tm(0.1))},
                    [], [vw(src, 8, 12)], "loc", len(topo.engines(core, hid)), after=sent[-1:])
         elif half == 0:
-            i = op({"g": (lambda: g.remote_dma(T["n%d" % t][:, 0:4], T[src][:, 4:8], T.sem["nL%d" % t], T.sem["loc"], p1, r1, bits(topo, core, lowd, 8, False)), 0.1)},
+            i = op({"g": (lambda: g.remote_dma(T["n%d" % t][:, 0:4], T[src][:, 4:8], T.sem["nL%d" % t], T.sem["loc"], p1, r1, bits(topo, core, lowd, 8, False)), tm(0.1))},
                    [], [vw(src, 4, 8)], "loc", 8, after=sent[-1:])
         else:
-            i = op({"g": (lambda: g.remote_dma_fused(tr, local_sem=T.sem["loc"]), 0.1)}, [], [vw(src)], "loc", 16, after=sent[-1:])
-        sent.append((i, False))
+            i = op({"g": (lambda: g.remote_dma_fused(tr, local_sem=T.sem["loc"]), tm(0.1))}, [], [vw(src)], "loc", 16, after=sent[-1:])
+        more("send" + k)
+        way = 1.0 if k == "n" else WIDE
         for h in (0, 1) if half is None else (half,):
-            op({"-": (None, (h + 1) * HOP + late)}, [vw("%s%d" % (k, t), h * HALF[k], (h + 1) * HALF[k])], [], "%s%s%d" % (k, "LH"[h], t), 8, after=[(i, True)])
-    sent = []
+            op({"-": (None, tm(-0.2, hop=h * way, far=way, first=(1 + 0.8 * h) * ((k, t) == ("q", 1))))}, [vw("%s%d" % (k, t), h * HALF[k], (h + 1) * HALF[k])], [],
+               "%s%s%d" % (k, "LH"[h], t), 8, after=[(i, True)], late=float(k != "n"))
+        sent.append((i, False))
 
-    load(vw("wy0"), T.why[:, :], "ld0", "y", DMA + 0.3)
-    load(vw("dr0"), T.drugs[:, :], "ld1", "s", DMA + 0.5)
-    load(vw("X", X0, X0 + D), T.eff[:, :], "ld2", "y", DMA + 2.0)
-    load(vw("lmI"), T.lim[:, :], "ld3", "s", DMA + 2.2)
-    load(vw("R", 16, 16 + D), T.rem[:, :], "ld4", "y", DMA + 5.0)
-    load(vw("Y", X0, X0 + D), T.eff[:, :], "ld5", "y", DMA + 7.0)
+    load(vw("wy0"), T.why[:, :], "ld0", "y", 0.3)
+    load(vw("dr0"), T.drugs[:, :], "ld1", "s", 0.5)
+    load(vw("lmI"), T.lim[:, :], "ld3", "y", 0.6)
+    load(vw("X", X0, XS), T.eff[:, :], "ld2", "y", 2.0)
+    load(vw("R", X0, XS), T.rem[:, :], "ld4", "y", 5.0)
+    load(vw("Y", X0, XS), T.eff[:, :], "ld5", "y", 6.5)
+    fill(vw("on"), 1.0)
     iota(vw("kI"), [[1, 1]], 0, 1)
+    pick(vw("Ib"), vw("on"), [[-1, 128]], A.is_equal, 0.0, 0)
     iota(vw("gid"), [[1, 8], [0, 16]], 0)
     iota(vw("cid"), [[1, 128]], 0)
     iota(vw("aid"), [[0, 8], [1, 16]], 0)
     iota(vw("g8"), [[1, 8]], 0)
-    ts(vw("aI"), vw("kI"), 15, A.bitwise_and)
-    ts(vw("gI"), vw("kI"), 4, A.arith_shift_right)
-    ts(vw("hI"), vw("kI"), 31, A.bitwise_and)
-    for n in "kagh":
+    for n, c, f in (("a", 15, A.bitwise_and), ("g", 4, A.arith_shift_right), ("h", 31, A.bitwise_and), ("t", 63, A.bitwise_and)):
+        ts(vw(n + "I"), vw("kI"), c, f)
+    for n in "kaght":
         aff(vw(n + "c"), vw(n + "I"))
     ts(vw("bo"), vw("gid"), vw("gc"), A.is_equal)
-    ts(vw("Ib"), vw("cid"), vw("kc"), A.is_equal)
-    tt(vw("M0"), vw("bo"), vw("Ib"), A.add)
-    ts(vw("bj"), vw("aid", 0, 16), vw("ac"), A.is_equal, -1.0, A.add)
-    ts(vw("b1"), vw("aid", 0, 16), vw("ac"), A.is_equal)
-    ts(vw("c3"), vw("cid"), vw("kc"), A.is_equal, -256.0, A.mult)
-    tt(vw("M2"), vw("c3"), vw("bo"), A.add)
     ts(vw("bo8f"), vw("g8"), vw("gc"), A.is_equal)
-    ts(vw("m16"), vw("aid"), vw("ac"), A.is_equal)
-    fill(vw("on"), 1.0)
-    fill(vw("on32"), 1.0, "vg")
-    fill(row("kr", 0, 128), 255.0)
-    fill(row("kr", 128, 256), 256.0)
-    for n, c in (("Im256", -256.0), ("I256", 256.0), ("I32", 1.0), ("I20", 131072.0), ("Im20", -131072.0), ("I2k", 2048.0), ("Im2k", -2048.0), ("I4k", 4096.0), ("I19", 2.0 ** 19), ("Im19", -2.0 ** 19), ("I16", 16.0), ("Im16", -16.0),
-                 ("ImQ", -float(16 + D)), ("IpQ", float(16 + D)), ("Im64", -64.0), ("IH", HUGE), ("I2H", 2 * HUGE), ("Ig", -HUGE / 32768)):
+    for a in (0, 128):
+        ts(vw("m16", a, a + 128), vw("aid"), vw("ac"), A.is_equal)
+    for n, c, st, z in (("d0r", 1.0, 16, -2.0 ** 31), ("d0k", 16.0, 16, -2.0 ** 31), ("d0m", 64.0, 16, -2.0 ** 31), ("d0b", 1.0, 16, -8192.0), ("d0a", 0.0, 64, BIG)):
+        fill(vw(n), c)
+        fill(vw(n, 0, None, st), z)
+    ts(vw("d0s"), vw("aid"), 0.0, A.not_equal)
+    fill(vw("on32"), 1.0)
+    fill(vw("cK"), -31.0)
+    for n, c in (("Im32", -32.0), ("I32", 1.0), ("I32m", -1.0), ("Im", -1.0), ("I16", 16.0), ("Im16", -16.0), ("Im64", -64.0), ("I64", 64.0), ("I17", 131072.0),
+                 ("I4k", 4096.0), ("Im4k", -4096.0), ("Im1k", -1024.0), ("IH", HUGE), ("ImH", -HUGE), ("I2H", 2 * HUGE), ("ImQ", -float(XS)), ("IpQ", float(XS))):
         aff(vw(n), vw("Ib"), c)
-    for n, c in (("bo32", 1.0), ("bo256", 256.0), ("boS", -2048.0), ("boT", 32768.0), ("boU", -32768.0)):
+    for n, c in (("bo32", 1.0), ("bo256", 256.0), ("boT", 4096.0), ("boU", -4096.0)):
         aff(vw(n), vw("bo"), c)
-    for n, src, c, b in (("dum", "kc", 1.0, float(XS)), ("ndum", "kc", -1.0, -float(XS)), ("b16p", "kc", 16.0, 15.0), ("a32", "ac", 1.0 / 32, 0.0),
-                         ("k17", "kc", 16.0, 0.0), ("limf", "lmI", 16.0, 120.0), ("m15", "aid", -1.0, 15.0), ("tie16", "aid", -16.0, 240.0)):
+    for n, src, c, b in (("dum", "kI", 1.0, float(XS)), ("a1c", "aI", 1.0, 1.0), ("a32", "aI", 1.0 / 32, 0.0), ("limf", "lmI", 16.0, 0.0), ("m15", "aid", -1.0, 15.0)):
         aff(vw(n), vw(src), c, b)
-    for n, a, c in (("bo8", 0, 1.0), ("w3", 0, 16.0), ("w3", 8, 512.0), ("w3", 16, 512.0), ("wd", 0, 4096.0), ("wd", 8, 4096.0), ("wm", 0, -256.0),
-                    ("wa", 0, -4096.0), ("wa", 8, -4096.0), ("wr2", 0, -8192.0), ("wr2", 8, -8192.0), ("bo8k", 0, vw("b16p")), ("bo8d", 0, vw("dum")),
-                    ("bo8n", 0, -1.0), ("bo16", 0, 16.0), ("bo8a", 0, vw("ac")), ("bo64", 0, 64.0), ("bo8p", 0, vw("k17"))):
+    for n, a, c in (("bo8", 0, 1.0), ("w3", 0, 16.0), ("wd", 0, 1024.0), ("wd", 8, 1024.0), ("wm", 0, -256.0), ("wa", 0, -2048.0), ("wa", 8, -2048.0),
+                    ("bo8d", 0, vw("dum")), ("bo8n", 0, -1.0), ("bo8a", 0, vw("a1c")), ("bo64", 0, 64.0), ("c4k", 0, 4096.0)):
         aff(vw(n, a, a + 8), vw("bo8f"), c)
-    aff(row("tie2", 0, 128), row("aid"), -256.0, 3840.0 - 128)
-    aff(row("tie2", 128, 256), row("aid"), -256.0, 3840.0 + 8192)
     for n in "XY":
-        fill(vw(n, 0, 16), 0.0, "vg")
-        fill(vw(n, 16, 32), -1.0, "vg")
-        fill(vw(n, XS, XW), 0.0, "vg")
-    fill(vw("R", 0, 16), -16, "vg")
-    for n, c, z in (("d0s", 1.0, 0.0), ("d0m", 0.0, -2 * BIG), ("d0b", 1.0, -8192.0)):
-        fill(vw(n), c, "vg")
-        fill(vw(n, 0, None, 16), z)
-    for n, c, z in (("d0p", 2.0, 0.0), ("d0h", 0.5, 0.0), ("d1h", 0.0, 32768.0)):
-        fill(row(n), c)
-        fill(row(n, 0, None, 16), z)
-    scan(row("pwr"), row("d0p"), row("on32"), A.mult, A.max)
-    scan(row("pwd"), row("d0h"), row("d1h"), A.mult, A.add)
-    aff(row("pay", 0, 128), row("m15"))
-    aff(row("pay", 128, 256), row("pwd"), 1.0 / 256, -0.125)
-    ts(row("pay", 256, 384), row("pwd"), 256.0, A.min)
-    fill(row("hlf"), 2.0)
-    fill(row("hlf", 0, None, 8), 0.0)
-    scan(row("wr"), row("hlf"), row("on"), A.mult, A.max)
-    ts(vw("pz", 0, 1), vw("aI"), 8.0, A.is_lt)
-    ts(vw("pz", 1, 2), vw("aI"), 8.0, A.is_ge)
-    mm(vw("pB", 500, 501), row("wr"), row("on", 0, 1))
-    ts(vw("pc"), vw("pz", 0, 2), vw("pB", 500, 501), A.mult)
-    aff(row("far"), row("pwd"))
-    mm(vw("pB", 502, 503), row("far"), row("on", 0, 1))
-    aff(vw("pwc"), vw("pB", 502, 503))
-    fill(row("pw20"), -131072.0)
-    fill(row("far"), HUGE / 4)
-    fill(vw("n16"), 0, "vg")
-    for s, c in enumerate((1.0, 2.0 ** 22, 2.25 * HUGE, -2.25 * HUGE)):
-        fill(row("ini", s, None, 4), c)
+        fill(vw(n, 0, X0), -1.0)
+        fill(vw(n, XS, XW), 0.0)
+    fill(vw("R", 0, X0), -X0)
+    act(vw("pwb"), vw("aI"), LN2, 0.0, F.Exp, us=1.35)
+    first, pwa = [(len(ops) - 1, False)], vw("pwa")
+    aff(pwa, vw("pwb"))
+    for b, f in ((0, A.is_lt), (1, A.is_ge)):
+        ts(vw("pc", 2 + b, 3 + b), vw("aI"), 5.0, f, -140.0, A.mult)
+        ts(vw("pc", b, b + 1), vw("aI"), LN2, A.mult, vw("pc", 2 + b, 3 + b), A.add)
+    aff(vw("Ipw"), vw("Ib"), pwa)
+    fill(row("low"), -131072.0 - 8388608.0)
+    tt(vw("pk"), vw("I4k", 1, 128, 2), vw("Ib", 0, 128, 2), A.add)
+    aff(vw("pk1"), vw("bo", 0, 128, 2))
+    aff(vw("pk2"), vw("bo", 0, 128, 2), 4096.0)
+    for n, a, b in (("less", -4096.0, -float(X0)), ("mid", -2040.0 * 4096, -2040.0), ("far", -2048.0 * 69632, 2048.0 * 17)):
+        pair(n, 0, 1, a, b)
+    for s, (a, b) in enumerate(((1.0, 0.0), (2.0 ** 23, 0.0), (2048.0 * 12288, 2048.0 * 17), (-2048.0 * 61440, -2048.0 * 17))):
+        pair("ini", s, 4, a, b)
     for s, c in enumerate((0.0, 2048.0, 2048.0)):
         fill(vw("qd", s, None, 4), c)
-    for n, st, b, k in (("8", 1, 0, 8), ("k", 16, 15, 8), ("16", 1, 0, 16)):
-        iota(vw("l%sI" % n), [[st, k]], b)
-        copy(vw("L" + n.upper()), vw("l%sI" % n))
+    iota(vw("l16I"), [[1, 16]], 0)
+    aff(vw("L16"), vw("l16I"))
+    aff(vw("L8"), vw("l16I", 0, 8))
     ts(vw("c1"), vw("cid"), vw("kc"), A.is_gt, 64.0, A.mult)
-    aff(vw("c2"), vw("Ib"), -32.0, 1.0)
-    tt(vw("c1"), vw("c1"), vw("c2"), A.add)
-    tt(vw("cm"), vw("c1"), vw("bo"), A.mult)
-    aff(vw("k16"), vw("ac"), -2048.0, 15 * 2048.0)
-    aff(vw("c3"), vw("bo"), vw("k16"))
-    tt(vw("boE"), vw("c3"), vw("I2H"), A.subtract)
-    aff(row("mk2", 0, 128), row("m15"), 2048.0)
-    aff(row("mk2", 128, 256), row("m15"), -2048.0)
-    fill(vw("d0a"), 0.0, "vg")
-    fill(vw("d0a", 0, None, 128), BIG)
+    tt(vw("c2"), vw("c1"), vw("bo"), A.mult)
+    tt(vw("cm"), vw("c2"), vw("Im32"), A.add)
+    tt(vw("cmb"), vw("cm"), vw("bo"), A.add)
     fill(vw("Z"), 0.0)
     aff(vw("Z", 15, 143, 16), vw("bo8f"))
     iota(vw("eI"), [[1, 32], [0, 16]], 0)
     ts(vw("E"), vw("eI"), vw("hc"), A.is_equal)
     for w in range(8):
-        ts(vw("sl", 128 * w, 128 * w + 128), vw("on"), vw("bo8f", w, w + 1), A.mult, 4096.0, A.mult)
-    for w in range(4):
-        ts(vw("tri", 128 * w, 128 * w + 128), vw("cid"), vw("kc"), A.is_ge, BIG, A.mult)
-    iota(vw("TQ"), [[1, XS - 16]], 0)
+        aff(vw("sl", 64 * w, 64 * w + 64), vw("on", 0, 64), vw("c4k", w, w + 1))
+    ts(vw("tri", 0, 63), vw("cid", 0, 63), vw("tc"), A.is_ge, BIG, A.mult)
+    fill(vw("tri", 63, 64), 0.0)
 
-    an = vw("pC", 0, 128)
-    if DBL:
-        iota(vw("wI"), [[0, 16], [1, 16]], 0)
-        iota(vw("dl"), [[-1, 16], [1, 16]], 0)
-        iota(vw("pofI"), [[0, 2], [16, 64]], 0)
-        ts(vw("c15"), vw("aI"), 15.0, A.is_equal)
-        ts(vw("c14"), vw("aI"), 14.0, A.is_equal, 2.0, A.mult)
-        ts(vw("a16"), vw("aI"), 16.0, A.mult)
-        ts(vw("n15"), vw("aI"), 15.0, A.is_lt)
-        ts(vw("Kc"), vw("wI"), vw("ac"), A.is_equal)
-        ts(vw("Kc", 15, 256, 16), vw("wI", 0, 16), 0.0, A.mult, vw("c14"), A.add)
-        fill(vw("Kc", 0, 256, 17), 0.0)
-        ts(vw("Kd"), vw("dl"), vw("c15"), A.mult)
-        tt(vw("K"), vw("Kd"), vw("Kc"), A.add)
-        ts(vw("l0"), vw("wy0"), vw("a16"), A.add)
-        tt(vw("qc"), vw("wy0"), vw("pofI"), A.add)
-        copy(vw("lu1"), vw("qc"))
-        aff(vw("pofm"), vw("pofI"), 1.0, vw("ac"))
-        fill(vw("Zc", 128, 144), 0.0)
-        aff(vw("Zc", 0, 128), vw("Ib"), vw("c15"))
-        mm(vw("pB", 503, 504), row("pwr"), row("on", 0, 1))
-        ts(vw("pw14"), vw("pB", 503, 504), vw("n15"), A.mult)
-        fill(vw("Zw"), 0.0)
-        aff(vw("Zw", 15, 143, 16), vw("bo8f"), vw("pw14"))
-        turn[0] = 0
-        for a in range(0, 128, 32):
-            aff(flat("WA", a, a + 32), ind(vw("K"), vw("l0", a, a + 32)))
-            more("K_%d" % a)
-        mm(an, row("pwr"), row("on"), True, False)
-
-        def masked(src, a, b, stop):
-            for m in range(16):
-                mm(vw("pC", a, b), vw("Zw", 15 - m, 143 - m), flat(src, a, b, m), False, stop and m == 15)
-            run(16)
-        for r, (src, dst) in enumerate((("WA", "WB"), ("WB", "WA"), ("WA", "WB"))):
-            for h in (0, 1):
-                lo = 64 * h
-                for a in (lo, lo + 32):
-                    if TWIN and a not in HELP:
-                        aff(flat("xc", a, a + 32), flat(src, a, a + 32))
-                        more("tw%d_%d" % (r, a))
-                    if a in HELP:
-                        aff(flat("mn", a, a + 32), ind(flat(src, lo, lo + 64), vw("lu%d" % 2 ** r, a, a + 32)), 1.0, 0.0, "s")
-                        more("g%d_%d" % (r, a))
-                        tt(flat(dst, a, a + 32), flat("mn", a, a + 32), flat(src, a, a + 32), A.add)
-                    else:
-                        tt(flat(dst, a, a + 32), ind(flat(src, lo, lo + 64), vw("lu%d" % 2 ** r, a, a + 32)), flat("xc" if TWIN else src, a, a + 32), A.add)
-                    more("d%d_%d" % (r, a))
-                o = vw(("pE", "pF")[h], 0, 64)
-                mm(o, vw("Ib"), vw("pofm", lo, lo + 64), True, False)
-                for m in range(16):
-                    mm(o, vw("Zc", 15 - m, 143 - m), flat(dst, lo, lo + 64, m), False, m == 15)
-                run(16)
-                copy(vw("lu%d" % 2 ** (r + 1), lo, lo + 64), o)
-                more("lu%d_%d" % (r, h))
-        for lo in (0, 64):
-            masked("WB", lo, lo + 64, False)
-        for lo in (0, 64):
-            for a in range(lo, lo + 64, 16):
-                aff(flat("x2", a, a + 16), ind(flat("WB", lo, lo + 64), vw("lu8", a, a + 16)))
-                more("l_%d" % a)
-            masked("x2", lo, lo + 64, lo == 64)
-        turn[0] = None
-    else:
-        aff(vw("nw"), vw("wy0"), -1.0, 16.0)
-        ts(vw("rt"), vw("wy0"), vw("ac"), A.is_equal, 17.0, A.mult)
-        tt(vw("N", 0, 128), vw("nw"), vw("rt"), A.max)
-    for h in (0, 1):
-        for b in () if DBL else (0, 1):
-            aff(vw("M", 128 * h + 64 * b, 128 * h + 64 * b + 64), vw("on", 0, 64), vw("pc", b, b + 1))
-    for s in range(0 if DBL else 16):
+    ts(vw("rt"), vw("wy0"), vw("ac"), A.is_equal, vw("a1c"), A.mult)
+    for h in (0, 64):
+        tt(vw("N", h, h + 64), vw("rt", h, h + 64), vw("wy0", h, h + 64), A.subtract)
+        act(vw("M", 2 * h, 2 * h + 64), vw("on", 0, 64), 0.0, vw("pc", 0, 1), F.Exp)
+        ops[-1]["after"] += first
+        more("Mi", -9.7)
+        act(vw("M", 11 * 256 + 2 * h + 64, 11 * 256 + 2 * h + 128), vw("on", 0, 64), 0.0, vw("pc", 1, 2), F.Exp)
+        ops[-1]["after"] += first
+        more("Ml", -5.0)
+    tt(vw("M2"), vw("bo"), vw("Im32"), A.add)
+    for s in range(16):
         j = 15 - s
-        bj, n0, n = vw("B", 128 * s, 128 * s + 128), row("n0r", 128 * s, 128 * s + 128), vw("N", 128 * s, 128 * s + 128)
-        relu(bj, vw("M0"), vw("bj", j, j + 1))
-        aff(n0, row("on"), float(16 - j))
-        if s < 15:
-            z = vw(("pC", "pD")[s % 2], 0, 128)
-            mm(z, n0, row("kr", 0, 128), True, False)
-            aj = vw("Aj", 128 * s, 128 * s + 128)
-            ts(aj, vw("M2"), vw("b1", j, j + 1), A.min)
-            mm(z, aj, n, False, True)
-            tt(vw("N", 128 * s + 128, 128 * s + 256), z, n, A.max)
+        aj, bj = vw("Aj", 128 * s, 128 * s + 128), vw("B", 128 * s, 128 * s + 128)
+        pick(bj, vw("Ib"), [[-16, 8], [0, 16]], A.not_equal, 1.0, -j)
+        more("B", 0.4 * s - 10.4)
+        sent[:] = [(len(ops) - 1, False)]
+        if j:
+            ts(aj, vw("M2"), vw("m16", j, j + 1), A.min)
         for h in (0, 1):
-            p = ("pE", "pF", "pG", "pH")[2 * h + s % 2]
-            m, m2 = [vw("M", 256 * k + 128 * h, 256 * k + 128 * h + 128) for k in (s % 2, 1 - s % 2)]
-            if h == 0:
-                aff(vw("Dn", 128 * (s % 8), 128 * (s % 8) + 128), n, -256.0, 256.0 * (16 - j), "s")
-            for b in (0, 64):
-                mm(vw(p, b, b + 64), vw("Ib"), vw("Dn", 128 * (s % 8) + 64 * h, 128 * (s % 8) + 64 * h + 64), b == 0, False)
-            run(2)
-            mm(vw(p, 0, 128), bj, m, False, True)
-            tt(m2, vw(p, 0, 128), m, A.max)
-    for h in () if DBL else (0, 1):
-        mm(vw("pC", 64 * h, 64 * h + 64), vw("Ib"), vw("M", 128 * h, 128 * h + 64), True, False)
-        mm(vw("pC", 64 * h, 64 * h + 64), vw("I256"), vw("M", 128 * h + 64, 128 * h + 128), False, True)
+            c = 128 * s + 64 * h
+            n, d = vw("N", c, c + 64), vw("Dn", c, c + 64)
+            if j:
+                z = vw(("pC", "pD", "pE", "pF")[2 * h + (s % 2 if j > 4 else 0)], 0, 64)
+                mm(z, row("on", n=j), row("cK", n=j), True, False)
+                mm(z, aj, n, False, True)
+                tt(vw("N", c + 128, c + 192), z, n, A.max)
+                more("N", STEP * (s - 16) - 0.6 + 0.1 * h)
+            aff(d, n, -131072.0, -131072.0 * j)
+            more("Dn" if s > 8 else "Dv", STEP * (s - 17) - 0.4 + 0.1 * h)
+            for b in (0,) if j > 4 else (0, 1):
+                z, lo = vw((("pG", "pH"), ("pD", "pF"), ("pB", "pA"))[2 if s < 6 and s % 2 else b][h], 0, 64), 2 * c + 64 * b
+                mm(z, vw("Ib"), d, True, False)
+                mm(z, bj, vw("M", lo, lo + 64), False, True)
+                if s > 6:
+                    run(2)
+                tt(vw("M", lo + 256, lo + 320), z, vw("M", lo, lo + 64), A.max)
+                more("M", STEP * (s - 16) - 0.3 + 0.1 * h + 0.05 * b)
+    an = vw("pC", 0, 128)
     aff(vw("wy32"), vw("wy0"), 1.0 / 32)
+    mm(an, vw("Ib"), vw("wy32"), True, False)
+    for h in (0, 1):
+        for b in (0, 64):
+            mm(vw("pC", 64 * h, 64 * h + 64), vw("Ib"), vw("M", 4096 + 128 * h + b, 4096 + 128 * h + b + 64), False, h + b == 65)
+        run(2)
     qf, q2f = vw("qd", 3, None, 4), vw("sq", 3, None, 4)
     ts(vw("eR"), vw("dr0"), float(D), A.is_ge)
-    aff(vw("qa"), vw("dr0"), 1.0, 16.0)
-    aff(vw("qb"), vw("eR"), float(16 + D))
+    aff(vw("qa"), vw("dr0"), 1.0, float(X0))
+    aff(vw("qb"), vw("eR"), float(XS))
     tt(qf, vw("qa"), vw("qb"), A.subtract)
-    copy(vw("q0"), qf)
+    aff(vw("q0"), qf)
     aff(vw("lim8"), vw("I32", 0, 128, 16), vw("limf"))
+    mm(vw("pB", 400, 408), vw("on32"), vw("lim8"))
+    aff(vw("limP"), vw("pB", 400, 408))
+    QB, win, tp = ("pC", "pE"), vw("pB", 128, 256), vw("pD", 384, 448)
 
     def rows(t):
-        q = "q%d" % t
         for a, b in zip(CUT1, CUT1[1:]):
-            turn[0] = 0 if t == 0 else turn[0]
-            xgath(t, "x", q, a, b)
-            if t == 0:
-                more("x0_%d" % a)
-                turn[0] = None
-        p = "pA"
+            xgath(t, "x", "q%d" % t, a, b)
+            if t == 1 and a >= H:
+                del ops[-1]["alts"]["v"]
+        p = "pF" if t else "pB"
         mm(vw(p, 384, 392), vw("eR"), vw("bo8"))
-        mm(vw(p, 392, 400), vw("eR"), vw("wm"), True, False)
-        mm(vw(p, 392, 400), vw("on32"), vw("lim8"), False, True)
-        aff(vw("n0"), vw(p, 384, 392), BIG, (-BIG if t else 0.0) - 16000.0)
-        tt(vw("thr"), vw(p, 392, 400), vw("n0"), A.min)
-        mm(vw("pA", 0, 384), row("on"), row("pay"), True, False)
-        for m in range(16):
-            mm(vw("pA", m, 384, 16), flat("x", 0, 128, m), vw("w3"), False, m == 15)
-            if m % 8 == 7:
-                run(8)
-        scan(vw("mr", 128, 384), vw("d0m", 0, 256), vw("pA", 128, 384), A.add, A.max)
-        more("mr1")
+        mm(vw(p, 392, 400), vw("eR"), vw("wm"))
+        run(2)
         if t:
-            scan(vw("mr", 0, 128), vw("d0m", 0, 128), vw("pA", 0, 128), A.add, A.max)
-            more("mr0")
+            mm(vw(p, 400, 408), vw("eN"), vw("bo8a"))
+        aff(vw("n0"), vw(p, 384, 392), BIG, (-BIG if t else 0.0) - 16000.0)
+        tt(vw("thr"), vw("limP"), vw("n0"), A.min)
+        tt(vw("sn"), vw(p, 392, 400), vw("thr"), A.add)
+        k = 16 if t else 4
+        for m in range(16):
+            mm(vw("pA", m, 128, 16), flat("x", 0, 128, m), vw("w3"), m == 0, m == 15)
+            if m % k == k - 1:
+                run(k, "keys")
+        scan(vw("mr"), vw("d0r"), vw("pA", 0, 128), A.add, A.max)
         scan(vw("sm"), vw("d0s"), vw("pA", 0, 128), A.mult, A.add)
-        ts(vw("nz"), vw("mr", 143, 384, 16), 255, A.bitwise_and)
-        if t == 0:
-            for a in (0, 8):
-                tt(vw("dz", a, a + 8), last("sm"), vw("thr"), A.is_ge)
-            tt(vw("pz"), vw("nz"), vw("dz"), A.mult)
-            for a, b in ((0, "I256"), (8, "Ib")):
-                aff(vw("pwB", 16 * a, 16 * a + 128), ind(vw("pz", a, a + 8), vw("L8")))
-                mm(vw("pB", 0, 128), vw("pwB", 16 * a, 16 * a + 128), vw(b), a == 0, a == 8)
-        for a, b in zip(CUT1, CUT1[1:]):
-            if not DK:
-                aff(flat("RA", a, b), ind(vw("R"), vw(q, a, b)), 1.0, 16.0)
-                more("RA_%d" % a)
+        ts(vw("nz"), last("mr"), 15, A.bitwise_and)
 
     def sums(t):
+        mm(tp, row("on", n=2), row("mid", n=2), True, False)
+        mm(tp, vw("eR"), vw("pk1"), False, False)
+        mm(tp, vw("eR"), vw("pk2"), False, False)
+        run(3)
         for m in range(16):
-            mm(vw("pD", 256, 384), vw("Ib"), flat("x", 0, 128, m), m == 0, False)
-            if m % 4 == 3:
-                run(4)
-        mm(vw("pD", 256, 384), vw("bo"), vw("eR"), False, t == 0)
-
-    QB = ("pC", "pE")
-
-    def quad(s, a, b, stop=False):
-        for h in (0, 1):
-            mm(vw(QB[h], s, 256, 4), a, vw(b, 64 * h, 64 * h + 64), False, stop)
-    win = vw("pB", 128, 256)
+            mm(tp, flat("x", 0, 128, m), vw("pk"), False, m == 15 and not t)
+            if m % 8 == 7:
+                run(8, "sums%d" % m)
 
     def kept(t):
         q, v = "q%d" % t, "v%d" % t
-        ts(vw("q16"), vw(q), 0.0, A.add)
-        zero(vw("eR"), vw("q16"))
-        mm(vw("pF", 0, 128), vw("cm"), vw("eR"))
-        relu(vw("e0"), vw("pF", 0, 128), 17.0)
-        zero(vw("eN"), vw("e0"))
-        if not DK:
-            mm(vw("pF", 128, 136), vw("eN"), vw("bo8a"))
-            aff(vw("e8"), vw("pF", 128, 136))
-            tt(vw("AE"), ind(vw("e8"), vw("L8")), vw("m16"), A.mult)
-            mm(vw("pF", 136, 144), vw("m16"), vw("bo8p"), True, False)
-            mm(vw("pF", 136, 144), vw("AE"), vw("bo8"), False, True)
-            copy(vw("le"), vw("pF", 136, 144))
+        aff(vw("q16"), vw(q))
+        zero(vw("eR"), vw(q))
+        for o in ops[-2:] if t == 1 else ():
+            del o["alts"]["v"]
+        mm(vw("pG", 0, 128), vw("cm"), vw("eR"))
+        relu(vw("eN"), vw("pG", 0, 128), -1.0 / 32)
         rows(t)
-        tt(vw("th2"), vw("thr"), last("sm"), A.subtract)
-        aff(vw("tb"), ind(vw("th2"), vw("L8")), 1.0 / 32, -1024.0)
-        aff(vw("kb"), ind(vw("mr", 0, 128), vw("LK")), 1.0 / 256, 1280 - 0.498046875)
-        ts(vw("k8"), last("mr"), 255, A.bitwise_and)
-        aff(vw("kl"), ind(vw("k8"), vw("L8")))
+        tt(vw("ke"), vw("pF", 400, 408), last("mr"), A.add)
+        aff(vw("k8"), vw("ke"), 1.0 / 16, -0.46875)
+        aff(vw("kb"), ind(vw("k8"), vw("L8")), 1.0, -2040.0)
+        tt(vw("th2"), vw("sn"), last("sm"), A.subtract)
+        aff(vw("tb"), ind(vw("th2"), vw("L8")), 1.0 / 16, vw("cb"))
         mm(vw("pB", 0, 128), vw(v), vw("I32"))
-        aff(vw("aP", 0, 128), vw("pB", 0, 128), 256.0)
-        aff(vw("aP", 128, 256), vw("pB", 0, 128))
-        tt(vw("pr"), ind(vw("nz"), vw("L16")), vw("aP"), A.mult)
+        act(vw("pwB"), ind(vw("nz"), vw("L8")), LN2, 0.0, F.Exp)
+        tt(vw("pr"), vw("pB", 0, 128), vw("pwB"), A.mult)
         ts(vw("bb"), vw("pr"), 32768, A.bitwise_and)
-        for a in (0, 128):
-            aff(vw("gb", a, a + 128), vw("bb", a, a + 128))
-            more("gb%d" % a)
-        ts(vw("s8"), last("mr"), 15, A.bitwise_and)
-        tt(vw("okK"), ind(vw("s8"), vw("L8")), vw("m15"), A.is_equal)
+        aff(vw("gb"), vw("bb"))
+        tt(vw("okK"), ind(vw("nz"), vw("L8")), vw("m15"), A.is_equal)
         for p in QB:
-            mm(vw(p, 0, 256), row("on"), row("ini", 0, 256), True, False)
-            mm(vw(p, 3, 256, 4), row("mk2", 128, 256), row("on", 0, 64), False, False)
-        for s, a, b in ((2, "boE", "eN"), (3, "IH", "eN"), (2, "kb", "Im19"), (3, "kb", "I19"), (2, "kl", "Im2k"), (3, "kl", "I2k"), (1, "tb", "I4k")):
-            quad(s, vw(a), b)
-        for a in (0, 128):
-            for s in (2, 3):
-                quad(s, vw("gb", a, a + 128), "Ig")
-        mm(win, row("on"), row("far"), True, False)
-        mm(win, row("mk2", 0, 128), row("on"), False, False)
+            mm(vw(p, 0, 256), row("on", n=2), row("ini", n=2), True, False)
+        for l in (((2, "ImH", "eN"), (3, "IH", "eN")), ((1, "tb", "I4k"),), ((2, "kb", "Im4k"), (3, "kb", "I4k")), ((2, "gb", "Im1k"), (3, "gb", "Im1k"))):
+            for h in (0, 1):
+                for s, a, b in l:
+                    mm(vw(QB[h], s, 256, 4), vw(a), vw(b, 64 * h, 64 * h + 64), False, False)
+                run(len(l))
+        mm(win, row("on", n=2), row("far", n=2), True, False)
         mm(win, vw("IH"), vw("eN"), False, False)
-        mm(win, vw("kb"), vw("Im19"), False, False)
-        mm(win, vw("kl"), vw("Im2k"), False, False)
+        mm(win, vw("kb"), vw("Im4k"), False, False)
         mm(win, vw("okK"), vw("I2H"), False, False)
         sums(t)
 
     def entered(t, q2):
-        n = vw("n%d" % t)
         for h in (0, 1):
             a, b, nh = 64 * h, 64 * h + 64, vw("n%d" % t, 4 * h, 4 * h + 4)
             aff(vw("xe", a, b), ind(XG(t), nh), 1.0, 0.0, "s")
@@ -726,241 +682,227 @@ def member(g, core, rank, T, topo):
             more("nq%d" % h)
             tt(vw("qd", 4 * a + 3, 4 * b, 4), vw("q16", a, b), vw("nq", a, b), A.add)
             more("qd%d" % h)
-            for s, c in ((1, "boS"), (2, "boT"), (3, "boU")):
+            for s, c in ((1, "boU"), (2, "boT"), (3, "boU")):
                 mm(vw(QB[h], s, 256, 4), vw(c), vw("xe", a, b), False, s == 3)
             run(3)
             scan(vw("sq", 4 * a, 4 * b), vw(QB[h], 0, 256), vw("qd", 4 * a, 4 * b), A.max, A.min)
             more("sq%d" % h)
-            copy(vw(q2, a, b), vw("sq", 4 * a + 3, 4 * b, 4))
+            aff(vw(q2, a, b), vw("sq", 4 * a + 3, 4 * b, 4))
             more("qo%d" % h)
         mm(win, vw("boT"), vw("xe"), False, True)
-        mm(vw("pD", 256, 384), vw("Ib"), vw("xe"), False, True)
-        relu(vw("w"), win, 0.0)
-        if not DK:
-            aff(vw("RN"), ind(vw("R"), n), 1.0, 16.0)
-            copy(ind(vw("RA"), vw("le")), vw("RN"))
+        mm(tp, vw("xe"), vw("pk"), False, True)
+        relu(vw("w"), win)
 
     def update(t):
-        tt(vw("rm"), qf, q2f, A.subtract)
-        tt(vw("yq"), vw("rm"), vw("w"), A.min)
-        act(vw("sg"), vw("yq"), 1.0, 0.0, F.Sign, vw("cj"))
-        for p in ("pG", "pH"):
-            mm(vw(p), vw("Ib"), vw("tri"), True, False)
+        rm, y8 = vw("pF", 128, 256), vw("pB", 256, 264)
+        mm(rm, vw("Ib"), qf, True, False)
+        mm(rm, vw("Im"), q2f, False, True)
+        tt(vw("yq"), rm, vw("w"), A.min if t else A.mult)
         for w in range(8):
-            p = vw("pG" if w < 4 else "pH", 128 * (w % 4), 128 * (w % 4) + 128)
-            mm(p, vw("sl", 128 * w, 128 * w + 128), vw("yq"), False, w % 4 == 3)
-            if w % 4 == 3:
-                run(4)
-        mm(vw("pB", 256, 264), vw("yq"), vw("bo8"))
-        aff(vw("y8"), vw("pB", 256, 264), -4096.0)
-        for a, p in ((0, "pG"), (512, "pH")):
-            for w in range(4):
-                act(vw("eq", a + 128 * w, a + 128 * w + 128), vw(p, 128 * w, 128 * w + 128), 1.0, vw("y8", a // 128 + w, a // 128 + w + 1), F.Abs)
-                more("eq%d" % (a // 512))
-            scan(vw("ab", a, a + 512), vw("d0a"), vw("eq", a, a + 512), A.add, A.min)
-            more("ab%d" % (a // 512))
-        mm(vw("pB", 264, 272), vw("yq"), vw("bo8"), True, False)
-        mm(vw("pB", 264, 272), vw("sg"), vw("bo16"), False, True)
-        aff(vw("ya"), vw("pB", 264, 272), -1.0, vw("dum"))
-        tt(vw("du"), vw("ab", 127, 1024, 128), vw("ya"), A.min)
-        if t < VI - 1:
-            mm(vw("pB", 280, 281), vw("on32"), vw("cj"))
-            aff(vw("cn"), vw("pB", 280, 281), 1.0, 281600.0)
-            aff(vw("cz"), vw("cn"), 1.0 / 256, -0.498046875)
-            aff(vw("cc"), vw("cz"), -256.0, vw("cn"))
-            aff(vw("limc"), vw("cc"), 16.0, vw("limf"))
-            aff(vw("lim8"), vw("I32", 0, 128, 16), vw("limc"))
-        tt(vw("AS"), ind(vw("du"), vw("L8")), vw("m16"), A.mult)
-        mm(vw("pB", 288, 296), vw("m16"), vw("bo8d"), True, False)
+            mm(vw("pG", 64 * w, 64 * w + 64), vw("Ib"), vw("tri"), w == 0, False)
+        run(8, None if t else "tri")
+        for h in (0, 64):
+            for w in range(8):
+                mm(vw("pG", 64 * w, 64 * w + 63, 1, h, h + 64), vw("sl", 64 * w, 64 * w + 64), vw("yq", h, h + 63), False, w == 7)
+        run(16, "near")
+        mm(y8, vw("yq"), vw("bo8"))
+        aff(vw("ym"), y8, -4096.0)
+        for w in range(8):
+            act(vw("eq", 64 * w, 64 * w + 64), vw("pG", 64 * w, 64 * w + 64), 1.0, vw("ym", w, w + 1), F.Abs)
+        scan(vw("ab"), vw("d0a"), vw("eq"), A.add, A.min)
+        aff(vw("ya"), y8, -1.0, vw("dum"))
+        tt(vw("du"), vw("ab", 63, 512, 64), vw("ya"), A.min)
+        listed(vw("pH", 0, 8), "yq", "l0")
+        tt(vw("AS"), ind(vw("du"), vw("L8")), vw("m16", 0, 128), A.mult)
+        mm(vw("pB", 288, 296), vw("m16", 0, 128), vw("bo8d"), True, False)
         mm(vw("pB", 288, 296), vw("AS"), vw("bo8n"), False, True)
-        copy(vw("ls"), vw("pB", 288, 296))
-        aff(vw("ti"), vw("pD", 256, 384), 0.0625)
-        tt(vw("xs"), ind(vw("XY"[t % 2]), vw("ls")), vw("ti"), A.add)
-        ts(vw("xn"), vw("xs"), 0.5, A.mult, -0.484375, A.add)
-        copy(ind(vw("YX"[t % 2]), vw("ls")), vw("xn"))
-        more("up")
+        aff(vw("ls"), vw("pB", 288, 296))
+        if t < VI - 1:
+            act(vw("sg"), y8, 1.0, 0.0, F.Sign, vw("cj"))
+            aff(vw("cjb"), vw("cj"))
+            mm(vw("pB", 280, 281), vw("on"), vw("cjb"))
+            aff(vw("cI"), vw("pB", 280, 281))
+            ts(vw("cA"), vw("cI"), 255, A.bitwise_and)
+            aff(vw("cb"), vw("cA"), 1.0, -2048.0)
+        ts(vw("tH"), tp, 1.5 * 2 ** 35, A.add, 1.5 * 2 ** 35, A.subtract)
+        tt(vw("tU", 0, 128, 2), tp, vw("tH"), A.subtract)
+        aff(vw("tU", 1, 128, 2), vw("tH"), 1.0 / 4096)
+        more("tV")
+        mm(vw("pE", 256, 384), vw("tU"), vw("Ib"), True, False)
+        aff(vw("xb"), ind(vw(tab(t)), vw("l0")))
+        more("xs")
+        mm(vw("pE", 256, 384), vw("I16"), vw("xb"), False, True)
+        aff(vw("xn"), vw("pE", 256, 384), 1.0 / 32, 63.75 - 0.484375)
+        for h in (1, 0):
+            aff(ind(vw(tab(t + 1)), vw("ls", 4 * h, 4 * h + 4)), vw("xn", 64 * h, 64 * h + 64), 1.0, 0.0, "v")
+            more("up" + "LH"[h])
+
+    def over(t, h):
+        a, b = (X0, X0 + 560, XS)[h:h + 2]
+        pick(vw(tab(t), a, b), vw(tab(t + 1), a, b), [[0, b - a]], A.is_ge, 0.0, 0)
+        more("over%d" % h)
+        ops[-1]["after"] += sent[-1:]
+        sent.append((len(ops) - 1, False))
 
     for t in range(VI):
-        q, v = "q%d" % t, "v%d" % t
-        end = t == VI - 1
+        v, end = "v%d" % t, t == VI - 1
+        tag[1] = t
         q2 = "q2u" if end else "qo%d" % (t + 1)
         if t:
+            tag[0] = "1" if t == 1 else ""
             kept(t)
-            turn[0] = t
+            tag[0] = ""
+            if end:
+                aff(vw("a1"), vw(v), 1.0, 8388608.0)
+                more("a2", t * TURN - 2.4)
+                mm(vw("pH", 128, 256), row("low"), row("on"), True, False)
+                mm(vw("pH", 128, 256), vw("I32"), vw("a1"), False, False)
+                mm(vw("pH", 128, 256), vw("I32m"), vw(v), False, False)
+                run(3)
             entered(t, q2)
         else:
             rows(0)
-            turn[0] = 0
+            tt(vw("dz"), last("sm"), vw("sn"), A.is_ge)
+            act(vw("pw"), vw("nz"), LN2, 0.0, F.Exp)
+            tt(vw("pz"), vw("pw"), vw("dz"), A.mult)
+            aff(vw("pwB"), ind(vw("pz"), vw("L8")))
+            mm(vw("pB", 0, 128), vw("pwB"), vw("Ib"))
             aff(vw("pwR"), vw("pB", 0, 128))
-            turn[0] = None
-            ts(vw("w"), vw("pB", 0, 128), vw("pwc"), A.is_equal, 4096.0, A.mult)
-            tt(vw("pr", 0, 128), an, vw("pwR"), A.mult)
-            tt(vw(v), an, vw("wy32"), A.add)
-            ts(vw("bb", 0, 128), vw("pr", 0, 128), 32768, A.bitwise_and)
-            tt(vw("qc"), qf, vw("bb", 0, 128), A.subtract)
-            turn[0] = 0
-            copy(vw(q2), vw("qc"))
-            more("qo0")
-            relu(q2f, vw("qc"), 0.0)
+            ts(vw("w"), vw("pB", 0, 128), pwa, A.mult, 32768.0, A.is_equal)
+            tt(vw("pr"), an, vw("pwR"), A.mult)
+            aff(vw(v), an)
+            ts(vw("bb"), vw("pr"), 32768, A.bitwise_and)
+            mm(vw("pA", 0, 128), vw("Ib"), qf)
+            tt(vw(q2), vw("pA", 0, 128), vw("bb"), A.subtract)
+            aff(q2f, vw(q2))
             sums(0)
+        tag[0] = "9" if end else ""
         if not end:
             send("q", t + 1)
+        for a in () if t else range(0, XS, 444):
+            iota(vw("TQ", a, a + 444), [[1, 444]], a)
+            ops[-1]["after"] += sent[-1:]
         zero(vw("e2"), q2f)
         for a, b in zip(CUT2, CUT2[1:]):
-            xgath(t, "x2", q2, a, b, 16.0, -2048.0, "vs" if t else "s" if a in CUT2[1::2] else "v")
-            if t == 0:
-                more("x2")
+            xgath(t, "x2", q2, a, b, 16.0, -2048.0)
         ku = vw("pC", 0, 128)
-        mm(ku, row("on"), row("tie16"), True, False)
+        mm(ku, vw("e2"), vw("bo256"), True, False)
         for m in range(16):
             mm(ku, flat("x2", 0, 128, m), vw("I16"), False, False)
         run(16)
-        mm(ku, vw("e2"), vw("bo256"), False, False)
         for a, b in zip(CUT2, CUT2[1:]):
             scan(flat("bs", a, b), flat("d0b", 0, b - a), flat("x2", a, b), A.add, A.max)
             more("bs_%d" % a)
-        bl = vw("bs", 15, 2048, 16)
-        aff(vw("lo"), bl, 0.0625, 1280 - 0.46875, "v")
-        mm(ku, bl, vw("Ib"), False, False)
+        aff(vw("lo"), last("bs"), 0.0625, 1280 - 0.46875)
+        mm(ku, last("bs"), vw("Ib"), False, False)
         mm(ku, vw("lo"), vw("Im16"), False, True)
-        e = 0 if end else 128
+        eQ = vw("eQ")
+        mm(vw("pA", 128, 256), vw("cmb" if end else "cm"), vw("e2"))
         if end:
-            mm(vw("pA", 0, 128), vw("e2"), vw("cm"))
-        mm(vw("pA", 128, 256), vw("cm"), vw("e2"))
-        relu(vw("e3", e, 256), vw("pA", e, 256), 17.0)
-        zero(vw("e1", 128 + e, 384), vw("e3", e, 256))
-        eQ = vw("e1", 256, 384)
-        aff(vw("a1"), vw(v), 1.0, 8388608.0)
-        aff(vw("a2"), vw("a1"), 1.0, -8388608.0)
-        if end:
-            aff(vw("e1", 0, 128), vw("e1", 128, 256), 64.0)
-            aff(vw("fR"), vw("e2"), -32.0, 32.0)
+            ts(eQ, vw("pA", 128, 256), -17.0, A.is_le)
+            mm(vw("pH", 128, 256), vw("Ib"), vw("e2"), False, True)
+            aff(vw("qa"), vw("pH", 128, 256), -32.0, -32.0 * 131072)
         else:
-            aff(vw("aM"), vw("a2"), 1.0, vw("a32"))
+            relu(eQ, vw("pA", 128, 256), -1.0 / 32)
+            mm(vw("pA", 256, 384), vw("I4k"), q2f)
+            tt(vw("t3"), vw("pA", 256, 384), vw(v), A.min)
+            aff(vw("a1"), vw("t3"), 1.0, 8388608.0)
         update(t)
-        scan(vw("mk"), vw("d0m", 0, 128), ku, A.add, A.max)
+        scan(vw("mk"), vw("d0k"), ku, A.add, A.max)
         aff(vw("cP"), ku, -1.0 / 4096, 1222.5 - 1.0 / 8192)
         ts(vw("r8"), last("mk"), 15, A.bitwise_and)
-        if DK:
-            tt(vw("ok"), ind(vw("r8"), vw("L8")), vw("m15"), A.is_equal)
-            mm(vw("pA", 384, 512), vw("ok"), vw("Ib"))
-            more("okm")
-            tt(vw("AL"), vw("pA", 384, 512), q2f, A.mult)
-            if not end:
-                tt(vw("oka"), vw("pA", 384, 512), vw("aM"), A.mult)
-            for c in range(16):
-                mm(vw("pD", 0, 8), vw("Z", 15 - c, 143 - c), vw("AL", c, 128, 16), c == 0, c == 15)
-            run(16)
-            more("dk")
-            copy(vw("lk"), vw("pD", 0, 8))
-            ts(vw("cd"), ind(vw("R"), vw("lk")), 16.0, A.add)
-        else:
-            tt(vw("AL"), ind(vw("r8"), vw("L8")), vw("m16"), A.mult)
-            mm(vw("pA", 256, 264), vw("m16"), vw("bo8k"), True, False)
-            mm(vw("pA", 256, 264), vw("AL"), vw("bo8n"), False, True)
-            copy(vw("lk"), vw("pA", 256, 264))
-            copy(vw("cd"), ind(vw("RA"), vw("lk")))
-            tt(vw("ok"), ind(vw("r8"), vw("L8")), vw("m15"), A.is_equal)
-            mm(vw("pA", 384, 512), vw("ok"), vw("Ib"))
-        nq = vw("pF", 0, 128)
-        nv = vw("pC", 0, 128)
+        tt(vw("ok"), ind(vw("r8"), vw("L8")), vw("m15"), A.is_equal)
+        okR, nv = vw("pA", 384, 512), vw("pC", 0, 128)
+        mm(okR, vw("ok"), vw("Ib"))
+        tt(vw("AL"), okR, q2f, A.mult)
         if not end:
-            mm(vw("pC", 128, 256), vw("I32"), vw(v), True, False)
-            mm(vw("pC", 128, 256), vw("Im20"), eQ, False, True)
-            aff(vw("t3"), vw("pC", 128, 256))
-            mm(nv, row("pw20"), row("on"), True, False)
-            mm(nv, row("pwr"), row("on"), False, False)
-            mm(nv, vw("I20"), eQ, False, False)
-            if not DK:
-                tt(vw("oka"), vw("pA", 384, 512), vw("aM"), A.mult)
-            mm(nv, vw("bo32"), vw("oka"), False, True)
+            tt(vw("oka"), okR, vw("a1"), A.mult)
+        aff(vw("okb"), okR, vw("a32"))
+        listed(vw("pD", 0, 8), "AL", "lk")
+        aff(vw("cd"), ind(vw("R"), vw("lk")), 1.0, float(X0))
+        if not end:
+            mm(nv, row("low"), row("on"), True, False)
+            mm(nv, vw("bo32"), vw("oka"), False, False)
+            mm(nv, vw("I17"), eQ, False, False)
+            mm(nv, vw("Ipw"), eQ, False, False)
+            mm(nv, vw("bo"), vw("okb"), False, True)
             tt(vw("vo%d" % (t + 1)), nv, vw("t3"), A.max)
             send("v", t + 1)
         bank = {2: "pF", 3: "pG", 0: "pE", 1: "pH"}
-        for n in (2, 3, 0, 1):
+        for n in bank:
             mm(vw(bank[n]), vw("cP", 0, 128, 1, 32 * n, 32 * n + 32), vw("E", 0, 512, 1, 32 * n, 32 * n + 32), True, n % 2 == 0)
+            more("far%d" % n)
             if n % 2 == 0:
-                aff(flat("vf", 16 * n, 16 * n + 32), vw(bank[n]), 1.0, -1100.0, "s")
+                aff(flat("vf", 32 * n, 32 * n + 32), vw(bank[n]), 1.0, -1100.0, "s")
                 more("vf%d" % n)
-        sb = ("pD", "pD")
-        if DK:
-            aff(vw("cd16"), ind(vw("R"), vw("lk")), 1.0, 16.0)
-            aff(vw("chi"), ind(vw("R"), vw("lk")), 1.0 / 64, 128.25 - 0.4921875)
-        else:
-            ts(vw("cd16"), vw("cd"), 0.0, A.add)
-            ts(vw("chi"), vw("cd"), 1.0 / 64, A.mult, 128 - 0.4921875, A.add)
-
-        def summed(src, n, w, stop):
+        aff(vw("cd16"), vw("cd"))
+        aff(vw("chi"), vw("cd16"), 1.0 / 64, 192 - 0.4921875)
+        for n in bank:
             a, b = 32 * n, 32 * n + 32
-            for j in range(16):
-                mm(vw(sb[n // 2], 128 + j, 384, 16, a, b), flat(src, a, b, j), vw(w), False, stop and j == 15)
-            run(16)
-        mm(vw("pD", 128, 384), row("on"), row("tie2"), True, False)
-        for h in (1, 0):
-            lo, hi = 64 * h, 64 * h + 64
-            n = 2 * h
-            tt(flat("mn", lo, lo + 32), ind(XG(t), vw("cd", lo, lo + 32)), flat("vf", 16 * n, 16 * n + 32), A.subtract)
-            more("mn_%d" % lo)
-            c = hi if h else hi - SHARE
-            xgath(t, "mn", "cd", lo + 32, c, -1.0, 0.0, "s")
-            if c < hi:
-                xgath(t, "mn", "cd", c, hi, -1.0, 0.0, "v")
-                more("mn_v")
-            mm(vw(bank[n + 1]), vw("Ib"), flat("mn", lo + 32, hi), False, True)
-            ts(flat("xc", lo, lo + 32), flat("mn", lo, lo + 32), 0.0, A.max, 2.0, A.mult)
+            if n % 2 == 0:
+                tt(flat("mn", a, b), ind(XG(t), vw("cd", a, b)), flat("vf", a, b), A.subtract)
+                more("mn_%d" % a)
+                ts(flat("xc", a, b), flat("mn", a, b), 0.0, A.max)
+            else:
+                for c, d in ((a, b - SHARE), (b - SHARE, b)) if n == 1 else ((a, b),):
+                    xgath(t, "mn", "cd", c, d, -1.0)
+                mm(vw(bank[n]), vw("Ib"), flat("mn", a, b), False, True)
+                more("near%d" % n)
+                act(flat("xc", a, b), vw(bank[n]), 0.5, -550.0, F.Abs)
             more("xc%d" % n)
-            act(flat("xc", lo + 32, hi), vw(bank[n + 1]), 1.0, -1100.0, F.Abs)
-            more("xc%d" % (n + 1))
+        mm(vw("pD", 256, 384), vw("cd16"), vw("Ib"), True, False)
         mm(vw("pD", 128, 256), vw("chi"), vw("Ib"), False, False)
-        mm(vw("pD", 256, 384), vw("cd16"), vw("Ib"), False, False)
         mm(vw("pD", 256, 384), vw("chi"), vw("Im64"), False, False)
-        run(3)
+        run(2)
         for n in (2, 0):
-            summed("mn", n, "wd", False)
+            for j in range(16):
+                mm(vw("pD", 128 + j, 384, 16, 32 * n, 32 * n + 32), flat("mn", 32 * n, 32 * n + 32, j), vw("wd"), False, False)
+            run(16, "lin%d" % n)
         for j in range(16):
             mm(vw("pD", 128 + j, 384, 16), flat("xc", 0, 128, j), vw("wa"), False, j == 15)
-        run(16)
+        run(16, "score")
         if not end:
-            scan(vw("ms"), vw("d0m", 0, 256), vw("pD", 128, 384), A.add, A.max)
-            ts(vw("n16", 0, 16), vw("ms", 15, 256, 16), 255, A.bitwise_and)
-            for a in (0, 8):
-                o = vw("AN", 16 * a, 16 * a + 128)
-                tt(o, ind(vw("n16", a, a + 8), vw("L8")), vw("m16"), A.mult)
-                more("AN%d" % a)
-                mm(vw("pH", 0, 8), o, vw("bo8" if a else "bo64"), a == 0, a == 8)
-            copy(vw("no%d" % (t + 1), 4, 12), vw("pH", 0, 8))
+            over(t, 0)
+        scan(vw("ms"), vw("d0m"), vw("pD", 128, 384), A.add, A.max)
+        ts(vw("n16"), last("ms"), 63, A.bitwise_and)
+        if not end:
+            tt(vw("AN"), ind(vw("n16"), vw("L16")), vw("m16"), A.mult)
+            for a in (0, 128):
+                mm(vw("pH", 0, 8), vw("AN", a, a + 128), vw("bo8" if a else "bo64"), a == 0, a == 128)
+            run(2)
+            aff(vw("no%d" % (t + 1), 4, 12), vw("pH", 0, 8), 1.0, 0.0, "vs" if t else "v")
             send("n", t + 1, 1)
             send("n", t + 1, 0)
-            copy(ind(vw("XY"[t % 2]), vw("ls")), vw("xn"))
-            more("up2")
-        if end:
-            aff(vw("okb"), vw("pA", 384, 512), vw("ac"))
-            mm(nv, vw("bo"), vw("okb"))
-            tt(vw("fr"), vw(v), vw("a2"), A.subtract)
-            tt(vw("fr"), vw("fr"), vw("fR"), A.mult)
-            tt(vw("t3"), nv, eQ, A.mult)
-            tt(vw("yw"), vw("fr"), vw("t3"), A.add)
-            store(T.yq[:, :], vw("yw"), "st1", "y", DMA + 0.3)
-            store(T.yx[:, :], vw("X", X0, X0 + D), "st0", "y", DMA + 1.6)
-            mm(nq, vw("ImQ"), eQ, True, False)
-            mm(nq, vw("IpQ"), vw("e2"), False, False)
-            mm(nq, vw("Ib"), q2f, False, False)
-            scan(vw("ms"), vw("d0m", 0, 256), vw("pD", 128, 384), A.add, A.max)
-            ts(vw("n16", 0, 16), vw("ms", 15, 256, 16), 255, A.bitwise_and)
-            for a in (0, 8):
-                o = vw("AN", 16 * a, 16 * a + 128)
-                tt(o, ind(vw("n16", a, a + 8), vw("L8")), vw("e1", 16 * a, 16 * a + 128), A.mult)
+            over(t, 1)
+        else:
+            mm(nv, vw("bo"), vw("okb"), True, False)
+            mm(nv, vw("I64"), eQ, False, True)
+            act(vw("t3"), nv, 32.0, -2048.0, F.Relu)
+            tt(vw("yw"), vw("qa"), vw("t3"), A.max)
+            store(T.yq[:, :], vw("yw"), "st1", "y", 0.3)
+            store(T.yx[:, :], vw("X", X0, XS), "st0", "y", 1.6)
+            old, new = vw("pA", 0, 128), vw("pF", 0, 128)
+            mm(old, vw("ImQ"), eQ, True, False)
+            mm(old, vw("IpQ"), vw("e2"), False, False)
+            mm(old, vw("Ib"), q2f, False, True)
+            run(3)
+            aff(vw("qb"), old, 1.0, -float(X0))
+            mm(new, row("on", n=2), row("less", n=2), True, False)
+            mm(new, vw("I4k"), eQ, False, False)
+            for a, x, w in ((0, "s", "I64"), (8, "v", "Ib")):
+                aff(vw("AN", 16 * a, 16 * a + 128), ind(vw("n16", a, a + 8), vw("L8")), 1.0, 0.0, x)
                 more("AN%d" % a)
-                mm(nq, o, vw("Ib"), False, a == 8)
-            aff(vw("yt"), nq, 1.0, -16.0)
-            store(T.yp[:, :], vw("yt"), "st2", "s", DMA + 0.3)
+                mm(new, vw("AN", 16 * a, 16 * a + 128), vw(w), False, a == 8)
+            tt(vw("yt"), new, vw("qb"), A.max)
+            store(T.yp[:, :], vw("yt"), "st2", "s", 0.3)
 
     if "plan" not in PLAN:
-        PLAN["plan"] = order(ops, links(ops))
-    pre, place, seq = PLAN["plan"]
+        PLAN["pre"] = links(ops)
+        PLAN["plan"] = order(ops, PLAN["pre"])
+    pre, (place, start, seq) = PLAN["pre"], PLAN["plan"]
     cnt, tok, snap, known = {}, {}, {}, {q: {} for q in Q}
     for i in seq:
-        o, q = ops[i], place[i][0]
+        o, q = ops[i], place[i]
         s = o["sem"] or ES[q]
         cnt[s] = cnt.get(s, 0) + o["inc"]
         tok[i] = (s, cnt[s])
@@ -969,9 +911,9 @@ def member(g, core, rank, T, topo):
             continue
         best = {}
         for j, hard in pre[i].items():
-            if (hard or place[j][0] != q) and tok[j][0] != "loc" and tok[j][1] > best.get(tok[j][0], (0, 0))[0]:
+            if (hard or place[j] != q) and tok[j][0] != "loc" and tok[j][1] > best.get(tok[j][0], (0, 0))[0]:
                 best[tok[j][0]] = (tok[j][1], j)
-        for k, (c, j) in sorted(best.items(), key=lambda e: -place[e[1][1]][2]):
+        for k, (c, j) in sorted(best.items(), key=lambda e: -start[e[1][1]]):
             if known[q].get(k, 0) < c:
                 Q[q].wait_ge(T.sem[k], c)
                 known[q][k] = c

import numpy as np
from concourse.bass import DstId, RemoteDMATransfer
from concourse.mybir import dt, AluOpType, AxisListType, ActivationFunctionType

A = AluOpType
F = ActivationFunctionType
NR, VI, H, L, D = 8, 4, 64, 128, 1760
STRIDE = (4, 1)
X0 = 16
XS = X0 + D
XW = XS + 128
BIG = 2.0 ** 24
HUGE = 2.0 ** 27
LN2 = 0.6931471805599453
f32, b16, h16, i32, u16 = "float32", "bfloat16", "float16", "int32", "uint16"
SB = {"X": (XW, b16), "Y": (XW, b16), "R": (XS, i32), "TQ": (XS, f32), "M": (17 * 256, h16)}
for _w, _d, _names in (
        (1, i32, "lmI kI aI gI hI tI cI cA"), (1, f32, "kc ac gc hc tc a1c a32 dum pwa limf cj cb"), (1, b16, "pwb cjb"), (4, f32, "pc"),
        (8, f32, "g8 c4k bo8f lim8 limP n0 thr sn th2 dz pw pz ym ya du"), (8, i32, "nz ke k8 r8"), (8, b16, "bo8 bo8n bo8a bo64 wm w3 sg"), (8, h16, "bo8d"),
        (8, u16, "L8 l0 ls lk"), (16, i32, "l16I n16"), (16, u16, "L16"), (16, b16, "wa wd"),
        (64, b16, "cK tri pk pk1 pk2 mid"), (64, f32, "tH"),
        (128, b16, "on cid gid aid Ib Im I16 Im16 Im32 I64 Im64 I17 I4k Im4k Im1k IH ImH I2H ImQ IpQ Ipw bo bo256 boT boU cm cmb c1 c2 M2 m15 d0s d0r d0k far low less"),
        (128, f32, "I32 I32m bo32 on32"), (144, b16, "Z"), (256, b16, "m16 d0m ini"), (512, b16, "eI E sl d0a"), (640, b16, "d0b"),
        (128, i32, "dr0 wy0 mr mk pr bb xn"), (128, b16, "rt wy32 eN eR e2 eQ xe xb pwB gb okK ok okb w chi"), (128, f32, "qa qb a1 t3 sm pwR oka yt yw"),
        (128, h16, "nq q16 tb kb yq lo cP AL AS cd16 tU"), (128, u16, "q2u cd"), (256, i32, "ms"), (256, h16, "AN"), (512, h16, "qd sq"), (512, b16, "eq ab"),
        (2048, b16, "B Aj N Dn x x2 xc mn vf"), (2048, h16, "bs")):
    SB.update({_k: (_w, _d) for _k in _names.split()})
ALONE = ("dr0", "wy0", "lmI", "yt", "yw")
ALIAS, SCRATCH, _wide = {}, {}, {}
for _k, (_w, _d) in SB.items():
    if _w > 1024 or _k in ALONE:
        SCRATCH[_k] = ("sbuf", [128, _w], _d)
    else:
        ALIAS[_k] = ("p_" + _d, _wide.get(_d, 0))
        _wide[_d] = _wide.get(_d, 0) + -(-_w // 16) * 16
for _d, _w in _wide.items():
    SCRATCH["p_" + _d] = ("sbuf", [128, _w], _d)
for _t in range(VI):
    SCRATCH["q%d" % _t] = ("sbuf", [128, L], u16)
    SCRATCH["v%d" % _t] = ("sbuf", [128, L], f32)
for _t in range(1, VI):
    SCRATCH["qo%d" % _t] = ("sbuf", [128, L], u16)
    SCRATCH["vo%d" % _t] = ("sbuf", [128, L], f32)
    SCRATCH["rq%d" % _t] = ("sbuf", [128, H], u16)
    SCRATCH["rv%d" % _t] = ("sbuf", [128, H], f32)
    SCRATCH["n%d" % _t] = ("sbuf", [128, 8], u16)
    SCRATCH["no%d" % _t] = ("sbuf", [128, 16], u16)
    SCRATCH["rn%d" % _t] = ("sbuf", [128, 4], u16)
PS = ("pA", "pB", "pC", "pD", "pE", "pF", "pG", "pH")
for _p in PS:
    SCRATCH[_p] = ("psum", [128, 512], f32)
SEMAPHORES = ["ev", "es", "et", "eg", "loc"] + ["ld%d" % _t for _t in range(6)] + ["st%d" % _t for _t in range(3)]
for _t in range(1, VI):
    SEMAPHORES += ["%s%d" % (_n, _t) for _n in ("qL", "qH", "vL", "vH", "nL", "nH", "rq", "rv", "rn")]
HALF = {"q": H, "v": H, "n": 4}
CUT1, CUT2, SHARE = range(0, 129, 16), (0, 32, 64, 104, 128), 16
CLOCKS = (((1, 0.86e-3, 1.25e-3, 3.2e-3, 0.48e-3, 0.9, 1.2, 2.5, 1.0, 1.0), 0.2, 1.25),
          ((1, 0.88e-3, 0.95e-3, 2.0e-3, 0.46e-3, 1.1, 1.5, 3.5, 1.5, 1.5), 0.29, 1.0),
          ((1, 1.0e-3, 1.1e-3, 2.5e-3, 0.75e-3, 1.0, 1.2, 3.0, 1.5, 1.3), 0.2, 0.5),
          ((1, 1.2e-3, 1.7e-3, 4.8e-3, 0.6e-3, 1.0, 1.2, 3.0, 1.5, 1.2), 0.2, 0.5))
TURN, STEP, WIDE, SWAPS, HEAT, SEED = 14.1, 0.52, 1.5, 24000, 0.2, 12
TABLE = {
    "v": """x_48 -8.19 eR -7.25 x_112 -4.86 x_96 -4.49 n0 -3.8 q16 -3.75 thr -3.55 sn -3.3 mr -2.76 nz -2.45 sm -2.4 ke -2.29 k8 -2.03 th2 -1.98 pr -1.77 bb -1.46 okK -1.35
            nq0 -0.86 qd0 -0.53 sq0 -0.22 nq1 0 qd1 0.33 sq1 0.64 w 0.86 qo1 1.06 e2 1.12 tH 1.17 yq 1.32 x2_64 1.43 bs_0 2.28 bs_32 2.5 bs_104 2.72 bs_64 2.89
            tV 3.16 tU 3.22 ab 3.31 du 3.73 mk 3.95 AS 4.06 r8 4.27 t3 4.33 ok 4.53 a1 4.74 upH 4.96 AL 5.21 upL 5.41 oka 5.67 lk 6.24 cA 6.29 cd 6.49 vo 6.7
            cd16 7.3 mn_48 6.9 mn_64 7.33 mn_0 8.02 xc2 8.71 xc0 8.93 ms 10.04 cb 10.26 n16 10.46 AN 10.71 no 11.55 0qo 1.06 0sq 1.3 0mr -2.9 0nz -2.6 0sm -2.8 0dz -2.5 0pz -2.05 0w 0.9 0thr -3.7 0sn -3.4""",
    "s": """x_0 -7.92 x_16 -7.53 x_80 -4.92 eN -4.53 x_32 -4.42 x_64 -4.04 pwB -2.2 tb -1.72 kb -1.5 gb -1.15 xe0 -0.86 xe1 -0.06 qo0 0.2 x2_32 0.46 x2_0 1.16 x2_104 1.87
            ym 2.41 ya 2.47 eq 2.67 l0 3.11 eQ 3.16 lo 3.36 xs 3.47 cP 4.26 xn 4.37 ls 4.7 sg 4.76 cjb 5.03 vf2 5.09 vf0 5.53 cI 5.95 okb 6.03 mn_96 6.91 mn_32 7.62
            chi 8 xc3 8.26 xc1 8.7 0pwb -11.2 0pw -2.35 0pwB -1.8 0pwR -1.1 0v 0.6 0limf -5.2 0lim8 -4.9 0limP -4.3 0n0 -4""",
    "t": """pGcmeR -5.1 pFeRbo8 -6.9 pFeNbo8a -4.19 pGIbtri -4.16 keys -3.45 pBvI32 -2.72 pEonini -2.47 pDonmid -2.35 pEImHeN -2.25 sums7 -2.16 sums15 -1.92 pConini -1.67
            pCImHeN -1.55 pCtbI4k -1.3 pEtbI4k -1.26 pCkbIm4k -1.07 pCgbIm1k -0.84 pCboUxe -0.52 pEkbIm4k -0.42 pBonfar -0.36 pBIHeN -0.3 pBkbIm4k -0.24
            pBokKI2H -0.18 pEgbIm1k -0.12 pEboUxe 0.28 pDxepk 0.38 pBboTxe 0.41 pFIbqd 0.64 pFImsq 1.06 pCe2bo256 1.32 pAcme2 1.38 pByqbo8 1.63 near 1.66 pHZyq 2.15
            pCx2I16 2.65 pCbsIb 3.63 pCloIm16 3.69 pEtUIb 3.75 pEI16xb 3.9 pHlowon -1.9 9pHIbe2 1.5 9pHZyq 3.8 9l0 4.4 9xs 4.7 9pEI16xb 5.1 9xn 5.4 9upH 5.7 9upL 6.1 pAI4ksq 3.96 pBm16bo8d 4.02 pBASbo8n 4.47 far2 4.57 pAokIb 4.94 far0 5 pBoncjb 5.29
            pClowon 5.32 pDZAL 5.52 pCbo32oka 6.03 pCI17eQ 6.28 pCIpweQ 6.34 pCbookb 6.4 far1 6.46 far3 6.71 pDcd16Ib 7.16 near3 7.82 near1 8.2 pDchiIb 8.4 lin2 8.55
            lin0 8.91 score 9.35 pHANbo64 11.28 0keys -3.8 0pDonmid 0.1 0sums7 0.2 0sums15 0.8 0pCIbM -0.1 tri 0.5""",
    "g": "sendq 1.37 sendv 7.01 over0 8.91 sendn 11.8 over1 12 0l16I -6 0cid -5.5 0eI -3.8 0TQ -2.7"}
DUE = {k: float(t) for l in TABLE.values() for k, t in zip(l.split()[::2], l.split()[1::2])}
ENG = {k: q for q, l in TABLE.items() for k in l.split()[::2]}
ENG.update({"0Dn": "s", "0Dv": "v"})
for _k in range(8):
    DUE["0x_%d" % (16 * _k)], ENG["0x_%d" % (16 * _k)] = -9.6 + 0.37 * _k, "s"
DUE.update({"1x_48": -4.86, "1x_32": -4.49, "1x_64": -4.85, "1x_80": -4.45, "1x_96": -4.05, "1x_112": -3.65, "1eR": -4.95, "1pGcmeR": -4.6, "1pFeRbo8": -4.5, "1eN": -3.25,
            "1q16": -2.0, "1n0": -3.2, "1thr": -2.9, "1sn": -2.6, "1keys": -2.7})
ENG.update({"1x_48": "v", "1x_32": "v", "1x_96": "s", "1x_112": "s", "1eR": "s", "1n0": "s"})
PLAN = {}


def relay_of(core, dst, topo):
    c = [n for n in topo.cores_of(core) if n != core and topo.may_write(n, dst)]
    return ([n for n in c if topo.die(n) == topo.die(core)] + c)[0]


def bits(topo, src, dst, n, top):
    e = topo.engines(src, dst)
    e = e[len(e) - n:] if top else e[:n]
    return sum(1 << k for k in e)


def rank_program(g, core, T, topo):
    rank = T.rank_of(core)
    if rank is None:
        for r, c in enumerate(T.cores):
            dst = T.cores[(r + STRIDE[1]) % NR]
            if relay_of(c, dst, topo) == core:
                relay(g, core, c, dst, T, topo)
        return
    member(g, core, rank, T, topo)


def relay(g, core, src, dst, T, topo):
    rid, pid = topo.addr(dst, core)
    m = bits(topo, core, dst, 8, False)
    for t in range(1, VI):
        for k in "qvn":
            g.wait_ge(T.sem["r%s%d" % (k, t)], len(topo.engines(src, core)) if k == "n" else 8)
            g.remote_dma(T["%s%d" % (k, t)][:, HALF[k]:2 * HALF[k]], T["r%s%d" % (k, t)][:, :], T.sem["%sH%d" % (k, t)], T.sem["loc"], pid, rid, m)
    g.wait_ge(T.sem["loc"], 24 * (VI - 1))


def clash(a, b):
    if a["lo"] >= b["hi"] or b["lo"] >= a["hi"] or a["r0"] >= b["r1"] or b["r0"] >= a["r1"]:
        return False
    return not (a["st"] > 1 and a["st"] == b["st"] and (a["lo"] - b["lo"]) % a["st"])


def covers(a, b):
    return a["st"] == 1 and a["lo"] <= b["lo"] and b["hi"] <= a["hi"] and a["r0"] <= b["r0"] and b["r1"] <= a["r1"]


def links(ops):
    recs, pre = {}, []
    for i, o in enumerate(ops):
        d = dict(o["after"])
        acc = [(a, True) for a in o["outs"]] + [(a, False) for a in o["ins"]]
        for a, wr in acc:
            l = recs.setdefault(a["n"], [])
            if a["n"] in PS:
                for b, bw, j in l[-1:] + [r for r in l if r[1] and not wr and "t" not in ops[r[2]]["alts"] and clash(a, r[0])]:
                    d[j] = d.get(j, False) or (bw and "t" not in ops[j]["alts"])
                continue
            for b, bw, j in l:
                if (wr or bw) and clash(a, b):
                    d[j] = True
        for a, wr in acc:
            l = recs[a["n"]]
            if wr and a["n"] not in PS:
                l[:] = [b for b in l if not covers(a, b[0])]
            l.append((a, wr, i))
        d.pop(i, None)
        pre.append(d)
    return pre


def order(ops, pre):
    n, K = len(ops), range(len(CLOCKS))
    dot = lambda c, k: sum(a * b for a, b in zip(c, CLOCKS[k][0]))
    cost = [[{q: dot(c, k) for q, (_, c) in o["alts"].items()} for o in ops] for k in K]
    lat = [[dot(o["lat"], k) for o in ops] for k in K]
    pl, behind = [], []
    for p in pre:
        b = 0
        for j in p:
            b |= behind[j]
        pl.append([(j, hard) for j, hard in p.items() if not b >> j & 1])
        for j, hard in p.items():
            b |= hard << j
        behind.append(b)
    pj = [[j for j, _ in p] for p in pl]
    ends = sorted(set(range(n)) - {j for p in pre for j in p})
    name = [o["name"] for o in ops]
    look = lambda table, k: table.get(k, table.get(k.lstrip("19")))
    wait = [[[(j, lat[k][j] + CLOCKS[k][1], hard) for j, hard in p] for p in pl] for k in K]
    sure = lambda i, j, hard: hard or not set(cost[0][i]) & set(cost[0][j])
    firms = [[[(j, d) for j, d, hard in p if sure(i, j, hard)] for i, p in enumerate(w)] for w in wait]
    softs = [[[(j, d) for j, d, hard in p if not sure(i, j, hard) and len(cost[0][i]) + len(cost[0][j]) > 2] for i, p in enumerate(w)] for w in wait]

    def place():
        due = [VI * TURN] * n
        for i in range(n - 1, -1, -1):
            t = look(DUE, name[i])
            t = ops[i].get("due") if t is None else ops[i]["visit"] * TURN + t
            due[i] = due[i] - min(cost[0][i].values()) - lat[0][i] if t is None else t
            for j, hard in pl[i]:
                due[j] = min(due[j], due[i] - (CLOCKS[0][1] if hard or set(cost[0][j]) != set(cost[0][i]) else 0.0))
        for i in range(n):
            for j in pj[i]:
                due[i] = max(due[i], due[j] + 1e-6)
        busy, q, s, e = {k: [] for k in "vstgy-"}, [None] * n, [0.0] * n, [0.0] * n
        for i in sorted(range(n), key=lambda k: due[k]):
            best, want = None, look(ENG, name[i])
            for k, c in cost[0][i].items():
                if want in cost[0][i] and want != k:
                    continue
                t = max([e[j] + d + ops[j]["late"] if hard or q[j] != k else e[j] for j, d, hard in wait[0][i]] + [0.0])
                for a, b in busy[k]:
                    if b > t + 1e-9 and a < t + c - 1e-9:
                        t = b
                f = t + c + (0.15 if k == "v" else 0.0)
                if best is None or f < best[0]:
                    best = (f, k, t, c)
            _, q[i], s[i], c = best
            e[i] = s[i] + c
            if q[i] != "-":
                busy[q[i]] = sorted(busy[q[i]] + [(s[i], e[i])])
        return q, sorted(range(n), key=lambda k: (s[k], k))

    def run(q, seq, k):
        c, firm, soft = cost[k], firms[k], softs[k]
        e, free = [0.0] * n, {x: 0.0 for x in "vstgy-"}
        for i in seq:
            x = q[i]
            t = free[x]
            for j, d in firm[i]:
                if e[j] + d > t:
                    t = e[j] + d
            for j, d in soft[i]:
                if q[j] != x and e[j] + d > t:
                    t = e[j] + d
            e[i] = free[x] = t + c[i][x]
            free["-"] = 0.0
        return e

    def pairs(q, before, e, k, i):
        l = []
        while i is not None:
            t, y = e[i] - cost[k][i][q[i]] - 1e-9, None
            for j, d, hard in wait[k][i]:
                if (e[j] + d if hard or q[j] != q[i] else e[j]) >= t:
                    y = j
            if y is None and q[i] != "-" and before[i] is not None and e[before[i]] >= t:
                y = before[i]
                l.append((y, i))
            i = y
        return l

    def judge(q, key, limit):
        seq = np.argsort(key, kind="stable").tolist()
        es, ws = [], []
        for k in K:
            es.append(run(q, seq, k))
            ws.append((max(es[k][i] + lat[k][i] for i in ends) + 0.3 * sum(es[k]) / n) * CLOCKS[k][2])
            if sum(ws) > limit[k]:
                return None
        at = [0.0] * n
        for p, i in enumerate(seq):
            at[i] = es[0][i] - cost[0][i][q[i]] + p * 1e-7
        seq = np.argsort(at, kind="stable").tolist()
        before, last, l = [None] * n, {}, []
        for j in seq:
            before[j], last[q[j]] = last.get(q[j]), j
        for k, e in enumerate(es):
            l += pairs(q, before, e, k, max(ends, key=lambda i: e[i] + lat[k][i])) + pairs(q, before, e, k, draw(n))[:4]
        return sum(ws), l, (q, at, seq), ws, [round(max(e[i] + lat[k][i] for i in ends), 2) for k, e in enumerate(es)]
    seed = [SEED]

    def draw(k):
        seed[0] = (seed[0] * 1103515245 + 12345) % 2 ** 31
        return (seed[0] >> 8) % k
    seen, kin = {}, {}
    for i, o in enumerate(ops):
        k = seen[(o["visit"], name[i])] = seen.get((o["visit"], name[i]), 0) + 1
        kin.setdefault((name[i], k), []).append(i)
    kin = {i: l for l in kin.values() for i in l}
    q, seq = place()
    now = best = judge(q, np.argsort(seq), [1e9] * len(K))
    PLAN["ends"] = best[4]
    for step in range(SWAPS):
        q, key = list(now[2][0]), list(now[2][1])
        pull = False
        for _ in range(1 + (draw(4) == 0)):
            a, b = now[1][draw(len(now[1]))]
            i, sign = ((a, 1.0), (b, -1.0))[draw(2)]
            if len(cost[0][i]) > 1 and draw(3) == 0:
                k = [k for k in cost[0][i] if k != q[i]][0]
                for j in kin[i]:
                    q[j] = k if k in cost[0][j] else q[j]
            else:
                d = abs(key[b] - key[a]) + (1e-4, 1e-4, 0.1, 0.3, 0.8, 2.0)[draw(6)]
                pull = pull or sign < 0
                for j in kin[i]:
                    key[j] += sign * d
        if pull:
            for i in range(n - 1, -1, -1):
                x = key[i]
                for j in pj[i]:
                    if key[j] >= x:
                        key[j] = x - 1e-6
        else:
            for i in range(n):
                x = key[i]
                for j in pj[i]:
                    if key[j] >= x:
                        key[i] = x = key[j] + 1e-6
        r = judge(q, key, [sum(now[3][:k + 1]) + 0.6 for k in K[:-1]] + [now[0] + HEAT * (1 - step / SWAPS) * draw(100) / 100])
        if r:
            now = r
            if r[0] < best[0]:
                best = r
    PLAN["ends2"] = best[4]
    return best[2]


def member(g, core, rank, T, topo):
    Q = {"v": g.vector, "s": g.scalar, "t": g.tensor, "g": g, "y": g.sync}
    ES = {"v": "ev", "s": "es", "t": "et", "g": "eg"}
    ops, sent, loaded = [], [], {}
    tag = ["0", 0]

    def vw(name, lo=0, hi=None, st=1, r0=0, r1=128):
        d, nm = SB[name][1] if name in SB else SCRATCH[name][2], name.rstrip("0123") if name not in SB else name
        if hi is None:
            hi = SB[name][0] if name in SB else SCRATCH[name][1][1]
        if name in ALIAS:
            name, o = ALIAS[name]
            lo, hi = lo + o, hi + o
        ap = T[name][r0:r1, lo:hi:st] if st > 1 else T[name][r0:r1, lo:hi]
        return {"ap": ap, "n": name, "lo": lo, "hi": hi, "st": st, "x": None, "r0": r0, "r1": r1, "k": len(range(lo, hi, st)), "b": 2 if "16" in d else 4, "d": d, "name": nm}

    def ind(w, o):
        return dict(w, ap=w["ap"].indirect(o["ap"]), x=o, k=16 * o["k"])

    def tm(us=0.0, cyc=0, gat=0, sca=0, pe=0, hop=0, dma=0, first=0, long=0, far=0):
        return (us, cyc, gat, sca, pe, hop, dma, first, long, far)

    def op(alts, outs, ins, sem=None, inc=1, lat=tm(), after=(), late=0.0):
        r = []
        for a in ins + [a["x"] for a in outs]:
            if isinstance(a, dict):
                r.append(a)
                if a["x"]:
                    r.append(a["x"])
        ops.append({"alts": alts, "outs": outs, "ins": r, "sem": sem, "inc": inc, "lat": lat, "after": list(after), "late": late, "visit": tag[1],
                    "name": tag[0] + (outs[0]["name"] if outs else "out")})
        return len(ops) - 1

    def more(name, due=None):
        ops[-1]["name"] = tag[0] + name
        if due is not None:
            ops[-1]["due"] = due

    def P(a):
        return a["ap"] if isinstance(a, dict) else a

    def vcost(o, ins, rate=1.0):
        if o["x"]:
            return tm(0.05, sca=o["k"])
        if ins and ins[0]["x"]:
            return tm(0.05, gat=o["k"])
        if rate == 1.0 and all(a["b"] == 2 for a in [o] + ins):
            rate /= 2
        return tm(cyc=max(64, rate * o["k"]))

    def scost(o, i, us=0.0):
        return tm(0.065, gat=o["k"]) if i["x"] else tm(us, max(64, o["k"]))

    def tt(o, a, b, f):
        r = 1.0 if a["n"] in PS or b["n"] in PS else 2.0
        op({"v": (lambda: g.vector.tensor_tensor(P(o), P(a), P(b), f), vcost(o, [a, b], r))}, [o], [a, b])

    def tsf(o, a, s1, f1, s2=None, f2=None):
        if s2 is None:
            return lambda: g.vector.tensor_scalar(P(o), P(a), P(s1), None, f1)
        return lambda: g.vector.tensor_scalar(P(o), P(a), P(s1), P(s2), f1, f2)

    def ts(o, a, s1, f1, s2=None, f2=None):
        op({"v": (tsf(o, a, s1, f1, s2, f2), vcost(o, [a]))}, [o], [a, s1, s2])

    def scan(o, d0, d1, f0, f1):
        op({"v": (lambda: g.vector.tensor_tensor_scan(P(o), P(d0), P(d1), 0.0, f0, f1), vcost(o, [d0, d1]))}, [o], [d0, d1])

    def fill(o, c):
        op({"v": (lambda: g.vector.memset(P(o), c), vcost(o, []))}, [o], [])

    def actf(o, i, scale, bias, func):
        return lambda: g.scalar.activation(P(o), P(i), func, bias=P(bias), scale=P(scale))

    def act(o, i, scale, bias, func, acc=None, us=0.0):
        if acc is None:
            op({"s": (actf(o, i, scale, bias, func), scost(o, i, us))}, [o], [i, scale, bias])
        else:
            op({"s": (lambda: g.scalar.activation(P(o), P(i), func, bias=P(bias), scale=P(scale), accum_out=P(acc)), scost(o, i, 0.02))}, [o, acc], [i, scale, bias])

    def aff(o, i, scale=1.0, bias=0.0, qs="vs"):
        if isinstance(scale, float) and isinstance(bias, float) and (scale, bias) == (1.0, 0.0):
            fv = lambda: g.vector.tensor_copy(P(o), P(i))
        else:
            fv = tsf(o, i, scale, A.mult, bias, A.add)
        alts = {"v": (fv, vcost(o, [i])), "s": (actf(o, i, scale, bias, F.Identity), scost(o, i))}
        op({q: alts[q] for q in qs}, [o], [i, scale, bias])

    def relu(o, i, scale=1.0):
        op({"v": (tsf(o, i, scale, A.mult, 0.0, A.max), vcost(o, [i])), "s": (actf(o, i, scale, 0.0, F.Relu), scost(o, i))}, [o], [i])

    def zero(o, i):
        op({"v": (tsf(o, i, 0.0, A.is_equal), vcost(o, [i])), "s": (actf(o, i, -1.0, 1.0, F.Relu), scost(o, i))}, [o], [i])

    def mm(o, a, b, start=True, stop=True):
        c = max(min(64, a["k"]), b["k"]) * (4 if a["b"] == 4 else 1)
        op({"t": (lambda: g.tensor.matmul(P(o), P(a), P(b), start, stop), tm(pe=c))}, [o], [a, b])
        more(o["name"] + a["name"] + b["name"])

    def run(k, name=None):
        l = ops[-k:]
        del ops[-k:]
        fs = [o["alts"]["t"][0] for o in l]
        op({"t": (lambda: [f() for f in fs][-1], tm(pe=sum(o["alts"]["t"][1][4] for o in l)))}, [a for o in l for a in o["outs"]], [a for o in l for a in o["ins"]])
        ops[-1]["name"] = tag[0] + name if name else l[0]["name"]

    def load(o, src, sem, q, us):
        loaded[q] = [(op({q: (lambda: Q[q].dma_start(P(o), src), tm(0.05))}, [o], [], sem, 16, tm(dma=1, long=us), loaded.get(q, [])), False)]

    def store(dst, i, sem, q, us):
        op({q: (lambda: Q[q].dma_start(dst, P(i)), tm(0.05))}, [], [i], sem, 16, tm(dma=1, long=us))
        more(sem)

    def iotaf(o, pat, base, cm):
        if o["d"] == i32:
            return lambda: g.iota(P(o), pat, base, cm)
        return lambda: g.iota(P(o), pat, base, cm, allow_small_or_imprecise_dtypes=True)

    def iota(o, pat, base, cm=0):
        op({"g": (iotaf(o, pat, base, cm), tm(0.13, 2 * o["k"]))}, [o], [])

    def pick(o, i, pat, f, c, base):
        op({"g": (lambda: g.affine_select(P(o), P(i), pat, f, c, base, 1), tm(0.17, 2 * o["k"]))}, [o], [i])

    def flat(name, a, b, m=None):
        return vw(name, 16 * a, 16 * b) if m is None else vw(name, 16 * a + m, 16 * b, 16)

    def last(name):
        return vw(name, 15, None, 16)

    def row(name, lo=0, hi=None, st=1, n=1):
        return vw(name, lo, hi, st, 0, n)

    def pair(name, lo, st, a, b):
        fill(row(name, lo, None, st, 2), b)
        fill(row(name, lo, None, st), a)

    def tab(t):
        return "XY"[t % 2]

    def XG(t):
        return vw(tab(t), 0, XS)

    def xgath(t, dst, lst, a, b, scale=1.0, bias=0.0):
        aff(flat(dst, a, b), ind(XG(t), vw(lst, a, b)), scale, bias)
        more("%s_%d" % (dst, a))

    def listed(o, src, dst):
        for c in range(16):
            mm(o, vw("Z", 15 - c, 143 - c), vw(src, c, 128, 16), c == 0, c == 15)
        run(16)
        aff(vw(dst), o)

    def send(k, t, half=None):
        src = "%so%d" % (k, t)
        lowd = T.cores[(rank + STRIDE[0]) % NR]
        hid = relay_of(core, T.cores[(rank + STRIDE[1]) % NR], topo)
        r1, p1 = topo.addr(lowd, core)
        r2, p2 = topo.addr(hid, core)
        tr = [RemoteDMATransfer(dst_ids=[DstId(rid=r1, pnc=p1)], dma_engine_mask=bits(topo, core, lowd, 8, False), remote_sem=T.sem["%sL%d" % (k, t)],
                                src=T[src][:, 0:HALF[k]], dst=T["%s%d" % (k, t)][:, 0:HALF[k]]),
              RemoteDMATransfer(dst_ids=[DstId(rid=r2, pnc=p2)], dma_engine_mask=bits(topo, core, hid, 8, True), remote_sem=T.sem["r%s%d" % (k, t)],
                                src=T[src][:, HALF[k]:2 * HALF[k]], dst=T["r%s%d" % (k, t)][:, :])]
        if half == 1:
            i = op({"g": (lambda: g.remote_dma(T["rn%d" % t][:, :], T[src][:, 8:12], T.sem["rn%d" % t], T.sem["loc"], p2, r2, topo.mask(core, hid)), tm(0.1))},
                   [], [vw(src, 8, 12)], "loc", len(topo.engines(core, hid)), after=sent[-1:])
        elif half == 0:
            i = op({"g": (lambda: g.remote_dma(T["n%d" % t][:, 0:4], T[src][:, 4:8], T.sem["nL%d" % t], T.sem["loc"], p1, r1, bits(topo, core, lowd, 8, False)), tm(0.1))},
                   [], [vw(src, 4, 8)], "loc", 8, after=sent[-1:])
        else:
            i = op({"g": (lambda: g.remote_dma_fused(tr, local_sem=T.sem["loc"]), tm(0.1))}, [], [vw(src)], "loc", 16, after=sent[-1:])
        more("send" + k)
        way = 1.0 if k == "n" else WIDE
        for h in (0, 1) if half is None else (half,):
            op({"-": (None, tm(-0.2, hop=h * way, far=way, first=(1 + 0.8 * h) * ((k, t) == ("q", 1))))}, [vw("%s%d" % (k, t), h * HALF[k], (h + 1) * HALF[k])], [],
               "%s%s%d" % (k, "LH"[h], t), 8, after=[(i, True)], late=float(k != "n"))
        sent.append((i, False))

    load(vw("wy0"), T.why[:, :], "ld0", "y", 0.3)
    load(vw("dr0"), T.drugs[:, :], "ld1", "s", 0.5)
    load(vw("lmI"), T.lim[:, :], "ld3", "y", 0.6)
    load(vw("X", X0, XS), T.eff[:, :], "ld2", "y", 2.0)
    load(vw("R", X0, XS), T.rem[:, :], "ld4", "y", 5.0)
    load(vw("Y", X0, XS), T.eff[:, :], "ld5", "y", 6.5)
    fill(vw("on"), 1.0)
    iota(vw("kI"), [[1, 1]], 0, 1)
    pick(vw("Ib"), vw("on"), [[-1, 128]], A.is_equal, 0.0, 0)
    iota(vw("gid"), [[1, 8], [0, 16]], 0)
    iota(vw("cid"), [[1, 128]], 0)
    iota(vw("aid"), [[0, 8], [1, 16]], 0)
    iota(vw("g8"), [[1, 8]], 0)
    for n, c, f in (("a", 15, A.bitwise_and), ("g", 4, A.arith_shift_right), ("h", 31, A.bitwise_and), ("t", 63, A.bitwise_and)):
        ts(vw(n + "I"), vw("kI"), c, f)
    for n in "kaght":
        aff(vw(n + "c"), vw(n + "I"))
    ts(vw("bo"), vw("gid"), vw("gc"), A.is_equal)
    ts(vw("bo8f"), vw("g8"), vw("gc"), A.is_equal)
    for a in (0, 128):
        ts(vw("m16", a, a + 128), vw("aid"), vw("ac"), A.is_equal)
    for n, c, st, z in (("d0r", 1.0, 16, -2.0 ** 31), ("d0k", 16.0, 16, -2.0 ** 31), ("d0m", 64.0, 16, -2.0 ** 31), ("d0b", 1.0, 16, -8192.0), ("d0a", 0.0, 64, BIG)):
        fill(vw(n), c)
        fill(vw(n, 0, None, st), z)
    ts(vw("d0s"), vw("aid"), 0.0, A.not_equal)
    fill(vw("on32"), 1.0)
    fill(vw("cK"), -31.0)
    for n, c in (("Im32", -32.0), ("I32", 1.0), ("I32m", -1.0), ("Im", -1.0), ("I16", 16.0), ("Im16", -16.0), ("Im64", -64.0), ("I64", 64.0), ("I17", 131072.0),
                 ("I4k", 4096.0), ("Im4k", -4096.0), ("Im1k", -1024.0), ("IH", HUGE), ("ImH", -HUGE), ("I2H", 2 * HUGE), ("ImQ", -float(XS)), ("IpQ", float(XS))):
        aff(vw(n), vw("Ib"), c)
    for n, c in (("bo32", 1.0), ("bo256", 256.0), ("boT", 4096.0), ("boU", -4096.0)):
        aff(vw(n), vw("bo"), c)
    for n, src, c, b in (("dum", "kI", 1.0, float(XS)), ("a1c", "aI", 1.0, 1.0), ("a32", "aI", 1.0 / 32, 0.0), ("limf", "lmI", 16.0, 0.0), ("m15", "aid", -1.0, 15.0)):
        aff(vw(n), vw(src), c, b)
    for n, a, c in (("bo8", 0, 1.0), ("w3", 0, 16.0), ("wd", 0, 1024.0), ("wd", 8, 1024.0), ("wm", 0, -256.0), ("wa", 0, -2048.0), ("wa", 8, -2048.0),
                    ("bo8d", 0, vw("dum")), ("bo8n", 0, -1.0), ("bo8a", 0, vw("a1c")), ("bo64", 0, 64.0), ("c4k", 0, 4096.0)):
        aff(vw(n, a, a + 8), vw("bo8f"), c)
    for n in "XY":
        fill(vw(n, 0, X0), -1.0)
        fill(vw(n, XS, XW), 0.0)
    fill(vw("R", 0, X0), -X0)
    act(vw("pwb"), vw("aI"), LN2, 0.0, F.Exp, us=1.35)
    first, pwa = [(len(ops) - 1, False)], vw("pwa")
    aff(pwa, vw("pwb"))
    for b, f in ((0, A.is_lt), (1, A.is_ge)):
        ts(vw("pc", 2 + b, 3 + b), vw("aI"), 5.0, f, -140.0, A.mult)
        ts(vw("pc", b, b + 1), vw("aI"), LN2, A.mult, vw("pc", 2 + b, 3 + b), A.add)
    aff(vw("Ipw"), vw("Ib"), pwa)
    fill(row("low"), -131072.0 - 8388608.0)
    tt(vw("pk"), vw("I4k", 1, 128, 2), vw("Ib", 0, 128, 2), A.add)
    aff(vw("pk1"), vw("bo", 0, 128, 2))
    aff(vw("pk2"), vw("bo", 0, 128, 2), 4096.0)
    for n, a, b in (("less", -4096.0, -float(X0)), ("mid", -2040.0 * 4096, -2040.0), ("far", -2048.0 * 69632, 2048.0 * 17)):
        pair(n, 0, 1, a, b)
    for s, (a, b) in enumerate(((1.0, 0.0), (2.0 ** 23, 0.0), (2048.0 * 12288, 2048.0 * 17), (-2048.0 * 61440, -2048.0 * 17))):
        pair("ini", s, 4, a, b)
    for s, c in enumerate((0.0, 2048.0, 2048.0)):
        fill(vw("qd", s, None, 4), c)
    iota(vw("l16I"), [[1, 16]], 0)
    aff(vw("L16"), vw("l16I"))
    aff(vw("L8"), vw("l16I", 0, 8))
    ts(vw("c1"), vw("cid"), vw("kc"), A.is_gt, 64.0, A.mult)
    tt(vw("c2"), vw("c1"), vw("bo"), A.mult)
    tt(vw("cm"), vw("c2"), vw("Im32"), A.add)
    tt(vw("cmb"), vw("cm"), vw("bo"), A.add)
    fill(vw("Z"), 0.0)
    aff(vw("Z", 15, 143, 16), vw("bo8f"))
    iota(vw("eI"), [[1, 32], [0, 16]], 0)
    ts(vw("E"), vw("eI"), vw("hc"), A.is_equal)
    for w in range(8):
        aff(vw("sl", 64 * w, 64 * w + 64), vw("on", 0, 64), vw("c4k", w, w + 1))
    ts(vw("tri", 0, 63), vw("cid", 0, 63), vw("tc"), A.is_ge, BIG, A.mult)
    fill(vw("tri", 63, 64), 0.0)

    ts(vw("rt"), vw("wy0"), vw("ac"), A.is_equal, vw("a1c"), A.mult)
    for h in (0, 64):
        tt(vw("N", h, h + 64), vw("rt", h, h + 64), vw("wy0", h, h + 64), A.subtract)
        act(vw("M", 2 * h, 2 * h + 64), vw("on", 0, 64), 0.0, vw("pc", 0, 1), F.Exp)
        ops[-1]["after"] += first
        more("Mi", -9.7)
        act(vw("M", 11 * 256 + 2 * h + 64, 11 * 256 + 2 * h + 128), vw("on", 0, 64), 0.0, vw("pc", 1, 2), F.Exp)
        ops[-1]["after"] += first
        more("Ml", -5.0)
    tt(vw("M2"), vw("bo"), vw("Im32"), A.add)
    for s in range(16):
        j = 15 - s
        aj, bj = vw("Aj", 128 * s, 128 * s + 128), vw("B", 128 * s, 128 * s + 128)
        pick(bj, vw("Ib"), [[-16, 8], [0, 16]], A.not_equal, 1.0, -j)
        more("B", 0.4 * s - 10.4)
        sent[:] = [(len(ops) - 1, False)]
        if j:
            ts(aj, vw("M2"), vw("m16", j, j + 1), A.min)
        for h in (0, 1):
            c = 128 * s + 64 * h
            n, d = vw("N", c, c + 64), vw("Dn", c, c + 64)
            if j:
                z = vw(("pC", "pD", "pE", "pF")[2 * h + (s % 2 if j > 4 else 0)], 0, 64)
                mm(z, row("on", n=j), row("cK", n=j), True, False)
                mm(z, aj, n, False, True)
                tt(vw("N", c + 128, c + 192), z, n, A.max)
                more("N", STEP * (s - 16) - 0.6 + 0.1 * h)
            aff(d, n, -131072.0, -131072.0 * j)
            more("Dn" if s > 8 else "Dv", STEP * (s - 17) - 0.4 + 0.1 * h)
            for b in (0,) if j > 4 else (0, 1):
                z, lo = vw((("pG", "pH"), ("pD", "pF"), ("pB", "pA"))[2 if s < 6 and s % 2 else b][h], 0, 64), 2 * c + 64 * b
                mm(z, vw("Ib"), d, True, False)
                mm(z, bj, vw("M", lo, lo + 64), False, True)
                if s > 6:
                    run(2)
                tt(vw("M", lo + 256, lo + 320), z, vw("M", lo, lo + 64), A.max)
                more("M", STEP * (s - 16) - 0.3 + 0.1 * h + 0.05 * b)
    an = vw("pC", 0, 128)
    aff(vw("wy32"), vw("wy0"), 1.0 / 32)
    mm(an, vw("Ib"), vw("wy32"), True, False)
    for h in (0, 1):
        for b in (0, 64):
            mm(vw("pC", 64 * h, 64 * h + 64), vw("Ib"), vw("M", 4096 + 128 * h + b, 4096 + 128 * h + b + 64), False, h + b == 65)
        run(2)
    qf, q2f = vw("qd", 3, None, 4), vw("sq", 3, None, 4)
    ts(vw("eR"), vw("dr0"), float(D), A.is_ge)
    aff(vw("qa"), vw("dr0"), 1.0, float(X0))
    aff(vw("qb"), vw("eR"), float(XS))
    tt(qf, vw("qa"), vw("qb"), A.subtract)
    aff(vw("q0"), qf)
    aff(vw("lim8"), vw("I32", 0, 128, 16), vw("limf"))
    mm(vw("pB", 400, 408), vw("on32"), vw("lim8"))
    aff(vw("limP"), vw("pB", 400, 408))
    QB, win, tp = ("pC", "pE"), vw("pB", 128, 256), vw("pD", 384, 448)

    def rows(t):
        for a, b in zip(CUT1, CUT1[1:]):
            xgath(t, "x", "q%d" % t, a, b)
            if t == 1 and a >= H:
                del ops[-1]["alts"]["v"]
        p = "pF" if t else "pB"
        mm(vw(p, 384, 392), vw("eR"), vw("bo8"))
        mm(vw(p, 392, 400), vw("eR"), vw("wm"))
        run(2)
        if t:
            mm(vw(p, 400, 408), vw("eN"), vw("bo8a"))
        aff(vw("n0"), vw(p, 384, 392), BIG, (-BIG if t else 0.0) - 16000.0)
        tt(vw("thr"), vw("limP"), vw("n0"), A.min)
        tt(vw("sn"), vw(p, 392, 400), vw("thr"), A.add)
        k = 16 if t else 4
        for m in range(16):
            mm(vw("pA", m, 128, 16), flat("x", 0, 128, m), vw("w3"), m == 0, m == 15)
            if m % k == k - 1:
                run(k, "keys")
        scan(vw("mr"), vw("d0r"), vw("pA", 0, 128), A.add, A.max)
        scan(vw("sm"), vw("d0s"), vw("pA", 0, 128), A.mult, A.add)
        ts(vw("nz"), last("mr"), 15, A.bitwise_and)

    def sums(t):
        mm(tp, row("on", n=2), row("mid", n=2), True, False)
        mm(tp, vw("eR"), vw("pk1"), False, False)
        mm(tp, vw("eR"), vw("pk2"), False, False)
        run(3)
        for m in range(16):
            mm(tp, flat("x", 0, 128, m), vw("pk"), False, m == 15 and not t)
            if m % 8 == 7:
                run(8, "sums%d" % m)

    def kept(t):
        q, v = "q%d" % t, "v%d" % t
        aff(vw("q16"), vw(q))
        zero(vw("eR"), vw(q))
        for o in ops[-2:] if t == 1 else ():
            del o["alts"]["v"]
        mm(vw("pG", 0, 128), vw("cm"), vw("eR"))
        relu(vw("eN"), vw("pG", 0, 128), -1.0 / 32)
        rows(t)
        tt(vw("ke"), vw("pF", 400, 408), last("mr"), A.add)
        aff(vw("k8"), vw("ke"), 1.0 / 16, -0.46875)
        aff(vw("kb"), ind(vw("k8"), vw("L8")), 1.0, -2040.0)
        tt(vw("th2"), vw("sn"), last("sm"), A.subtract)
        aff(vw("tb"), ind(vw("th2"), vw("L8")), 1.0 / 16, vw("cb"))
        mm(vw("pB", 0, 128), vw(v), vw("I32"))
        act(vw("pwB"), ind(vw("nz"), vw("L8")), LN2, 0.0, F.Exp)
        tt(vw("pr"), vw("pB", 0, 128), vw("pwB"), A.mult)
        ts(vw("bb"), vw("pr"), 32768, A.bitwise_and)
        aff(vw("gb"), vw("bb"))
        tt(vw("okK"), ind(vw("nz"), vw("L8")), vw("m15"), A.is_equal)
        for p in QB:
            mm(vw(p, 0, 256), row("on", n=2), row("ini", n=2), True, False)
        for l in (((2, "ImH", "eN"), (3, "IH", "eN")), ((1, "tb", "I4k"),), ((2, "kb", "Im4k"), (3, "kb", "I4k")), ((2, "gb", "Im1k"), (3, "gb", "Im1k"))):
            for h in (0, 1):
                for s, a, b in l:
                    mm(vw(QB[h], s, 256, 4), vw(a), vw(b, 64 * h, 64 * h + 64), False, False)
                run(len(l))
        mm(win, row("on", n=2), row("far", n=2), True, False)
        mm(win, vw("IH"), vw("eN"), False, False)
        mm(win, vw("kb"), vw("Im4k"), False, False)
        mm(win, vw("okK"), vw("I2H"), False, False)
        sums(t)

    def entered(t, q2):
        for h in (0, 1):
            a, b, nh = 64 * h, 64 * h + 64, vw("n%d" % t, 4 * h, 4 * h + 4)
            aff(vw("xe", a, b), ind(XG(t), nh), 1.0, 0.0, "s")
            more("xe%d" % h)
            tt(vw("nq", a, b), ind(vw("TQ"), nh), vw("eN", a, b), A.mult)
            more("nq%d" % h)
            tt(vw("qd", 4 * a + 3, 4 * b, 4), vw("q16", a, b), vw("nq", a, b), A.add)
            more("qd%d" % h)
            for s, c in ((1, "boU"), (2, "boT"), (3, "boU")):
                mm(vw(QB[h], s, 256, 4), vw(c), vw("xe", a, b), False, s == 3)
            run(3)
            scan(vw("sq", 4 * a, 4 * b), vw(QB[h], 0, 256), vw("qd", 4 * a, 4 * b), A.max, A.min)
            more("sq%d" % h)
            aff(vw(q2, a, b), vw("sq", 4 * a + 3, 4 * b, 4))
            more("qo%d" % h)
        mm(win, vw("boT"), vw("xe"), False, True)
        mm(tp, vw("xe"), vw("pk"), False, True)
        relu(vw("w"), win)

    def update(t):
        rm, y8 = vw("pF", 128, 256), vw("pB", 256, 264)
        mm(rm, vw("Ib"), qf, True, False)
        mm(rm, vw("Im"), q2f, False, True)
        tt(vw("yq"), rm, vw("w"), A.min if t else A.mult)
        for w in range(8):
            mm(vw("pG", 64 * w, 64 * w + 64), vw("Ib"), vw("tri"), w == 0, False)
        run(8, None if t else "tri")
        for h in (0, 64):
            for w in range(8):
                mm(vw("pG", 64 * w, 64 * w + 63, 1, h, h + 64), vw("sl", 64 * w, 64 * w + 64), vw("yq", h, h + 63), False, w == 7)
        run(16, "near")
        mm(y8, vw("yq"), vw("bo8"))
        aff(vw("ym"), y8, -4096.0)
        for w in range(8):
            act(vw("eq", 64 * w, 64 * w + 64), vw("pG", 64 * w, 64 * w + 64), 1.0, vw("ym", w, w + 1), F.Abs)
        scan(vw("ab"), vw("d0a"), vw("eq"), A.add, A.min)
        aff(vw("ya"), y8, -1.0, vw("dum"))
        tt(vw("du"), vw("ab", 63, 512, 64), vw("ya"), A.min)
        listed(vw("pH", 0, 8), "yq", "l0")
        tt(vw("AS"), ind(vw("du"), vw("L8")), vw("m16", 0, 128), A.mult)
        mm(vw("pB", 288, 296), vw("m16", 0, 128), vw("bo8d"), True, False)
        mm(vw("pB", 288, 296), vw("AS"), vw("bo8n"), False, True)
        aff(vw("ls"), vw("pB", 288, 296))
        if t < VI - 1:
            act(vw("sg"), y8, 1.0, 0.0, F.Sign, vw("cj"))
            aff(vw("cjb"), vw("cj"))
            mm(vw("pB", 280, 281), vw("on"), vw("cjb"))
            aff(vw("cI"), vw("pB", 280, 281))
            ts(vw("cA"), vw("cI"), 255, A.bitwise_and)
            aff(vw("cb"), vw("cA"), 1.0, -2048.0)
        ts(vw("tH"), tp, 1.5 * 2 ** 35, A.add, 1.5 * 2 ** 35, A.subtract)
        tt(vw("tU", 0, 128, 2), tp, vw("tH"), A.subtract)
        aff(vw("tU", 1, 128, 2), vw("tH"), 1.0 / 4096)
        more("tV")
        mm(vw("pE", 256, 384), vw("tU"), vw("Ib"), True, False)
        aff(vw("xb"), ind(vw(tab(t)), vw("l0")))
        more("xs")
        mm(vw("pE", 256, 384), vw("I16"), vw("xb"), False, True)
        aff(vw("xn"), vw("pE", 256, 384), 1.0 / 32, 63.75 - 0.484375)
        for h in (1, 0):
            aff(ind(vw(tab(t + 1)), vw("ls", 4 * h, 4 * h + 4)), vw("xn", 64 * h, 64 * h + 64), 1.0, 0.0, "v")
            more("up" + "LH"[h])

    def over(t, h):
        a, b = (X0, X0 + 560, XS)[h:h + 2]
        pick(vw(tab(t), a, b), vw(tab(t + 1), a, b), [[0, b - a]], A.is_ge, 0.0, 0)
        more("over%d" % h)
        ops[-1]["after"] += sent[-1:]
        sent.append((len(ops) - 1, False))

    for t in range(VI):
        v, end = "v%d" % t, t == VI - 1
        tag[1] = t
        q2 = "q2u" if end else "qo%d" % (t + 1)
        if t:
            tag[0] = "1" if t == 1 else ""
            kept(t)
            tag[0] = ""
            if end:
                aff(vw("a1"), vw(v), 1.0, 8388608.0)
                more("a2", t * TURN - 2.4)
                mm(vw("pH", 128, 256), row("low"), row("on"), True, False)
                mm(vw("pH", 128, 256), vw("I32"), vw("a1"), False, False)
                mm(vw("pH", 128, 256), vw("I32m"), vw(v), False, False)
                run(3)
            entered(t, q2)
        else:
            rows(0)
            tt(vw("dz"), last("sm"), vw("sn"), A.is_ge)
            act(vw("pw"), vw("nz"), LN2, 0.0, F.Exp)
            tt(vw("pz"), vw("pw"), vw("dz"), A.mult)
            aff(vw("pwB"), ind(vw("pz"), vw("L8")))
            mm(vw("pB", 0, 128), vw("pwB"), vw("Ib"))
            aff(vw("pwR"), vw("pB", 0, 128))
            ts(vw("w"), vw("pB", 0, 128), pwa, A.mult, 32768.0, A.is_equal)
            tt(vw("pr"), an, vw("pwR"), A.mult)
            aff(vw(v), an)
            ts(vw("bb"), vw("pr"), 32768, A.bitwise_and)
            mm(vw("pA", 0, 128), vw("Ib"), qf)
            tt(vw(q2), vw("pA", 0, 128), vw("bb"), A.subtract)
            aff(q2f, vw(q2))
            sums(0)
        tag[0] = "9" if end else ""
        if not end:
            send("q", t + 1)
        for a in () if t else range(0, XS, 444):
            iota(vw("TQ", a, a + 444), [[1, 444]], a)
            ops[-1]["after"] += sent[-1:]
        zero(vw("e2"), q2f)
        for a, b in zip(CUT2, CUT2[1:]):
            xgath(t, "x2", q2, a, b, 16.0, -2048.0)
        ku = vw("pC", 0, 128)
        mm(ku, vw("e2"), vw("bo256"), True, False)
        for m in range(16):
            mm(ku, flat("x2", 0, 128, m), vw("I16"), False, False)
        run(16)
        for a, b in zip(CUT2, CUT2[1:]):
            scan(flat("bs", a, b), flat("d0b", 0, b - a), flat("x2", a, b), A.add, A.max)
            more("bs_%d" % a)
        aff(vw("lo"), last("bs"), 0.0625, 1280 - 0.46875)
        mm(ku, last("bs"), vw("Ib"), False, False)
        mm(ku, vw("lo"), vw("Im16"), False, True)
        eQ = vw("eQ")
        mm(vw("pA", 128, 256), vw("cmb" if end else "cm"), vw("e2"))
        if end:
            ts(eQ, vw("pA", 128, 256), -17.0, A.is_le)
            mm(vw("pH", 128, 256), vw("Ib"), vw("e2"), False, True)
            aff(vw("qa"), vw("pH", 128, 256), -32.0, -32.0 * 131072)
        else:
            relu(eQ, vw("pA", 128, 256), -1.0 / 32)
            mm(vw("pA", 256, 384), vw("I4k"), q2f)
            tt(vw("t3"), vw("pA", 256, 384), vw(v), A.min)
            aff(vw("a1"), vw("t3"), 1.0, 8388608.0)
        update(t)
        scan(vw("mk"), vw("d0k"), ku, A.add, A.max)
        aff(vw("cP"), ku, -1.0 / 4096, 1222.5 - 1.0 / 8192)
        ts(vw("r8"), last("mk"), 15, A.bitwise_and)
        tt(vw("ok"), ind(vw("r8"), vw("L8")), vw("m15"), A.is_equal)
        okR, nv = vw("pA", 384, 512), vw("pC", 0, 128)
        mm(okR, vw("ok"), vw("Ib"))
        tt(vw("AL"), okR, q2f, A.mult)
        if not end:
            tt(vw("oka"), okR, vw("a1"), A.mult)
        aff(vw("okb"), okR, vw("a32"))
        listed(vw("pD", 0, 8), "AL", "lk")
        aff(vw("cd"), ind(vw("R"), vw("lk")), 1.0, float(X0))
        if not end:
            mm(nv, row("low"), row("on"), True, False)
            mm(nv, vw("bo32"), vw("oka"), False, False)
            mm(nv, vw("I17"), eQ, False, False)
            mm(nv, vw("Ipw"), eQ, False, False)
            mm(nv, vw("bo"), vw("okb"), False, True)
            tt(vw("vo%d" % (t + 1)), nv, vw("t3"), A.max)
            send("v", t + 1)
        bank = {2: "pF", 3: "pG", 0: "pE", 1: "pH"}
        for n in bank:
            mm(vw(bank[n]), vw("cP", 0, 128, 1, 32 * n, 32 * n + 32), vw("E", 0, 512, 1, 32 * n, 32 * n + 32), True, n % 2 == 0)
            more("far%d" % n)
            if n % 2 == 0:
                aff(flat("vf", 32 * n, 32 * n + 32), vw(bank[n]), 1.0, -1100.0, "s")
                more("vf%d" % n)
        aff(vw("cd16"), vw("cd"))
        aff(vw("chi"), vw("cd16"), 1.0 / 64, 192 - 0.4921875)
        for n in bank:
            a, b = 32 * n, 32 * n + 32
            if n % 2 == 0:
                tt(flat("mn", a, b), ind(XG(t), vw("cd", a, b)), flat("vf", a, b), A.subtract)
                more("mn_%d" % a)
                ts(flat("xc", a, b), flat("mn", a, b), 0.0, A.max)
            else:
                for c, d in ((a, b - SHARE), (b - SHARE, b)) if n == 1 else ((a, b),):
                    xgath(t, "mn", "cd", c, d, -1.0)
                mm(vw(bank[n]), vw("Ib"), flat("mn", a, b), False, True)
                more("near%d" % n)
                act(flat("xc", a, b), vw(bank[n]), 0.5, -550.0, F.Abs)
            more("xc%d" % n)
        mm(vw("pD", 256, 384), vw("cd16"), vw("Ib"), True, False)
        mm(vw("pD", 128, 256), vw("chi"), vw("Ib"), False, False)
        mm(vw("pD", 256, 384), vw("chi"), vw("Im64"), False, False)
        run(2)
        for n in (2, 0):
            for j in range(16):
                mm(vw("pD", 128 + j, 384, 16, 32 * n, 32 * n + 32), flat("mn", 32 * n, 32 * n + 32, j), vw("wd"), False, False)
            run(16, "lin%d" % n)
        for j in range(16):
            mm(vw("pD", 128 + j, 384, 16), flat("xc", 0, 128, j), vw("wa"), False, j == 15)
        run(16, "score")
        if not end:
            over(t, 0)
        scan(vw("ms"), vw("d0m"), vw("pD", 128, 384), A.add, A.max)
        ts(vw("n16"), last("ms"), 63, A.bitwise_and)
        if not end:
            tt(vw("AN"), ind(vw("n16"), vw("L16")), vw("m16"), A.mult)
            for a in (0, 128):
                mm(vw("pH", 0, 8), vw("AN", a, a + 128), vw("bo8" if a else "bo64"), a == 0, a == 128)
            run(2)
            aff(vw("no%d" % (t + 1), 4, 12), vw("pH", 0, 8), 1.0, 0.0, "vs" if t else "v")
            send("n", t + 1, 1)
            send("n", t + 1, 0)
            over(t, 1)
        else:
            mm(nv, vw("bo"), vw("okb"), True, False)
            mm(nv, vw("I64"), eQ, False, True)
            act(vw("t3"), nv, 32.0, -2048.0, F.Relu)
            tt(vw("yw"), vw("qa"), vw("t3"), A.max)
            store(T.yq[:, :], vw("yw"), "st1", "y", 0.3)
            store(T.yx[:, :], vw("X", X0, XS), "st0", "y", 1.6)
            old, new = vw("pA", 0, 128), vw("pF", 0, 128)
            mm(old, vw("ImQ"), eQ, True, False)
            mm(old, vw("IpQ"), vw("e2"), False, False)
            mm(old, vw("Ib"), q2f, False, True)
            run(3)
            aff(vw("qb"), old, 1.0, -float(X0))
            mm(new, row("on", n=2), row("less", n=2), True, False)
            mm(new, vw("I4k"), eQ, False, False)
            for a, x, w in ((0, "s", "I64"), (8, "v", "Ib")):
                aff(vw("AN", 16 * a, 16 * a + 128), ind(vw("n16", a, a + 8), vw("L8")), 1.0, 0.0, x)
                more("AN%d" % a)
                mm(new, vw("AN", 16 * a, 16 * a + 128), vw(w), False, a == 8)
            tt(vw("yt"), new, vw("qb"), A.max)
            store(T.yp[:, :], vw("yt"), "st2", "s", 0.3)

    if "plan" not in PLAN:
        PLAN["pre"] = links(ops)
        PLAN["plan"] = order(ops, PLAN["pre"])
    pre, (place, start, seq) = PLAN["pre"], PLAN["plan"]
    cnt, tok, snap, known = {}, {}, {}, {q: {} for q in Q}
    for i in seq:
        o, q = ops[i], place[i]
        s = o["sem"] or ES[q]
        cnt[s] = cnt.get(s, 0) + o["inc"]
        tok[i] = (s, cnt[s])
        if q == "-":
            snap[i] = {}
            continue
        best = {}
        for j, hard in pre[i].items():
            if (hard or place[j] != q) and tok[j][0] != "loc" and tok[j][1] > best.get(tok[j][0], (0, 0))[0]:
                best[tok[j][0]] = (tok[j][1], j)
        for k, (c, j) in sorted(best.items(), key=lambda e: -start[e[1][1]]):
            if known[q].get(k, 0) < c:
                Q[q].wait_ge(T.sem[k], c)
                known[q][k] = c
                for k2, c2 in snap[j].items():
                    known[q][k2] = max(known[q].get(k2, 0), c2)
        r = o["alts"][q][0]()
        if s != "loc":
            r.then_inc(T.sem[s], o["inc"])
        snap[i] = dict(known[q])
    for s in SEMAPHORES:
        if cnt.get(s):
            g.wait_ge(T.sem[s], cnt[s])
